import numpy as np, ml_dtypes
CORES = [9,25,41,57]
N = 4
BF = ml_dtypes.bfloat16
W, NS, TS = 4096, 256, 6
B = W // NS
def parts(rng):
    size = rng.choice(np.array([256, 256, 256, 64, 16]), (N, 8, 1, W))
    x = (rng.random((N, 8, 16, W)) * size).astype(np.int64)
    v = rng.integers(0, W, (N, 8, 16, W)); s = rng.integers(0, W, (N, 8, 16, NS)); z = rng.integers(0, 256, (N, 8, 16, NS)); w = rng.integers(0, 256, (N, 8, 16))
    h = np.where(rng.random((N, 8, 16)) < 0.75, rng.integers(0, 600, (N, 8, 16)), rng.integers(600, 1600, (N, 8, 16)))
    return x, v, s, z, w, h, rng.integers(0, 2, (N, 8, NS))
def pack(x, v, s, z, w, h, a):
    return {"reg": np.ascontiguousarray(x.reshape(N, 128, W)).astype(np.float32).astype(BF), "vw": np.ascontiguousarray((v[..., :W // 2] + W * v[..., W // 2:]).reshape(N, 128, W // 2)).astype(np.int32),
            "scan": np.ascontiguousarray(s.reshape(N, 128, NS)).astype(np.int32), "z0": np.ascontiguousarray(z.reshape(N, 128, NS)).astype(np.float32).astype(BF),
            "wt": np.ascontiguousarray(w.reshape(N, 128, 1)).astype(np.int32), "th": np.ascontiguousarray(h.reshape(N, 128, 1)).astype(np.int32), "warm": np.ascontiguousarray(a).astype(np.int32)}
def setup_inputs(rng):
    return pack(*parts(rng))
def setup_inputs_corners(rng):
    x, v, s, z, w, h, a = parts(rng); i = np.arange(NS)[None, :]; k = np.arange(16)[:, None]; d = np.arange(W)[None, :]
    for q in range(N):
        for g in range(8):
            c = (g + 3 * q) % 8
            x[q, g][:, ::7] = 0; x[q, g][:, 3::7] = 255; x[q, g][:, W - 1] = 255
            if (q + g) % 3 == 0: a[q, g] = 0
            if (q + g) % 3 == 1: a[q, g] = 1
            if c == 0: s[q, g] = 0; w[q, g] = 255
            if c == 1: s[q, g] = W - 1; h[q, g] = 4079
            if c == 2: s[q, g] = B * i + k % B; h[q, g] = 0
            if c == 3: s[q, g] = B * rng.integers(0, NS, (16, NS)); w[q, g] = 0; h[q, g] = 0; a[q, g] = rng.integers(0, 2, NS)
            if c == 4: s[q, g] = (16 * i + k + 1) % W; v[q, g] = np.where(k >= 0, (d + 1) % W, 0)
            if c == 5: v[q, g] = np.where(k >= 0, d, 0); w[q, g] = 255 * rng.integers(0, 2, 16)
            if c == 6: v[q, g] = (W - 1) * rng.integers(0, 2, (1, W)); h[q, g] = 4079 * rng.integers(0, 2, 16)
            if c == 7: s[q, g] = B * rng.integers(0, NS, (16, NS)) + B - 1; a[q, g] = rng.integers(0, 2, NS); h[q, g] = 0
            if c % 3 == 0: z[q, g] = 0
            if c % 3 == 1: z[q, g] = 255
    return pack(x, v, s, z, w, h, a)
def setup_inputs_crowd(rng):
    x, v, s, z, w, h, a = parts(rng); h = rng.integers(0, 1000, (N, 8, 16))
    for q in range(N):
        for g in range(8):
            pl = rng.permutation(W)[:4]; x[q, g][:, pl[:3]] = rng.integers(200, 256, (16, 3)); x[q, g][:, pl[3]] = 0
            s[q, g] = rng.choice(pl[:1 + 2 * (g % 2)], (16, NS)); a[q, g] = 1
            if g % 4 == 1: w[q, g] = 0
            if g % 4 == 2: w[q, g] = 255
            o = int(rng.integers(0, NS)) if g < 7 else NS - 1
            if q % 4 == 3:
                a[q, g] = 0
                if g == 7: a[q, g, o] = 1
            elif (q % 4 == 1 and g == 7) or (q % 4 == 2 and g % 2 == 1):
                way = (g // 2 + q) % 3
                if way == 0: a[q, g, o] = 0
                else: s[q, g, :, o] = pl[3]
                if way == 2: s[q, g, int(rng.integers(0, 16)), o] = pl[0]
    return pack(x, v, s, z, w, h, a)
def setup_inputs_ends(rng):
    x = np.where(rng.random((N, 8, 1, W)) < 0.5, 255 * rng.integers(0, 2, (N, 8, 1, W)), 255 * rng.integers(0, 2, (N, 8, 16, W)))
    x[..., 0] = 0; x[..., W - 1] = 255; x[:, 1, :, 0] = 255; x[:, 1, :, W - 1] = 0
    e = (W - 1) * rng.integers(0, 2, (N, 8, 16, W // 2)); c = rng.random(e.shape) < 0.7
    v = np.concatenate([np.where(c, e, rng.integers(0, W, e.shape)), np.where(c, e, rng.integers(0, W, e.shape))], axis=3)
    s = np.where(rng.random((N, 8, 16, NS)) < 0.72, (W - 1) * rng.integers(0, 2, (N, 8, 16, NS)), rng.integers(0, W, (N, 8, 16, NS)))
    z = np.where(rng.random((N, 8, 1, NS)) < 0.5, 255 * rng.integers(0, 2, (N, 8, 1, NS)), 255 * rng.integers(0, 2, (N, 8, 16, NS)))
    w = 255 * rng.integers(0, 2, (N, 8, 16)); w[:, 2] = 255; w[:, 6] = 255
    w[:, 3] = 0; w[:, 3, 15] = 255; w[:, 3, 0] = 2; w[:, 7] = w[:, 3]; w[0, 7] = 255
    h = 4079 * rng.integers(0, 2, (N, 8, 16)); h[..., 0] = 4079; h[..., 8] = 0; h[..., 15] = 0
    a = (rng.random((N, 8, NS)) < 0.6).astype(np.int64); i = np.arange(NS); last = i[i % 8 == 7]; one = i[i % 8 == 6]; two = i[i % 8 == 1]; three = i[i % 8 == 5]; late = 5 * B - 1
    for q in range(N):
        b = (N - 1 - q) % 2 == 0
        v[q, :, :, W - 1] = W - 1 if b else 0; v[q, :, :, W // 2 - 1] = W - 1 if b else 0
        s[q][:, :, last] = W - 1; z[q][:, :, last] = 0 if b else 255; a[q][:, last] = 1
        if b:
            both = np.concatenate([one, two]); s[q][:, :, both] = 0; z[q][:, :, both] = 255; a[q][:, both] = 1
            s[q][:, 15, one] = W - 1; s[q][:, 8, two] = W - 1
            for g in (3, 7):
                x[q, g][:, late] = 0; s[q, g][:, 4] = W - 1; z[q, g][:, 4] = 0; a[q, g, 4] = 1
                s[q, g][:, three] = 0; s[q, g][15, three] = W - 1; s[q, g][8, three] = late; z[q, g][:, three] = 0; a[q, g, three] = 1
    s[0, :, 3] = W - 1; s[0, :, 15] = W - 1; s[0, 1, 3] = 0; s[0, 1, 15] = 0; a[0] = 1; a[0, 0, 0] = 0
    return pack(x, v, s, z, w, h, a)
def setup_inputs_spread(rng):
    x, v, s, z, w, h, a = parts(rng)
    x = (np.exp2(8 * rng.random((N, 8, 1, W))) * rng.random((N, 8, 16, W))).astype(np.int64)
    z = (np.exp2(8 * rng.random((N, 8, 1, NS))) * rng.random((N, 8, 16, NS))).astype(np.int64)
    w = np.minimum(np.exp2(8 * rng.random((N, 8, 16))).astype(np.int64), 255); h = np.minimum(np.exp2(12 * rng.random((N, 8, 16))).astype(np.int64) - 1, 4079)
    p = rng.choice(np.array([0.5, 1.0, 2.0, 3.0]), (N, 8, 1, 1))
    s = np.minimum((W * rng.random((N, 8, 16, NS)) ** p).astype(np.int64), W - 1); v = np.minimum((W * rng.random((N, 8, 16, W)) ** p).astype(np.int64), W - 1)
    a = (rng.random((N, 8, NS)) < rng.choice(np.array([0.1, 0.5, 0.9]), (N, 8, 1))).astype(np.int64)
    return pack(x, v, s, z, w, h, a)
def setup_inputs_ties(rng):
    x, v, s, z, w, h, a = parts(rng); lane = np.arange(16)[:, None]
    for q in range(N):
        for g in range(8):
            if g % 2 == 0:
                c = (0, 16, 1000, 4079)[(g // 2 + q) % 4]
                m = np.minimum(np.maximum(c + rng.integers(-1, 2, W), 0), 4080)
                x[q, g] = m // 16 + ((lane + rng.integers(0, 16, W)) % 16 < m % 16); h[q, g] = c
                z[q, g] = z[q, g] * rng.integers(0, 2, (1, NS)); a[q, g] = rng.random(NS) < 0.8
            else:
                x[q, g] = rng.integers(0, 16, (16, W)); x[q, g][:, W // 2:] = x[q, g][:, :W // 2]
                s[q, g, 1::2] = (s[q, g, 0::2] + W // 2) % W; h[q, g] = rng.integers(10, 70, 16); z[q, g] = rng.integers(0, 16, (16, NS))
                x[q, g][:, 5] = 255; x[q, g, (g + q) % 16, 5] = 254; x[q, g][:, W - 1] = 255
                s[q, g][:, NS - 2:] = 5; s[q, g, 15, NS - 2:] = W - 1; z[q, g][:, NS - 2:] = 0; a[q, g, NS - 2:] = 1
                if g % 4 == 3:
                    x[q, g][:, W - 3] = 0; x[q, g][:, W // 2 - 3] = 0; w[q, g, 0] = 1; w[q, g, 1] = 16
                    s[q, g][:, 4:6] = W - 3; z[q, g][:, 4:6] = 0; z[q, g, 0, 4:6] = 11; z[q, g, 1, 4:6] = W // 16 - 2; a[q, g, 4:6] = 1
    return pack(x, v, s, z, w, h, a)
def check_inputs(d):
    bad = []
    for k, lo, hi in (("reg", 0, 255), ("vw", 0, W * W - 1), ("scan", 0, W - 1), ("z0", 0, 255), ("wt", 0, 255), ("th", 0, 4079), ("warm", 0, 1)):
        a = np.asarray(d[k]).astype(np.float64)
        if not (np.min(a) >= lo and np.max(a) <= hi): bad.append("range of " + k)
        elif np.any(a != np.floor(a)): bad.append("whole numbers in " + k)
    return bad
def pick(x, ix):
    return np.take_along_axis(x, ix.reshape(N, 8, 1, 16 * NS), 3).reshape(N, 8, 16, 16, NS)
def reference(reg, vw, scan, z0, wt, th, warm):
    X = reg.astype(np.float32).astype(np.int32).reshape(N, 8, 16, W); pk = vw.astype(np.int64).reshape(N, 8, 16, W // 2)
    V = np.concatenate([pk % W, pk // W], axis=3)
    S = scan.astype(np.int64).reshape(N, 8, 16, NS); z = z0.astype(np.float32).astype(np.int32).reshape(N, 8, 16, NS)
    wl = wt.astype(np.int64).reshape(N, 8, 16, 1); theta = th.astype(np.int64).reshape(N, 8, 16, 1); new = warm == 0
    last = np.zeros((N, 8, 16, 16, NS), np.int32); m = np.zeros((N, 8, 16, NS), np.int64); A = np.zeros((N, 1, 1, 1), np.int64)
    row37 = 37 * np.arange(16).reshape(1, 1, 16, 1); sc = np.arange(NS)
    for t in range(TS):
        C = pick(X, S)
        moved = (np.add.reduce(np.abs(C - last), axis=2) > theta + A % 32) & ~new[:, :, None, :]
        m = m + moved; some = np.any(moved, axis=2)
        clean = ~new & ~some; borrow = some & (np.add.reduce(m, axis=2) >= 2); has = clean | borrow
        key = 4096 * m + np.add.reduce(np.abs(C - z[:, :, :, None, :]), axis=2)
        donor = np.argmax(key, axis=2)
        dr = np.take_along_axis(S, donor[:, :, None, :], 2)
        F = np.where(borrow[:, :, None, :], np.take_along_axis(V, dr, 3), S)
        D = pick(X, F); y = (np.max(D, axis=3) + np.min(D, axis=3)) >> 1
        z = np.where(has[:, :, None, :], np.abs(y - z), z)
        u = np.add.reduce(wl * z, axis=2, keepdims=True) % W
        place = B * sc + u[:, :, 0, :] % B
        X = X.copy(); V = V.copy()
        for r in range(N):
            for odd in range(2):
                q = (r + odd * (1 + t % 3)) % N
                gi, si = np.nonzero(has[r] & (sc % 2 == odd)); pl = place[r][gi, si]
                X[q][gi, :, pl] = y[r][gi, :, si]
                if t < TS - 1: V[q][gi, :, pl] = F[r][gi, :, si]
        S = np.where(has[:, :, None, :], (((F * u) >> 5) + F + row37 + A) % W, S)
        m = np.where(has[:, :, None, :], 0, m); new = has; last = C
        A = np.add.reduce(borrow.astype(np.int64).reshape(N, 8 * NS), axis=1).reshape(N, 1, 1, 1)
    return {"yx": X.reshape(N, 128, W).astype(np.float32).astype(BF), "ys": S.reshape(N, 128, NS).astype(np.float32), "yz": z.reshape(N, 128, NS).astype(np.float32).astype(BF)}

@@ -1,0 +1,771 @@
+import math
+from concourse.bass import DstId, RemoteDMATransfer
+from concourse.mybir import AluOpType, AxisListType, ActivationFunctionType
+
+OP = AluOpType
+AF = ActivationFunctionType
+W, NS, TS, NR = 4096, 256, 6, 4
+WD = W + NS
+SO = WD
+SN = SO + NS
+MAGIC = 12582912.0
+
+B, F, I, U = "bfloat16", "float32", "int32", "uint16"
+SB = {
+    "X": (WD, B), "T2": (WD, B), "VS": (SN + NS, I), "VW": (2048, I),
+    "M": (W, B), "G2": (W, B), "D": (W, B), "MX": (W, B), "MN": (W, B), "ZX0": (W, B), "ZX1": (W, B),
+    "ZA0": (512, B), "ZA1": (512, B), "ZR": (256, B), "SR": (256, I), "S16": (256, U), "SF": (256, F),
+    "WI": (8, I), "TI": (8, I), "WM": (256, I), "WMF": (256, F), "CF": (32, F), "PI": (16, I),
+    "JF": (128, F), "RF": (128, F), "GF": (128, F), "IF": (128, F), "IB": (128, B), "IH": (128, B),
+    "IN": (128, B), "IG": (128, B), "BD": (128, B), "AP": (128, B), "MR": (128, F), "WBD": (128, B),
+    "ONF": (128, F), "ONB": (128, B), "M2B": (128, B), "CQ": (128, B), "RKW": (128 * 6, B), "TMP": (128, F), "CMP": (128, B),
+    "DC": (8, F), "W1": (16, B), "W2": (96, B), "WG": (16, B), "EQT": (8, F), "BT": (8, F), "I8": (32, F),
+    "BI0": (256, F), "BI": (256, B), "NQ": (256, F), "QD": (16, F), "QP": (32, F), "RH": (32, F), "Q16": (16, F),
+    "MK0": (1024, B), "MKB": (1024, B), "MKN": (128, B), "OLD": (256, B), "AB": (256, F), "LS": (16, U),
+    "MV": (256, B), "KEY": (256, F), "RR": (256, F), "EQ": (256, F), "ZZ": (256, F), "SC": (256, F), "CN": (256, F),
+    "BO": (16, B), "HS0": (16, F), "HS1": (16, F), "THR": (16, F), "TH2": (16, F), "DB": (16, F), "E1": (256, F), "E2": (256, B), "DCB": (16, B),
+    "MH": (256, F), "HX": (256, B), "DL": (16, U), "UI": (16, I), "UA": (16, I),
+    "FB": (256 * TS, U), "YB": (256 * TS, B), "LB": (32 * TS, U),
+    "RY": (128 * TS, B), "RFF": (128 * TS, U), "RL": (8 * TS, U),
+    "DD": (256, B), "AD": (256, B), "SG": (256, B), "TN": (256, B),
+    "UR": (256, I), "PR": (256, I), "PR2": (256, I), "AI": (8, I), "OS": (256, F), "OZ": (256, B),
+}
+PS = ["PK0", "PK1", "PSU", "PA0", "PA1", "PD0", "PD1", "PF"]
+SCRATCH = {k: ("sbuf", [128, v[0]], v[1]) for k, v in SB.items()}
+SCRATCH.update({k: ("psum", [128, 512], F) for k in PS})
+NDMA = 24
+SEMAPHORES = (["qV", "qA", "qP", "qG", "sent"] + ["d%d" % k for k in range(NDMA)]
+              + ["ra%d" % t for t in range(TS)] + ["rb%d" % t for t in range(TS)])
+
+PAR = {"cyc": 0.00083 * 1.15, "pe": 0.00042 * 1.3, "gat": 1.55, "sca": 3.5, "hop": 0.16, "pass": 4, "pool": 1.3,
+       "mch": 512, "gch": 1024, "dch": 1024, "zact": 0, "rem": 3.0, "alt": (0, 768), "c0v": (0, 1, 4), "r0v": (), "soft": "", "seed": 2, "tries": 10000, "ach": 256, "zi": (7, 3), "abr": (0, 1), "gv": 0, "dda": (1, 0),
+       "cuts": ([0, 1024, 2048], [0, 1024, 2048]),
+       "order": {"g0": 10, "m0": 12, "a0": 14, "g1": 16, "m1": 18, "d0": 20, "a1": 22, "d1": 24, "s0": 30, "y0": 32,
+                 "s1": 26, "y1": 28, "u0": 40, "u1": 36, "x0": 34, "x1": 35, "out": 50}}
+LATE = 10000
+PER = {"FB": 256, "YB": 256, "LB": 32, "RY": 128, "RFF": 128, "RL": 8}
+KEPT = {}
+
+
+def vw(name, lo=0, hi=None, step=1, p1=128):
+    if hi is None:
+        hi = SB[name][0] if name in SB else 512
+    return (name, lo, hi, step, p1)
+
+
+def ind(win, off):
+    return ("@", win, off)
+
+
+def width(v):
+    if v[0] == "@":
+        return 16 * width(v[2])
+    return (v[2] - v[1] + v[3] - 1) // v[3]
+
+
+def two(v):
+    n = v[1][0] if v[0] == "@" else v[0]
+    return n in SB and SB[n][1] in (B, U)
+
+
+def clash(a, b):
+    if a[2] <= b[1] or b[2] <= a[1]:
+        return False
+    if a[3] > 1 and a[3] == b[3] and (a[1] - b[1]) % a[3] != 0:
+        return False
+    return True
+
+
+def build(rank, cores, topo):
+    ops = []
+    rank_now = [LATE]
+    step, nth = [-1], {}
+
+    def at(t, name):
+        rank_now[0] = 100 * t + PAR["order"][name] if name else LATE
+
+    def add(eng, cost, rd, wr, call, **kw):
+        r, w = [], []
+        for v in rd:
+            if isinstance(v, tuple):
+                r += [v[1], v[2]] if v[0] == "@" else [v]
+        for v in wr:
+            if v[0] == "@":
+                w.append(v[1])
+                r.append(v[2])
+            else:
+                w.append(v)
+        o = {"eng": eng, "cost": cost, "r": r, "w": w, "call": call, "pr": rank_now[0]}
+        o.update(kw)
+        x = w[0] if w else (r[0] if r else ("", 0))
+        name = x[0][:2] if x[0][:2] in ("ZA", "ZX", "HS") else x[0]
+        key = ["i", "a", "", "", "", "", "z"][step[0] + 1] + eng + name + str(x[1] % PER.get(name, 8192))
+        nth[key] = nth.get(key, 0) + 1
+        o["key"], o["step"] = key + "_" * (nth[key] - 1), max(step[0], 0)
+        ops.append(o)
+
+    cyc = PAR["cyc"]
+
+    def vcost(out, ins, per):
+        n = width(out)
+        if out[0] == "@":
+            return 0.05 + n * PAR["sca"] * cyc
+        if ins[0][0] == "@":
+            return 0.05 + n * PAR["gat"] * cyc
+        return max(64, n * per) * cyc
+
+    def half(*vs):
+        return 0.5 if all(two(v) for v in vs) else 1
+
+    def cp(out, a):
+        add("V", vcost(out, [a], half(out, a)) if width(out) >= width(a) else 64 * cyc, [a], [out], ("tensor_copy", out, a))
+
+    def tt(out, a, b, op):
+        per = 1 if (a[0] in PS or b[0] in PS) else 2
+        add("V", vcost(out, [a], per), [a, b], [out], ("tensor_tensor", out, a, b, op))
+
+    def ts(out, a, s1, op0, s2=None, op1=None):
+        c = ("tensor_scalar", out, a, s1, s2, op0) + ((op1,) if op1 is not None else ())
+        add("V", vcost(out, [a], half(out, a)), [a, s1, s2], [out], c)
+
+    def scan(out, d0, d1, op0, op1):
+        add("V", vcost(out, [d0], half(out, d0, d1)), [d0, d1], [out], ("tensor_tensor_scan", out, d0, d1, 0.0, op0, op1))
+
+    def mset(out, val):
+        add("V", vcost(out, [out], half(out)), [], [out], ("memset", out, val))
+
+    def act(out, a, func, bias=0.0, scale=1.0):
+        n = width(out)
+        c = 0.065 + n * PAR["gat"] * cyc if a[0] == "@" else max(64, n) * cyc + 0.03
+        add("A", c, [a, bias, scale], [out], ("activation", out, a, func, bias, scale))
+
+    def mm(terms, start=True, stop=True):
+        c = sum(max(64, width(t[2])) * (1 if two(t[2]) else 4) * PAR["pe"] for t in terms)
+        add("P", c, [x for t in terms for x in t[1:]], [t[0] for t in terms], ("mm", terms, start, stop), goon=not start)
+
+    def iota(out, pat, base, cm):
+        add("G", (0.13 + 2 * width(out) * 0.00083) * PAR["pool"], [], [out], ("iota", out, pat, base, cm))
+
+    def asel(out, a, pat, op, base, cm):
+        add("G", (0.17 + 2 * width(out) * 0.00083) * PAR["pool"], [a], [out], ("affine_select", out, a, pat, op, 0.0, base, cm))
+
+    nd = [0]
+
+    def dma(q, out, a, lat):
+        rd = [a] if a[0] != "$" else []
+        wr = [out] if out[0] != "$" else []
+        add(q, 0.1, rd, wr, ("dma", out, a), sem="d%d" % nd[0], lat=lat)
+        nd[0] += 1
+
+    def col(name, j):
+        return vw(name, j, j + 1)
+
+    dma("S", vw("SR"), ("$", "scan", 0, 256), 2.0)
+    dma("S", vw("ZR"), ("$", "z0", 0, 256), 2.0)
+    for j in range(4):
+        dma("S", vw("X", 1024 * j, 1024 * j + 1024), ("$", "reg", 1024 * j, 1024 * j + 1024), 2.6 + 0.9 * j)
+    dma("A", col("TI", 0), ("$", "th", 0, 1), 2.0)
+    dma("A", vw("WM", p1=8), ("$", "warm", 0, 256), 2.0)
+    dma("A", col("WI", 0), ("$", "wt", 0, 1), 2.0)
+    for j in range(2):
+        dma("S", vw("VW", 1024 * j, 1024 * j + 1024), ("$", "vw", 1024 * j, 1024 * j + 1024), 7.0 + 1.8 * j)
+
+    iota(vw("PI", 0, 1), [[0, 1]], 0, 1)
+    iota(vw("GF"), [[1, 8], [0, 16]], 0, 0)
+    iota(vw("RF"), [[0, 8], [1, 16]], 0, 0)
+    iota(vw("JF"), [[1, 128]], 0, 0)
+    ts(vw("PI", 1, 2), vw("PI", 0, 1), 15, OP.bitwise_and)
+    ts(vw("PI", 2, 3), vw("PI", 0, 1), 4, OP.arith_shift_right)
+    ts(vw("PI", 3, 4), vw("PI", 0, 1), 1, OP.arith_shift_right, 7, OP.bitwise_and)
+    cp(vw("CF", 0, 4), vw("PI", 0, 4))
+    ts(col("CF", 4), col("CF", 1), 8.0, OP.is_lt)
+    ts(vw("BD"), vw("GF"), col("CF", 2), OP.is_equal)
+    ts(vw("CMP"), vw("RF"), col("CF", 3), OP.is_equal)
+    tt(vw("AP"), vw("CMP"), vw("BD"), OP.mult)
+    ts(col("CF", 13), col("CF", 4), -255.0, OP.mult)
+    ts(col("CF", 14), col("CF", 4), -16.0, OP.mult)
+    ts(vw("EQT"), vw("JF", 8, 16), col("CF", 1), OP.is_equal)
+    ts(vw("BT"), vw("EQT"), 16.0, OP.mult, col("CF", 13), OP.add)
+    ts(vw("DC"), vw("GF", 0, 128, 16), col("CF", 2), OP.is_equal)
+    ts(vw("IF"), vw("JF"), col("CF", 0), OP.is_equal)
+    act(vw("IB"), vw("IF"), AF.Identity)
+    act(vw("IH"), vw("IF"), AF.Identity, scale=0.5)
+    act(vw("IN"), vw("IF"), AF.Identity, scale=-1.0)
+    act(vw("IG"), vw("IF"), AF.Identity, scale=-8192.0)
+    ts(vw("MR"), vw("RF"), col("CF", 1), OP.is_equal)
+    mset(vw("ONF"), 1.0)
+    mset(vw("ONB"), 1.0)
+    mset(vw("M2B"), -2.0)
+    mset(vw("CQ"), -0.25)
+    for name in ("VS", "X", "T2"):
+        iota(vw(name, W, WD), [[0, NS]], 0, 0)
+    iota(vw("MK0"), [[0, 1024]], 1, 0)
+    asel(vw("MK0"), vw("MK0"), [[0, 64], [1, 16]], OP.is_gt, 0, 0)
+    iota(vw("MKB"), [[0, 1024]], 256, 0)
+    asel(vw("MKB"), vw("MKB"), [[0, 64], [1, 16]], OP.is_equal, 0, 0)
+    mset(vw("MKN"), 0.0)
+    mset(vw("MKN", 0, 128, 16), -1048576.0)
+    ts(vw("I8", 0, 8), vw("JF", 0, 8), 1.0, OP.mult)
+    ts(vw("I8", 8, 16), vw("JF", 0, 8), 16.0, OP.mult, 15.0, OP.add)
+    cp(vw("LS"), vw("I8", 0, 16))
+    LC, L15 = vw("LS", 0, 8), vw("LS", 8, 16)
+    act(vw("W1", 0, 8), vw("DC"), AF.Identity, scale=32.0)
+    act(vw("DCB", 0, 8), vw("DC"), AF.Identity)
+    for t in range(TS):
+        act(vw("W2", 16 * t, 16 * t + 8), vw("DC"), AF.Identity, scale=col("CF", 14) if t else -16.0)
+        act(vw("W2", 16 * t + 8, 16 * t + 16), vw("DC"), AF.Identity, scale=col("EQT", t) if t else 1.0)
+    for t in range(1, TS):
+        asel(vw("RKW", 128 * t, 128 * t + 128), vw("BD"), [[0, 8], [1, 16]], OP.is_equal, -(8 + t), 0)
+    cp(col("CF", 5), col("TI", 0))
+    cp(col("CF", 6), col("WI", 0))
+    ts(col("CF", 7), col("CF", 5), -1.0, OP.mult, -0.5, OP.add)
+    ts(col("CF", 8), col("CF", 1), 37.0, OP.mult)
+    ts(col("CF", 10), col("CF", 1), 37.0, OP.mult)
+    act(vw("WG", 0, 8), vw("DC"), AF.Identity, scale=col("CF", 6))
+    act(vw("WBD"), vw("BD"), AF.Identity, scale=col("CF", 6))
+    ts(vw("Q16"), vw("JF", 0, 16), 16.0, OP.mult, col("CF", 1), OP.add)
+    act(vw("QD"), vw("Q16"), AF.Identity, bias=float(SO))
+    for h in range(2):
+        ts(col("CF", 15 + h), col("CF", 0), 31.0, OP.mult, float(16 * (1 - h) - W - 128 * h), OP.add)
+        ts(col("CF", 17 + h), col("CF", 0), -1.0, OP.mult, float(-SO - 128 * h), OP.add)
+        act(vw("QP", 16 * h, 16 * h + 8), vw("Q16", 8 * h, 8 * h + 8), AF.Identity, bias=float(W))
+        act(vw("QP", 16 * h + 8, 16 * h + 16), vw("Q16", 8 * h, 8 * h + 8), AF.Identity)
+        act(vw("RH", 16 * h, 16 * h + 8), vw("DC"), AF.Identity, scale=col("CF", 15 + h))
+        act(vw("RH", 16 * h + 8, 16 * h + 16), vw("DC"), AF.Identity, scale=256.0)
+        act(vw("NQ", 128 * h, 128 * h + 128), vw("ONF"), AF.Identity, scale=col("CF", 17 + h))
+    act(vw("TMP"), vw("IF"), AF.Identity, scale=col("CF", 5))
+    mm([(vw("PF", 0, 128), vw("ONF"), vw("TMP"))])
+    ts(vw("BI0", 128, 256), vw("PF", 0, 128), -1.0, OP.mult, -1.0, OP.add)
+    act(vw("BI0", 0, 128), vw("RF"), AF.Identity, bias=15.0, scale=-1.0)
+    act(vw("BI", 0, 128), vw("RF"), AF.Identity, bias=15.0, scale=-1.0)
+    ts(vw("CMP"), vw("PF", 0, 128), col("CF", 5), OP.is_ge)
+    tt(vw("CMP"), vw("CMP"), vw("BD"), OP.mult)
+    mm([(vw("PF", 128, 256), vw("M2B"), vw("CMP"))])
+    act(vw("BI", 128, 256), vw("PF", 128, 256), AF.Identity)
+
+    for h in range(2):
+        src = vw("SR", 1 - h, 256, 2)
+        cp(vw("S16", 128 * h, 128 * h + 128), src)
+        cp(vw("SF", 128 * h, 128 * h + 128), src)
+        cp(vw("VS", SO + 128 * h, SO + 128 * h + 128), src)
+        cp(vw("ZA0", 128 * h, 128 * h + 128), vw("ZR", 1 - h, 256, 2))
+    for k in range(16):
+        if k < PAR["zi"][0]:
+            act(vw("ZX0", k, W, 16), vw("ZA0", 0, 256), AF.Copy)
+        elif k < PAR["zi"][0] + PAR["zi"][1]:
+            asel(vw("ZX0", k, W, 16), vw("ZA0", 0, 256), [[0, 256]], OP.is_ge, 1, 0)
+        else:
+            cp(vw("ZX0", k, W, 16), vw("ZA0", 0, 256))
+
+    def turn_lists():
+        for h in range(2):
+            o = vw("PSU", 128 * h, 128 * h + 128)
+            mm([(o, vw("IF"), vw("NQ", 128 * h, 128 * h + 128)), (o, vw("SF", 128 * h, 128 * h + 128), vw("IF"))])
+    turn_lists()
+    cp(vw("WMF", p1=8), vw("WM", p1=8))
+    for h in range(2):
+        mm([(vw("PD1", 8 * h, 8 * h + 8), vw("WMF", 1 - h, 256, 2, 8), vw("IF", 0, 8, 1, 8))])
+    ts(vw("HS1"), vw("PD1", 0, 16), -1.0, OP.mult, 1.0, OP.add)
+    ts(vw("THR"), vw("PD1", 0, 16), 65536.0, OP.mult)
+    for h in range(2):
+        act(vw("HX", 128 * h, 128 * h + 128), ind(vw("HS1", 8 * h, 8 * h + 8), LC), AF.Copy)
+    for j in range(8):
+        bank = vw(["PK0", "PK1", "PA0", "PA1"][j % 4])
+        mm([(bank, vw("AP"), vw("X", 512 * j, 512 * j + 512))])
+        act(vw("T2", 512 * j, 512 * j + 512), bank, AF.Identity, bias=col("BT", 0))
+    for j in range(4):
+        src = vw("VW", 512 * j, 512 * j + 512)
+        ts(vw("VS", 512 * j, 512 * j + 512), src, 4095, OP.bitwise_and)
+        ts(vw("VS", 2048 + 512 * j, 2048 + 512 * j + 512), src, 12, OP.arith_shift_right)
+
+    def hv(name, h, n=128, base=0):
+        return vw(name, base + n * h, base + n * h + n)
+
+    def settle_lists(t):
+        for h in range(2):
+            cp(hv("SF", h), ind(vw("VS", SO, SN + NS), vw("LB", 32 * t + 16 * h + 8, 32 * t + 16 * h + 16)))
+        if t < TS - 1:
+            cp(vw("VS", SO, SN), vw("SF"))
+        if t < TS - 2:
+            cp(vw("S16"), vw("SF"))
+            turn_lists()
+
+    me = cores[rank]
+    for t in range(TS):
+        last = t == TS - 1
+        step[0] = t
+        nth.clear()
+        zx = "ZX%d" % (max(t - 1, 0) % 2)
+        za, zb = "ZA%d" % (t % 2), "ZA%d" % ((t + 1) % 2)
+        hs, hp = "HS%d" % (t % 2), "HS%d" % ((t + 1) % 2)
+        for h in range(2):
+            pk, pa = "PK%d" % h, "PA%d" % h
+            at(t, "m%d" % h)
+            lo, hi = PAR["alt"]
+            b = 2048 * h
+            while b < 2048 * h + 2048:
+                a = b
+                b = a + (PAR["ach"] if lo <= a < hi and t else min(PAR["mch"], 512 - a % 512))
+                rows = ind(vw("X", 0, W), vw("S16", a // 16, b // 16))
+                if t == 0:
+                    j = a // 512
+                    bank = vw(["PD0", "PD1", "PF"][j % 3])
+                    if j in PAR["c0v"]:
+                        cp(vw("G2", a, b), rows)
+                    else:
+                        act(vw("G2", a, b), rows, AF.Copy)
+                    mm([(bank, vw("IN"), vw(zx, a, b)), (bank, vw("IB"), vw("G2", a, b))])
+                    if j in PAR["r0v"]:
+                        ts(vw("M", a, b), bank, 0.0, OP.max)
+                    else:
+                        act(vw("M", a, b), bank, AF.Relu)
+                elif lo <= a < hi:
+                    bank = vw(["PA1", "PF"][a // (b - a) % 2], 0, b - a)
+                    act(vw("D", a, b), rows, AF.Copy)
+                    mm([(bank, vw("IN"), vw(zx, a, b)), (bank, vw("IB"), vw("D", a, b))])
+                    act(vw("M", a, b), bank, AF.Relu)
+                else:
+                    tt(vw("M", a, b), rows, vw(zx, a, b), OP.max)
+            at(t, "g%d" % h)
+            for a in range(2048 * h, 2048 * h + 2048 if t else 0, PAR["gch"]):
+                b = a + PAR["gch"]
+                rows = ind(vw("T2", 0, W), vw("S16", a // 16, b // 16))
+                if a >= W - PAR["gv"]:
+                    cp(vw("G2", a, b), rows)
+                else:
+                    act(vw("G2", a, b), rows, AF.Copy)
+            at(t, "a%d" % h)
+            first = [(vw(pk, 0, 256), vw("IF"), vw("BI0")) if t == 0 else (vw(pk, 0, 256), vw("IB"), vw("BI")),
+                     (vw(pk, 128, 256), vw("IG"), hv("HX", h))]
+            if t > 0:
+                first.append((vw(pk, 0, 128), vw("IB"), hv("MV", h)))
+            mm(first, stop=False)
+            mm([(vw(pk, k, 128, 16), vw("M", 2048 * h + k, 2048 * h + 2048, 16), vw("W1", 0, 8)) for k in range(16)], start=False, stop=False)
+            mm([(vw(pk, k, 256, 16), vw("G2", 2048 * h + k, 2048 * h + 2048, 16), vw("W2", 16 * t, 16 * t + 16)) for k in range(16)], start=False)
+            ts(hv("MV", h), vw(pk, 128, 256), 0.0, OP.is_ge, 65536.0, OP.mult)
+            tt(hv("KEY", h), vw(pk, 0, 128), hv("MV", h), OP.add)
+            scan(hv("RR", h), vw("MKN"), hv("KEY", h), OP.add, OP.max)
+            scan(hv("CN", h), vw("MK0", 0, 128), hv("MV", h), OP.mult, OP.add)
+            tt(hv("EQ", h), ind(hv("RR", h), L15), hv("KEY", h), OP.is_equal)
+            cn = vw("CN", 128 * h + 15, 128 * h + 128, 16)
+            tt(hv("BO", h, 8), cn, hv("THR", h, 8), OP.is_gt)
+            tt(hv(hs, h, 8), cn, hv("THR", h, 8), OP.not_equal)
+            tt(hv("ZZ", h), hv("PSU", h), hv("EQ", h), OP.mult)
+            scan(hv("SC", h), vw("MK0", 0, 128), hv("ZZ", h), OP.mult, OP.add)
+            tt(hv("DB", h, 8), vw("SC", 128 * h + 15, 128 * h + 128, 16), hv("BO", h, 8), OP.mult)
+            tt(hv("E1", h), ind(hv("DB", h, 8), LC), vw("MR"), OP.mult)
+            mm([(vw(pa, 0, 8), vw("IF"), hv("QD", h, 8))], stop=False)
+            mm([(vw(pa, 0, 8), hv("E1", h), vw("DC"))], start=False)
+            cp(hv("DL", h, 8), vw(pa, 0, 8))
+            cp(hv("FB", h, 128, 256 * t), ind(vw("VS", 0, SN), hv("DL", h, 8)))
+            at(t, None)
+            tt(hv("MH", h), ind(hv(hs, h, 8), LC), vw("MR"), OP.mult)
+            if not last:
+                act(hv("HX", h), ind(hv(hs, h, 8), LC), AF.Copy)
+        if t > 0:
+            settle_lists(t - 1)
+        if not last:
+            mm([(vw("PD0", 256, 272), vw("ONB"), vw("BO"))])
+            add("V", 64 * cyc, [vw("PD0", 256, 272)], [col("CF", 9)], ("tensor_reduce", col("CF", 9), vw("PD0", 256, 272)))
+            cp(col("AI", 0), col("CF", 9))
+            ts(col("AI", 1), col("AI", 0), 31, OP.bitwise_and)
+            ts(col("CF", 12), col("AI", 1), -1.0, OP.mult, col("CF", 7), OP.add)
+            tt(col("CF", 10 + (t + 1) % 2), col("CF", 9), col("CF", 8), OP.add)
+            tt(vw("TH2"), vw(hp), vw(hs), OP.subtract)
+            ts(vw("THR"), vw("TH2"), 32768.0, OP.mult, 32768.0, OP.add)
+        for h in range(2):
+            pa = "PA%d" % h
+            yv, fv = hv("YB", h, 128, 256 * t), hv("FB", h, 128, 256 * t)
+            at(t, "d%d" % h)
+            for a in range(2048 * h, 2048 * h + 2048, PAR["dch"]):
+                b = a + PAR["dch"]
+                act(vw("D", a, b), ind(vw("X", 0, W), vw("FB", 256 * t + a // 16, 256 * t + b // 16)), AF.Copy)
+            cuts = PAR["cuts"][h]
+            at(t, "s%d" % h)
+            for a, b in zip(cuts[:-1], cuts[1:]):
+                a, b = a + 2048 * h, b + 2048 * h
+                scan(vw("MX", a, b), vw("MK0", 0, b - a), vw("D", a, b), OP.mult, OP.max)
+                scan(vw("MN", a, b), vw("MKB", 0, b - a), vw("D", a, b), OP.add, OP.min)
+            at(t, "y%d" % h)
+            py = vw(pa, 128, 256)
+            mm([(py, vw("IB"), vw("CQ"))], stop=False)
+            mm([(py, vw("IH"), vw("MX", 2048 * h + 15, 2048 * h + 2048, 16))], start=False, stop=False)
+            mm([(py, vw("IH"), vw("MN", 2048 * h + 15, 2048 * h + 2048, 16))], start=False)
+            ts(yv, py, MAGIC, OP.add, MAGIC, OP.subtract)
+            if h == 0:
+                dst = cores[(rank + 1 + t % 3) % NR]
+                pairs = [(vw("RY", 128 * t, 128 * t + 128), yv)] + ([] if last else [(vw("RFF", 128 * t, 128 * t + 128), fv)])
+                add("G", 0.5, [p[1] for p in pairs], [], ("send", dst, pairs, "ra%d" % t))
+                add("R", 0.0, [], [p[0] for p in pairs], None, sem="ra%d" % t, after=len(ops) - 1, lat=PAR["rem"], cnt=len(topo.engines(me, dst)))
+            pd, pk = vw("PD%d" % h, 256, 384), "PK%d" % h
+            av = hv(za, h, 128, 256)
+            if PAR["abr"][h]:
+                mm([(pd, vw("IN"), hv(za, h)), (pd, vw("IB"), vw("CQ"))], stop=False)
+                mm([(pd, vw("IH"), vw("MX", 2048 * h + 15, 2048 * h + 2048, 16))], start=False, stop=False)
+                mm([(pd, vw("IH"), vw("MN", 2048 * h + 15, 2048 * h + 2048, 16))], start=False)
+                act(hv("AB", h), pd, AF.Abs)
+                ts(av, hv("AB", h), MAGIC, OP.add, MAGIC, OP.subtract)
+            else:
+                mm([(pd, vw("IN"), hv(za, h))], stop=False)
+                mm([(pd, vw("IB"), yv)], start=False)
+                act(av, pd, AF.Abs)
+            mm([(vw(pa, 16, 24), av, vw("WG", 0, 8))])
+            cp(hv("UI", h, 8), vw(pa, 16, 24))
+            ts(hv("UA", h, 8), hv("UI", h, 8), 15, OP.bitwise_and)
+            tt(hv("E2", h), ind(hv("UA", h, 8), LC), hv("MH", h), OP.mult)
+            mm([(vw(pk, 256, 272), vw("IF"), hv("QP", h, 16)), (vw(pk, 256, 272), hv("MH", h), hv("RH", h, 16))], stop=False)
+            mm([(vw(pk, 256, 264), hv("E2", h), vw("DCB", 0, 8))], start=False)
+            lb = hv("LB", h, 16, 32 * t)
+            cp(lb, vw(pk, 256, 272))
+            if h == 0:
+                pairs = [(vw("RL", 8 * t, 8 * t + 8), vw("LB", 32 * t, 32 * t + 8))]
+                add("G", 0.5, [pairs[0][1]], [], ("send", dst, pairs, "rb%d" % t))
+                add("R", 0.0, [], [pairs[0][0]], None, sem="rb%d" % t, after=len(ops) - 1, lat=PAR["rem"] - 0.5, cnt=len(topo.engines(me, dst)))
+            at(t, None)
+            mm([(hv("PSU", h, 128, 256), vw("WBD"), av)])
+            cp(hv("UR", h), hv("PSU", h, 128, 256))
+            act(hv(zb, h), ind(vw(za), vw("LB", 32 * t + 16 * h + 8, 32 * t + 16 * h + 16)), AF.Copy)
+        for j in range(2):
+            pd = "PD%d" % j
+            if j == 0:
+                ys, fs, ls = vw("RY", 128 * t, 128 * t + 128), vw("RFF", 128 * t, 128 * t + 128), vw("RL", 8 * t, 8 * t + 8)
+            else:
+                ys, fs, ls = hv("YB", 1, 128, 256 * t), hv("FB", 1, 128, 256 * t), vw("LB", 32 * t + 16, 32 * t + 24)
+            at(t, "x%d" % j)
+            if not last:
+                if PAR["dda"][j]:
+                    act(hv("OLD", j), ind(vw("X"), ls), AF.Copy)
+                else:
+                    tt(hv("DD", j), ind(vw("X"), ls), ys, OP.subtract)
+            cp(ind(vw("X"), ls), ys)
+            at(t, "u%d" % j)
+            if not last:
+                if PAR["dda"][j]:
+                    mm([(vw(pd, 128, 256), vw("IN"), ys), (vw(pd, 128, 256), vw("IB"), hv("OLD", j))])
+                    act(hv("AD", j), vw(pd, 128, 256), AF.Abs)
+                else:
+                    act(hv("AD", j), hv("DD", j), AF.Abs)
+                mm([(vw(pd, 0, 128), vw("BD"), hv("AD", j))])
+                act(hv("SG", j), vw(pd, 0, 128), AF.Sign, bias=col("CF", 12))
+                mm([(vw(pd, 128, 256), vw("AP"), ys), (vw(pd, 128, 256), vw("RKW", 128 * (t + 1), 128 * (t + 2)), hv("SG", j))])
+                act(hv("TN", j), vw(pd, 128, 256), AF.Identity, bias=col("BT", t + 1))
+                cp(ind(vw("T2"), ls), hv("TN", j))
+                at(t, None)
+                cp(ind(vw("VS", 0, WD), ls), fs)
+        if last:
+            at(t, "out")
+            for j in range(2):
+                dma("SA"[j], ("$", "yx", 2048 * j, 2048 * j + 2048), vw("X", 2048 * j, 2048 * j + 2048), 5.5)
+        at(t, None)
+        ts(vw("UR"), vw("UR"), 4095, OP.bitwise_and)
+        cp(vw("PF", 0, 256), vw("FB", 256 * t, 256 * t + 256))
+        tt(vw("PR"), vw("PF", 0, 256), vw("UR"), OP.mult)
+        act(vw("PF", 256, 512), vw("PF", 0, 256), AF.Identity, bias=col("CF", 10 + t % 2))
+        ts(vw("PR"), vw("PR"), 5, OP.arith_shift_right)
+        tt(vw("PR2"), vw("PF", 256, 512), vw("PR"), OP.add)
+        ts(vw("VS", SN, SN + NS), vw("PR2"), 4095, OP.bitwise_and)
+        if t < TS - 2:
+            for k in range(16):
+                o = vw("ZX%d" % ((t + 1) % 2), k, W, 16)
+                if k < PAR["zact"]:
+                    act(o, vw(zb, 0, 256), AF.Copy)
+                else:
+                    asel(o, vw(zb, 0, 256), [[0, 256]], OP.is_ge, 1, 0)
+    settle_lists(TS - 1)
+    zf = "ZA%d" % (TS % 2)
+    for h in range(2):
+        act(vw("OZ", 1 - h, 256, 2), hv(zf, h), AF.Copy)
+        act(vw("OS", 1 - h, 256, 2), hv("SF", h), AF.Copy)
+    dma("S", ("$", "yz", 0, 256), vw("OZ"), 2.0)
+    dma("S", ("$", "ys", 0, 256), vw("OS"), 2.0)
+    return ops
+
+
+def depend(ops):
+    seen = {}
+    for n, o in enumerate(ops):
+        dep, reads = set(), set()
+        if "after" in o:
+            dep.add(o["after"])
+        for v, w in [(v, False) for v in o["r"]] + [(v, True) for v in o["w"]]:
+            for m, u, uw in seen.get(v[0], []):
+                if m == n:
+                    continue
+                if v[0] in PS and (ops[m]["eng"] != o["eng"] or (o["eng"] == "P")):
+                    dep.add(m)
+                elif (w or uw) and clash(u, v):
+                    dep.add(m)
+                    if uw:
+                        reads.add(m)
+        o["dep"] = dep
+        o["soft"] = {m for m in dep if ops[m]["eng"] == o["eng"] and "sem" not in ops[m] and "sem" not in o
+                     and ((o["eng"] in PAR["soft"] and m not in reads) or (o["eng"] == "P" and o["goon"]))}
+        for v, w in [(v, False) for v in o["r"]] + [(v, True) for v in o["w"]]:
+            lst = seen.setdefault(v[0], [])
+            if w and v[0] not in PS:
+                lst[:] = [e for e in lst if not (v[3] == 1 and v[4] == 128 and v[1] <= e[1][1] and e[1][2] <= v[2])]
+            lst.append((n, v, w))
+
+
+def schedule(ops):
+    n = len(ops)
+    pred = [list(o["dep"]) for o in ops]
+    succ = [[] for _ in ops]
+    for i in range(n):
+        for d in pred[i]:
+            succ[d].append(i)
+    pr = [o["pr"] for o in ops]
+    for i in range(n - 1, -1, -1):
+        for d in pred[i]:
+            pr[d] = min(pr[d], pr[i])
+    prio = sorted(range(n), key=lambda i: (pr[i], i))
+    best = None
+    for _ in range(PAR["pass"]):
+        start, end = place(ops, prio, pred, False)
+        if best is None or max(end) < best[0]:
+            best = (max(end), sorted(range(n), key=lambda i: (start[i], i)))
+        back = sorted(range(n), key=lambda i: (-end[i], -i))
+        _s, bend = place(ops, back, succ, True)
+        prio = sorted(range(n), key=lambda i: (-bend[i], i))
+    return improve(ops, best[1])
+
+
+def improve(ops, order):
+    n, hop = len(ops), PAR["hop"]
+    anc, pred, succ = [0] * n, [], [[] for _ in ops]
+    for i, o in enumerate(ops):
+        keep, m = [], 0
+        for d in sorted(o["dep"], reverse=True):
+            if not (m >> d) & 1:
+                keep.append(d)
+                succ[d].append(i)
+                m |= anc[d] | (1 << d)
+        anc[i] = m
+        pred.append(keep)
+    keys, base = [o["key"] for o in ops], [100 * o["step"] for o in ops]
+    st = place(ops, order, pred, False)[0]
+    mark = [st[i] for i in range(n) if keys[i].endswith("VMV0")]
+    fine = {}
+    for t in (4, 1, 3, 2, 0, 5):
+        for i in range(n):
+            if ops[i]["step"] == t:
+                fine[keys[i]] = (st[i] - mark[t]) / (mark[3] - mark[2]) * 100
+
+    gaps = [[(d, 0.0 if d in ops[i]["soft"] else hop) for d in pred[i]] for i in range(n)]
+    kind = [(o["eng"], o["cost"], o.get("lat", 0.0)) for o in ops]
+
+    def rate(f):
+        pr = [base[i] + f[keys[i]] for i in range(n)]
+        for i in range(n - 1, -1, -1):
+            p = pr[i]
+            for d in pred[i]:
+                if p < pr[d]:
+                    pr[d] = p
+        st, en = [0.0] * n, [0.0] * n
+        busy = {e: [] for e in "VAPGS"}
+        for i in sorted(range(n), key=lambda j: pr[j]):
+            r = 0.0
+            for d, x in gaps[i]:
+                x += en[d]
+                if x > r:
+                    r = x
+            e, c, lat = kind[i]
+            if e != "R":
+                iv = busy[e]
+                m = k = len(iv)
+                while k and iv[k - 1][1] > r:
+                    k -= 1
+                while k < m and iv[k][0] < r + c:
+                    r = iv[k][1]
+                    k += 1
+                iv.insert(k, (r, r + c))
+            st[i] = r
+            en[i] = r + c + lat
+        return max(en), st, en, pr
+
+    def chain(st, en):
+        before = {(ops[i]["eng"], round(st[i] + ops[i]["cost"], 6)): i for i in range(n)}
+        i, pairs = max(range(n), key=lambda j: en[j]), []
+        while True:
+            b = max(pred[i], key=lambda d: en[d]) if pred[i] else None
+            j = before.get((ops[i]["eng"], round(st[i], 6)))
+            if b is not None and en[b] + (0 if b in ops[i]["soft"] else hop) >= st[i] - 1e-6:
+                i = b
+            elif j is not None and j != i:
+                pairs.append((j, i))
+                i = j
+            else:
+                return pairs
+
+    seed = [PAR["seed"]]
+
+    def rnd():
+        seed[0] = (seed[0] * 1103515245 + 12345) % 2147483648
+        return seed[0] / 2147483648
+
+    cur, st, en, pr = rate(fine)
+    best, pairs = (cur, st), chain(st, en)
+    for it in range(PAR["tries"]):
+        f = dict(fine)
+        j, i = pairs[int(rnd() * len(pairs))]
+        u = rnd()
+        if u < 0.4:
+            f[keys[i]] = pr[j] - base[i] - 0.01 - rnd() * rnd() * 3
+        else:
+            p = pr[i] + 0.01 + rnd() * rnd() * 6 if u < 0.8 else pr[j] + rnd() * 30
+            todo, seen = [j], set()
+            while todo:
+                x = todo.pop()
+                if x not in seen and x != i:
+                    seen.add(x)
+                    f[keys[x]] = max(f[keys[x]], p - base[x])
+                    todo += [y for y in succ[x] if pr[y] < p]
+        v, st, en, pr2 = rate(f)
+        if v <= cur - (0.15 * (1 - it / PAR["tries"]) + 1e-4) * math.log(rnd() + 1e-12):
+            fine, cur, pr, pairs = f, v, pr2, chain(st, en)
+            if v < best[0]:
+                best = (v, st)
+    return sorted(range(n), key=lambda i: (best[1][i] if pred[i] or "sem" not in ops[i] else -1.0, i))
+
+
+def place(ops, prio, pred, lat_first):
+    hop = PAR["hop"]
+    end = [0.0] * len(ops)
+    start = [0.0] * len(ops)
+    busy = {}
+    for i in prio:
+        o = ops[i]
+        e = o["eng"]
+        r = 0.0
+        for d in pred[i]:
+            x = end[d] + (0.0 if (d in o["soft"] or i in ops[d]["soft"]) else hop)
+            if x > r:
+                r = x
+        lat = o.get("lat", 0.0)
+        if lat_first:
+            r += lat
+        c = o["cost"]
+        if e != "R":
+            iv = busy.setdefault(e, [])
+            k = len(iv)
+            while k > 0 and iv[k - 1][1] > r:
+                k -= 1
+            while k < len(iv) and iv[k][0] < r + c:
+                r = max(r, iv[k][1])
+                k += 1
+            iv.insert(k, (r, r + c))
+        start[i] = r
+        end[i] = r + c + (0.0 if lat_first else lat)
+    return start, end
+
+
+def rank_program(g, core, T, topo):
+    rank = T.rank_of(core)
+    if rank is None:
+        return
+    ops = build(rank, list(T.cores), topo)
+    depend(ops)
+    if "order" not in KEPT:
+        KEPT["order"] = schedule(ops)
+    order = KEPT["order"]
+    pos = {i: k for k, i in enumerate(order)}
+    known = {}
+    for i in order:
+        o = ops[i]
+        o["wait"] = []
+        if o["eng"] == "R":
+            continue
+        need = {}
+        for d in o["dep"]:
+            p = ops[d]
+            if d in o["soft"]:
+                continue
+            key = p.get("sem") or p["eng"]
+            if key not in need or pos[d] > pos[need[key]]:
+                need[key] = d
+        for key, d in need.items():
+            if known.get((o["eng"], key), -1) < pos[d]:
+                known[(o["eng"], key)] = pos[d]
+                o["wait"].append(d)
+                ops[d]["mark"] = True
+    queue = {"V": g.vector, "A": g.scalar, "P": g.tensor, "G": g, "S": g.sync}
+    count = {}
+    sent = 0
+
+    def ap(v):
+        if not isinstance(v, tuple):
+            return v
+        if v[0] == "@":
+            return ap(v[1]).indirect(ap(v[2]))
+        if v[0] == "$":
+            t = T[v[1]]
+            return t[:] if v[3] - v[2] == t.shape[1] else t[:, v[2]:v[3]]
+        t = T[v[0]]
+        if v[3] == 1:
+            return t[0:v[4], v[1]:v[2]]
+        return t[0:v[4], v[1]:v[2]:v[3]]
+
+    tail = []
+    for i in order:
+        o = ops[i]
+        e = o["eng"]
+        if e == "R":
+            o["sig"] = (o["sem"], o["cnt"])
+            continue
+        q = queue[e]
+        for d in o["wait"]:
+            s, c = ops[d]["sig"]
+            q.wait_ge(T.sem[s], c)
+        c = o["call"]
+        if c[0] == "send":
+            dst, pairs, sem = c[1], c[2], c[3]
+            rid, pid = topo.addr(dst)[0], topo.addr(dst)[1]
+            eng = topo.engines(core, dst)
+            if len(pairs) == 1:
+                g.remote_dma(ap(pairs[0][0]), ap(pairs[0][1]), T.sem[sem], T.sem["sent"], pid, rid, topo.mask(core, dst))
+            else:
+                k = len(eng) // len(pairs)
+                g.remote_dma_fused([RemoteDMATransfer(dst_ids=[DstId(rid=rid, pnc=pid)], dma_engine_mask=sum(1 << x for x in eng[k * j:k * j + k]),
+                                                      remote_sem=T.sem[sem], src=ap(p[1]), dst=ap(p[0])) for j, p in enumerate(pairs)], local_sem=T.sem["sent"])
+            sent += len(eng)
+            continue
+        if c[0] == "dma":
+            q.dma_start(ap(c[1]), ap(c[2])).then_inc(T.sem[o["sem"]], 16)
+            o["sig"] = (o["sem"], 16)
+            if not o.get("mark"):
+                tail.append(o["sem"])
+            continue
+        if c[0] == "mm":
+            for k, t in enumerate(c[1]):
+                ins = q.matmul(ap(t[0]), ap(t[1]), ap(t[2]), c[2] and k == 0, c[3] and k == len(c[1]) - 1)
+        elif c[0] == "activation":
+            if c[3] == AF.Copy:
+                ins = q.activation(ap(c[1]), ap(c[2]), c[3])
+            else:
+                ins = q.activation(ap(c[1]), ap(c[2]), c[3], bias=ap(c[4]), scale=ap(c[5]))
+        elif c[0] == "tensor_reduce":
+            ins = q.tensor_reduce(ap(c[1]), ap(c[2]), AxisListType.X, OP.add)
+        elif c[0] == "iota":
+            if SB[c[1][0]][1] == I:
+                ins = q.iota(ap(c[1]), c[2], c[3], c[4])
+            else:
+                ins = q.iota(ap(c[1]), c[2], c[3], c[4], allow_small_or_imprecise_dtypes=True)
+        elif c[0] == "affine_select":
+            ins = q.affine_select(ap(c[1]), ap(c[2]), c[3], c[4], c[5], c[6], c[7])
+        elif c[0] == "tensor_copy":
+            ins = q.tensor_copy(ap(c[1]), ap(c[2]))
+        elif c[0] == "tensor_tensor":
+            ins = q.tensor_tensor(ap(c[1]), ap(c[2]), ap(c[3]), c[4])
+        elif c[0] == "tensor_scalar":
+            ins = q.tensor_scalar(*[ap(x) for x in c[1:]])
+        elif c[0] == "tensor_tensor_scan":
+            ins = q.tensor_tensor_scan(*[ap(x) for x in c[1:]])
+        else:
+            ins = q.memset(ap(c[1]), c[2])
+        if o.get("mark"):
+            count[e] = count.get(e, 0) + 1
+            ins.then_inc(T.sem["q" + e], 1)
+            o["sig"] = ("q" + e, count[e])
+    g.wait_ge(T.sem["sent"], sent)
+    for s in tail:
+        g.sync.wait_ge(T.sem[s], 16)

@@ -5,45 +5,49 @@ from concourse.mybir import AluOpType, AxisListType, ActivationFunctionType
 OP = AluOpType
 AF = ActivationFunctionType
 W, NS, TS, NR = 4096, 256, 6, 4
-WD = W + NS
-SO = WD
-SN = SO + NS
+WD = 2 * W
+Z0 = NS * (TS + 1)
+V0 = Z0 + 128
+H0 = V0 + W
 MAGIC = 12582912.0
 
 B, F, I, U = "bfloat16", "float32", "int32", "uint16"
 SB = {
-    "X": (WD, B), "T2": (WD, B), "VS": (SN + NS, I), "VW": (2048, I),
+    "X": (WD, B), "T2": (WD, B), "VS": (H0 + NS * (TS - 1), I), "VW": (2048, I),
     "M": (W, B), "G2": (W, B), "D": (W, B), "MX": (W, B), "MN": (W, B), "ZX0": (W, B), "ZX1": (W, B),
-    "ZA0": (512, B), "ZA1": (512, B), "ZR": (256, B), "SR": (256, I), "S16": (256, U), "SF": (256, F),
+    "ZA0": (256, B), "ZA1": (256, B), "ZR": (256, B), "SR": (256, I), "S16": (256, U), "SF": (256, F),
     "WI": (8, I), "TI": (8, I), "WM": (256, I), "WMF": (256, F), "CF": (32, F), "PI": (16, I),
-    "JF": (128, F), "RF": (128, F), "GF": (128, F), "IF": (128, F), "IB": (128, B), "IH": (128, B),
-    "IN": (128, B), "IG": (128, B), "BD": (128, B), "AP": (128, B), "MR": (128, F), "WBD": (128, B),
-    "ONF": (128, F), "ONB": (128, B), "M2B": (128, B), "CQ": (128, B), "RKW": (128 * 6, B), "TMP": (128, F), "CMP": (128, B),
-    "DC": (8, F), "W1": (16, B), "W2": (96, B), "WG": (16, B), "EQT": (8, F), "BT": (8, F), "I8": (32, F),
-    "BI0": (256, F), "BI": (256, B), "NQ": (256, F), "QD": (16, F), "QP": (32, F), "RH": (32, F), "Q16": (16, F),
-    "MK0": (1024, B), "MKB": (1024, B), "MKN": (128, B), "OLD": (256, B), "AB": (256, F), "LS": (16, U),
-    "MV": (256, B), "KEY": (256, F), "RR": (256, F), "EQ": (256, F), "ZZ": (256, F), "SC": (256, F), "CN": (256, F),
-    "BO": (16, B), "HS0": (16, F), "HS1": (16, F), "THR": (16, F), "TH2": (16, F), "DB": (16, F), "E1": (256, F), "E2": (256, B), "DCB": (16, B),
-    "MH": (256, F), "HX": (256, B), "DL": (16, U), "UI": (16, I), "UA": (16, I),
-    "FB": (256 * TS, U), "YB": (256 * TS, B), "LB": (32 * TS, U),
-    "RY": (128 * TS, B), "RFF": (128 * TS, U), "RL": (8 * TS, U),
-    "DD": (256, B), "AD": (256, B), "SG": (256, B), "TN": (256, B),
-    "UR": (256, I), "PR": (256, I), "PR2": (256, I), "AI": (8, I), "OS": (256, F), "OZ": (256, B),
+    "JF": (144, F), "RF": (128, F), "GF": (128, F), "IF": (128, F), "IB": (128, B), "IH": (128, B),
+    "IN": (128, B), "IG": (128, B), "IK": (128, B), "IS": (128, B), "BD": (128, B), "MR": (128, F), "WBD": (128, B),
+    "ONF": (128, F), "ONB": (128, B), "CQ": (128, B), "CU": (128, B), "TMP": (128, F), "TM2": (128, F), "DI": (128, F),
+    "WO": (144, B), "WS": (128, B), "AP": (128, B), "AP2": (128, B), "APN": (128, B), "QS": (128, B), "BS": (16, F), "L15": (8, U),
+    "YW": (256, B), "S4": (256, U), "C2": (W, B), "KB": (256, F), "HX": (32, B), "BZ": (128, B), "XM": (256, F), "MZ": (256, B), "WB2": (128, B), "WBN": (128, B),
+    "DC": (8, F), "DC8": (8, F), "DCN": (8, F), "DCM": (8, F), "W1": (16, B), "WK": (16, B), "WR": (32, B), "BT": (16, F),
+    "BI0": (128, F), "BI": (128, B), "QP": (32, F), "Q16": (16, F),
+    "CT": (1024, B), "MK0": (512, B), "MKB": (512, B), "MKN": (128, B), "OLD": (256, B), "LS": (8, U),
+    "SG": (256, B), "KEY": (256, F), "NE": (256, F), "SC": (256, F), "CN": (256, B), "NH": (16, F), "XB": (16, F),
+    "BO": (16, B), "HS0": (16, B), "HS1": (16, B), "THR": (16, F), "TH2": (16, F), "DB": (16, F), "E1": (256, F), "E2": (256, F),
+    "WT0": (16, B), "WT1": (16, B), "WW": (16, B), "DL": (16, U), "C7": (128, B), "C64": (8, B), "NB": (16, F), "NH0": (16, F), "E3": (256, F),
+    "FB": (256, U), "FO": (128 * TS + 128, I), "YB": (256 * TS, B), "LB": (32 * TS, U),
+    "RY": (128 * TS, B), "RL": (8 * TS, U),
+    "DD": (256, B), "HI": (256, B), "TN": (256, B), "UR": (256, F), "UB": (256, B),
+    "PR": (256, I), "PR2": (256, I), "AI": (8, I), "OS": (256, F), "OZ": (256, B),
 }
-PS = ["PK0", "PK1", "PSU", "PA0", "PA1", "PD0", "PD1", "PF"]
+PS = ["PK0", "PK1", "PU", "PA0", "PA1", "PD0", "PD1", "PF"]
 SCRATCH = {k: ("sbuf", [128, v[0]], v[1]) for k, v in SB.items()}
 SCRATCH.update({k: ("psum", [128, 512], F) for k in PS})
 NDMA = 24
 SEMAPHORES = (["qV", "qA", "qP", "qG", "sent"] + ["d%d" % k for k in range(NDMA)]
-              + ["ra%d" % t for t in range(TS)] + ["rb%d" % t for t in range(TS)])
+              + ["r%s%d" % (x, t) for x in "abc" for t in range(TS)])
 
-PAR = {"cyc": 0.00083 * 1.15, "pe": 0.00042 * 1.3, "gat": 1.55, "sca": 3.5, "hop": 0.16, "pass": 4, "pool": 1.3,
-       "mch": 512, "gch": 1024, "dch": 1024, "zact": 0, "rem": 3.0, "alt": (0, 768), "c0v": (0, 1, 4), "r0v": (), "soft": "", "seed": 2, "tries": 10000, "ach": 256, "zi": (7, 3), "abr": (0, 1), "gv": 0, "dda": (1, 0),
-       "cuts": ([0, 1024, 2048], [0, 1024, 2048]),
+PAR = {"cyc": 0.00083 * 1.1, "pe": 0.00042 * 1.3, "gat": 1.55, "sca": 3.5, "hop": 0.2, "pass": 4, "heat": 0.15, "tries2": 16000, "heat2": 0.4, "pool": 1.3,
+       "mch": (256,) * 8, "gch": 512, "dch": 512, "rem": 3.0, "alt": (0, 1, 4), "abk": ("PA0",), "ywv": (1, 1), "c0v": (0, 1, 4), "r0v": (), "seed": 2, "tries": 2000,
+       "ach": 256, "zi": (7, 3), "abr": (0, 0), "gv": (2, 3), "dv": (), "both": 1, "jo": (1, 0), "ml": (0, 0), "sv": 1, "dda": (0, 0), "tna": (1, 1), "xm": (1, 0), "parts": (((0, 96), (96, 128)), ((0, 96), (96, 128))), "ho": (1, 0), "mz": (1, 1),
+       "cuts": ([0, 512, 1024, 1536, 2048], [0, 512, 1024, 1536, 2048]),
        "order": {"g0": 10, "m0": 12, "a0": 14, "g1": 16, "m1": 18, "d0": 20, "a1": 22, "d1": 24, "s0": 30, "y0": 32,
                  "s1": 26, "y1": 28, "u0": 40, "u1": 36, "x0": 34, "x1": 35, "out": 50}}
 LATE = 10000
-PER = {"FB": 256, "YB": 256, "LB": 32, "RY": 128, "RFF": 128, "RL": 8}
+PER = {"YB": 256, "LB": 32, "RY": 128, "RL": 8, "FO": 128}
 KEPT = {}
 
 
@@ -51,6 +55,10 @@ def vw(name, lo=0, hi=None, step=1, p1=128):
     if hi is None:
         hi = SB[name][0] if name in SB else 512
     return (name, lo, hi, step, p1)
+
+
+def made(t):
+    return NS * (TS - 1 - max(t, -1))
 
 
 def ind(win, off):
@@ -70,6 +78,8 @@ def two(v):
 
 def clash(a, b):
     if a[2] <= b[1] or b[2] <= a[1]:
+        return False
+    if len(a) > 5 and len(b) > 5 and a[5] != b[5]:
         return False
     if a[3] > 1 and a[3] == b[3] and (a[1] - b[1]) % a[3] != 0:
         return False
@@ -98,8 +108,11 @@ def build(rank, cores, topo):
         o = {"eng": eng, "cost": cost, "r": r, "w": w, "call": call, "pr": rank_now[0]}
         o.update(kw)
         x = w[0] if w else (r[0] if r else ("", 0))
-        name = x[0][:2] if x[0][:2] in ("ZA", "ZX", "HS") else x[0]
-        key = ["i", "a", "", "", "", "", "z"][step[0] + 1] + eng + name + str(x[1] % PER.get(name, 8192))
+        name = x[0][:2] if x[0][:2] in ("ZA", "ZX", "HS", "WT") else x[0]
+        c0 = x[1] % PER.get(name, 8192)
+        if name == "VS":
+            c0 = H0 + (x[1] - H0) % NS if x[1] >= H0 else x[1] % NS if x[1] < Z0 else x[1]
+        key = ["i", "a", "", "", "", "", "z"][step[0] + 1] + eng + name + str(c0)
         nth[key] = nth.get(key, 0) + 1
         o["key"], o["step"] = key + "_" * (nth[key] - 1), max(step[0], 0)
         ops.append(o)
@@ -118,7 +131,7 @@ def build(rank, cores, topo):
         return 0.5 if all(two(v) for v in vs) else 1
 
     def cp(out, a):
-        add("V", vcost(out, [a], half(out, a)) if width(out) >= width(a) else 64 * cyc, [a], [out], ("tensor_copy", out, a))
+        add("V", vcost(out, [a], half(out, a)), [a], [out], ("tensor_copy", out, a))
 
     def tt(out, a, b, op):
         per = 1 if (a[0] in PS or b[0] in PS) else 2
@@ -134,14 +147,14 @@ def build(rank, cores, topo):
     def mset(out, val):
         add("V", vcost(out, [out], half(out)), [], [out], ("memset", out, val))
 
-    def act(out, a, func, bias=0.0, scale=1.0):
+    def act(out, a, func=AF.Identity, bias=0.0, scale=1.0):
         n = width(out)
         c = 0.065 + n * PAR["gat"] * cyc if a[0] == "@" else max(64, n) * cyc + 0.03
         add("A", c, [a, bias, scale], [out], ("activation", out, a, func, bias, scale))
 
-    def mm(terms, start=True, stop=True):
-        c = sum(max(64, width(t[2])) * (1 if two(t[2]) else 4) * PAR["pe"] for t in terms)
-        add("P", c, [x for t in terms for x in t[1:]], [t[0] for t in terms], ("mm", terms, start, stop), goon=not start)
+    def mm(terms, start=True, stop=True, goon=True):
+        c = sum(max(min(64, width(t[1])), width(t[2])) * (1 if two(t[2]) else 4) * PAR["pe"] for t in terms)
+        add("P", c, [x for t in terms for x in t[1:]], [t[0] for t in terms], ("mm", terms, start, stop), goon=goon and not start)
 
     def iota(out, pat, base, cm):
         add("G", (0.13 + 2 * width(out) * 0.00083) * PAR["pool"], [], [out], ("iota", out, pat, base, cm))
@@ -160,6 +173,9 @@ def build(rank, cores, topo):
     def col(name, j):
         return vw(name, j, j + 1)
 
+    def hv(name, h, n=128, base=0):
+        return vw(name, base + n * h, base + n * h + n)
+
     dma("S", vw("SR"), ("$", "scan", 0, 256), 2.0)
     dma("S", vw("ZR"), ("$", "z0", 0, 256), 2.0)
     for j in range(4):
@@ -173,122 +189,136 @@ def build(rank, cores, topo):
     iota(vw("PI", 0, 1), [[0, 1]], 0, 1)
     iota(vw("GF"), [[1, 8], [0, 16]], 0, 0)
     iota(vw("RF"), [[0, 8], [1, 16]], 0, 0)
-    iota(vw("JF"), [[1, 128]], 0, 0)
+    iota(vw("JF"), [[1, 144]], 0, 0)
+    mset(vw("X", W, W + 16), 0.0)
+    for a in range(W, WD, 512):
+        iota(vw("X", max(a, W + 16), a + 512), [[0, a + 512 - max(a, W + 16)]], 0, 0)
     ts(vw("PI", 1, 2), vw("PI", 0, 1), 15, OP.bitwise_and)
     ts(vw("PI", 2, 3), vw("PI", 0, 1), 4, OP.arith_shift_right)
     ts(vw("PI", 3, 4), vw("PI", 0, 1), 1, OP.arith_shift_right, 7, OP.bitwise_and)
     cp(vw("CF", 0, 4), vw("PI", 0, 4))
-    ts(col("CF", 4), col("CF", 1), 8.0, OP.is_lt)
     ts(vw("BD"), vw("GF"), col("CF", 2), OP.is_equal)
-    ts(vw("CMP"), vw("RF"), col("CF", 3), OP.is_equal)
-    tt(vw("AP"), vw("CMP"), vw("BD"), OP.mult)
-    ts(col("CF", 13), col("CF", 4), -255.0, OP.mult)
-    ts(col("CF", 14), col("CF", 4), -16.0, OP.mult)
-    ts(vw("EQT"), vw("JF", 8, 16), col("CF", 1), OP.is_equal)
-    ts(vw("BT"), vw("EQT"), 16.0, OP.mult, col("CF", 13), OP.add)
-    ts(vw("DC"), vw("GF", 0, 128, 16), col("CF", 2), OP.is_equal)
-    ts(vw("IF"), vw("JF"), col("CF", 0), OP.is_equal)
-    act(vw("IB"), vw("IF"), AF.Identity)
-    act(vw("IH"), vw("IF"), AF.Identity, scale=0.5)
-    act(vw("IN"), vw("IF"), AF.Identity, scale=-1.0)
-    act(vw("IG"), vw("IF"), AF.Identity, scale=-8192.0)
+    ts(vw("DC"), vw("GF", 0, 128, 16), 0.0, OP.add, col("CF", 2), OP.is_equal)
+    ts(vw("IF"), vw("JF", 0, 128), col("CF", 0), OP.is_equal)
     ts(vw("MR"), vw("RF"), col("CF", 1), OP.is_equal)
+    for name, x in (("IB", 1.0), ("IH", 0.5), ("IN", -1.0), ("IG", -8192.0), ("IK", 32768.0), ("IS", 2048.0)):
+        act(vw(name), vw("IF"), scale=x)
     mset(vw("ONF"), 1.0)
     mset(vw("ONB"), 1.0)
-    mset(vw("M2B"), -2.0)
     mset(vw("CQ"), -0.25)
-    for name in ("VS", "X", "T2"):
-        iota(vw(name, W, WD), [[0, NS]], 0, 0)
-    iota(vw("MK0"), [[0, 1024]], 1, 0)
-    asel(vw("MK0"), vw("MK0"), [[0, 64], [1, 16]], OP.is_gt, 0, 0)
-    iota(vw("MKB"), [[0, 1024]], 256, 0)
-    asel(vw("MKB"), vw("MKB"), [[0, 64], [1, 16]], OP.is_equal, 0, 0)
-    mset(vw("MKN"), 0.0)
-    mset(vw("MKN", 0, 128, 16), -1048576.0)
-    ts(vw("I8", 0, 8), vw("JF", 0, 8), 1.0, OP.mult)
-    ts(vw("I8", 8, 16), vw("JF", 0, 8), 16.0, OP.mult, 15.0, OP.add)
-    cp(vw("LS"), vw("I8", 0, 16))
-    LC, L15 = vw("LS", 0, 8), vw("LS", 8, 16)
-    act(vw("W1", 0, 8), vw("DC"), AF.Identity, scale=32.0)
-    act(vw("DCB", 0, 8), vw("DC"), AF.Identity)
-    for t in range(TS):
-        act(vw("W2", 16 * t, 16 * t + 8), vw("DC"), AF.Identity, scale=col("CF", 14) if t else -16.0)
-        act(vw("W2", 16 * t + 8, 16 * t + 16), vw("DC"), AF.Identity, scale=col("EQT", t) if t else 1.0)
-    for t in range(1, TS):
-        asel(vw("RKW", 128 * t, 128 * t + 128), vw("BD"), [[0, 8], [1, 16]], OP.is_equal, -(8 + t), 0)
+    mset(vw("CU"), -16.0)
+    mset(vw("CU", p1=1), -15.5)
+    mset(col("CF", 12), 0.5)
+    iota(vw("VS", Z0, V0), [[0, V0 - Z0]], W, 0)
+    mset(vw("C7"), -7.5)
+    mset(vw("C64"), (V0 - Z0) / 16384)
+    iota(vw("NB", 0, 4), [[0, 2], [128, 2]], made(-1) - Z0, 1)
+    iota(vw("NB", 4, 12), [[-NS, 4], [128, 2]], made(0) - Z0 + 2 * NS, 1)
+    act(vw("NB", 0, 12), vw("NB", 0, 12), scale=1.0 / 8192)
+    for name, x, y in (("MK0", 1.0, 0.0), ("MKB", 0.0, 256.0), ("MKN", 0.0, -256.0)):
+        mset(vw(name), x)
+        mset(vw(name, step=16), y)
+    cp(vw("LS"), vw("JF", 0, 8))
+    LC = vw("LS")
+    ts(vw("L15"), vw("JF", 0, 8), 16.0, OP.mult, 15.0, OP.add)
+    act(vw("W1", 0, 8), vw("DC"), scale=32.0 / 32768)
+    act(vw("DC8"), vw("DC"), scale=8192.0)
+    act(vw("DCN"), vw("DC"), scale=-16.0 / 32768)
+    act(vw("DCM"), vw("DC"), scale=-1.0)
+    ts(col("CF", 14), col("MR", 2), 1.0 / 64, OP.mult)
+    ts(col("CF", 15), col("MR", 3), 1.0 / 8192, OP.mult, col("CF", 14), OP.add)
+    act(vw("WK", 0, 8), vw("DC"), scale=col("CF", 15))
+    act(vw("WK", 8, 16), vw("WK", 0, 8), scale=-1.0)
+    ts(col("CF", 7), col("CF", 1), 8.0, OP.is_ge)
+    ts(col("CF", 13), col("MR", 4), 8192.0, OP.mult, col("CF", 7), OP.add)
+    ts(col("CF", 21), col("CF", 1), 2.0, OP.is_lt)
+    ts(col("CF", 16), col("MR", 4), 16384.0, OP.mult, col("CF", 21), OP.add)
+    act(vw("BZ"), vw("BD"), scale=32.0 / 32768)
+    for t in range(2):
+        act(hv("WR", 2 * t, 8), vw("DCN"), scale=col("CF", 16) if t else 1.0)
+        act(hv("WR", 2 * t + 1, 8), vw("DC"), scale=col("CF", 13) if t else 1.0)
+    ts(col("CF", 4), col("CF", 2), 16.0, OP.mult, 15.0, OP.add)
+    ts(vw("WO"), vw("JF"), col("CF", 4), OP.is_equal)
+    tt(vw("WS"), vw("WO", 14, 142), vw("WO", 15, 143), OP.add)
+    ts(col("CF", 17), col("CF", 3), 8.0, OP.add)
+    ts(vw("TM2"), vw("RF"), col("CF", 17), OP.is_equal)
+    tt(vw("AP"), vw("TM2"), vw("BD"), OP.mult)
+    act(vw("AP2"), vw("AP"), scale=2.0)
+    act(vw("APN"), vw("AP"), scale=-1.0)
+    act(vw("QS"), vw("JF", 0, 128), scale=col("MR", 3))
+    iota(vw("BS"), [[1, 8], [0, 2]], 1, 0)
+    ts(vw("BT"), vw("JF", 0, 16), (H0 - V0) / 128, OP.add, col("MR", 2), OP.mult)
+    ts(col("CF", 20), col("CF", 7), -255.0, OP.mult)
+    ts(vw("BS"), vw("BS"), col("MR", 4), OP.mult, col("CF", 20), OP.add)
+    tt(vw("BT"), vw("BT"), vw("BS"), OP.add)
     cp(col("CF", 5), col("TI", 0))
     cp(col("CF", 6), col("WI", 0))
-    ts(col("CF", 7), col("CF", 5), -1.0, OP.mult, -0.5, OP.add)
     ts(col("CF", 8), col("CF", 1), 37.0, OP.mult)
     ts(col("CF", 10), col("CF", 1), 37.0, OP.mult)
-    act(vw("WG", 0, 8), vw("DC"), AF.Identity, scale=col("CF", 6))
-    act(vw("WBD"), vw("BD"), AF.Identity, scale=col("CF", 6))
+    act(vw("WBD"), vw("BD"), scale=col("CF", 6))
+    act(vw("WB2"), vw("WBD"), scale=2.0)
+    act(vw("WBN"), vw("WBD"), scale=-1.0)
     ts(vw("Q16"), vw("JF", 0, 16), 16.0, OP.mult, col("CF", 1), OP.add)
-    act(vw("QD"), vw("Q16"), AF.Identity, bias=float(SO))
     for h in range(2):
-        ts(col("CF", 15 + h), col("CF", 0), 31.0, OP.mult, float(16 * (1 - h) - W - 128 * h), OP.add)
-        ts(col("CF", 17 + h), col("CF", 0), -1.0, OP.mult, float(-SO - 128 * h), OP.add)
-        act(vw("QP", 16 * h, 16 * h + 8), vw("Q16", 8 * h, 8 * h + 8), AF.Identity, bias=float(W))
-        act(vw("QP", 16 * h + 8, 16 * h + 16), vw("Q16", 8 * h, 8 * h + 8), AF.Identity)
-        act(vw("RH", 16 * h, 16 * h + 8), vw("DC"), AF.Identity, scale=col("CF", 15 + h))
-        act(vw("RH", 16 * h + 8, 16 * h + 16), vw("DC"), AF.Identity, scale=256.0)
-        act(vw("NQ", 128 * h, 128 * h + 128), vw("ONF"), AF.Identity, scale=col("CF", 17 + h))
-    act(vw("TMP"), vw("IF"), AF.Identity, scale=col("CF", 5))
+        ts(vw("QP", 16 * h, 16 * h + 8), vw("Q16", 0, 8), 32.0, OP.mult, 16.0 * (1 - h) + 7.5, OP.add)
+        act(vw("QP", 16 * h + 8, 16 * h + 16), vw("Q16", 8 * h, 8 * h + 8))
+    act(vw("TMP"), vw("IF"), scale=col("CF", 5))
     mm([(vw("PF", 0, 128), vw("ONF"), vw("TMP"))])
-    ts(vw("BI0", 128, 256), vw("PF", 0, 128), -1.0, OP.mult, -1.0, OP.add)
-    act(vw("BI0", 0, 128), vw("RF"), AF.Identity, bias=15.0, scale=-1.0)
-    act(vw("BI", 0, 128), vw("RF"), AF.Identity, bias=15.0, scale=-1.0)
-    ts(vw("CMP"), vw("PF", 0, 128), col("CF", 5), OP.is_ge)
-    tt(vw("CMP"), vw("CMP"), vw("BD"), OP.mult)
-    mm([(vw("PF", 128, 256), vw("M2B"), vw("CMP"))])
-    act(vw("BI", 128, 256), vw("PF", 128, 256), AF.Identity)
+    act(vw("BI0"), vw("PF", 0, 128), scale=-1.0)
+    act(vw("BI"), vw("RF"), scale=-1.0 / 32768)
+    ts(col("CF", 18), col("CF", 1), 0.0, OP.is_gt, -1.0 / 8192, OP.mult)
+    ts(vw("TM2"), vw("JF", 1, 129), col("CF", 0), OP.is_equal, col("CF", 18), OP.mult)
+    act(vw("DI"), vw("IF"), scale=1.0 / 8192)
+    tt(vw("DI"), vw("DI"), vw("TM2"), OP.add)
 
     for h in range(2):
         src = vw("SR", 1 - h, 256, 2)
-        cp(vw("S16", 128 * h, 128 * h + 128), src)
-        cp(vw("SF", 128 * h, 128 * h + 128), src)
-        cp(vw("VS", SO + 128 * h, SO + 128 * h + 128), src)
-        cp(vw("ZA0", 128 * h, 128 * h + 128), vw("ZR", 1 - h, 256, 2))
+        cp(hv("S16", h), src)
+        cp(hv("SF", h), src)
+        cp(hv("VS", h, 128, made(-1)), src)
+        cp(hv("ZA0", h), vw("ZR", 1 - h, 256, 2))
     for k in range(16):
         if k < PAR["zi"][0]:
-            act(vw("ZX0", k, W, 16), vw("ZA0", 0, 256), AF.Copy)
+            act(vw("ZX0", k, W, 16), vw("ZA0"), AF.Copy)
         elif k < PAR["zi"][0] + PAR["zi"][1]:
-            asel(vw("ZX0", k, W, 16), vw("ZA0", 0, 256), [[0, 256]], OP.is_ge, 1, 0)
+            asel(vw("ZX0", k, W, 16), vw("ZA0"), [[0, 256]], OP.is_ge, 1, 0)
         else:
-            cp(vw("ZX0", k, W, 16), vw("ZA0", 0, 256))
-
-    def turn_lists():
-        for h in range(2):
-            o = vw("PSU", 128 * h, 128 * h + 128)
-            mm([(o, vw("IF"), vw("NQ", 128 * h, 128 * h + 128)), (o, vw("SF", 128 * h, 128 * h + 128), vw("IF"))])
-    turn_lists()
+            cp(vw("ZX0", k, W, 16), vw("ZA0"))
     cp(vw("WMF", p1=8), vw("WM", p1=8))
     for h in range(2):
         mm([(vw("PD1", 8 * h, 8 * h + 8), vw("WMF", 1 - h, 256, 2, 8), vw("IF", 0, 8, 1, 8))])
     ts(vw("HS1"), vw("PD1", 0, 16), -1.0, OP.mult, 1.0, OP.add)
-    ts(vw("THR"), vw("PD1", 0, 16), 65536.0, OP.mult)
-    for h in range(2):
-        act(vw("HX", 128 * h, 128 * h + 128), ind(vw("HS1", 8 * h, 8 * h + 8), LC), AF.Copy)
-    for j in range(8):
-        bank = vw(["PK0", "PK1", "PA0", "PA1"][j % 4])
-        mm([(bank, vw("AP"), vw("X", 512 * j, 512 * j + 512))])
-        act(vw("T2", 512 * j, 512 * j + 512), bank, AF.Identity, bias=col("BT", 0))
+    ts(vw("THR"), vw("PD1", 0, 16), 8.0, OP.mult)
+
+    def mark_new(hs):
+        for h in range(2):
+            act(vw("HX", 16 * h, 16 * h + 8), hv(hs, h, 8), scale=1.0 / 128)
+            act(vw("HX", 16 * h + 8, 16 * h + 16), hv(hs, h, 8))
+    mark_new("HS1")
+
+    def blocks():
+        ts(vw("S4"), vw("S16"), 1.0 / 16, OP.mult, -15.0 / 32, OP.add)
     for j in range(4):
         src = vw("VW", 512 * j, 512 * j + 512)
-        ts(vw("VS", 512 * j, 512 * j + 512), src, 4095, OP.bitwise_and)
-        ts(vw("VS", 2048 + 512 * j, 2048 + 512 * j + 512), src, 12, OP.arith_shift_right)
+        ts(hv("VS", j, 512, V0), src, 4095, OP.bitwise_and)
+        ts(hv("VS", j, 512, V0 + 2048), src, 12, OP.arith_shift_right)
 
-    def hv(name, h, n=128, base=0):
-        return vw(name, base + n * h, base + n * h + n)
+    def first_table():
+        dma("S", vw("T2", 0, W), vw("X", W, WD), 4.0)
+        mm([(vw("PU", 0, 256), vw("WO", 15 - a, 143 - a), hv("X", a, 256)) for a in range(16)])
+        lane = [hv("CT", l, 256) for l in range(4)]
+        act(lane[0], vw("PU", 0, 256), AF.Copy)
+        tt(lane[1], vw("PU", 0, 256), lane[0], OP.subtract)
+        iota(lane[3], [[0, 2], [1, 128]], 0, 0)
+        iota(lane[2], [[1, 2], [0, 128]], 0, 0)
+        ts(col("CF", 19), col("CF", 1), 2.0, OP.mult)
+        act(lane[2], lane[2], bias=col("CF", 19))
+        for l in range(4):
+            dma("S", vw("T2", 0, W) + (l, 16), lane[l], 2.5)
 
     def settle_lists(t):
         for h in range(2):
-            cp(hv("SF", h), ind(vw("VS", SO, SN + NS), vw("LB", 32 * t + 16 * h + 8, 32 * t + 16 * h + 16)))
-        if t < TS - 1:
-            cp(vw("VS", SO, SN), vw("SF"))
-        if t < TS - 2:
-            cp(vw("S16"), vw("SF"))
-            turn_lists()
+            cp(hv("SF" if t == TS - 1 else "S16", h), ind(vw("VS", made(t), Z0), vw("LB", 32 * t + 16 * h + 8, 32 * t + 16 * h + 16)))
 
     me = cores[rank]
     for t in range(TS):
@@ -298,88 +328,141 @@ def build(rank, cores, topo):
         zx = "ZX%d" % (max(t - 1, 0) % 2)
         za, zb = "ZA%d" % (t % 2), "ZA%d" % ((t + 1) % 2)
         hs, hp = "HS%d" % (t % 2), "HS%d" % ((t + 1) % 2)
-        for h in range(2):
-            pk, pa = "PK%d" % h, "PA%d" % h
-            at(t, "m%d" % h)
-            lo, hi = PAR["alt"]
-            b = 2048 * h
-            while b < 2048 * h + 2048:
-                a = b
-                b = a + (PAR["ach"] if lo <= a < hi and t else min(PAR["mch"], 512 - a % 512))
-                rows = ind(vw("X", 0, W), vw("S16", a // 16, b // 16))
-                if t == 0:
-                    j = a // 512
-                    bank = vw(["PD0", "PD1", "PF"][j % 3])
-                    if j in PAR["c0v"]:
-                        cp(vw("G2", a, b), rows)
-                    else:
-                        act(vw("G2", a, b), rows, AF.Copy)
-                    mm([(bank, vw("IN"), vw(zx, a, b)), (bank, vw("IB"), vw("G2", a, b))])
-                    if j in PAR["r0v"]:
-                        ts(vw("M", a, b), bank, 0.0, OP.max)
-                    else:
-                        act(vw("M", a, b), bank, AF.Relu)
-                elif lo <= a < hi:
-                    bank = vw(["PA1", "PF"][a // (b - a) % 2], 0, b - a)
-                    act(vw("D", a, b), rows, AF.Copy)
-                    mm([(bank, vw("IN"), vw(zx, a, b)), (bank, vw("IB"), vw("D", a, b))])
+        wt = "WT%d" % (t % 2)
+        dst = cores[(rank + 1 + t % 3) % NR]
+        lands = [(hv("RY", t), hv("RL", t, 8)), (hv("YB", 1, 128, 256 * t), vw("LB", 32 * t + 16, 32 * t + 24))]
+
+        def send(there, here, sem, lat):
+            add("G", 0.5, [here], [], ("send", dst, [(there, here)], sem + str(t)))
+            add("R", 0.0, [], [there], None, sem=sem + str(t), after=len(ops) - 1, lat=lat, cnt=len(topo.engines(me, dst)))
+
+        for j in range(8 if t else 0):
+            at(t, "m%d" % (j // 4))
+            n = PAR["ach"] if j in PAR["alt"] else PAR["mch"][j]
+            for a in range(512 * j, 512 * j + 512, n):
+                b = a + n
+                rows = ind(vw("YW"), vw("S4", a // 16, b // 16))
+                if j in PAR["alt"]:
+                    bank = vw(PAR["abk"][a // n % len(PAR["abk"])], 0, n)
+                    act(vw("C2", a, b), rows, AF.Copy)
+                    mm([(bank, vw("IN"), vw(zx, a, b)), (bank, vw("IB"), vw("C2", a, b))])
                     act(vw("M", a, b), bank, AF.Relu)
                 else:
                     tt(vw("M", a, b), rows, vw(zx, a, b), OP.max)
+        for h in range(2):
+            pk, pa = "PK%d" % h, "PA%d" % h
+            at(t, "m%d" % h)
+            for j in range(4 * h, 4 * h + 4 if t == 0 else 0):
+                a, b = 512 * j, 512 * j + 512
+                rows = ind(vw("X", 0, W), vw("S16", a // 16, b // 16))
+                bank = vw(["PD0", "PD1", "PU"][j % 3])
+                if j in PAR["c0v"]:
+                    cp(vw("G2", a, b), rows)
+                else:
+                    act(vw("G2", a, b), rows, AF.Copy)
+                mm([(bank, vw("IN"), vw(zx, a, b)), (bank, vw("IB"), vw("G2", a, b))])
+                if j in PAR["r0v"]:
+                    ts(vw("M", a, b), bank, 0.0, OP.max)
+                else:
+                    act(vw("M", a, b), bank, AF.Relu)
             at(t, "g%d" % h)
             for a in range(2048 * h, 2048 * h + 2048 if t else 0, PAR["gch"]):
                 b = a + PAR["gch"]
                 rows = ind(vw("T2", 0, W), vw("S16", a // 16, b // 16))
-                if a >= W - PAR["gv"]:
+                if a // PAR["gch"] in PAR["gv"]:
                     cp(vw("G2", a, b), rows)
                 else:
                     act(vw("G2", a, b), rows, AF.Copy)
             at(t, "a%d" % h)
-            first = [(vw(pk, 0, 256), vw("IF"), vw("BI0")) if t == 0 else (vw(pk, 0, 256), vw("IB"), vw("BI")),
-                     (vw(pk, 128, 256), vw("IG"), hv("HX", h))]
-            if t > 0:
-                first.append((vw(pk, 0, 128), vw("IB"), hv("MV", h)))
-            mm(first, stop=False)
-            mm([(vw(pk, k, 128, 16), vw("M", 2048 * h + k, 2048 * h + 2048, 16), vw("W1", 0, 8)) for k in range(16)], start=False, stop=False)
-            mm([(vw(pk, k, 256, 16), vw("G2", 2048 * h + k, 2048 * h + 2048, 16), vw("W2", 16 * t, 16 * t + 16)) for k in range(16)], start=False)
-            ts(hv("MV", h), vw(pk, 128, 256), 0.0, OP.is_ge, 65536.0, OP.mult)
-            tt(hv("KEY", h), vw(pk, 0, 128), hv("MV", h), OP.add)
-            scan(hv("RR", h), vw("MKN"), hv("KEY", h), OP.add, OP.max)
-            scan(hv("CN", h), vw("MK0", 0, 128), hv("MV", h), OP.mult, OP.add)
-            tt(hv("EQ", h), ind(hv("RR", h), L15), hv("KEY", h), OP.is_equal)
+
+            def lanes(bank, c, n, name, ks, wts, q):
+                return [(vw(bank, c + k, c + k + 16 * n - 15, 16, q[1]) + (q[0], 1),
+                         vw(name, 2048 * h + 16 * q[0] + k, 2048 * h + 16 * q[1], 16), wts) for k in ks]
+            parts = PAR["parts"][h]
+            key, rho, dp = vw(pk, 0, 128), vw(pk, 128, 256), vw(pa, 256, 384)
+            if t:
+                more = [(key, vw("IB"), hv("SG", h)), (key, vw("ONB", p1=8 * t), vw("ONB", p1=8 * t))]
+            else:
+                more = [(vw(pk, 0, 128, 1, 32 * j + 32) + (32 * j, 1), hv(za, 4 * h + j, 32), vw("BZ")) for j in range(4) if 4 * h + j not in PAR["alt"]]
+            mm([(key, vw("IB"), vw("BI")), (rho, vw("IF"), vw("BI0"))] + more, stop=False)
+            news = [(vw(pk, k, 256, 16), vw("IG"), hv("HX", h, 16)) for k in range(16)]
+            mm(news[:15], start=False, stop=False)
+            act(hv("NH0", h, 8), hv("THR", h, 8), bias=col("NB", 2 * t + h), scale=(made(t - 2) - made(t - 3)) / 32768)
+            late = PAR["ml"][h] or t == 0
+            ms = [lanes(pk, 0, 8, "M", range(16), vw("W1", 0, 8), q) for q in (parts if late else [(0, 128)])]
+            gs = [lanes(pk, 0, 16, "G2", range(16), hv("WR", min(t, 1), 16), q) for q in parts]
+            sums = [x for pair in zip(gs, ms) for x in pair] if late else ms + gs
+            for x in sums:
+                mm(x + news[15:] * (x is sums[-1]), start=False, stop=x is sums[-1])
+            ts(hv("SG", h), rho, col("CF", 12), OP.is_gt, 8.0, OP.mult)
+            if t:
+                ts(vw(pk, 384, 512), rho, 8192.0 * t - 6135.5, OP.is_gt, 128.0, OP.mult)
+                tt(vw(pk, 256, 384), key, hv("SG", h), OP.add)
+                tt(hv("KB", h), vw(pk, 384, 512), hv("KEY", h), OP.add)
+                tt(hv("KEY", h), vw(pk, 256, 384), hv("KB", h), OP.min)
+            else:
+                tt(hv("KEY", h), key, hv("SG", h), OP.add)
+            if t:
+                mm([(vw(pa, 271, 384, 16), vw("IB"), vw("C64"))], stop=False)
+                for q in parts:
+                    steps = lanes(pa, 256, 8, "G2", range(16), vw("WK", 0, 8), q) + lanes(pa, 255, 8, "G2", range(1, 16), vw("WK", 8, 16), q)
+                    mm(steps[:16], start=False, stop=False)
+                    mm(steps[16:] + ([(vw(pa, 271, 384, 16), vw("IB"), vw("C64"))] if q == parts[-1] else []), start=False, stop=q == parts[-1])
+            else:
+                mm([(dp, hv("SF", h), vw("DI"))] + [(vw(pa, 271, 384, 16), vw("IB"), vw("C64"))] * 2)
+            scan(hv("CN", h), vw("MK0", 0, 128), hv("SG", h), OP.mult, OP.add)
+            scan(vw(pk, 256, 384), vw("MKN"), hv("KEY", h), OP.add, OP.max)
+            tt(hv("NE", h), vw(pk, 256, 384), hv("KEY", h), OP.not_equal)
+            scan(hv("SC", h), hv("NE", h), dp, OP.mult, OP.add)
             cn = vw("CN", 128 * h + 15, 128 * h + 128, 16)
             tt(hv("BO", h, 8), cn, hv("THR", h, 8), OP.is_gt)
             tt(hv(hs, h, 8), cn, hv("THR", h, 8), OP.not_equal)
-            tt(hv("ZZ", h), hv("PSU", h), hv("EQ", h), OP.mult)
-            scan(hv("SC", h), vw("MK0", 0, 128), hv("ZZ", h), OP.mult, OP.add)
-            tt(hv("DB", h, 8), vw("SC", 128 * h + 15, 128 * h + 128, 16), hv("BO", h, 8), OP.mult)
-            tt(hv("E1", h), ind(hv("DB", h, 8), LC), vw("MR"), OP.mult)
-            mm([(vw(pa, 0, 8), vw("IF"), hv("QD", h, 8))], stop=False)
-            mm([(vw(pa, 0, 8), hv("E1", h), vw("DC"))], start=False)
-            cp(hv("DL", h, 8), vw(pa, 0, 8))
-            cp(hv("FB", h, 128, 256 * t), ind(vw("VS", 0, SN), hv("DL", h, 8)))
+            tt(hv("NH", h, 8), hv(hs, h, 8), hv("NH0", h, 8), OP.mult)
+            tt(hv("XB", h, 8), hv("NH", h, 8), hv("BO", h, 8), OP.add)
+            if PAR["xm"][h]:
+                tt(hv("XM", h), ind(hv("XB", h, 8), LC), vw("MR"), OP.mult)
+                tt(hv("E1", h), ind(hv("SC", h), vw("L15")), hv("XM", h), OP.min)
+            else:
+                tt(hv("DB", h, 8), vw("SC", 128 * h + 15, 128 * h + 128, 16), hv("XB", h, 8), OP.min)
+                tt(hv("E1", h), ind(hv("DB", h, 8), LC), vw("MR"), OP.mult)
+            mm([(vw(pa, 0, 8), hv("E1", h), vw("DC8"))])
+            ts(hv("DL", h, 8), vw(pa, 0, 8), float(Z0 - made(t - 2)), OP.add)
+            cp(hv("FB", h), ind(vw("VS", made(t - 2), H0 + NS * t), hv("DL", h, 8)))
             at(t, None)
-            tt(hv("MH", h), ind(hv(hs, h, 8), LC), vw("MR"), OP.mult)
-            if not last:
-                act(hv("HX", h), ind(hv(hs, h, 8), LC), AF.Copy)
-        if t > 0:
+            ts(hv(wt, h, 8), vw(pa, 0, 8), 0.0, OP.is_equal, 0.125, OP.mult)
+            if last:
+                tt(hv("WW", h, 8), hv("WT0", h, 8), hv("WT1", h, 8), OP.min)
+            fi = hv("FO", t + h) if h == 0 or last else vw("VS", H0 + NS * t + 128, H0 + NS * t + 256)
+            cp(fi, hv("FB", h))
+            if h == 0 and not last:
+                send(vw("VS", H0 + NS * t, H0 + NS * t + 128), fi, "rc", PAR["rem"] + 0.5)
+            ts(hv("PF", h, 128, 256), hv("FB", h), col("CF", 10 + t % 2), OP.add)
+        if t == 0:
+            first_table()
+        elif not last:
             settle_lists(t - 1)
         if not last:
+            blocks()
             mm([(vw("PD0", 256, 272), vw("ONB"), vw("BO"))])
             add("V", 64 * cyc, [vw("PD0", 256, 272)], [col("CF", 9)], ("tensor_reduce", col("CF", 9), vw("PD0", 256, 272)))
             cp(col("AI", 0), col("CF", 9))
             ts(col("AI", 1), col("AI", 0), 31, OP.bitwise_and)
-            ts(col("CF", 12), col("AI", 1), -1.0, OP.mult, col("CF", 7), OP.add)
-            tt(col("CF", 10 + (t + 1) % 2), col("CF", 9), col("CF", 8), OP.add)
+            ts(col("CF", 12), col("AI", 1), 0.5 - 8 * 255 + 8192 * (t + 1), OP.add)
+            act(col("CF", 10 + (t + 1) % 2), col("CF", 9), bias=col("CF", 8))
             tt(vw("TH2"), vw(hp), vw(hs), OP.subtract)
-            ts(vw("THR"), vw("TH2"), 32768.0, OP.mult, 32768.0, OP.add)
+            act(vw("THR"), vw("TH2"), bias=4.0, scale=4.0)
+            mark_new(hs)
         for h in range(2):
-            pa = "PA%d" % h
-            yv, fv = hv("YB", h, 128, 256 * t), hv("FB", h, 128, 256 * t)
+            pa, pk = "PA%d" % h, "PK%d" % h
+            yv = hv("YB", h, 128, 256 * t)
             at(t, "d%d" % h)
             for a in range(2048 * h, 2048 * h + 2048, PAR["dch"]):
                 b = a + PAR["dch"]
-                act(vw("D", a, b), ind(vw("X", 0, W), vw("FB", 256 * t + a // 16, 256 * t + b // 16)), AF.Copy)
+                rows = ind(vw("X", 0, W + 16), vw("FB", a // 16, b // 16))
+                if a // PAR["dch"] in PAR["dv"]:
+                    cp(vw("D", a, b), rows)
+                else:
+                    act(vw("D", a, b), rows, AF.Copy)
             cuts = PAR["cuts"][h]
             at(t, "s%d" % h)
             for a, b in zip(cuts[:-1], cuts[1:]):
@@ -393,84 +476,93 @@ def build(rank, cores, topo):
             mm([(py, vw("IH"), vw("MN", 2048 * h + 15, 2048 * h + 2048, 16))], start=False)
             ts(yv, py, MAGIC, OP.add, MAGIC, OP.subtract)
             if h == 0:
-                dst = cores[(rank + 1 + t % 3) % NR]
-                pairs = [(vw("RY", 128 * t, 128 * t + 128), yv)] + ([] if last else [(vw("RFF", 128 * t, 128 * t + 128), fv)])
-                add("G", 0.5, [p[1] for p in pairs], [], ("send", dst, pairs, "ra%d" % t))
-                add("R", 0.0, [], [p[0] for p in pairs], None, sem="ra%d" % t, after=len(ops) - 1, lat=PAR["rem"], cnt=len(topo.engines(me, dst)))
-            pd, pk = vw("PD%d" % h, 256, 384), "PK%d" % h
-            av = hv(za, h, 128, 256)
-            if PAR["abr"][h]:
-                mm([(pd, vw("IN"), hv(za, h)), (pd, vw("IB"), vw("CQ"))], stop=False)
-                mm([(pd, vw("IH"), vw("MX", 2048 * h + 15, 2048 * h + 2048, 16))], start=False, stop=False)
-                mm([(pd, vw("IH"), vw("MN", 2048 * h + 15, 2048 * h + 2048, 16))], start=False)
-                act(hv("AB", h), pd, AF.Abs)
-                ts(av, hv("AB", h), MAGIC, OP.add, MAGIC, OP.subtract)
+                send(hv("RY", t), yv, "ra", PAR["rem"])
+            pd = vw("PD%d" % h, 256, 384)
+            av = hv(zb, h)
+            mm([(pd, vw("IN"), hv(za, h))], stop=False)
+            mm([(pd, vw("IB"), yv)], start=False)
+            act(av, pd, AF.Abs)
+            pu = vw(pk, 384, 512)
+            if PAR["mz"][h]:
+                tt(hv("MZ", h), yv, hv(za, h), OP.max)
+                mm([(pu, vw("IB"), vw("C7")), (pu, hv(za, h), vw("WBN"))], stop=False)
+                mm([(pu, yv, vw("WBN"))], start=False, stop=False)
+                mm([(pu, hv("MZ", h), vw("WB2"))], start=False)
             else:
-                mm([(pd, vw("IN"), hv(za, h))], stop=False)
-                mm([(pd, vw("IB"), yv)], start=False)
-                act(av, pd, AF.Abs)
-            mm([(vw(pa, 16, 24), av, vw("WG", 0, 8))])
-            cp(hv("UI", h, 8), vw(pa, 16, 24))
-            ts(hv("UA", h, 8), hv("UI", h, 8), 15, OP.bitwise_and)
-            tt(hv("E2", h), ind(hv("UA", h, 8), LC), hv("MH", h), OP.mult)
-            mm([(vw(pk, 256, 272), vw("IF"), hv("QP", h, 16)), (vw(pk, 256, 272), hv("MH", h), hv("RH", h, 16))], stop=False)
-            mm([(vw(pk, 256, 264), hv("E2", h), vw("DCB", 0, 8))], start=False)
-            lb = hv("LB", h, 16, 32 * t)
-            cp(lb, vw(pk, 256, 272))
+                mm([(pu, vw("IB"), vw("C7"))], stop=False)
+                mm([(pu, av, vw("WBD"))], start=False)
+            tt(hv("E2", h), pu, vw("MR"), OP.mult)
+            ts(hv("E3", h), hv("E2", h), -16 * MAGIC, OP.add, 16 * MAGIC, OP.add)
+            pl = vw(pa, 384, 400)
+            mm([(pl, vw("IF"), hv("QP", h, 16)), (vw(pa, 384, 392), vw("IK"), hv(wt, h, 8)), (vw(pa, 392, 400), vw("IS"), hv(wt, h, 8))]
+               + ([(vw(pa, 392, 400), vw("IS"), hv("WW", h, 8))] if last else []), stop=False)
+            mm([(vw(pa, 384, 392), hv("E2", h), vw("DC"))], start=False, stop=False)
+            mm([(vw(pa, 384, 392), hv("E3", h), vw("DCM"))], start=False)
+            cp(hv("LB", h, 16, 32 * t), pl)
             if h == 0:
-                pairs = [(vw("RL", 8 * t, 8 * t + 8), vw("LB", 32 * t, 32 * t + 8))]
-                add("G", 0.5, [pairs[0][1]], [], ("send", dst, pairs, "rb%d" % t))
-                add("R", 0.0, [], [pairs[0][0]], None, sem="rb%d" % t, after=len(ops) - 1, lat=PAR["rem"] - 0.5, cnt=len(topo.engines(me, dst)))
+                send(hv("RL", t, 8), vw("LB", 32 * t, 32 * t + 8), "rb", PAR["rem"] - 0.5)
+            for j in PAR["ho"] if h == 1 and not last else ():
+                at(t, "u%d" % j)
+                if PAR["ywv"][j]:
+                    cp(vw("YW", 1 - j, 256, 2), lands[j][0])
+                else:
+                    act(vw("YW", 1 - j, 256, 2), lands[j][0], AF.Copy)
+                mm([(vw("PU", 0, 128), vw("WS"), lands[j][0])])
+                act(hv("HI", j), vw("PU", 0, 128), scale=col("MR", 1))
             at(t, None)
-            mm([(hv("PSU", h, 128, 256), vw("WBD"), av)])
-            cp(hv("UR", h), hv("PSU", h, 128, 256))
-            act(hv(zb, h), ind(vw(za), vw("LB", 32 * t + 16 * h + 8, 32 * t + 16 * h + 16)), AF.Copy)
-        for j in range(2):
-            pd = "PD%d" % j
-            if j == 0:
-                ys, fs, ls = vw("RY", 128 * t, 128 * t + 128), vw("RFF", 128 * t, 128 * t + 128), vw("RL", 8 * t, 8 * t + 8)
-            else:
-                ys, fs, ls = hv("YB", 1, 128, 256 * t), hv("FB", 1, 128, 256 * t), vw("LB", 32 * t + 16, 32 * t + 24)
+            mm([(hv("PF", h), vw("CU"), vw("ONB")), (hv("PF", h), vw("WBD"), av)])
+            act(hv("UR", h), hv("PF", h), bias=MAGIC * W)
+            act(hv("UB", h), hv("UR", h), bias=-MAGIC * W)
+            mm([(hv("PU", h, 128, 256), vw("WBD"), av), (hv("PU", h, 128, 256), vw("IN"), hv("UB", h))])
+            fi = hv("FO", t + h) if h == 0 or last else vw("VS", H0 + NS * t + 128, H0 + NS * t + 256)
+            tt(hv("PR", h), fi, hv("PU", h, 128, 256), OP.mult)
+            ts(hv("PR", h), hv("PR", h), 5, OP.arith_shift_right)
+            tt(hv("PR2", h), hv("PR", h), hv("PF", h, 128, 256), OP.add)
+            ts(hv("VS", h, 128, made(t)), hv("PR2", h), 4095, OP.bitwise_and)
+
+        def look(j):
             at(t, "x%d" % j)
             if not last:
-                if PAR["dda"][j]:
-                    act(hv("OLD", j), ind(vw("X"), ls), AF.Copy)
-                else:
-                    tt(hv("DD", j), ind(vw("X"), ls), ys, OP.subtract)
+                act(hv("OLD", j), ind(vw("X"), lands[j][1]), AF.Copy)
+                if not PAR["dda"][j]:
+                    tt(hv("DD", j), ind(vw("X"), lands[j][1]), lands[j][0], OP.max)
+        if PAR["both"]:
+            look(0)
+            look(1)
+        for j in PAR["jo"]:
+            ys, ls = lands[j]
+            if not PAR["both"]:
+                look(j)
+            at(t, "x%d" % j)
             cp(ind(vw("X"), ls), ys)
             at(t, "u%d" % j)
             if not last:
+                pd = vw("PD%d" % j, 0, 128)
+                first = [(pd, vw("IB"), vw("QS")), (pd, vw("WS"), ys), (pd, vw("IN"), hv("HI", j))]
                 if PAR["dda"][j]:
-                    mm([(vw(pd, 128, 256), vw("IN"), ys), (vw(pd, 128, 256), vw("IB"), hv("OLD", j))])
-                    act(hv("AD", j), vw(pd, 128, 256), AF.Abs)
+                    pe = vw("PA%d" % j, 128, 256)
+                    mm(first, stop=False)
+                    mm([(pe, vw("IN"), ys)], stop=False)
+                    mm([(pe, vw("IB"), hv("OLD", j))], start=False)
+                    act(hv("DD", j), pe, AF.Abs)
+                    mm([(pd, vw("AP"), hv("DD", j))], start=False)
                 else:
-                    act(hv("AD", j), hv("DD", j), AF.Abs)
-                mm([(vw(pd, 0, 128), vw("BD"), hv("AD", j))])
-                act(hv("SG", j), vw(pd, 0, 128), AF.Sign, bias=col("CF", 12))
-                mm([(vw(pd, 128, 256), vw("AP"), ys), (vw(pd, 128, 256), vw("RKW", 128 * (t + 1), 128 * (t + 2)), hv("SG", j))])
-                act(hv("TN", j), vw(pd, 128, 256), AF.Identity, bias=col("BT", t + 1))
+                    mm(first + [(pd, vw("APN"), ys)], stop=False)
+                    mm([(pd, vw("APN"), hv("OLD", j))], start=False, stop=False)
+                    mm([(pd, vw("AP2"), hv("DD", j))], start=False)
+                if PAR["tna"][j]:
+                    act(hv("TN", j), pd, bias=col("BT", 2 * t + j))
+                else:
+                    ts(hv("TN", j), pd, col("BT", 2 * t + j), OP.add)
                 cp(ind(vw("T2"), ls), hv("TN", j))
-                at(t, None)
-                cp(ind(vw("VS", 0, WD), ls), fs)
         if last:
             at(t, "out")
             for j in range(2):
                 dma("SA"[j], ("$", "yx", 2048 * j, 2048 * j + 2048), vw("X", 2048 * j, 2048 * j + 2048), 5.5)
         at(t, None)
-        ts(vw("UR"), vw("UR"), 4095, OP.bitwise_and)
-        cp(vw("PF", 0, 256), vw("FB", 256 * t, 256 * t + 256))
-        tt(vw("PR"), vw("PF", 0, 256), vw("UR"), OP.mult)
-        act(vw("PF", 256, 512), vw("PF", 0, 256), AF.Identity, bias=col("CF", 10 + t % 2))
-        ts(vw("PR"), vw("PR"), 5, OP.arith_shift_right)
-        tt(vw("PR2"), vw("PF", 256, 512), vw("PR"), OP.add)
-        ts(vw("VS", SN, SN + NS), vw("PR2"), 4095, OP.bitwise_and)
         if t < TS - 2:
             for k in range(16):
-                o = vw("ZX%d" % ((t + 1) % 2), k, W, 16)
-                if k < PAR["zact"]:
-                    act(o, vw(zb, 0, 256), AF.Copy)
-                else:
-                    asel(o, vw(zb, 0, 256), [[0, 256]], OP.is_ge, 1, 0)
+                asel(vw("ZX%d" % ((t + 1) % 2), k, W, 16), vw(zb), [[0, 256]], OP.is_ge, 1, 0)
     settle_lists(TS - 1)
     zf = "ZA%d" % (TS % 2)
     for h in range(2):
@@ -484,7 +576,7 @@ def build(rank, cores, topo):
 def depend(ops):
     seen = {}
     for n, o in enumerate(ops):
-        dep, reads = set(), set()
+        dep = set()
         if "after" in o:
             dep.add(o["after"])
         for v, w in [(v, False) for v in o["r"]] + [(v, True) for v in o["w"]]:
@@ -495,15 +587,12 @@ def depend(ops):
                     dep.add(m)
                 elif (w or uw) and clash(u, v):
                     dep.add(m)
-                    if uw:
-                        reads.add(m)
         o["dep"] = dep
-        o["soft"] = {m for m in dep if ops[m]["eng"] == o["eng"] and "sem" not in ops[m] and "sem" not in o
-                     and ((o["eng"] in PAR["soft"] and m not in reads) or (o["eng"] == "P" and o["goon"]))}
+        o["soft"] = {m for m in dep if ops[m]["eng"] == o["eng"] == "P" and o["goon"]}
         for v, w in [(v, False) for v in o["r"]] + [(v, True) for v in o["w"]]:
             lst = seen.setdefault(v[0], [])
             if w and v[0] not in PS:
-                lst[:] = [e for e in lst if not (v[3] == 1 and v[4] == 128 and v[1] <= e[1][1] and e[1][2] <= v[2])]
+                lst[:] = [e for e in lst if not (v[3] == 1 and v[4] == 128 and len(v) == 5 and v[1] <= e[1][1] and e[1][2] <= v[2])]
             lst.append((n, v, w))
 
 
@@ -542,43 +631,46 @@ def improve(ops, order):
                 m |= anc[d] | (1 << d)
         anc[i] = m
         pred.append(keep)
-    keys, base = [o["key"] for o in ops], [100 * o["step"] for o in ops]
+    names = {}
+    keys = [names.setdefault(o["key"], len(names)) for o in ops]
+    base = [100 * o["step"] for o in ops]
     st = place(ops, order, pred, False)[0]
-    mark = [st[i] for i in range(n) if keys[i].endswith("VMV0")]
-    fine = {}
+    mark = [st[i] for i in range(n) if ops[i]["key"].endswith("VKEY0")]
+    fine = [0.0] * len(names)
     for t in (4, 1, 3, 2, 0, 5):
         for i in range(n):
             if ops[i]["step"] == t:
                 fine[keys[i]] = (st[i] - mark[t]) / (mark[3] - mark[2]) * 100
 
     gaps = [[(d, 0.0 if d in ops[i]["soft"] else hop) for d in pred[i]] for i in range(n)]
-    kind = [(o["eng"], o["cost"], o.get("lat", 0.0)) for o in ops]
+    kind = [(gaps[i], "VAPGSR".index(o["eng"]), o["cost"], o.get("lat", 0.0)) for i, o in enumerate(ops)]
+    edges = [(i, d) for i in range(n - 1, -1, -1) for d in pred[i]]
+    both = list(zip(base, keys))
 
     def rate(f):
-        pr = [base[i] + f[keys[i]] for i in range(n)]
-        for i in range(n - 1, -1, -1):
-            p = pr[i]
-            for d in pred[i]:
-                if p < pr[d]:
-                    pr[d] = p
+        pr = [b + f[k] for b, k in both]
+        for i, d in edges:
+            if pr[i] < pr[d]:
+                pr[d] = pr[i]
         st, en = [0.0] * n, [0.0] * n
-        busy = {e: [] for e in "VAPGS"}
-        for i in sorted(range(n), key=lambda j: pr[j]):
+        busy = [([], []) for _ in range(5)]
+        for _p, i in sorted(zip(pr, range(n))):
             r = 0.0
-            for d, x in gaps[i]:
+            gap, e, c, lat = kind[i]
+            for d, x in gap:
                 x += en[d]
                 if x > r:
                     r = x
-            e, c, lat = kind[i]
-            if e != "R":
-                iv = busy[e]
-                m = k = len(iv)
-                while k and iv[k - 1][1] > r:
+            if e < 5:
+                lo, hi = busy[e]
+                m = k = len(hi)
+                while k and hi[k - 1] > r:
                     k -= 1
-                while k < m and iv[k][0] < r + c:
-                    r = iv[k][1]
+                while k < m and lo[k] < r + c:
+                    r = hi[k]
                     k += 1
-                iv.insert(k, (r, r + c))
+                lo.insert(k, r)
+                hi.insert(k, r + c)
             st[i] = r
             en[i] = r + c + lat
         return max(en), st, en, pr
@@ -587,9 +679,9 @@ def improve(ops, order):
         before = {(ops[i]["eng"], round(st[i] + ops[i]["cost"], 6)): i for i in range(n)}
         i, pairs = max(range(n), key=lambda j: en[j]), []
         while True:
-            b = max(pred[i], key=lambda d: en[d]) if pred[i] else None
+            b, x = max(gaps[i], key=lambda p: en[p[0]] + p[1]) if pred[i] else (None, 0)
             j = before.get((ops[i]["eng"], round(st[i], 6)))
-            if b is not None and en[b] + (0 if b in ops[i]["soft"] else hop) >= st[i] - 1e-6:
+            if b is not None and en[b] + x >= st[i] - 1e-6:
                 i = b
             elif j is not None and j != i:
                 pairs.append((j, i))
@@ -603,28 +695,58 @@ def improve(ops, order):
         seed[0] = (seed[0] * 1103515245 + 12345) % 2147483648
         return seed[0] / 2147483648
 
-    cur, st, en, pr = rate(fine)
-    best, pairs = (cur, st), chain(st, en)
-    for it in range(PAR["tries"]):
-        f = dict(fine)
-        j, i = pairs[int(rnd() * len(pairs))]
-        u = rnd()
-        if u < 0.4:
-            f[keys[i]] = pr[j] - base[i] - 0.01 - rnd() * rnd() * 3
-        else:
-            p = pr[i] + 0.01 + rnd() * rnd() * 6 if u < 0.8 else pr[j] + rnd() * 30
-            todo, seen = [j], set()
-            while todo:
-                x = todo.pop()
-                if x not in seen and x != i:
-                    seen.add(x)
-                    f[keys[x]] = max(f[keys[x]], p - base[x])
-                    todo += [y for y in succ[x] if pr[y] < p]
-        v, st, en, pr2 = rate(f)
-        if v <= cur - (0.15 * (1 - it / PAR["tries"]) + 1e-4) * math.log(rnd() + 1e-12):
-            fine, cur, pr, pairs = f, v, pr2, chain(st, en)
-            if v < best[0]:
-                best = (v, st)
+    def strict(f):
+        pr = [b + f[k] for b, k in both]
+        for i, d in edges:
+            if pr[i] < pr[d]:
+                pr[d] = pr[i]
+        st, en = [0.0] * n, [0.0] * n
+        free = [0.0] * 6
+        for _p, i in sorted(zip(pr, range(n))):
+            gap, e, c, lat = kind[i]
+            r = free[e]
+            for d, x in gap:
+                x += en[d]
+                if x > r:
+                    r = x
+            st[i] = r
+            r += c
+            if e < 5:
+                free[e] = r
+            en[i] = r + lat
+        return max(en), st, en, pr
+
+    best = None
+    for rate, tries, heat in ((rate, PAR["tries"], PAR["heat"]), (strict, PAR["tries2"], PAR["heat2"])):
+        if best:
+            st = best[1]
+            mark = [st[i] for i in range(n) if ops[i]["key"].endswith("VKEY0")]
+            for t in (4, 1, 3, 2, 0, 5):
+                for i in range(n):
+                    if ops[i]["step"] == t:
+                        fine[keys[i]] = (st[i] - mark[t]) / (mark[3] - mark[2]) * 100
+        cur, st, en, pr = rate(fine)
+        best, pairs = min(best or (1e9,), (cur, st)), chain(st, en)
+        for it in range(tries):
+            f = list(fine)
+            j, i = pairs[int(rnd() * len(pairs))]
+            u = rnd()
+            if u < 0.4:
+                f[keys[i]] = pr[j] - base[i] - 0.001 - rnd() ** 3 * 3
+            else:
+                p = pr[i] + 0.001 + rnd() ** 3 * 6 if u < 0.8 else pr[j] + rnd() * 30
+                todo, seen = [j], set()
+                while todo:
+                    x = todo.pop()
+                    if x not in seen and x != i:
+                        seen.add(x)
+                        f[keys[x]] = max(f[keys[x]], p - base[x])
+                        todo += [y for y in succ[x] if pr[y] < p]
+            v, st, en, pr2 = rate(f)
+            if v <= cur - (heat * (1 - it / tries) + 1e-4) * math.log(rnd() + 1e-12):
+                fine, cur, pr, pairs = f, v, pr2, chain(st, en) or pairs
+                if v < best[0]:
+                    best = (v, st)
     return sorted(range(n), key=lambda i: (best[1][i] if pred[i] or "sem" not in ops[i] else -1.0, i))
 
 
@@ -701,6 +823,8 @@ def rank_program(g, core, T, topo):
             t = T[v[1]]
             return t[:] if v[3] - v[2] == t.shape[1] else t[:, v[2]:v[3]]
         t = T[v[0]]
+        if len(v) > 5:
+            return t[v[5]:v[4]:v[6], v[1]:v[2]:v[3]]
         if v[3] == 1:
             return t[0:v[4], v[1]:v[2]]
         return t[0:v[4], v[1]:v[2]:v[3]]
@@ -720,14 +844,8 @@ def rank_program(g, core, T, topo):
         if c[0] == "send":
             dst, pairs, sem = c[1], c[2], c[3]
             rid, pid = topo.addr(dst)[0], topo.addr(dst)[1]
-            eng = topo.engines(core, dst)
-            if len(pairs) == 1:
-                g.remote_dma(ap(pairs[0][0]), ap(pairs[0][1]), T.sem[sem], T.sem["sent"], pid, rid, topo.mask(core, dst))
-            else:
-                k = len(eng) // len(pairs)
-                g.remote_dma_fused([RemoteDMATransfer(dst_ids=[DstId(rid=rid, pnc=pid)], dma_engine_mask=sum(1 << x for x in eng[k * j:k * j + k]),
-                                                      remote_sem=T.sem[sem], src=ap(p[1]), dst=ap(p[0])) for j, p in enumerate(pairs)], local_sem=T.sem["sent"])
-            sent += len(eng)
+            g.remote_dma(ap(pairs[0][0]), ap(pairs[0][1]), T.sem[sem], T.sem["sent"], pid, rid, topo.mask(core, dst))
+            sent += len(topo.engines(core, dst))
             continue
         if c[0] == "dma":
             q.dma_start(ap(c[1]), ap(c[2])).then_inc(T.sem[o["sem"]], 16)

@@ -1,5 +1,3 @@
-import math
-from concourse.bass import DstId, RemoteDMATransfer
 from concourse.mybir import AluOpType, AxisListType, ActivationFunctionType
 
 OP = AluOpType
@@ -10,45 +8,105 @@ Z0 = NS * (TS + 1)
 V0 = Z0 + 128
 H0 = V0 + W
 MAGIC = 12582912.0
+KU = 2.0 ** -14
+RU = 2.0 ** -30
+LOW = -(4095 << 12) - 1
 
 B, F, I, U = "bfloat16", "float32", "int32", "uint16"
 SB = {
-    "X": (WD, B), "T2": (WD, B), "VS": (H0 + NS * (TS - 1), I), "VW": (2048, I),
-    "M": (W, B), "G2": (W, B), "D": (W, B), "MX": (W, B), "MN": (W, B), "ZX0": (W, B), "ZX1": (W, B),
-    "ZA0": (256, B), "ZA1": (256, B), "ZR": (256, B), "SR": (256, I), "S16": (256, U), "SF": (256, F),
+    "X": (WD, B), "VS": (H0 + NS * (TS - 1), I), "TB": (256, B), "YW": (256, B), "SEL": (2048, B),
+    "M": (W, B), "G2": (W, B), "D": (W, B), "MX": (W, B), "MN": (W, B), "ZX0": (W, B), "ZX1": (W, B), "C2": (W, B),
+    "ZA0": (256, B), "ZA1": (256, B), "ZR": (256, B), "SR": (256, I), "S16": (256, U), "SF": (256, F), "B16": (256, B), "S4": (256, U),
     "WI": (8, I), "TI": (8, I), "WM": (256, I), "WMF": (256, F), "CF": (32, F), "PI": (16, I),
-    "JF": (144, F), "RF": (128, F), "GF": (128, F), "IF": (128, F), "IB": (128, B), "IH": (128, B),
-    "IN": (128, B), "IG": (128, B), "IK": (128, B), "IS": (128, B), "BD": (128, B), "MR": (128, F), "WBD": (128, B),
-    "ONF": (128, F), "ONB": (128, B), "CQ": (128, B), "CU": (128, B), "TMP": (128, F), "TM2": (128, F), "DI": (128, F),
-    "WO": (144, B), "WS": (128, B), "AP": (128, B), "AP2": (128, B), "APN": (128, B), "QS": (128, B), "BS": (16, F), "L15": (8, U),
-    "YW": (256, B), "S4": (256, U), "C2": (W, B), "KB": (256, F), "HX": (32, B), "BZ": (128, B), "XM": (256, F), "MZ": (256, B), "WB2": (128, B), "WBN": (128, B),
-    "DC": (8, F), "DC8": (8, F), "DCN": (8, F), "DCM": (8, F), "W1": (16, B), "WK": (16, B), "WR": (32, B), "BT": (16, F),
-    "BI0": (128, F), "BI": (128, B), "QP": (32, F), "Q16": (16, F),
-    "CT": (1024, B), "MK0": (512, B), "MKB": (512, B), "MKN": (128, B), "OLD": (256, B), "LS": (8, U),
-    "SG": (256, B), "KEY": (256, F), "NE": (256, F), "SC": (256, F), "CN": (256, B), "NH": (16, F), "XB": (16, F),
-    "BO": (16, B), "HS0": (16, B), "HS1": (16, B), "THR": (16, F), "TH2": (16, F), "DB": (16, F), "E1": (256, F), "E2": (256, F),
-    "WT0": (16, B), "WT1": (16, B), "WW": (16, B), "DL": (16, U), "C7": (128, B), "C64": (8, B), "NB": (16, F), "NH0": (16, F), "E3": (256, F),
-    "FB": (256, U), "FO": (128 * TS + 128, I), "YB": (256 * TS, B), "LB": (32 * TS, U),
-    "RY": (128 * TS, B), "RL": (8 * TS, U),
-    "DD": (256, B), "HI": (256, B), "TN": (256, B), "UR": (256, F), "UB": (256, B),
-    "PR": (256, I), "PR2": (256, I), "AI": (8, I), "OS": (256, F), "OZ": (256, B),
+    "JF": (144, F), "RF": (128, F), "GF": (128, F), "IF": (128, F), "INF": (128, F), "IF8": (128, F), "IN8": (128, F),
+    "IB": (128, B), "IH": (128, B), "IN": (128, B), "IK": (128, B), "IS": (128, B), "I4": (128, B), "IN4": (128, B),
+    "IP": (128, B), "IM": (128, B), "IQ": (128, B),
+    "BD": (128, B), "MR": (128, F), "WBD": (128, B), "ONF": (128, F), "ONB": (128, B), "CQ": (128, B), "CU": (128, B),
+    "CA": (128, B), "CM": (128, B), "C7": (128, B), "CB": (56, B), "TMP": (128, F), "TM2": (128, F), "DI": (128, F), "DJ": (128, B),
+    "WO": (144, B), "WS": (128, B), "AP": (128, B), "AP2": (128, B), "APN": (128, B), "L15": (8, U), "LS": (8, U),
+    "BZ": (128, B), "XM": (128, F), "MZ": (256, B), "WB2": (128, B), "WBN": (128, B), "HT": (128, B), "GS": (256, B),
+    "DC": (16, F), "DC8": (8, F), "DCM": (16, F), "W1": (8, B), "WR": (40, B),
+    "BI0": (128, F), "BI1": (128, F), "BI": (128, B), "QP": (32, F), "QL": (8, B), "Q16": (16, F),
+    "MK0": (512, B), "MKB": (512, B), "MKN": (128, B),
+    "UW": (256, B), "SG0": (256, B), "SG1": (256, B), "KS": (256, F), "KEY": (256, F), "NE": (256, F), "SC": (256, F), "CN": (256, B),
+    "C1": (256, F), "NH": (16, F), "XB": (16, F), "BO": (16, B), "HS0": (16, B), "HS1": (16, B), "THR": (16, F), "TH2": (16, F),
+    "DB": (16, F), "E1": (256, F), "E2": (256, F), "E3": (256, F), "WT0": (16, B), "WT1": (16, B), "WW": (16, B), "DL": (16, U),
+    "NB": (16, F), "NH0": (16, F), "FI": (256, I), "FB": (256 * TS, U), "FF": (256, F), "YB": (256 * TS, B), "LB": (64 * TS, U),
+    "RY": (128 * TS, B), "RP": (16, B), "RV": (128 * TS, U), "DD": (256, B), "DR": (256, B), "HI": (256, B), "UR": (256, F),
+    "PR": (256, F), "PR2": (256, I), "AI": (8, I), "OS": (256, F), "OZ": (256, B),
 }
 PS = ["PK0", "PK1", "PU", "PA0", "PA1", "PD0", "PD1", "PF"]
-SCRATCH = {k: ("sbuf", [128, v[0]], v[1]) for k, v in SB.items()}
+SHARE = {}
+for _k, _v in SB.items():
+    if _v[0] == 128 and _v[1] in (B, F) and _k != "XM":
+        SHARE[_k] = ("K" + _v[1], 128 * sum(x[0] == "K" + _v[1] for x in SHARE.values()))
+SCRATCH = {k: ("sbuf", [128, v[0]], v[1]) for k, v in SB.items() if k not in SHARE}
+SCRATCH.update({"K" + d: ("sbuf", [128, 128 * sum(x[0] == "K" + d for x in SHARE.values())], d) for d in (B, F)})
 SCRATCH.update({k: ("psum", [128, 512], F) for k in PS})
-NDMA = 24
+NDMA = 16
 SEMAPHORES = (["qV", "qA", "qP", "qG", "sent"] + ["d%d" % k for k in range(NDMA)]
-              + ["r%s%d" % (x, t) for x in "abc" for t in range(TS)])
+              + ["r%s%d" % (x, t) for x in "abc" for t in range(TS)] + ["rd%d" % (TS - 1)])
 
-PAR = {"cyc": 0.00083 * 1.1, "pe": 0.00042 * 1.3, "gat": 1.55, "sca": 3.5, "hop": 0.2, "pass": 4, "heat": 0.15, "tries2": 16000, "heat2": 0.4, "pool": 1.3,
-       "mch": (256,) * 8, "gch": 512, "dch": 512, "rem": 3.0, "alt": (0, 1, 4), "abk": ("PA0",), "ywv": (1, 1), "c0v": (0, 1, 4), "r0v": (), "seed": 2, "tries": 2000,
-       "ach": 256, "zi": (7, 3), "abr": (0, 0), "gv": (2, 3), "dv": (), "both": 1, "jo": (1, 0), "ml": (0, 0), "sv": 1, "dda": (0, 0), "tna": (1, 1), "xm": (1, 0), "parts": (((0, 96), (96, 128)), ((0, 96), (96, 128))), "ho": (1, 0), "mz": (1, 1),
-       "cuts": ([0, 512, 1024, 1536, 2048], [0, 512, 1024, 1536, 2048]),
-       "order": {"g0": 10, "m0": 12, "a0": 14, "g1": 16, "m1": 18, "d0": 20, "a1": 22, "d1": 24, "s0": 30, "y0": 32,
-                 "s1": 26, "y1": 28, "u0": 40, "u1": 36, "x0": 34, "x1": 35, "out": 50}}
-LATE = 10000
-PER = {"YB": 256, "LB": 32, "RY": 128, "RL": 8, "FO": 128}
-KEPT = {}
+PAR = {
+    "alt": {0: ("PK0", "PA1"), 7: ("PA1", "PU")},
+    "mcut": list(range(0, W + 1, 256)), "dv": (), "old": (0, 0), "xm": 1, "mz": 2, "ba": 0, "ya": 0, "so": 0,
+    "gv": (0,),
+    "cuts": ([0, 512, 1024, 1536, 1856, 2048], [0, 512, 1024, 1536, 2048]),
+    "dvl": (),
+    "c0v": (3, 4), "f0": (1, 2),
+    "zi": (6, 5),
+    "sets": ((("G2", 0, 64), ("M", 0, 128), ("G2", 64, 96), ("G2", 96, 128)), (("G2", 0, 96), ("M", 0, 96), ("G2", 96, 128), ("M", 96, 128))),
+}
+STEP = """VUW0 +VPR128 PU.INC2 PK0.INUW PD1.B1BI PA0.IPUW VSG0 VM2816 VCN0 VKS0 +VVS0 VHS0 VBO0 VKEY0 VM2304 VNH0 VPK0256 AM3584 AG23584 AM3840
+ANH08 PD1.G2WR PD1.MW1 VXB0 +VPR2128 VNE0 VXM0 VSC0 +VVS128 VE10 +VX0_ PD1.G2WR_ PD1.MSG VUW128 PA0.E1DC PA1.B1CB PK0.IBWB PA1.IPUW PK1.INUW VDL0
+VSG128 VFB0 VKS128 VCN128 VWT0 GFB0 VFF0 VKEY128 VHS8 VBO8 VPK1256 AD1856 VNH8 VTH20 PD0.ONBO PA0.IBCQ VMN1856 VNE128 VMX1856 VCF9 VXB8 AD0 AD512
+AD1536 VSC128 VMN0 VDB8 VMX0 VE1128 PD1.INZA PU.HSIB PK1.IBWB PA1.E1DC VMX512 VMN512 VDL8 VMX1536 VMN1536 VFB128 AD1024 VMX1024 VMN1024 VSF0 APF256
+AD2048 AD2560 RRV0 PA0.IHMX PA0.IHMN PD0.INZA VYB0 PD0.IBYW AD3072 AZA0 AD3584 GYB0 VWT8 VAI0 VPF384 VMZ0 VB160 VMN2048 PK0.YBWB PA1.IBCQ PA0.IFWT
+PK0.MZWB VE20 VMN2560 VE30 PA0.E2DC PA0.E3DC PF.CUZA VMX2560 VMX3072 AUR0 AHT0 VLB0 VMX2048 VMN3072 RRY0 PU.INZA VMX3584 VMN3584 PA1.IHMX VAI1 VS40
+VVS6016 PA1.IHMN VCF12 VPR0 VYW0 VVS6017 VMZ128 VPR20 PD1.IBYW PU.WSYW PK1.YWWB PK1.MZWB ATHR0 ACF10 AZA128 AHI128 VE2128 GLB0 RLB48 PA1.IFWT
+PA0.WSHI PU.WSRY PF.CUZA_ PA1.E2DC VYW1 VE3128 -VM1536 -AC20 PA1.E3DC VLB24 -VM768 VDD128 VDD0 VDR128 VRP0 -VM2048 VDR0 -VM1280 -VM512 -VM1792
+GZX15 GZX8 GZX7 GZX13 GZX6 GZX14 GZX2 GZX12 GZX10 GZX1 GZX11 GZX3 GZX9 GZX4 GZX0 GZX5 -PD0.B1BI -PK0.INC2 AHI0 PA0.WSHI_ PA0.APDD PA0.APDR PA0.SERP
+PA0.APDD_ PA0.APDR_ -ANH00 -AC2256 AUR128 -AC23840 -AM0 -AC23584 -PA1.INC2 ATB0 ATB1 -AM256 -AG2512 -AG21024 -AG21536 -AG23072 -AG22560 -AG22048
+-VG20 -VM1024 PU.INZA_ -PK0.IFUW -PA1.INC2_ -PA0.B1CB -PK1.IFUW -PD0.G2WR -PD0.MW1 -VM3328 -VM2560 -VM3072 VX0 -PD0.G2WR_ -PD0.G2SG"""
+FIRST = """iSX4112 iGPI0 iGJF0 iGGF0 iGRF0 iVCB0 iVONF0 iVCU0 iVPI2 iVPI3 iVPI1 iVCF0 iVCQ0 iVVS1792 iGNB4 iGNB0 iGCB16 iVIF0 iVMKB0 iVCF17 iVBD0
+iVDC0 iVCF18 iVCF4 iVCU0_ iVCA0 iVTM20 iVONB0 iVCF7 iVZA128 iVZA0 iVCF5 iGZX8 iGQL0 iGZX7 iGZX9 iGZX6 iGZX10 iGSEL1024 iVC70 iVMK00 iVMR0 iVMKN0
+iVCF15 iVZX15 iVWMF0 iVZX11 iVSF0 iPD1.WMIF iAIH0 iAI40 iAIS0 iAIB0 iAWR0 iAW10 iADC80 iANB0 iAIK0 iAWR8 iAIF80 iAZX5 iAZX0 iATMP0 iABZ0 iAZX2
+iAIP0 iVAP0 iVDC8 iVQ160 iPF.ONTM iPD1.WMIF_ iAAP20 iAIN0 iAZX3 iABI0 iAZX1 iABI00 iAZX4 iAIN80 iABI10 iAQP8 iVS16128 iVZX14 iVTHR0 iVQP24 iVS160
+iVZX12 aANH00 iVTM20_ iVX4096 iVLS0 iVHS0 iVCM0 iVSF128 iVZX13 iVMKN0_ aVB160 iVL150 iVCB8 iVMK00_ iVWO0 iVQP0 iGSEL512 iGSEL0 iGSEL1536 iGGS0
+iGSEL2 iGGS128 iVCF13 aVS40 iVCF6 aVG21536 iVCF12 iVVS128 aPK1.IBBZ aPK0.IBBZ aPK0.INHS aAG20 aPD0.ING2 aPA1.ING2 aPK1.INHS aAG21024 aAG2512 aAM0
+aAM1536 aPK0.G2WR aAG23072 aAG22560 aVM1024 aVM512 aVG22048 iVCF14 iVVS4480 iVDI0 aPK0.MW1 aPK0.G2WR_ aPK0.MHS aPD0.ING2_ aPU.ING2 aPA0.SFCB
+aAG23584 aAM2048 aVSG0 iVVS0 aVCN0 aVKEY0 aVHS0 aVBO0 aPD1.ING2 aPK1.G2WR aVPK0256 aVNH0 iVVS3968 aVXB0 aVNE0 aVXM0 aVSC0 iVVS5504 aVE10
+aPD0.ING2_2 aAM2560 aAM3072 iADCM0 iAWBD0 aAM3584 iADJ0 aANH08 iACB16 iAWBN0 aPA0.E1DC iVVS4992 aPK1.MW1 aPK1.G2WR_ aPK1.MHS aPA1.SFCB aVDL0 aVFI0
+aVWT0 iVMKB0_ iVCF10 aVFB0 aVSG128 iAWB20 iAWR16 aAD1024 iAINF0 aAD1536 aVFF0 aAD0 aAD1856 iAWR24 aAD512 aAPF256 aVCN128 aVKEY128 aVHS8 aVPK1256
+aVBO8 aVNH8 aVNE128 iVWS0 aVXB8 aVSC128 aVMN1024 aGFB0 aRRV0 aVDB8 aVMN1536 aVMX1536 aVE1128 aPD0.ONBO aPU.HSIB aPA1.E1DC aPK1.IBWB aVMX1024 aVMN0
+aVDL8 aVMX1856 aVMN1856 aVFI128 aVMX0 aVFB128 aVMX512 aVMN512 aAD3584 aAD3072 aPA0.IBCQ aPK0.IBWB aPA0.IHMX aPA0.IHMN aVWT8 aVPF384 aVCF9 aVYB0
+aVTH20 aVMZ0 aPD1.INZA aPK0.YBWB aVMN3584 iVCA0_ aPK0.MZWB aPD0.INZA aAD2560 aAD2048 aPA1.IBCQ aVE20 aVMX3072 aVE30 aVMX3584 iVCF8 aPA0.IFWT
+aPA0.E2DC aPD0.IBYW aPA0.E3DC aAZA0 aAHT0 aPF.CUZA aGYB0 aRRY0 aVMN2560 aVLB0 aVMX2560 aVMN3072 aVMX2048 aVMN2048 aATHR0 iAAPN0 aAUR0 iAWR32 iAIN40
+iAIQ0 aPA1.IHMX aPA1.IHMN aPU.INZA aGLB0 aRLB48 aVVS6016 aVAI0 aVYW0 aPD1.IBYW aPK1.YWWB aVMZ128 aPK1.MZWB aVPR0 aVAI1 aPU.WSYW aPA1.IFWT aVE2128
+aAZA128 iAIM0 aAHI128 aVYW1 aPA1.E2DC aVPR20 aVE3128 aPA1.E3DC VM512 aVLB24 VM2560 aVDD128 aVDD0 aVDR128 aVRP0 VM1536 aVDR0 aVCF12 VM1280 VM1024
+aPU.WSRY aPA0.WSHI aPF.CUZA_ PK1.IFMK aGZX9 aGZX15 aGZX2 aGZX8 aGZX5 aGZX10 aGZX4 aGZX3 aGZX1 aGZX0 aGZX7 aGZX12 aGZX14 aGZX13 aGZX11 aGZX6 AC23584
+AC20 PK0.INC2 ANH00 aAUR128 aAHI0 aPA0.WSHI_ AC2256 AC23840 aACF10 AM0 aPA0.APDD aPA0.APDR aPA0.SERP aPA0.APDD_ aPA0.APDR_ aATB0 aATB1 PA1.INC2
+AM256 AG2512 AG21024 AG21536 VM1792 VG20 VM768 VM3072 VM3328 PD0.B1BI aPU.INZA_ PA1.INC2_ PA0.B1CB aVPR128 PD0.G2WR PD0.MW1 VM2816 PD0.G2WR_
+PD0.G2SG aVVS6017 VUW0 PU.INC2 PK0.IFMK PK0.INUW aVVS0 VSG0 VC10 VCN0 PD1.B1BI PA0.INC1 AG22048 ANH08 AG23072 AG22560 AM3840 AM3584 AG23584
+PD1.G2WR VKS0 VHS0 VBO0 VKEY0 VNH0 VM2048 VPK0256 VXB0 VM2304 VNE0 VXM0 VSC0 aVX0 VE10 PD1.MW1 PD1.G2WR_ PA0.E1DC PD1.MSG aVX0_ VDL0 aVPR2128
+VUW128 PA1.B1CB PK0.IBWB PK1.INUW VFI0 VSG128 VFB0 VKS128 VCN128 VC1128 VKEY128 VHS8 aVVS128 VPK1256 VBO8 VWT0 VNH8 PA1.INC1 VNE128 VFF0 VXB8
+VSC128 AD0 GFB0 AD1536 AD512 RRV0 VMN0 VDB8 VMX0 VE1128 VMX1536 PA1.E1DC VMN512 VDL8 VTH20 AD1856 VMX1856 VMN1856 VFI128 VMN1536 VWT8 AD1024
+APF256 ATHR0 VFB128"""
+LAST = """zVM768 VDD128 zVM1792 VDR128 VRP0 VDD0 zVM1280 VDR0 ATHR0 zANH00 AHI128 zAC20 zPK1.IFUW PU.WSRY zAC2256 zPK0.INC2 PA0.WSHI zPA1.INC2
+PD1.IBYW AHI0 zAM0 zAC23840 zANH08 zAC23584 AZA128 PA0.WSHI_ PA0.APDD PA0.APDR PA0.SERP PA0.APDD_ PA0.APDR_ ATB1 ATB0 zAM256 zVM1536 zVM512 VPR20
+zAG2512 zVM3328 zVG20 zVM1024 zVM2048 zPD0.B1BI zPD1.B1BI PF.CUZA_ zPK0.IFUW zPD0.G2WR zAG21024 zAG21536 zPD0.MW1 zPD0.G2WR_ zPD0.G2SG zVM2560
+VCF12 VX0 AUR128 zAG22048 zAG22560 zAG23072 zVUW0 zVM2816 zVSG0 PU.INZA_ VPR128 zVCN0 zVKS0 zPK0.INUW zPA1.INC2_ zPA0.B1CB zPA0.IPUW zPD0.IBCQ
+zPU.INC2 zVHS0 zVBO0 zVKEY0 zVM3072 zVPK0256 zVNH0 zVM2304 zVXB0 zVNE0 zAM3840 zAG23584 zAM3584 zVXM0 zVSC0 zPD1.G2WR zPD1.MW1 zPD1.G2WR_ VVS6017
+zVE10 VX0_ zPD1.MSG zPA0.E1DC zVUW128 zVDL0 zPK1.INUW zPA1.B1CB zPA1.IPUW zPK0.IBWB zVSG128 zVFB0 zVKS128 zVCN128 zVWT0 zPA0.IBCQ zVKEY128 zAD0
+zAD1024 zAD512 zAD1536 zAD1856 zVHS8 zVPK1256 zVBO8 zVNH8 zVNE128 zVMN0 zVXB8 zVSC128 zVMX0 zVDB8 zVMN1024 zVE1128 zVMX1024 zPA1.E1DC zVMX512
+zVDL8 zVMN512 zPA0.IHMX zPA0.IHMN zPK1.IBWB zVFB128 zVMN1536 zVWW0 zVYB0 zVMX1536 zVFF0 ACF10 zAD2560 zAD2048 zAD3072 zAD3584 zGYB0 zVMZ0 zVMX1856
+zVMN1856 VPR2128 zVWT8 zPK0.YBWB zPK0.MZWB zPD0.IHMX zPD0.IHMN zPA0.IFQL zVE20 zVYB64 zVMN2560 zVE30 zVMX2560 zVMZ64 zPK0.IBWB_ zPA1.IBCQ
+zPD0.INZA zPA0.E2DC zVMN2048 zPA0.E3DC zPK0.YBWB_ zPK0.MZWB_ zPD0.IBYW zVLB8 zVMX2048 zVE20_ zVFF128 zVMX3072 zVMN3072 zVE30_ zPA1.IHMX zPA1.IHMN
+zPA0.IFWW zPA0.E2DC_ zPA0.E3DC_ zPD1.IBCQ zVMN3584 zVYB128 zVMX3584 zVMZ128 zVLB12 zVWW8 zAZA0 zAPF384 zAPF256 zPK1.YBWB zPF.CUZA zPD1.IHMX
+zPD1.IHMN zPK1.MZWB zPA1.IFWW zGLB8 zGYB64 zVYB192 zVE2128 zVMZ192 zVE3128 zPA1.E2DC zPK1.IBWB_ zAUR0 zPK1.YBWB_ zPA1.E3DC zPD1.INZA zPK1.MZWB_
+zPD1.IBYW zPU.INZA zAZA128 zAOZ1 zAOZ0 zRRY0 zRLB56 VVS0 zVLB24 zPA1.IFQL zVE2128_ zVX0 zVPR0 zVX0_ zVPR20 zVE3128_ zPA1.E2DC_ zPF.CUZA_ zPA1.E3DC_
+zVLB36 zVVS0 zVX2048 zGLB12 zRRY64 zRLB60 zSX0 zAOZ0_ zAUR128 zPU.INZA_ VVS128 zVPR128 zVX2048_ zVPR2128 zVVS128 zSX2048 zVSF0 zAOS1 zAOS0 zAOS0_"""
+PER = {"YB": 256, "LB": 64, "RY": 128, "RV": 128, "FB": 256}
 
 
 def vw(name, lo=0, hi=None, step=1, p1=128):
@@ -65,21 +123,8 @@ def ind(win, off):
     return ("@", win, off)
 
 
-def width(v):
-    if v[0] == "@":
-        return 16 * width(v[2])
-    return (v[2] - v[1] + v[3] - 1) // v[3]
-
-
-def two(v):
-    n = v[1][0] if v[0] == "@" else v[0]
-    return n in SB and SB[n][1] in (B, U)
-
-
 def clash(a, b):
     if a[2] <= b[1] or b[2] <= a[1]:
-        return False
-    if len(a) > 5 and len(b) > 5 and a[5] != b[5]:
         return False
     if a[3] > 1 and a[3] == b[3] and (a[1] - b[1]) % a[3] != 0:
         return False
@@ -88,13 +133,10 @@ def clash(a, b):
 
 def build(rank, cores, topo):
     ops = []
-    rank_now = [LATE]
     step, nth = [-1], {}
+    pool = []
 
-    def at(t, name):
-        rank_now[0] = 100 * t + PAR["order"][name] if name else LATE
-
-    def add(eng, cost, rd, wr, call, **kw):
+    def add(eng, rd, wr, call, **kw):
         r, w = [], []
         for v in rd:
             if isinstance(v, tuple):
@@ -105,69 +147,55 @@ def build(rank, cores, topo):
                 r.append(v[2])
             else:
                 w.append(v)
-        o = {"eng": eng, "cost": cost, "r": r, "w": w, "call": call, "pr": rank_now[0]}
+        o = {"eng": eng, "r": r, "w": w, "call": call}
         o.update(kw)
-        x = w[0] if w else (r[0] if r else ("", 0))
-        name = x[0][:2] if x[0][:2] in ("ZA", "ZX", "HS", "WT") else x[0]
+        x = w[0] if w else r[0]
+        name = x[0][:2] if x[0][:2] in ("ZA", "ZX", "HS", "WT", "SG") else x[0]
         c0 = x[1] % PER.get(name, 8192)
         if name == "VS":
             c0 = H0 + (x[1] - H0) % NS if x[1] >= H0 else x[1] % NS if x[1] < Z0 else x[1]
-        key = ["i", "a", "", "", "", "", "z"][step[0] + 1] + eng + name + str(c0)
+        c0 -= name == "CF" and c0 == 11
+        key = eng + name + str(c0)
+        if eng == "P":
+            key = name + "." + call[1][0][1][0][:2] + call[1][-1][2][0][:2].replace("YB", "YW")
+        key = ["i", "a", "", "", "", "", "z"][step[0] + 1] + key
         nth[key] = nth.get(key, 0) + 1
-        o["key"], o["step"] = key + "_" * (nth[key] - 1), max(step[0], 0)
+        o["key"], o["step"] = key + ["", "_", "_2", "_3"][nth[key] - 1], max(step[0], 0)
         ops.append(o)
 
-    cyc = PAR["cyc"]
-
-    def vcost(out, ins, per):
-        n = width(out)
-        if out[0] == "@":
-            return 0.05 + n * PAR["sca"] * cyc
-        if ins[0][0] == "@":
-            return 0.05 + n * PAR["gat"] * cyc
-        return max(64, n * per) * cyc
-
-    def half(*vs):
-        return 0.5 if all(two(v) for v in vs) else 1
-
     def cp(out, a):
-        add("V", vcost(out, [a], half(out, a)), [a], [out], ("tensor_copy", out, a))
+        add("V", [a], [out], ("tensor_copy", out, a))
 
     def tt(out, a, b, op):
-        per = 1 if (a[0] in PS or b[0] in PS) else 2
-        add("V", vcost(out, [a], per), [a, b], [out], ("tensor_tensor", out, a, b, op))
+        add("V", [a, b], [out], ("tensor_tensor", out, a, b, op))
 
     def ts(out, a, s1, op0, s2=None, op1=None):
-        c = ("tensor_scalar", out, a, s1, s2, op0) + ((op1,) if op1 is not None else ())
-        add("V", vcost(out, [a], half(out, a)), [a, s1, s2], [out], c)
+        add("V", [a, s1, s2], [out], ("tensor_scalar", out, a, s1, s2, op0) + ((op1,) if op1 is not None else ()))
 
     def scan(out, d0, d1, op0, op1):
-        add("V", vcost(out, [d0], half(out, d0, d1)), [d0, d1], [out], ("tensor_tensor_scan", out, d0, d1, 0.0, op0, op1))
+        add("V", [d0, d1], [out], ("tensor_tensor_scan", out, d0, d1, 0.0, op0, op1))
 
     def mset(out, val):
-        add("V", vcost(out, [out], half(out)), [], [out], ("memset", out, val))
+        add("V", [], [out], ("memset", out, val))
 
     def act(out, a, func=AF.Identity, bias=0.0, scale=1.0):
-        n = width(out)
-        c = 0.065 + n * PAR["gat"] * cyc if a[0] == "@" else max(64, n) * cyc + 0.03
-        add("A", c, [a, bias, scale], [out], ("activation", out, a, func, bias, scale))
+        add("A", [a, bias, scale], [out], ("activation", out, a, func, bias, scale))
 
-    def mm(terms, start=True, stop=True, goon=True):
-        c = sum(max(min(64, width(t[1])), width(t[2])) * (1 if two(t[2]) else 4) * PAR["pe"] for t in terms)
-        add("P", c, [x for t in terms for x in t[1:]], [t[0] for t in terms], ("mm", terms, start, stop), goon=goon and not start)
+    def mm(terms, start=True, stop=True):
+        add("P", [x for t in terms for x in t[1:]], [t[0] for t in terms], ("mm", terms, start, stop), goon=not start)
 
     def iota(out, pat, base, cm):
-        add("G", (0.13 + 2 * width(out) * 0.00083) * PAR["pool"], [], [out], ("iota", out, pat, base, cm))
+        add("G", [], [out], ("iota", out, pat, base, cm), behind=pool[:1])
+        pool.append(len(ops) - 1)
 
     def asel(out, a, pat, op, base, cm):
-        add("G", (0.17 + 2 * width(out) * 0.00083) * PAR["pool"], [a], [out], ("affine_select", out, a, pat, op, 0.0, base, cm))
+        add("G", [a], [out], ("affine_select", out, a, pat, op, 0.0, base, cm), behind=pool[:1])
+        pool.append(len(ops) - 1)
 
     nd = [0]
 
-    def dma(q, out, a, lat):
-        rd = [a] if a[0] != "$" else []
-        wr = [out] if out[0] != "$" else []
-        add(q, 0.1, rd, wr, ("dma", out, a), sem="d%d" % nd[0], lat=lat)
+    def dma(q, out, a):
+        add(q, [a] if a[0] != "$" else [], [out] if out[0] != "$" else [], ("dma", out, a), sem="d%d" % nd[0])
         nd[0] += 1
 
     def col(name, j):
@@ -176,42 +204,50 @@ def build(rank, cores, topo):
     def hv(name, h, n=128, base=0):
         return vw(name, base + n * h, base + n * h + n)
 
-    dma("S", vw("SR"), ("$", "scan", 0, 256), 2.0)
-    dma("S", vw("ZR"), ("$", "z0", 0, 256), 2.0)
-    for j in range(4):
-        dma("S", vw("X", 1024 * j, 1024 * j + 1024), ("$", "reg", 1024 * j, 1024 * j + 1024), 2.6 + 0.9 * j)
-    dma("A", col("TI", 0), ("$", "th", 0, 1), 2.0)
-    dma("A", vw("WM", p1=8), ("$", "warm", 0, 256), 2.0)
-    dma("A", col("WI", 0), ("$", "wt", 0, 1), 2.0)
+    dma("S", vw("ZR"), ("$", "z0", 0, 256))
+    dma("A", col("TI", 0), ("$", "th", 0, 1))
+    dma("S", vw("SR"), ("$", "scan", 0, 256))
+    dma("A", vw("WM", p1=8), ("$", "warm", 0, 256))
+    dma("A", col("WI", 0), ("$", "wt", 0, 1))
     for j in range(2):
-        dma("S", vw("VW", 1024 * j, 1024 * j + 1024), ("$", "vw", 1024 * j, 1024 * j + 1024), 7.0 + 1.8 * j)
+        dma("S", hv("X", j, 2048), ("$", "reg", 2048 * j, 2048 * j + 2048))
+    for j in range(2):
+        dma("S", hv("VS", j, 1024, V0), ("$", "vw", 1024 * j, 1024 * j + 1024))
 
     iota(vw("PI", 0, 1), [[0, 1]], 0, 1)
     iota(vw("GF"), [[1, 8], [0, 16]], 0, 0)
     iota(vw("RF"), [[0, 8], [1, 16]], 0, 0)
     iota(vw("JF"), [[1, 144]], 0, 0)
     mset(vw("X", W, W + 16), 0.0)
-    for a in range(W, WD, 512):
-        iota(vw("X", max(a, W + 16), a + 512), [[0, a + 512 - max(a, W + 16)]], 0, 0)
+    dma("S", vw("X", W + 16, WD), vw("X", 16, W))
     ts(vw("PI", 1, 2), vw("PI", 0, 1), 15, OP.bitwise_and)
     ts(vw("PI", 2, 3), vw("PI", 0, 1), 4, OP.arith_shift_right)
     ts(vw("PI", 3, 4), vw("PI", 0, 1), 1, OP.arith_shift_right, 7, OP.bitwise_and)
     cp(vw("CF", 0, 4), vw("PI", 0, 4))
     ts(vw("BD"), vw("GF"), col("CF", 2), OP.is_equal)
-    ts(vw("DC"), vw("GF", 0, 128, 16), 0.0, OP.add, col("CF", 2), OP.is_equal)
+    for j in range(2):
+        ts(hv("DC", j, 8), vw("GF", 0, 128, 16), 0.0, OP.add, col("CF", 2), OP.is_equal)
+    DC = vw("DC", 0, 8)
     ts(vw("IF"), vw("JF", 0, 128), col("CF", 0), OP.is_equal)
     ts(vw("MR"), vw("RF"), col("CF", 1), OP.is_equal)
-    for name, x in (("IB", 1.0), ("IH", 0.5), ("IN", -1.0), ("IG", -8192.0), ("IK", 32768.0), ("IS", 2048.0)):
+    for name, x in (("IB", 1.0), ("IH", 0.5), ("IN", -1.0), ("IK", 32768.0), ("IS", 2048.0), ("I4", 4.0), ("IN4", -4.0),
+                    ("IP", 1.0 / 32), ("IM", -1.0 / 32), ("IQ", -1.0 / 16), ("INF", -1.0), ("IF8", 1.0 / 8192), ("IN8", -1.0 / 8192)):
         act(vw(name), vw("IF"), scale=x)
     mset(vw("ONF"), 1.0)
     mset(vw("ONB"), 1.0)
     mset(vw("CQ"), -0.25)
     mset(vw("CU"), -16.0)
     mset(vw("CU", p1=1), -15.5)
-    mset(col("CF", 12), 0.5)
-    iota(vw("VS", Z0, V0), [[0, V0 - Z0]], W, 0)
+    mset(vw("CA"), -32.0)
+    mset(vw("CA", p1=1), -24.5)
+    mset(vw("CM"), MAGIC * W)
+    mset(col("CF", 12), 0.5 * RU)
+    mset(vw("VS", Z0, V0), 1 << 24)
     mset(vw("C7"), -7.5)
-    mset(vw("C64"), (V0 - Z0) / 16384)
+    for j, x in enumerate([64, V0 - Z0 - 64 + 7.5]):
+        mset(hv("CB", j, 8), x / 256)
+    iota(vw("CB", 16, 56), [[NS // 128, TS - 1], [0, 8]], (H0 - Z0) // 128, 0)
+    act(vw("CB", 16, 56), vw("CB", 16, 56), scale=0.5)
     iota(vw("NB", 0, 4), [[0, 2], [128, 2]], made(-1) - Z0, 1)
     iota(vw("NB", 4, 12), [[-NS, 4], [128, 2]], made(0) - Z0 + 2 * NS, 1)
     act(vw("NB", 0, 12), vw("NB", 0, 12), scale=1.0 / 8192)
@@ -221,22 +257,16 @@ def build(rank, cores, topo):
     cp(vw("LS"), vw("JF", 0, 8))
     LC = vw("LS")
     ts(vw("L15"), vw("JF", 0, 8), 16.0, OP.mult, 15.0, OP.add)
-    act(vw("W1", 0, 8), vw("DC"), scale=32.0 / 32768)
-    act(vw("DC8"), vw("DC"), scale=8192.0)
-    act(vw("DCN"), vw("DC"), scale=-16.0 / 32768)
+    act(vw("W1"), DC, scale=2 * KU)
+    act(vw("DC8"), DC, scale=8192.0)
     act(vw("DCM"), vw("DC"), scale=-1.0)
-    ts(col("CF", 14), col("MR", 2), 1.0 / 64, OP.mult)
-    ts(col("CF", 15), col("MR", 3), 1.0 / 8192, OP.mult, col("CF", 14), OP.add)
-    act(vw("WK", 0, 8), vw("DC"), scale=col("CF", 15))
-    act(vw("WK", 8, 16), vw("WK", 0, 8), scale=-1.0)
     ts(col("CF", 7), col("CF", 1), 8.0, OP.is_ge)
-    ts(col("CF", 13), col("MR", 4), 8192.0, OP.mult, col("CF", 7), OP.add)
-    ts(col("CF", 21), col("CF", 1), 2.0, OP.is_lt)
-    ts(col("CF", 16), col("MR", 4), 16384.0, OP.mult, col("CF", 21), OP.add)
-    act(vw("BZ"), vw("BD"), scale=32.0 / 32768)
-    for t in range(2):
-        act(hv("WR", 2 * t, 8), vw("DCN"), scale=col("CF", 16) if t else 1.0)
-        act(hv("WR", 2 * t + 1, 8), vw("DC"), scale=col("CF", 13) if t else 1.0)
+    ts(col("CF", 13), col("CF", 7), RU, OP.mult)
+    ts(col("CF", 14), col("CF", 1), 2.0, OP.is_lt, -KU, OP.mult)
+    ts(col("CF", 15), col("CF", 7), -255.0, OP.mult)
+    act(vw("BZ"), vw("BD"), scale=2 * KU)
+    for j, x in enumerate((-KU, RU, col("MR", 2), col("CF", 13), col("CF", 14))):
+        act(hv("WR", j, 8), DC, scale=x)
     ts(col("CF", 4), col("CF", 2), 16.0, OP.mult, 15.0, OP.add)
     ts(vw("WO"), vw("JF"), col("CF", 4), OP.is_equal)
     tt(vw("WS"), vw("WO", 14, 142), vw("WO", 15, 143), OP.add)
@@ -245,42 +275,43 @@ def build(rank, cores, topo):
     tt(vw("AP"), vw("TM2"), vw("BD"), OP.mult)
     act(vw("AP2"), vw("AP"), scale=2.0)
     act(vw("APN"), vw("AP"), scale=-1.0)
-    act(vw("QS"), vw("JF", 0, 128), scale=col("MR", 3))
-    iota(vw("BS"), [[1, 8], [0, 2]], 1, 0)
-    ts(vw("BT"), vw("JF", 0, 16), (H0 - V0) / 128, OP.add, col("MR", 2), OP.mult)
-    ts(col("CF", 20), col("CF", 7), -255.0, OP.mult)
-    ts(vw("BS"), vw("BS"), col("MR", 4), OP.mult, col("CF", 20), OP.add)
-    tt(vw("BT"), vw("BT"), vw("BS"), OP.add)
+    for a in range(0, 2048, 512):
+        iota(vw("SEL", a, a + 512), [[0, 512]], 0, 0)
+    asel(vw("SEL", 2, 2048, 16), vw("ONB"), [[-1, 16], [-16, 8]], OP.is_equal, 0, 1)
+    for h in range(2):
+        asel(vw("GS", 128 * h, 128 * h + 128, 1, 16), vw("ONB", p1=16), [[-1, 8], [0, 16]], OP.is_equal, -8 * h, 1)
     cp(col("CF", 5), col("TI", 0))
     cp(col("CF", 6), col("WI", 0))
-    ts(col("CF", 8), col("CF", 1), 37.0, OP.mult)
-    ts(col("CF", 10), col("CF", 1), 37.0, OP.mult)
+    for j in (8, 10):
+        ts(col("CF", j), col("CF", 1), 37.0 * 32, OP.mult, -2.0 ** 23, OP.add)
     act(vw("WBD"), vw("BD"), scale=col("CF", 6))
     act(vw("WB2"), vw("WBD"), scale=2.0)
     act(vw("WBN"), vw("WBD"), scale=-1.0)
     ts(vw("Q16"), vw("JF", 0, 16), 16.0, OP.mult, col("CF", 1), OP.add)
     for h in range(2):
-        ts(vw("QP", 16 * h, 16 * h + 8), vw("Q16", 0, 8), 32.0, OP.mult, 16.0 * (1 - h) + 7.5, OP.add)
-        act(vw("QP", 16 * h + 8, 16 * h + 16), vw("Q16", 8 * h, 8 * h + 8))
+        ts(hv("QP", 3 * h, 8), vw("Q16", 0, 8), 32.0, OP.mult, 16.0 * (1 - h) + 7.5, OP.add)
+    act(vw("QP", 8, 24), vw("Q16"))
+    iota(vw("QL"), [[-W // 2, 2], [0, 4]], 0, 0)
     act(vw("TMP"), vw("IF"), scale=col("CF", 5))
     mm([(vw("PF", 0, 128), vw("ONF"), vw("TMP"))])
-    act(vw("BI0"), vw("PF", 0, 128), scale=-1.0)
-    act(vw("BI"), vw("RF"), scale=-1.0 / 32768)
+    act(vw("BI0"), vw("PF", 0, 128), scale=-RU)
+    act(vw("BI1"), vw("BI0"), bias=8 * 255 * RU)
+    act(vw("BI"), vw("RF"), scale=-KU / 16)
     ts(col("CF", 18), col("CF", 1), 0.0, OP.is_gt, -1.0 / 8192, OP.mult)
     ts(vw("TM2"), vw("JF", 1, 129), col("CF", 0), OP.is_equal, col("CF", 18), OP.mult)
-    act(vw("DI"), vw("IF"), scale=1.0 / 8192)
-    tt(vw("DI"), vw("DI"), vw("TM2"), OP.add)
+    tt(vw("DI"), vw("IF8"), vw("TM2"), OP.add)
+    act(vw("DJ"), vw("DI"), scale=1.0 / 16)
 
     for h in range(2):
         src = vw("SR", 1 - h, 256, 2)
         cp(hv("S16", h), src)
-        cp(hv("SF", h), src)
+        ts(hv("SF", h), src, -7.5, OP.add)
         cp(hv("VS", h, 128, made(-1)), src)
         cp(hv("ZA0", h), vw("ZR", 1 - h, 256, 2))
     for k in range(16):
         if k < PAR["zi"][0]:
             act(vw("ZX0", k, W, 16), vw("ZA0"), AF.Copy)
-        elif k < PAR["zi"][0] + PAR["zi"][1]:
+        elif k < sum(PAR["zi"]):
             asel(vw("ZX0", k, W, 16), vw("ZA0"), [[0, 256]], OP.is_ge, 1, 0)
         else:
             cp(vw("ZX0", k, W, 16), vw("ZA0"))
@@ -288,37 +319,12 @@ def build(rank, cores, topo):
     for h in range(2):
         mm([(vw("PD1", 8 * h, 8 * h + 8), vw("WMF", 1 - h, 256, 2, 8), vw("IF", 0, 8, 1, 8))])
     ts(vw("HS1"), vw("PD1", 0, 16), -1.0, OP.mult, 1.0, OP.add)
-    ts(vw("THR"), vw("PD1", 0, 16), 8.0, OP.mult)
-
-    def mark_new(hs):
-        for h in range(2):
-            act(vw("HX", 16 * h, 16 * h + 8), hv(hs, h, 8), scale=1.0 / 128)
-            act(vw("HX", 16 * h + 8, 16 * h + 16), hv(hs, h, 8))
-    mark_new("HS1")
-
-    def blocks():
-        ts(vw("S4"), vw("S16"), 1.0 / 16, OP.mult, -15.0 / 32, OP.add)
+    cp(vw("THR"), vw("PD1", 0, 16))
     for j in range(4):
-        src = vw("VW", 512 * j, 512 * j + 512)
-        ts(hv("VS", j, 512, V0), src, 4095, OP.bitwise_and)
-        ts(hv("VS", j, 512, V0 + 2048), src, 12, OP.arith_shift_right)
-
-    def first_table():
-        dma("S", vw("T2", 0, W), vw("X", W, WD), 4.0)
-        mm([(vw("PU", 0, 256), vw("WO", 15 - a, 143 - a), hv("X", a, 256)) for a in range(16)])
-        lane = [hv("CT", l, 256) for l in range(4)]
-        act(lane[0], vw("PU", 0, 256), AF.Copy)
-        tt(lane[1], vw("PU", 0, 256), lane[0], OP.subtract)
-        iota(lane[3], [[0, 2], [1, 128]], 0, 0)
-        iota(lane[2], [[1, 2], [0, 128]], 0, 0)
-        ts(col("CF", 19), col("CF", 1), 2.0, OP.mult)
-        act(lane[2], lane[2], bias=col("CF", 19))
-        for l in range(4):
-            dma("S", vw("T2", 0, W) + (l, 16), lane[l], 2.5)
+        ts(hv("VS", j, 512, V0 + 2048), hv("VS", j, 512, V0), 12, OP.arith_shift_right)
 
     def settle_lists(t):
-        for h in range(2):
-            cp(hv("SF" if t == TS - 1 else "S16", h), ind(vw("VS", made(t), Z0), vw("LB", 32 * t + 16 * h + 8, 32 * t + 16 * h + 16)))
+        ts(vw("SF"), ind(vw("VS", made(t), Z0), hv("LB", 1, 16, 64 * t)), 0.0 if t == TS - 1 else -7.5, OP.add)
 
     me = cores[rank]
     for t in range(TS):
@@ -328,90 +334,92 @@ def build(rank, cores, topo):
         zx = "ZX%d" % (max(t - 1, 0) % 2)
         za, zb = "ZA%d" % (t % 2), "ZA%d" % ((t + 1) % 2)
         hs, hp = "HS%d" % (t % 2), "HS%d" % ((t + 1) % 2)
+        sg, sp = "SG%d" % (t % 2), "SG%d" % ((t + 1) % 2)
         wt = "WT%d" % (t % 2)
         dst = cores[(rank + 1 + t % 3) % NR]
-        lands = [(hv("RY", t), hv("RL", t, 8)), (hv("YB", 1, 128, 256 * t), vw("LB", 32 * t + 16, 32 * t + 24))]
+        lands = [(hv("RY", t), hv("LB", 7, 8, 64 * t)), (hv("YB", 1, 128, 256 * t) if last else vw("YW", 0, 256, 2), hv("LB", 4, 8, 64 * t))]
 
-        def send(there, here, sem, lat):
-            add("G", 0.5, [here], [], ("send", dst, [(there, here)], sem + str(t)))
-            add("R", 0.0, [], [there], None, sem=sem + str(t), after=len(ops) - 1, lat=lat, cnt=len(topo.engines(me, dst)))
+        def send(there, here, sem):
+            add("G", [here], [], ("send", dst, there, here, sem + str(t)), behind=list(pool))
+            pool[:] = [len(ops) - 1]
+            add("R", [], [there], None, sem=sem + str(t), after=[len(ops) - 1], cnt=len(topo.engines(me, dst)))
 
-        for j in range(8 if t else 0):
-            at(t, "m%d" % (j // 4))
-            n = PAR["ach"] if j in PAR["alt"] else PAR["mch"][j]
-            for a in range(512 * j, 512 * j + 512, n):
-                b = a + n
-                rows = ind(vw("YW"), vw("S4", a // 16, b // 16))
-                if j in PAR["alt"]:
-                    bank = vw(PAR["abk"][a // n % len(PAR["abk"])], 0, n)
-                    act(vw("C2", a, b), rows, AF.Copy)
-                    mm([(bank, vw("IN"), vw(zx, a, b)), (bank, vw("IB"), vw("C2", a, b))])
-                    act(vw("M", a, b), bank, AF.Relu)
-                else:
-                    tt(vw("M", a, b), rows, vw(zx, a, b), OP.max)
+        def gather(out, rows, vector):
+            if vector:
+                cp(out, rows)
+            else:
+                act(out, rows, AF.Copy)
+
+        for a, b in zip(PAR["mcut"][:-1], PAR["mcut"][1:] if t else ()):
+            rows = ind(vw("YW"), vw("S4", a // 16, b // 16))
+            if a // 512 in PAR["alt"]:
+                bank = vw(PAR["alt"][a // 512][a // 256 % 2], 0, 256)
+                act(vw("C2", a, b), rows, AF.Copy)
+                mm([(bank, vw("IN"), vw(zx, a, b)), (bank, vw("IB"), vw("C2", a, b))])
+                act(vw("M", a, b), bank, AF.Relu)
+            else:
+                tt(vw("M", a, b), rows, vw(zx, a, b), OP.max)
         for h in range(2):
-            pk, pa = "PK%d" % h, "PA%d" % h
-            at(t, "m%d" % h)
-            for j in range(4 * h, 4 * h + 4 if t == 0 else 0):
+            pk, pa, pd = "PK%d" % h, "PA%d" % h, "PD%d" % h
+            for j in range(4 * h, 4 * h + 4):
                 a, b = 512 * j, 512 * j + 512
+                if t:
+                    gather(vw("G2", a, b), ind(vw("TB"), vw("S4", a // 16, b // 16)), j in PAR["gv"])
+                    continue
                 rows = ind(vw("X", 0, W), vw("S16", a // 16, b // 16))
-                bank = vw(["PD0", "PD1", "PU"][j % 3])
-                if j in PAR["c0v"]:
-                    cp(vw("G2", a, b), rows)
+                gather(vw("G2", a, b), rows, j in PAR["c0v"])
+                if j in PAR["f0"]:
+                    tt(vw("M", a, b), rows, vw(zx, a, b), OP.max)
                 else:
-                    act(vw("G2", a, b), rows, AF.Copy)
-                mm([(bank, vw("IN"), vw(zx, a, b)), (bank, vw("IB"), vw("G2", a, b))])
-                if j in PAR["r0v"]:
-                    ts(vw("M", a, b), bank, 0.0, OP.max)
-                else:
+                    bank = vw(["PD0", "PD1", "PU", "PA1", "PD0", "PD1", "PU", "PD0"][j])
+                    mm([(bank, vw("IN"), vw(zx, a, b)), (bank, vw("IB"), vw("G2", a, b))])
                     act(vw("M", a, b), bank, AF.Relu)
-            at(t, "g%d" % h)
-            for a in range(2048 * h, 2048 * h + 2048 if t else 0, PAR["gch"]):
-                b = a + PAR["gch"]
-                rows = ind(vw("T2", 0, W), vw("S16", a // 16, b // 16))
-                if a // PAR["gch"] in PAR["gv"]:
-                    cp(vw("G2", a, b), rows)
-                else:
-                    act(vw("G2", a, b), rows, AF.Copy)
-            at(t, "a%d" % h)
 
-            def lanes(bank, c, n, name, ks, wts, q):
-                return [(vw(bank, c + k, c + k + 16 * n - 15, 16, q[1]) + (q[0], 1),
-                         vw(name, 2048 * h + 16 * q[0] + k, 2048 * h + 16 * q[1], 16), wts) for k in ks]
-            parts = PAR["parts"][h]
-            key, rho, dp = vw(pk, 0, 128), vw(pk, 128, 256), vw(pa, 256, 384)
-            if t:
-                more = [(key, vw("IB"), hv("SG", h)), (key, vw("ONB", p1=8 * t), vw("ONB", p1=8 * t))]
+            def lanes(bank, c, n, name, wts, q0, q1):
+                return [(vw(bank, c + k, c + k + 16 * n - 15, 16, q1) + (q0, 1),
+                         vw(name, 2048 * h + 16 * q0 + k, 2048 * h + 16 * q1, 16), wts) for k in range(16)]
+            dp, ends, uw = vw(pa, 256, 384), vw(pa, 271, 384, 16), hv("UW", h)
+            act(hv("NH0", h, 8), hv("THR", h, 8), bias=col("NB", 2 * t + h), scale=(made(t - 2) - made(t - 3)) / 4096)
+            if t == 0:
+                key, rho, reset = vw(pk, 0, 128), vw(pk, 128, 256), vw("MKN")
+                more = [(vw(pk, 0, 128, 1, 32 * j + 32) + (32 * j, 1), hv(za, 4 * h + j, 32), vw("BZ"))
+                        for j in range(4) if 4 * h + j not in PAR["alt"] and 4 * h + j not in PAR["f0"]]
+                mm([(key, vw("IB"), vw("BI")), (rho, vw("IF"), vw("BI0"))] + more, stop=False)
+                news = [(vw(pk, 128 + k, 256, 16), vw("IN"), hv(hp, h, 8)) for k in range(16)]
+                mm(news[:15], start=False, stop=False)
+                for q0, q1 in ((0, 96), (96, 128)):
+                    mm(lanes(pk, 0, 16, "G2", vw("WR", 0, 16), q0, q1), start=False, stop=False)
+                    mm(lanes(pk, 0, 8, "M", vw("W1"), q0, q1) + news[15:] * (q0 > 0), start=False, stop=q0 > 0)
+                ts(hv(sg, h), rho, col("CF", 12), OP.is_gt)
+                tt(hv("KEY", h), key, hv(sg, h), OP.add)
+                mm([(dp, hv("SF", h), vw("DI")), (ends, vw("IP"), hv("CB", 0, 8)), (ends, vw("IP"), hv("CB", 1, 8))])
             else:
-                more = [(vw(pk, 0, 128, 1, 32 * j + 32) + (32 * j, 1), hv(za, 4 * h + j, 32), vw("BZ")) for j in range(4) if 4 * h + j not in PAR["alt"]]
-            mm([(key, vw("IB"), vw("BI")), (rho, vw("IF"), vw("BI0"))] + more, stop=False)
-            news = [(vw(pk, k, 256, 16), vw("IG"), hv("HX", h, 16)) for k in range(16)]
-            mm(news[:15], start=False, stop=False)
-            act(hv("NH0", h, 8), hv("THR", h, 8), bias=col("NB", 2 * t + h), scale=(made(t - 2) - made(t - 3)) / 32768)
-            late = PAR["ml"][h] or t == 0
-            ms = [lanes(pk, 0, 8, "M", range(16), vw("W1", 0, 8), q) for q in (parts if late else [(0, 128)])]
-            gs = [lanes(pk, 0, 16, "G2", range(16), hv("WR", min(t, 1), 16), q) for q in parts]
-            sums = [x for pair in zip(gs, ms) for x in pair] if late else ms + gs
-            for x in sums:
-                mm(x + news[15:] * (x is sums[-1]), start=False, stop=x is sums[-1])
-            ts(hv("SG", h), rho, col("CF", 12), OP.is_gt, 8.0, OP.mult)
-            if t:
-                ts(vw(pk, 384, 512), rho, 8192.0 * t - 6135.5, OP.is_gt, 128.0, OP.mult)
-                tt(vw(pk, 256, 384), key, hv("SG", h), OP.add)
-                tt(hv("KB", h), vw(pk, 384, 512), hv("KEY", h), OP.add)
-                tt(hv("KEY", h), vw(pk, 256, 384), hv("KB", h), OP.min)
-            else:
-                tt(hv("KEY", h), key, hv("SG", h), OP.add)
-            if t:
-                mm([(vw(pa, 271, 384, 16), vw("IB"), vw("C64"))], stop=False)
-                for q in parts:
-                    steps = lanes(pa, 256, 8, "G2", range(16), vw("WK", 0, 8), q) + lanes(pa, 255, 8, "G2", range(1, 16), vw("WK", 8, 16), q)
-                    mm(steps[:16], start=False, stop=False)
-                    mm(steps[16:] + ([(vw(pa, 271, 384, 16), vw("IB"), vw("C64"))] if q == parts[-1] else []), start=False, stop=q == parts[-1])
-            else:
-                mm([(dp, hv("SF", h), vw("DI"))] + [(vw(pa, 271, 384, 16), vw("IB"), vw("C64"))] * 2)
-            scan(hv("CN", h), vw("MK0", 0, 128), hv("SG", h), OP.mult, OP.add)
-            scan(vw(pk, 256, 384), vw("MKN"), hv("KEY", h), OP.add, OP.max)
+                diff, rho, key, ba = (hv(pd, j) for j in range(4))
+                reset, kept = hv(pk, 0), hv(pk, 1)
+                mm([(diff, hv("B16", h), vw("IB")), (diff, vw("IB"), vw("C7")), (rho, vw("IF"), vw("BI1")), (diff, hv("SF", h), vw("INF"))]
+                   + [(ba, hv("B16", h), vw("IQ")), (ba, vw("CA"), vw("ONB")), (ba, hv("SF", h), vw("IF"))] * (t == 1)
+                   + [(diff, vw("HT", p1=16), vw("GS", 128 * h, 128 * h + 128, 1, 16)), (key, vw("IB"), vw("BI"))], stop=False)
+                mm([(kept, vw("IF"), hv("KEY", h)), (kept, vw("ONB", p1=4), vw("ONB", p1=4))] + [(kept, vw("IN"), hv(sg, h))] * (t > 1)
+                   + [(reset, vw("IB"), vw("MKN"))] + [(kept, vw("I4"), uw)] * (t > 1), stop=False)
+                for x in PAR["sets"][h]:
+                    end = x == PAR["sets"][h][-1]
+                    mm((lanes(pd, 256, 8, "M", vw("W1"), *x[1:]) if x[0] == "M" else lanes(pd, 0, 24, "G2", vw("WR", 16, 40), *x[1:]))
+                       + [(key, vw("IB"), hv(sp, h))] * end, start=False, stop=end)
+                ts(uw, diff, 0.0, OP.not_equal, col("CF", 12), OP.max)
+                mm([(kept, vw("IN4"), uw), (kept, vw("IN4"), uw), (reset, vw("IN4"), uw),
+                    (vw(pk, 1, 128), vw("I4"), vw("UW", 128 * h, 128 * h + 127))], start=False)
+                tt(hv(sg, h), rho, uw, OP.is_gt)
+                tt(hv("KS", h), key, hv(sg, h), OP.add)
+                tt(hv("KEY", h), kept, hv("KS", h), OP.min)
+                mm([(dp, hv("B16", h), vw("DJ")), (ends, vw("IP"), hv("CB", t + 1, 8))], stop=False)
+                name, plus, minus = ("C1", "IF8", "IN8") if t == 1 else ("UW", "IM", "IP")
+                if t == 1:
+                    tt(hv("C1", h), ba, uw, OP.mult)
+                a = 128 * h
+                mm([(vw(pa, 256, 383), vw(minus), vw(name, a + 1, a + 128)), (vw(pa, 271, 368, 16), vw(plus), vw(name, a + 16, a + 128, 16)),
+                    (dp, vw(plus), hv(name, h))], start=False)
+            scan(hv("CN", h), vw("MK0", 0, 128), hv(sg, h), OP.mult, OP.add)
+            scan(vw(pk, 256, 384), reset, hv("KEY", h), OP.add, OP.max)
             tt(hv("NE", h), vw(pk, 256, 384), hv("KEY", h), OP.not_equal)
             scan(hv("SC", h), hv("NE", h), dp, OP.mult, OP.add)
             cn = vw("CN", 128 * h + 15, 128 * h + 128, 16)
@@ -419,147 +427,145 @@ def build(rank, cores, topo):
             tt(hv(hs, h, 8), cn, hv("THR", h, 8), OP.not_equal)
             tt(hv("NH", h, 8), hv(hs, h, 8), hv("NH0", h, 8), OP.mult)
             tt(hv("XB", h, 8), hv("NH", h, 8), hv("BO", h, 8), OP.add)
-            if PAR["xm"][h]:
-                tt(hv("XM", h), ind(hv("XB", h, 8), LC), vw("MR"), OP.mult)
-                tt(hv("E1", h), ind(hv("SC", h), vw("L15")), hv("XM", h), OP.min)
+            if h < PAR["xm"]:
+                tt(vw("XM"), ind(hv("XB", h, 8), LC), vw("MR"), OP.mult)
+                tt(hv("E1", h), ind(hv("SC", h), vw("L15")), vw("XM"), OP.min)
             else:
                 tt(hv("DB", h, 8), vw("SC", 128 * h + 15, 128 * h + 128, 16), hv("XB", h, 8), OP.min)
                 tt(hv("E1", h), ind(hv("DB", h, 8), LC), vw("MR"), OP.mult)
             mm([(vw(pa, 0, 8), hv("E1", h), vw("DC8"))])
             ts(hv("DL", h, 8), vw(pa, 0, 8), float(Z0 - made(t - 2)), OP.add)
-            cp(hv("FB", h), ind(vw("VS", made(t - 2), H0 + NS * t), hv("DL", h, 8)))
-            at(t, None)
+            rows, fb = ind(vw("VS", made(t - 2), H0 + NS * t), hv("DL", h, 8)), hv("FB", h, 128, 256 * t)
+            if t < 2:
+                ts(hv("FI", h), rows, LOW, OP.bitwise_and)
+                rows = hv("FI", h)
+            ts(fb, rows, float(W), OP.min)
             ts(hv(wt, h, 8), vw(pa, 0, 8), 0.0, OP.is_equal, 0.125, OP.mult)
             if last:
                 tt(hv("WW", h, 8), hv("WT0", h, 8), hv("WT1", h, 8), OP.min)
-            fi = hv("FO", t + h) if h == 0 or last else vw("VS", H0 + NS * t + 128, H0 + NS * t + 256)
-            cp(fi, hv("FB", h))
             if h == 0 and not last:
-                send(vw("VS", H0 + NS * t, H0 + NS * t + 128), fi, "rc", PAR["rem"] + 0.5)
-            ts(hv("PF", h, 128, 256), hv("FB", h), col("CF", 10 + t % 2), OP.add)
-        if t == 0:
-            first_table()
-        elif not last:
-            settle_lists(t - 1)
+                send(hv("RV", t), fb, "rc")
+                cp(vw("VS", H0 + NS * t + 1, H0 + NS * t + 256, 2), hv("RV", t))
+            if h == 0 or last:
+                cp(hv("FF", h), fb)
+                act(hv("PF", h, 128, 256), hv("FF", h), bias=col("CF", 10 + t % 2), scale=32.0)
+            else:
+                cp(vw("VS", H0 + NS * t, H0 + NS * t + 256, 2), fb)
+                ts(hv("PF", h, 128, 256), fb, 32.0, OP.mult, col("CF", 10 + t % 2), OP.add)
         if not last:
-            blocks()
-            mm([(vw("PD0", 256, 272), vw("ONB"), vw("BO"))])
-            add("V", 64 * cyc, [vw("PD0", 256, 272)], [col("CF", 9)], ("tensor_reduce", col("CF", 9), vw("PD0", 256, 272)))
+            if t:
+                settle_lists(t - 1)
+            if PAR["ba"]:
+                act(vw("OS"), vw("SF"), bias=16 * MAGIC)
+                act(vw("B16"), vw("OS"), bias=-16 * MAGIC)
+            else:
+                ts(vw("B16"), vw("SF"), 16 * MAGIC, OP.add, -16 * MAGIC, OP.add)
+            ts(vw("S4"), vw("B16"), 1.0 / 16, OP.mult)
+            mm([(vw("PD0", 384, 400), vw("ONB"), vw("BO"))])
+            add("V", [vw("PD0", 384, 400)], [col("CF", 9)], ("tensor_reduce", col("CF", 9), vw("PD0", 384, 400)))
             cp(col("AI", 0), col("CF", 9))
             ts(col("AI", 1), col("AI", 0), 31, OP.bitwise_and)
-            ts(col("CF", 12), col("AI", 1), 0.5 - 8 * 255 + 8192 * (t + 1), OP.add)
-            act(col("CF", 10 + (t + 1) % 2), col("CF", 9), bias=col("CF", 8))
+            ts(col("CF", 12), col("AI", 1), 0.5, OP.add, RU, OP.mult)
+            act(col("CF", 10 + (t + 1) % 2), col("CF", 9), bias=col("CF", 8), scale=32.0)
             tt(vw("TH2"), vw(hp), vw(hs), OP.subtract)
-            act(vw("THR"), vw("TH2"), bias=4.0, scale=4.0)
-            mark_new(hs)
+            act(vw("THR"), vw("TH2"), bias=0.5, scale=0.5)
+            mm([(vw("PU", 128, 256, 1, 16), vw(hs), vw("IB"))])
+            act(vw("HT", p1=16), vw("PU", 128, 256, 1, 16), scale=128.0)
         for h in range(2):
             pa, pk = "PA%d" % h, "PK%d" % h
-            yv = hv("YB", h, 128, 256 * t)
-            at(t, "d%d" % h)
-            for a in range(2048 * h, 2048 * h + 2048, PAR["dch"]):
-                b = a + PAR["dch"]
-                rows = ind(vw("X", 0, W + 16), vw("FB", a // 16, b // 16))
-                if a // PAR["dch"] in PAR["dv"]:
-                    cp(vw("D", a, b), rows)
-                else:
-                    act(vw("D", a, b), rows, AF.Copy)
-            cuts = PAR["cuts"][h]
-            at(t, "s%d" % h)
+            yv = lands[1][0] if h else hv("YB", 0, 128, 256 * t)
+            cuts = [2048 * h + a for a in PAR["cuts"][h]]
             for a, b in zip(cuts[:-1], cuts[1:]):
-                a, b = a + 2048 * h, b + 2048 * h
+                gather(vw("D", a, b), ind(vw("X", 0, W + 16), vw("FB", 256 * t + a // 16, 256 * t + b // 16)), a in PAR["dvl" if last else "dv"])
+            for a, b in zip(cuts[:-1], cuts[1:]):
                 scan(vw("MX", a, b), vw("MK0", 0, b - a), vw("D", a, b), OP.mult, OP.max)
                 scan(vw("MN", a, b), vw("MKB", 0, b - a), vw("D", a, b), OP.add, OP.min)
-            at(t, "y%d" % h)
-            py = vw(pa, 128, 256)
-            mm([(py, vw("IB"), vw("CQ"))], stop=False)
-            mm([(py, vw("IH"), vw("MX", 2048 * h + 15, 2048 * h + 2048, 16))], start=False, stop=False)
-            mm([(py, vw("IH"), vw("MN", 2048 * h + 15, 2048 * h + 2048, 16))], start=False)
-            ts(yv, py, MAGIC, OP.add, MAGIC, OP.subtract)
-            if h == 0:
-                send(hv("RY", t), yv, "ra", PAR["rem"])
-            pd = vw("PD%d" % h, 256, 384)
-            av = hv(zb, h)
+            for p, n in ((0, 64), (1, 64)) if last else ((0, 128),):
+                def part(v, p=p, n=n):
+                    return (v[0], v[1] + n * v[3] * p, min(v[2], v[1] + n * v[3] * (p + 1)), v[3], v[4])
+
+                def rows(v, p=p, n=n):
+                    return v[:4] + (n * p + n, n * p, 1)
+                py = vw("PD%d" % h, 0, n) if p else vw(pa, 128, 128 + n)
+                mm([(py, vw("IB"), vw("CQ", 0, n))], stop=False)
+                mm([(py, vw("IH"), part(vw("MX", 2048 * h + 15, 2048 * h + 2048, 16)))], start=False, stop=False)
+                mm([(py, vw("IH"), part(vw("MN", 2048 * h + 15, 2048 * h + 2048, 16)))], start=False)
+                ts(part(yv), py, MAGIC, OP.add, MAGIC, OP.subtract)
+                if h == 0:
+                    send(part(hv("RY", t)), part(yv), "rc" if p else "ra")
+                pu = rows(vw(pk, 384, 512))
+                tt(part(hv("MZ", h)), part(yv), part(hv(za, h)), OP.max)
+                mm([(pu, part(vw("IB")), vw("C7")), (pu, part(hv(za, h)), vw("WBN"))], stop=False)
+                mm([(pu, part(yv), vw("WBN"))], start=False, stop=False)
+                mm([(pu, part(hv("MZ", h)), vw("WB2"))], start=False)
+                tt(rows(hv("E2", h)), pu, rows(vw("MR")), OP.mult)
+                ts(rows(hv("E3", h)), rows(hv("E2", h)), -16 * MAGIC, OP.add, 16 * MAGIC, OP.add)
+                pi, pp, pc, both = vw(pa, 392, 400), hv(pa, h, 8, 384 + 8 * h), hv(pa, 1 - h, 8, 392 - 8 * h), hv(pa, 0, 16, 384 + 8 * h)
+                if last:
+                    both = hv(pa, p, 4, 392)
+                    mm([(both, vw("IF"), hv("QP", p, 4, 24 * h)), (both, vw("IK"), hv(wt, p, 4, 8 * h)), (both, vw("IB"), hv("QL", p, 4))]
+                       + [(pc, vw("IF"), hv("QP", 1 + h, 8)), (pc, vw("IS"), hv(wt, h, 8)), (pc, vw("IS"), hv("WW", h, 8))] * (p != h), stop=False)
+                    mm([(both, rows(hv("E2", h)), rows(hv("DC", p, 4)))], start=False, stop=False)
+                    mm([(both, rows(hv("E3", h)), rows(hv("DCM", p, 4)))], start=False)
+                    a, b = ((8, 12), (12, 24), (0, 12), (12, 16))[2 * h + p]
+                    cp(vw("LB", 64 * t + 24 * h + a, 64 * t + 24 * h + b), vw(pa, 384 + a, 384 + b))
+                    if h == 0:
+                        send(hv("LB", p, 4, 64 * t + 56), hv("LB", p, 4, 64 * t + 8), "rd" if p else "rb")
+                    continue
+                mm([(hv(pa, 0, 16, 392 - 8 * h), vw("IF"), hv("QP", h, 16)), (pp, vw("IN"), vw("C7", 0, 8)), (pp, vw("IK"), hv(wt, h, 8)),
+                    (pi, vw("IK"), hv(wt, h, 8)), (pc, vw("IS"), hv(wt, h, 8))], stop=False)
+                mm([(both, hv("E2", h), vw("DC"))], start=False, stop=False)
+                mm([(both, hv("E3", h), vw("DCM"))], start=False)
+                cp(hv("LB", h, 24, 64 * t), vw(pa, 384, 408))
+                if h == 0:
+                    send(hv("LB", 3, 16, 64 * t), hv("LB", 0, 16, 64 * t), "rb")
+            pd, av = vw("PD%d" % h, 256, 384), hv(zb, h)
             mm([(pd, vw("IN"), hv(za, h))], stop=False)
             mm([(pd, vw("IB"), yv)], start=False)
             act(av, pd, AF.Abs)
-            pu = vw(pk, 384, 512)
-            if PAR["mz"][h]:
-                tt(hv("MZ", h), yv, hv(za, h), OP.max)
-                mm([(pu, vw("IB"), vw("C7")), (pu, hv(za, h), vw("WBN"))], stop=False)
-                mm([(pu, yv, vw("WBN"))], start=False, stop=False)
-                mm([(pu, hv("MZ", h), vw("WB2"))], start=False)
-            else:
-                mm([(pu, vw("IB"), vw("C7"))], stop=False)
-                mm([(pu, av, vw("WBD"))], start=False)
-            tt(hv("E2", h), pu, vw("MR"), OP.mult)
-            ts(hv("E3", h), hv("E2", h), -16 * MAGIC, OP.add, 16 * MAGIC, OP.add)
-            pl = vw(pa, 384, 400)
-            mm([(pl, vw("IF"), hv("QP", h, 16)), (vw(pa, 384, 392), vw("IK"), hv(wt, h, 8)), (vw(pa, 392, 400), vw("IS"), hv(wt, h, 8))]
-               + ([(vw(pa, 392, 400), vw("IS"), hv("WW", h, 8))] if last else []), stop=False)
-            mm([(vw(pa, 384, 392), hv("E2", h), vw("DC"))], start=False, stop=False)
-            mm([(vw(pa, 384, 392), hv("E3", h), vw("DCM"))], start=False)
-            cp(hv("LB", h, 16, 32 * t), pl)
-            if h == 0:
-                send(hv("RL", t, 8), vw("LB", 32 * t, 32 * t + 8), "rb", PAR["rem"] - 0.5)
-            for j in PAR["ho"] if h == 1 and not last else ():
-                at(t, "u%d" % j)
-                if PAR["ywv"][j]:
-                    cp(vw("YW", 1 - j, 256, 2), lands[j][0])
-                else:
-                    act(vw("YW", 1 - j, 256, 2), lands[j][0], AF.Copy)
-                mm([(vw("PU", 0, 128), vw("WS"), lands[j][0])])
-                act(hv("HI", j), vw("PU", 0, 128), scale=col("MR", 1))
-            at(t, None)
+            if h and not last:
+                cp(vw("RP"), vw("LB", 64 * t + 40, 64 * t + 56))
+                for j in (1, 0):
+                    if j == 0:
+                        gather(vw("YW", 1, 256, 2), lands[0][0], not PAR["ya"])
+                    mm([(vw("PU", 0, 128), vw("WS"), lands[j][0])])
+                    act(hv("HI", j), vw("PU", 0, 128), scale=col("MR", 1))
+            u = hv("PU", h, 128, 256)
             mm([(hv("PF", h), vw("CU"), vw("ONB")), (hv("PF", h), vw("WBD"), av)])
             act(hv("UR", h), hv("PF", h), bias=MAGIC * W)
-            act(hv("UB", h), hv("UR", h), bias=-MAGIC * W)
-            mm([(hv("PU", h, 128, 256), vw("WBD"), av), (hv("PU", h, 128, 256), vw("IN"), hv("UB", h))])
-            fi = hv("FO", t + h) if h == 0 or last else vw("VS", H0 + NS * t + 128, H0 + NS * t + 256)
-            tt(hv("PR", h), fi, hv("PU", h, 128, 256), OP.mult)
-            ts(hv("PR", h), hv("PR", h), 5, OP.arith_shift_right)
+            mm([(u, vw("INF"), hv("UR", h)), (u, vw("ONB", p1=1), vw("CM", p1=1)), (u, vw("WBD"), av)])
+            tt(hv("PR", h), hv("FF", h) if h == 0 or last else vw("VS", H0 + NS * t, H0 + NS * t + 256, 2), u, OP.mult)
             tt(hv("PR2", h), hv("PR", h), hv("PF", h, 128, 256), OP.add)
-            ts(hv("VS", h, 128, made(t)), hv("PR2", h), 4095, OP.bitwise_and)
+            ts(hv("VS", h, 128, made(t)), hv("PR2", h), 5, OP.arith_shift_right, 4095, OP.bitwise_and)
 
-        def look(j):
-            at(t, "x%d" % j)
-            if not last:
-                act(hv("OLD", j), ind(vw("X"), lands[j][1]), AF.Copy)
-                if not PAR["dda"][j]:
-                    tt(hv("DD", j), ind(vw("X"), lands[j][1]), lands[j][0], OP.max)
-        if PAR["both"]:
-            look(0)
-            look(1)
-        for j in PAR["jo"]:
-            ys, ls = lands[j]
-            if not PAR["both"]:
-                look(j)
-            at(t, "x%d" % j)
-            cp(ind(vw("X"), ls), ys)
-            at(t, "u%d" % j)
-            if not last:
-                pd = vw("PD%d" % j, 0, 128)
-                first = [(pd, vw("IB"), vw("QS")), (pd, vw("WS"), ys), (pd, vw("IN"), hv("HI", j))]
-                if PAR["dda"][j]:
-                    pe = vw("PA%d" % j, 128, 256)
-                    mm(first, stop=False)
-                    mm([(pe, vw("IN"), ys)], stop=False)
-                    mm([(pe, vw("IB"), hv("OLD", j))], start=False)
-                    act(hv("DD", j), pe, AF.Abs)
-                    mm([(pd, vw("AP"), hv("DD", j))], start=False)
+        for j in range(0 if last else 2):
+            if PAR["old"][j]:
+                act(hv("DD", j), ind(vw("X"), lands[j][1]), AF.Copy)
+                tt(hv("DR", j), ind(vw("X"), lands[j][1]), lands[j][0], OP.max)
+            else:
+                tt(hv("DD", j), ind(vw("X"), lands[j][1]), lands[j][0], OP.subtract)
+                ts(hv("DR", j), hv("DD", j), 0.0, OP.max)
+        for p in range(2 if last else 1):
+            a = W // 2 * p
+            for j in (1, 0):
+                ys, ls = lands[j]
+                if last:
+                    cp(ind(vw("X", a, a + W + W // 2), hv(ls[0], p, 4, ls[1])), hv(ys[0], p, 64, ys[1]))
                 else:
-                    mm(first + [(pd, vw("APN"), ys)], stop=False)
-                    mm([(pd, vw("APN"), hv("OLD", j))], start=False, stop=False)
-                    mm([(pd, vw("AP2"), hv("DD", j))], start=False)
-                if PAR["tna"][j]:
-                    act(hv("TN", j), pd, bias=col("BT", 2 * t + j))
-                else:
-                    ts(hv("TN", j), pd, col("BT", 2 * t + j), OP.add)
-                cp(ind(vw("T2"), ls), hv("TN", j))
-        if last:
-            at(t, "out")
-            for j in range(2):
-                dma("SA"[j], ("$", "yx", 2048 * j, 2048 * j + 2048), vw("X", 2048 * j, 2048 * j + 2048), 5.5)
-        at(t, None)
+                    cp(ind(vw("X"), ls), ys)
+            if last:
+                dma("S", ("$", "yx", a, a + W // 2), vw("X", a, a + W // 2))
+        if not last:
+            for j in (1, 0):
+                mm([(hv("PA0", 1 - j), vw("WS"), lands[j][0])] + [(hv("PA0", 1 - j), vw("APN"), lands[j][0])] * PAR["old"][j]
+                   + [(hv("PA0", 1 - j), vw("IN"), hv("HI", j))], start=j == 1, stop=False)
+            for j in (1, 0):
+                if j == PAR["so"]:
+                    mm([(vw("PA0", k, 256, 16), hv("SEL", k), vw("RP")) for k in range(16)], start=False, stop=False)
+                mm([(hv("PA0", 1 - j), vw("APN"), hv("DD", j))], start=False, stop=False)
+                mm([(hv("PA0", 1 - j), vw("AP2"), hv("DR", j))], start=False, stop=j == 0)
+            for j in (1, 0):
+                act(vw("TB", 1 - j, 256, 2), hv("PA0", 1 - j), bias=col("CF", 15))
         if t < TS - 2:
             for k in range(16):
                 asel(vw("ZX%d" % ((t + 1) % 2), k, W, 16), vw(zb), [[0, 256]], OP.is_ge, 1, 0)
@@ -568,17 +574,15 @@ def build(rank, cores, topo):
     for h in range(2):
         act(vw("OZ", 1 - h, 256, 2), hv(zf, h), AF.Copy)
         act(vw("OS", 1 - h, 256, 2), hv("SF", h), AF.Copy)
-    dma("S", ("$", "yz", 0, 256), vw("OZ"), 2.0)
-    dma("S", ("$", "ys", 0, 256), vw("OS"), 2.0)
+    dma("A", ("$", "yz", 0, 256), vw("OZ"))
+    dma("A", ("$", "ys", 0, 256), vw("OS"))
     return ops
 
 
 def depend(ops):
     seen = {}
     for n, o in enumerate(ops):
-        dep = set()
-        if "after" in o:
-            dep.add(o["after"])
+        dep = set(o.get("after", ()))
         for v, w in [(v, False) for v in o["r"]] + [(v, True) for v in o["w"]]:
             for m, u, uw in seen.get(v[0], []):
                 if m == n:
@@ -587,8 +591,8 @@ def depend(ops):
                     dep.add(m)
                 elif (w or uw) and clash(u, v):
                     dep.add(m)
-        o["dep"] = dep
-        o["soft"] = {m for m in dep if ops[m]["eng"] == o["eng"] == "P" and o["goon"]}
+        o["soft"] = {m for m in dep if ops[m]["eng"] == o["eng"] and o.get("goon")} | (set(o.get("behind", ())) - dep)
+        o["dep"] = dep | o["soft"]
         for v, w in [(v, False) for v in o["r"]] + [(v, True) for v in o["w"]]:
             lst = seen.setdefault(v[0], [])
             if w and v[0] not in PS:
@@ -597,188 +601,24 @@ def depend(ops):
 
 
 def schedule(ops):
-    n = len(ops)
-    pred = [list(o["dep"]) for o in ops]
-    succ = [[] for _ in ops]
-    for i in range(n):
-        for d in pred[i]:
-            succ[d].append(i)
-    pr = [o["pr"] for o in ops]
-    for i in range(n - 1, -1, -1):
-        for d in pred[i]:
-            pr[d] = min(pr[d], pr[i])
-    prio = sorted(range(n), key=lambda i: (pr[i], i))
-    best = None
-    for _ in range(PAR["pass"]):
-        start, end = place(ops, prio, pred, False)
-        if best is None or max(end) < best[0]:
-            best = (max(end), sorted(range(n), key=lambda i: (start[i], i)))
-        back = sorted(range(n), key=lambda i: (-end[i], -i))
-        _s, bend = place(ops, back, succ, True)
-        prio = sorted(range(n), key=lambda i: (-bend[i], i))
-    return improve(ops, best[1])
-
-
-def improve(ops, order):
-    n, hop = len(ops), PAR["hop"]
-    anc, pred, succ = [0] * n, [], [[] for _ in ops]
+    calls = STEP.split()
+    step = {x.strip("+-"): k + len(calls) * (x.count("+") - x.count("-")) for k, x in enumerate(calls)}
+    first = {x: k - 10000 for k, x in enumerate(FIRST.split())}
+    last = {x: k + 10000 for k, x in enumerate(LAST.split())}
+    rank = []
     for i, o in enumerate(ops):
-        keep, m = [], 0
-        for d in sorted(o["dep"], reverse=True):
-            if not (m >> d) & 1:
-                keep.append(d)
-                succ[d].append(i)
-                m |= anc[d] | (1 << d)
-        anc[i] = m
-        pred.append(keep)
-    names = {}
-    keys = [names.setdefault(o["key"], len(names)) for o in ops]
-    base = [100 * o["step"] for o in ops]
-    st = place(ops, order, pred, False)[0]
-    mark = [st[i] for i in range(n) if ops[i]["key"].endswith("VKEY0")]
-    fine = [0.0] * len(names)
-    for t in (4, 1, 3, 2, 0, 5):
-        for i in range(n):
-            if ops[i]["step"] == t:
-                fine[keys[i]] = (st[i] - mark[t]) / (mark[3] - mark[2]) * 100
-
-    gaps = [[(d, 0.0 if d in ops[i]["soft"] else hop) for d in pred[i]] for i in range(n)]
-    kind = [(gaps[i], "VAPGSR".index(o["eng"]), o["cost"], o.get("lat", 0.0)) for i, o in enumerate(ops)]
-    edges = [(i, d) for i in range(n - 1, -1, -1) for d in pred[i]]
-    both = list(zip(base, keys))
-
-    def rate(f):
-        pr = [b + f[k] for b, k in both]
-        for i, d in edges:
-            if pr[i] < pr[d]:
-                pr[d] = pr[i]
-        st, en = [0.0] * n, [0.0] * n
-        busy = [([], []) for _ in range(5)]
-        for _p, i in sorted(zip(pr, range(n))):
-            r = 0.0
-            gap, e, c, lat = kind[i]
-            for d, x in gap:
-                x += en[d]
-                if x > r:
-                    r = x
-            if e < 5:
-                lo, hi = busy[e]
-                m = k = len(hi)
-                while k and hi[k - 1] > r:
-                    k -= 1
-                while k < m and lo[k] < r + c:
-                    r = hi[k]
-                    k += 1
-                lo.insert(k, r)
-                hi.insert(k, r + c)
-            st[i] = r
-            en[i] = r + c + lat
-        return max(en), st, en, pr
-
-    def chain(st, en):
-        before = {(ops[i]["eng"], round(st[i] + ops[i]["cost"], 6)): i for i in range(n)}
-        i, pairs = max(range(n), key=lambda j: en[j]), []
-        while True:
-            b, x = max(gaps[i], key=lambda p: en[p[0]] + p[1]) if pred[i] else (None, 0)
-            j = before.get((ops[i]["eng"], round(st[i], 6)))
-            if b is not None and en[b] + x >= st[i] - 1e-6:
-                i = b
-            elif j is not None and j != i:
-                pairs.append((j, i))
-                i = j
-            else:
-                return pairs
-
-    seed = [PAR["seed"]]
-
-    def rnd():
-        seed[0] = (seed[0] * 1103515245 + 12345) % 2147483648
-        return seed[0] / 2147483648
-
-    def strict(f):
-        pr = [b + f[k] for b, k in both]
-        for i, d in edges:
-            if pr[i] < pr[d]:
-                pr[d] = pr[i]
-        st, en = [0.0] * n, [0.0] * n
-        free = [0.0] * 6
-        for _p, i in sorted(zip(pr, range(n))):
-            gap, e, c, lat = kind[i]
-            r = free[e]
-            for d, x in gap:
-                x += en[d]
-                if x > r:
-                    r = x
-            st[i] = r
-            r += c
-            if e < 5:
-                free[e] = r
-            en[i] = r + lat
-        return max(en), st, en, pr
-
-    best = None
-    for rate, tries, heat in ((rate, PAR["tries"], PAR["heat"]), (strict, PAR["tries2"], PAR["heat2"])):
-        if best:
-            st = best[1]
-            mark = [st[i] for i in range(n) if ops[i]["key"].endswith("VKEY0")]
-            for t in (4, 1, 3, 2, 0, 5):
-                for i in range(n):
-                    if ops[i]["step"] == t:
-                        fine[keys[i]] = (st[i] - mark[t]) / (mark[3] - mark[2]) * 100
-        cur, st, en, pr = rate(fine)
-        best, pairs = min(best or (1e9,), (cur, st)), chain(st, en)
-        for it in range(tries):
-            f = list(fine)
-            j, i = pairs[int(rnd() * len(pairs))]
-            u = rnd()
-            if u < 0.4:
-                f[keys[i]] = pr[j] - base[i] - 0.001 - rnd() ** 3 * 3
-            else:
-                p = pr[i] + 0.001 + rnd() ** 3 * 6 if u < 0.8 else pr[j] + rnd() * 30
-                todo, seen = [j], set()
-                while todo:
-                    x = todo.pop()
-                    if x not in seen and x != i:
-                        seen.add(x)
-                        f[keys[x]] = max(f[keys[x]], p - base[x])
-                        todo += [y for y in succ[x] if pr[y] < p]
-            v, st, en, pr2 = rate(f)
-            if v <= cur - (heat * (1 - it / tries) + 1e-4) * math.log(rnd() + 1e-12):
-                fine, cur, pr, pairs = f, v, pr2, chain(st, en) or pairs
-                if v < best[0]:
-                    best = (v, st)
-    return sorted(range(n), key=lambda i: (best[1][i] if pred[i] or "sem" not in ops[i] else -1.0, i))
-
-
-def place(ops, prio, pred, lat_first):
-    hop = PAR["hop"]
-    end = [0.0] * len(ops)
-    start = [0.0] * len(ops)
-    busy = {}
-    for i in prio:
-        o = ops[i]
-        e = o["eng"]
-        r = 0.0
-        for d in pred[i]:
-            x = end[d] + (0.0 if (d in o["soft"] or i in ops[d]["soft"]) else hop)
-            if x > r:
-                r = x
-        lat = o.get("lat", 0.0)
-        if lat_first:
-            r += lat
-        c = o["cost"]
-        if e != "R":
-            iv = busy.setdefault(e, [])
-            k = len(iv)
-            while k > 0 and iv[k - 1][1] > r:
-                k -= 1
-            while k < len(iv) and iv[k][0] < r + c:
-                r = max(r, iv[k][1])
-                k += 1
-            iv.insert(k, (r, r + c))
-        start[i] = r
-        end[i] = r + c + (0.0 if lat_first else lat)
-    return start, end
+        if "sem" in o and not o["dep"]:
+            rank.append(i - 20000)
+        elif o["step"] <= 1 and o["key"] in first:
+            rank.append(first[o["key"]])
+        elif o["step"] >= 4 and o["key"] in last:
+            rank.append(last[o["key"]])
+        else:
+            rank.append(len(calls) * o["step"] + step.get(o["key"], 30000))
+    for i in range(len(ops) - 1, -1, -1):
+        for d in ops[i]["dep"]:
+            rank[d] = min(rank[d], rank[i])
+    return sorted(range(len(ops)), key=lambda i: (rank[i], i))
 
 
 def rank_program(g, core, T, topo):
@@ -787,29 +627,28 @@ def rank_program(g, core, T, topo):
         return
     ops = build(rank, list(T.cores), topo)
     depend(ops)
-    if "order" not in KEPT:
-        KEPT["order"] = schedule(ops)
-    order = KEPT["order"]
+    order = schedule(ops)
     pos = {i: k for k, i in enumerate(order)}
     known = {}
     for i in order:
         o = ops[i]
         o["wait"] = []
-        if o["eng"] == "R":
+        if o["call"] is None:
             continue
         need = {}
-        for d in o["dep"]:
-            p = ops[d]
-            if d in o["soft"]:
-                continue
-            key = p.get("sem") or p["eng"]
+        for d in o["dep"] - o["soft"]:
+            key = ops[d].get("sem") or ops[d]["eng"]
             if key not in need or pos[d] > pos[need[key]]:
                 need[key] = d
-        for key, d in need.items():
-            if known.get((o["eng"], key), -1) < pos[d]:
-                known[(o["eng"], key)] = pos[d]
+        mine = known.setdefault(o["eng"], {})
+        for key, d in sorted(need.items(), key=lambda x: -pos[x[1]]):
+            if mine.get(key, -1) < pos[d]:
+                mine[key] = pos[d]
                 o["wait"].append(d)
                 ops[d]["mark"] = True
+                for k, x in ops[d].get("knew", {}).items():
+                    mine[k] = max(mine.get(k, -1), x)
+        o["knew"] = dict(mine)
     queue = {"V": g.vector, "A": g.scalar, "P": g.tensor, "G": g, "S": g.sync}
     count = {}
     sent = 0
@@ -822,6 +661,9 @@ def rank_program(g, core, T, topo):
         if v[0] == "$":
             t = T[v[1]]
             return t[:] if v[3] - v[2] == t.shape[1] else t[:, v[2]:v[3]]
+        if v[0] in SHARE:
+            name, a = SHARE[v[0]]
+            v = (name, v[1] + a, v[2] + a) + v[3:]
         t = T[v[0]]
         if len(v) > 5:
             return t[v[5]:v[4]:v[6], v[1]:v[2]:v[3]]
@@ -832,20 +674,17 @@ def rank_program(g, core, T, topo):
     tail = []
     for i in order:
         o = ops[i]
-        e = o["eng"]
-        if e == "R":
+        e, c = o["eng"], o["call"]
+        if c is None:
             o["sig"] = (o["sem"], o["cnt"])
             continue
         q = queue[e]
         for d in o["wait"]:
-            s, c = ops[d]["sig"]
-            q.wait_ge(T.sem[s], c)
-        c = o["call"]
+            q.wait_ge(T.sem[ops[d]["sig"][0]], ops[d]["sig"][1])
         if c[0] == "send":
-            dst, pairs, sem = c[1], c[2], c[3]
-            rid, pid = topo.addr(dst)[0], topo.addr(dst)[1]
-            g.remote_dma(ap(pairs[0][0]), ap(pairs[0][1]), T.sem[sem], T.sem["sent"], pid, rid, topo.mask(core, dst))
-            sent += len(topo.engines(core, dst))
+            rid, pid = topo.addr(c[1])[:2]
+            g.remote_dma(ap(c[2]), ap(c[3]), T.sem[c[4]], T.sem["sent"], pid, rid, topo.mask(core, c[1]))
+            sent += len(topo.engines(core, c[1]))
             continue
         if c[0] == "dma":
             q.dma_start(ap(c[1]), ap(c[2])).then_inc(T.sem[o["sem"]], 16)

@@ -1,3 +1,4 @@
+import numpy as np
 from concourse.mybir import AluOpType, AxisListType, ActivationFunctionType
 
 OP = AluOpType
@@ -7,33 +8,36 @@ WD = 2 * W
 Z0 = NS * (TS + 1)
 V0 = Z0 + 128
 H0 = V0 + W
+UN = 1024
 MAGIC = 12582912.0
 KU = 2.0 ** -14
-RU = 2.0 ** -30
+RU = 2.0 ** -34
 LOW = -(4095 << 12) - 1
 
 B, F, I, U = "bfloat16", "float32", "int32", "uint16"
 SB = {
-    "X": (WD, B), "VS": (H0 + NS * (TS - 1), I), "TB": (256, B), "YW": (256, B), "SEL": (2048, B),
+    "X": (WD, B), "VS": (H0 + NS, I), "VB": (UN + 3 * NS, F), "TB": (256, B), "YW": (256, B), "SEL": (2048, B),
     "M": (W, B), "G2": (W, B), "D": (W, B), "MX": (W, B), "MN": (W, B), "ZX0": (W, B), "ZX1": (W, B), "C2": (W, B),
-    "ZA0": (256, B), "ZA1": (256, B), "ZR": (256, B), "SR": (256, I), "S16": (256, U), "SF": (256, F), "B16": (256, B), "S4": (256, U),
+    "ZA0": (256, B), "ZA1": (256, B), "ZR": (256, B), "SR": (256, I), "S16": (256, U), "S4": (256, U),
     "WI": (8, I), "TI": (8, I), "WM": (256, I), "WMF": (256, F), "CF": (32, F), "PI": (16, I),
-    "JF": (144, F), "RF": (128, F), "GF": (128, F), "IF": (128, F), "INF": (128, F), "IF8": (128, F), "IN8": (128, F),
-    "IB": (128, B), "IH": (128, B), "IN": (128, B), "IK": (128, B), "IS": (128, B), "I4": (128, B), "IN4": (128, B),
-    "IP": (128, B), "IM": (128, B), "IQ": (128, B),
-    "BD": (128, B), "MR": (128, F), "WBD": (128, B), "ONF": (128, F), "ONB": (128, B), "CQ": (128, B), "CU": (128, B),
-    "CA": (128, B), "CM": (128, B), "C7": (128, B), "CB": (56, B), "TMP": (128, F), "TM2": (128, F), "DI": (128, F), "DJ": (128, B),
+    "JF": (144, F), "RF": (128, F), "GF": (128, F), "IF": (128, F), "IF8": (128, F), "IN8": (128, F), "INH": (128, F), "IF32": (128, F),
+    "IB": (128, B), "IH": (128, B), "IG": (128, B), "IN": (128, B), "IK": (128, B), "IS": (128, B), "I8": (128, B), "J8": (128, B),
+    "IP": (128, B), "IM": (128, B), "IQ": (128, B), "IU": (128, B),
+    "BD": (128, B), "MR": (128, F), "WBD": (128, B), "ONF": (128, F), "ONB": (128, B), "ONN": (128, B), "CQ": (128, B), "CU": (128, B),
+    "CA": (128, B), "CM": (128, B), "C16": (128, B), "C01": (128, B), "CR": (8, B), "C15": (128, B), "CT": (8, B), "RP1": (8, B),
+    "RN1": (8, B), "BH": (128, B), "BL": (128, B), "C32": (128, B), "CL": (128, B), "W2": (128, B), "W2N": (128, B), "C23": (128, B), "GL": (128, B),
+    "C7": (128, B), "CB": (24, B), "CE": (40, B), "TMP": (128, F), "TM2": (128, F), "DI": (128, F), "DJ": (128, B), "DK": (128, B), "B16": (256, B),
     "WO": (144, B), "WS": (128, B), "AP": (128, B), "AP2": (128, B), "APN": (128, B), "L15": (8, U), "LS": (8, U),
-    "BZ": (128, B), "XM": (128, F), "MZ": (256, B), "WB2": (128, B), "WBN": (128, B), "HT": (128, B), "GS": (256, B),
-    "DC": (16, F), "DC8": (8, F), "DCM": (16, F), "W1": (8, B), "WR": (40, B),
-    "BI0": (128, F), "BI1": (128, F), "BI": (128, B), "QP": (32, F), "QL": (8, B), "Q16": (16, F),
+    "BZ": (128, B), "XM": (128, F), "WBN": (128, B), "WB2": (128, B), "WN2": (128, B), "MZ": (256, B), "HA0": (256, B), "HA1": (256, B), "GS": (256, B),
+    "DC": (16, B), "DU": (24, F), "W1": (8, B), "WR": (40, B),
+    "BI0": (128, F), "BI1": (128, F), "BI": (128, B), "QP": (32, F), "QL": (8, B), "Q16": (16, F), "QB": (16, B),
     "MK0": (512, B), "MKB": (512, B), "MKN": (128, B),
-    "UW": (256, B), "SG0": (256, B), "SG1": (256, B), "KS": (256, F), "KEY": (256, F), "NE": (256, F), "SC": (256, F), "CN": (256, B),
-    "C1": (256, F), "NH": (16, F), "XB": (16, F), "BO": (16, B), "HS0": (16, B), "HS1": (16, B), "THR": (16, F), "TH2": (16, F),
-    "DB": (16, F), "E1": (256, F), "E2": (256, F), "E3": (256, F), "WT0": (16, B), "WT1": (16, B), "WW": (16, B), "DL": (16, U),
-    "NB": (16, F), "NH0": (16, F), "FI": (256, I), "FB": (256 * TS, U), "FF": (256, F), "YB": (256 * TS, B), "LB": (64 * TS, U),
-    "RY": (128 * TS, B), "RP": (16, B), "RV": (128 * TS, U), "DD": (256, B), "DR": (256, B), "HI": (256, B), "UR": (256, F),
-    "PR": (256, F), "PR2": (256, I), "AI": (8, I), "OS": (256, F), "OZ": (256, B),
+    "UW": (256, B), "SG0": (256, B), "SG1": (256, B), "KEY": (256, F), "NE": (256, F), "SC": (256, F), "CN": (256, B),
+    "C1": (256, F), "NH": (16, F), "XB": (16, F), "BO": (16, B), "HS0": (16, B), "HS1": (16, B), "THR": (16, F),
+    "DB": (16, F), "E1": (256, F), "E2": (256, B), "WT0": (16, B), "WT1": (16, B), "WW": (16, B), "DL": (16, U),
+    "NB": (8, F), "FI": (256, I), "FB": (256 * TS, U), "FF": (256, F), "YB": (256 * TS, B), "LB": (64 * TS, U),
+    "RY": (128 * TS, B), "RP": (16, B), "RV": (128 * TS, U), "DD": (256, B), "DR": (256, B),
+    "PR": (256, F), "PR2": (256, I), "OS": (256, F), "OZ": (256, B),
 }
 PS = ["PK0", "PK1", "PU", "PA0", "PA1", "PD0", "PD1", "PF"]
 SHARE = {}
@@ -43,70 +47,33 @@ for _k, _v in SB.items():
 SCRATCH = {k: ("sbuf", [128, v[0]], v[1]) for k, v in SB.items() if k not in SHARE}
 SCRATCH.update({"K" + d: ("sbuf", [128, 128 * sum(x[0] == "K" + d for x in SHARE.values())], d) for d in (B, F)})
 SCRATCH.update({k: ("psum", [128, 512], F) for k in PS})
-NDMA = 16
+NDMA = 24
 SEMAPHORES = (["qV", "qA", "qP", "qG", "sent"] + ["d%d" % k for k in range(NDMA)]
               + ["r%s%d" % (x, t) for x in "abc" for t in range(TS)] + ["rd%d" % (TS - 1)])
 
 PAR = {
-    "alt": {0: ("PK0", "PA1"), 7: ("PA1", "PU")},
-    "mcut": list(range(0, W + 1, 256)), "dv": (), "old": (0, 0), "xm": 1, "mz": 2, "ba": 0, "ya": 0, "so": 0,
+    "alt": {0: "PA0", 7: "PA1"},
+    "acut": 256, "mcut": 256,
     "gv": (0,),
     "cuts": ([0, 512, 1024, 1536, 1856, 2048], [0, 512, 1024, 1536, 2048]),
-    "dvl": (),
-    "c0v": (3, 4), "f0": (1, 2),
-    "zi": (6, 5),
-    "sets": ((("G2", 0, 64), ("M", 0, 128), ("G2", 64, 96), ("G2", 96, 128)), (("G2", 0, 96), ("M", 0, 96), ("G2", 96, 128), ("M", 96, 128))),
+    "dv": (),
+    "run": 4,
+    "split": 1,
+    "xm": 2,
+    "ya": (0, 0),
+    "c0v": (1, 3), "r0v": (0, 2, 5),
+    "old": (1, 1), "yw": 1,
+    "zi": (0, 16),
+    "zv": (0, 0), "gp": (0, 0, 0), "sg": (((0, 128),), ((0, 128),)), "sm": (((0, 128),), ((0, 128),)), "sl": (((0, 128),), ((0, 128),)),
 }
-STEP = """VUW0 +VPR128 PU.INC2 PK0.INUW PD1.B1BI PA0.IPUW VSG0 VM2816 VCN0 VKS0 +VVS0 VHS0 VBO0 VKEY0 VM2304 VNH0 VPK0256 AM3584 AG23584 AM3840
-ANH08 PD1.G2WR PD1.MW1 VXB0 +VPR2128 VNE0 VXM0 VSC0 +VVS128 VE10 +VX0_ PD1.G2WR_ PD1.MSG VUW128 PA0.E1DC PA1.B1CB PK0.IBWB PA1.IPUW PK1.INUW VDL0
-VSG128 VFB0 VKS128 VCN128 VWT0 GFB0 VFF0 VKEY128 VHS8 VBO8 VPK1256 AD1856 VNH8 VTH20 PD0.ONBO PA0.IBCQ VMN1856 VNE128 VMX1856 VCF9 VXB8 AD0 AD512
-AD1536 VSC128 VMN0 VDB8 VMX0 VE1128 PD1.INZA PU.HSIB PK1.IBWB PA1.E1DC VMX512 VMN512 VDL8 VMX1536 VMN1536 VFB128 AD1024 VMX1024 VMN1024 VSF0 APF256
-AD2048 AD2560 RRV0 PA0.IHMX PA0.IHMN PD0.INZA VYB0 PD0.IBYW AD3072 AZA0 AD3584 GYB0 VWT8 VAI0 VPF384 VMZ0 VB160 VMN2048 PK0.YBWB PA1.IBCQ PA0.IFWT
-PK0.MZWB VE20 VMN2560 VE30 PA0.E2DC PA0.E3DC PF.CUZA VMX2560 VMX3072 AUR0 AHT0 VLB0 VMX2048 VMN3072 RRY0 PU.INZA VMX3584 VMN3584 PA1.IHMX VAI1 VS40
-VVS6016 PA1.IHMN VCF12 VPR0 VYW0 VVS6017 VMZ128 VPR20 PD1.IBYW PU.WSYW PK1.YWWB PK1.MZWB ATHR0 ACF10 AZA128 AHI128 VE2128 GLB0 RLB48 PA1.IFWT
-PA0.WSHI PU.WSRY PF.CUZA_ PA1.E2DC VYW1 VE3128 -VM1536 -AC20 PA1.E3DC VLB24 -VM768 VDD128 VDD0 VDR128 VRP0 -VM2048 VDR0 -VM1280 -VM512 -VM1792
-GZX15 GZX8 GZX7 GZX13 GZX6 GZX14 GZX2 GZX12 GZX10 GZX1 GZX11 GZX3 GZX9 GZX4 GZX0 GZX5 -PD0.B1BI -PK0.INC2 AHI0 PA0.WSHI_ PA0.APDD PA0.APDR PA0.SERP
-PA0.APDD_ PA0.APDR_ -ANH00 -AC2256 AUR128 -AC23840 -AM0 -AC23584 -PA1.INC2 ATB0 ATB1 -AM256 -AG2512 -AG21024 -AG21536 -AG23072 -AG22560 -AG22048
--VG20 -VM1024 PU.INZA_ -PK0.IFUW -PA1.INC2_ -PA0.B1CB -PK1.IFUW -PD0.G2WR -PD0.MW1 -VM3328 -VM2560 -VM3072 VX0 -PD0.G2WR_ -PD0.G2SG"""
-FIRST = """iSX4112 iGPI0 iGJF0 iGGF0 iGRF0 iVCB0 iVONF0 iVCU0 iVPI2 iVPI3 iVPI1 iVCF0 iVCQ0 iVVS1792 iGNB4 iGNB0 iGCB16 iVIF0 iVMKB0 iVCF17 iVBD0
-iVDC0 iVCF18 iVCF4 iVCU0_ iVCA0 iVTM20 iVONB0 iVCF7 iVZA128 iVZA0 iVCF5 iGZX8 iGQL0 iGZX7 iGZX9 iGZX6 iGZX10 iGSEL1024 iVC70 iVMK00 iVMR0 iVMKN0
-iVCF15 iVZX15 iVWMF0 iVZX11 iVSF0 iPD1.WMIF iAIH0 iAI40 iAIS0 iAIB0 iAWR0 iAW10 iADC80 iANB0 iAIK0 iAWR8 iAIF80 iAZX5 iAZX0 iATMP0 iABZ0 iAZX2
-iAIP0 iVAP0 iVDC8 iVQ160 iPF.ONTM iPD1.WMIF_ iAAP20 iAIN0 iAZX3 iABI0 iAZX1 iABI00 iAZX4 iAIN80 iABI10 iAQP8 iVS16128 iVZX14 iVTHR0 iVQP24 iVS160
-iVZX12 aANH00 iVTM20_ iVX4096 iVLS0 iVHS0 iVCM0 iVSF128 iVZX13 iVMKN0_ aVB160 iVL150 iVCB8 iVMK00_ iVWO0 iVQP0 iGSEL512 iGSEL0 iGSEL1536 iGGS0
-iGSEL2 iGGS128 iVCF13 aVS40 iVCF6 aVG21536 iVCF12 iVVS128 aPK1.IBBZ aPK0.IBBZ aPK0.INHS aAG20 aPD0.ING2 aPA1.ING2 aPK1.INHS aAG21024 aAG2512 aAM0
-aAM1536 aPK0.G2WR aAG23072 aAG22560 aVM1024 aVM512 aVG22048 iVCF14 iVVS4480 iVDI0 aPK0.MW1 aPK0.G2WR_ aPK0.MHS aPD0.ING2_ aPU.ING2 aPA0.SFCB
-aAG23584 aAM2048 aVSG0 iVVS0 aVCN0 aVKEY0 aVHS0 aVBO0 aPD1.ING2 aPK1.G2WR aVPK0256 aVNH0 iVVS3968 aVXB0 aVNE0 aVXM0 aVSC0 iVVS5504 aVE10
-aPD0.ING2_2 aAM2560 aAM3072 iADCM0 iAWBD0 aAM3584 iADJ0 aANH08 iACB16 iAWBN0 aPA0.E1DC iVVS4992 aPK1.MW1 aPK1.G2WR_ aPK1.MHS aPA1.SFCB aVDL0 aVFI0
-aVWT0 iVMKB0_ iVCF10 aVFB0 aVSG128 iAWB20 iAWR16 aAD1024 iAINF0 aAD1536 aVFF0 aAD0 aAD1856 iAWR24 aAD512 aAPF256 aVCN128 aVKEY128 aVHS8 aVPK1256
-aVBO8 aVNH8 aVNE128 iVWS0 aVXB8 aVSC128 aVMN1024 aGFB0 aRRV0 aVDB8 aVMN1536 aVMX1536 aVE1128 aPD0.ONBO aPU.HSIB aPA1.E1DC aPK1.IBWB aVMX1024 aVMN0
-aVDL8 aVMX1856 aVMN1856 aVFI128 aVMX0 aVFB128 aVMX512 aVMN512 aAD3584 aAD3072 aPA0.IBCQ aPK0.IBWB aPA0.IHMX aPA0.IHMN aVWT8 aVPF384 aVCF9 aVYB0
-aVTH20 aVMZ0 aPD1.INZA aPK0.YBWB aVMN3584 iVCA0_ aPK0.MZWB aPD0.INZA aAD2560 aAD2048 aPA1.IBCQ aVE20 aVMX3072 aVE30 aVMX3584 iVCF8 aPA0.IFWT
-aPA0.E2DC aPD0.IBYW aPA0.E3DC aAZA0 aAHT0 aPF.CUZA aGYB0 aRRY0 aVMN2560 aVLB0 aVMX2560 aVMN3072 aVMX2048 aVMN2048 aATHR0 iAAPN0 aAUR0 iAWR32 iAIN40
-iAIQ0 aPA1.IHMX aPA1.IHMN aPU.INZA aGLB0 aRLB48 aVVS6016 aVAI0 aVYW0 aPD1.IBYW aPK1.YWWB aVMZ128 aPK1.MZWB aVPR0 aVAI1 aPU.WSYW aPA1.IFWT aVE2128
-aAZA128 iAIM0 aAHI128 aVYW1 aPA1.E2DC aVPR20 aVE3128 aPA1.E3DC VM512 aVLB24 VM2560 aVDD128 aVDD0 aVDR128 aVRP0 VM1536 aVDR0 aVCF12 VM1280 VM1024
-aPU.WSRY aPA0.WSHI aPF.CUZA_ PK1.IFMK aGZX9 aGZX15 aGZX2 aGZX8 aGZX5 aGZX10 aGZX4 aGZX3 aGZX1 aGZX0 aGZX7 aGZX12 aGZX14 aGZX13 aGZX11 aGZX6 AC23584
-AC20 PK0.INC2 ANH00 aAUR128 aAHI0 aPA0.WSHI_ AC2256 AC23840 aACF10 AM0 aPA0.APDD aPA0.APDR aPA0.SERP aPA0.APDD_ aPA0.APDR_ aATB0 aATB1 PA1.INC2
-AM256 AG2512 AG21024 AG21536 VM1792 VG20 VM768 VM3072 VM3328 PD0.B1BI aPU.INZA_ PA1.INC2_ PA0.B1CB aVPR128 PD0.G2WR PD0.MW1 VM2816 PD0.G2WR_
-PD0.G2SG aVVS6017 VUW0 PU.INC2 PK0.IFMK PK0.INUW aVVS0 VSG0 VC10 VCN0 PD1.B1BI PA0.INC1 AG22048 ANH08 AG23072 AG22560 AM3840 AM3584 AG23584
-PD1.G2WR VKS0 VHS0 VBO0 VKEY0 VNH0 VM2048 VPK0256 VXB0 VM2304 VNE0 VXM0 VSC0 aVX0 VE10 PD1.MW1 PD1.G2WR_ PA0.E1DC PD1.MSG aVX0_ VDL0 aVPR2128
-VUW128 PA1.B1CB PK0.IBWB PK1.INUW VFI0 VSG128 VFB0 VKS128 VCN128 VC1128 VKEY128 VHS8 aVVS128 VPK1256 VBO8 VWT0 VNH8 PA1.INC1 VNE128 VFF0 VXB8
-VSC128 AD0 GFB0 AD1536 AD512 RRV0 VMN0 VDB8 VMX0 VE1128 VMX1536 PA1.E1DC VMN512 VDL8 VTH20 AD1856 VMX1856 VMN1856 VFI128 VMN1536 VWT8 AD1024
-APF256 ATHR0 VFB128"""
-LAST = """zVM768 VDD128 zVM1792 VDR128 VRP0 VDD0 zVM1280 VDR0 ATHR0 zANH00 AHI128 zAC20 zPK1.IFUW PU.WSRY zAC2256 zPK0.INC2 PA0.WSHI zPA1.INC2
-PD1.IBYW AHI0 zAM0 zAC23840 zANH08 zAC23584 AZA128 PA0.WSHI_ PA0.APDD PA0.APDR PA0.SERP PA0.APDD_ PA0.APDR_ ATB1 ATB0 zAM256 zVM1536 zVM512 VPR20
-zAG2512 zVM3328 zVG20 zVM1024 zVM2048 zPD0.B1BI zPD1.B1BI PF.CUZA_ zPK0.IFUW zPD0.G2WR zAG21024 zAG21536 zPD0.MW1 zPD0.G2WR_ zPD0.G2SG zVM2560
-VCF12 VX0 AUR128 zAG22048 zAG22560 zAG23072 zVUW0 zVM2816 zVSG0 PU.INZA_ VPR128 zVCN0 zVKS0 zPK0.INUW zPA1.INC2_ zPA0.B1CB zPA0.IPUW zPD0.IBCQ
-zPU.INC2 zVHS0 zVBO0 zVKEY0 zVM3072 zVPK0256 zVNH0 zVM2304 zVXB0 zVNE0 zAM3840 zAG23584 zAM3584 zVXM0 zVSC0 zPD1.G2WR zPD1.MW1 zPD1.G2WR_ VVS6017
-zVE10 VX0_ zPD1.MSG zPA0.E1DC zVUW128 zVDL0 zPK1.INUW zPA1.B1CB zPA1.IPUW zPK0.IBWB zVSG128 zVFB0 zVKS128 zVCN128 zVWT0 zPA0.IBCQ zVKEY128 zAD0
-zAD1024 zAD512 zAD1536 zAD1856 zVHS8 zVPK1256 zVBO8 zVNH8 zVNE128 zVMN0 zVXB8 zVSC128 zVMX0 zVDB8 zVMN1024 zVE1128 zVMX1024 zPA1.E1DC zVMX512
-zVDL8 zVMN512 zPA0.IHMX zPA0.IHMN zPK1.IBWB zVFB128 zVMN1536 zVWW0 zVYB0 zVMX1536 zVFF0 ACF10 zAD2560 zAD2048 zAD3072 zAD3584 zGYB0 zVMZ0 zVMX1856
-zVMN1856 VPR2128 zVWT8 zPK0.YBWB zPK0.MZWB zPD0.IHMX zPD0.IHMN zPA0.IFQL zVE20 zVYB64 zVMN2560 zVE30 zVMX2560 zVMZ64 zPK0.IBWB_ zPA1.IBCQ
-zPD0.INZA zPA0.E2DC zVMN2048 zPA0.E3DC zPK0.YBWB_ zPK0.MZWB_ zPD0.IBYW zVLB8 zVMX2048 zVE20_ zVFF128 zVMX3072 zVMN3072 zVE30_ zPA1.IHMX zPA1.IHMN
-zPA0.IFWW zPA0.E2DC_ zPA0.E3DC_ zPD1.IBCQ zVMN3584 zVYB128 zVMX3584 zVMZ128 zVLB12 zVWW8 zAZA0 zAPF384 zAPF256 zPK1.YBWB zPF.CUZA zPD1.IHMX
-zPD1.IHMN zPK1.MZWB zPA1.IFWW zGLB8 zGYB64 zVYB192 zVE2128 zVMZ192 zVE3128 zPA1.E2DC zPK1.IBWB_ zAUR0 zPK1.YBWB_ zPA1.E3DC zPD1.INZA zPK1.MZWB_
-zPD1.IBYW zPU.INZA zAZA128 zAOZ1 zAOZ0 zRRY0 zRLB56 VVS0 zVLB24 zPA1.IFQL zVE2128_ zVX0 zVPR0 zVX0_ zVPR20 zVE3128_ zPA1.E2DC_ zPF.CUZA_ zPA1.E3DC_
-zVLB36 zVVS0 zVX2048 zGLB12 zRRY64 zRLB60 zSX0 zAOZ0_ zAUR128 zPU.INZA_ VVS128 zVPR128 zVX2048_ zVPR2128 zVVS128 zSX2048 zVSF0 zAOS1 zAOS0 zAOS0_"""
-PER = {"YB": 256, "LB": 64, "RY": 128, "RV": 128, "FB": 256}
+PLAN = {"slow": 1.25, "gather": 1.56, "scatter": 3.8, "wake": 0.14, "lag": 0.09, "own": 0.02, "act": 0.02, "pe": 0.43e-3, "mm": 0.005, "pelag": 0.03,
+        "send": 0.7, "row": 0.04, "link": 1.0e4, "land": 1.9, "first": 4.0, "dma": 1.5, "bytes": 4.5e5, "look": 2.0, "passes": 400, "shake": 0.3,
+        "some": 0.3, "turn": 0, "moves": 2000, "give": 0.002}
+RANGE = [{}, {"slow": 1.0, "gather": 1.56}, {"slow": 1.1, "gather": 1.15, "scatter": 2.5, "lag": 0.0, "own": 0.11},
+         {"slow": 1.4, "gather": 1.95, "scatter": 5.0}]
+
+
+EVERY = {"YB": 256, "LB": 64, "RY": 128, "RV": 128, "FB": 256, "VS": 256, "VB": 256, "CE": 8, "DU": 8}
 
 
 def vw(name, lo=0, hi=None, step=1, p1=128):
@@ -117,6 +84,10 @@ def vw(name, lo=0, hi=None, step=1, p1=128):
 
 def made(t):
     return NS * (TS - 1 - max(t, -1))
+
+
+def slot(t):
+    return UN + NS * (1 + t % 2)
 
 
 def ind(win, off):
@@ -133,8 +104,8 @@ def clash(a, b):
 
 def build(rank, cores, topo):
     ops = []
-    step, nth = [-1], {}
     pool = []
+    lastdma, group, seen = {}, {}, {}
 
     def add(eng, rd, wr, call, **kw):
         r, w = [], []
@@ -149,18 +120,9 @@ def build(rank, cores, topo):
                 w.append(v)
         o = {"eng": eng, "r": r, "w": w, "call": call}
         o.update(kw)
-        x = w[0] if w else r[0]
-        name = x[0][:2] if x[0][:2] in ("ZA", "ZX", "HS", "WT", "SG") else x[0]
-        c0 = x[1] % PER.get(name, 8192)
-        if name == "VS":
-            c0 = H0 + (x[1] - H0) % NS if x[1] >= H0 else x[1] % NS if x[1] < Z0 else x[1]
-        c0 -= name == "CF" and c0 == 11
-        key = eng + name + str(c0)
-        if eng == "P":
-            key = name + "." + call[1][0][1][0][:2] + call[1][-1][2][0][:2].replace("YB", "YW")
-        key = ["i", "a", "", "", "", "", "z"][step[0] + 1] + key
-        nth[key] = nth.get(key, 0) + 1
-        o["key"], o["step"] = key + ["", "_", "_2", "_3"][nth[key] - 1], max(step[0], 0)
+        name = (eng,) + tuple((x[0].rstrip("01") if x[0] not in PS else x[0], x[1] % EVERY.get(x[0], WD)) for x in (w + r)[:3])
+        seen[name] = seen.get(name, 0) + 1
+        o["name"] = name + (seen[name],)
         ops.append(o)
 
     def cp(out, a):
@@ -181,22 +143,45 @@ def build(rank, cores, topo):
     def act(out, a, func=AF.Identity, bias=0.0, scale=1.0):
         add("A", [a, bias, scale], [out], ("activation", out, a, func, bias, scale))
 
-    def mm(terms, start=True, stop=True):
-        add("P", [x for t in terms for x in t[1:]], [t[0] for t in terms], ("mm", terms, start, stop), goon=not start)
+    def mm(terms, start=True, stop=True, pin=False, block=False):
+        bank = terms[0][0][0]
+        step = PAR["run"] if len(terms) >= 16 else len(terms) if block else 1
+        for k in range(0, len(terms), step):
+            some = terms[k:k + step]
+            first, end = start and k == 0, stop and k + step >= len(terms)
+            if first:
+                group[bank] = len(ops)
+            add("P", [x for t in some for x in t[1:]], [t[0] for t in some], ("mm", some, first, end), goon=not first,
+                group=group[bank], end=end, pin=pin, opens=True)
+
+    def whole(out, big, n=128):
+        return [(out, x, vw(big, 0, n)) for x in (vw("IB"), vw("IN"))]
 
     def iota(out, pat, base, cm):
-        add("G", [], [out], ("iota", out, pat, base, cm), behind=pool[:1])
-        pool.append(len(ops) - 1)
+        add("G", [], [out], ("iota", out, pat, base, cm))
 
     def asel(out, a, pat, op, base, cm):
         add("G", [a], [out], ("affine_select", out, a, pat, op, 0.0, base, cm), behind=pool[:1])
-        pool.append(len(ops) - 1)
+        if pool:
+            pool.append(len(ops) - 1)
+
+    def widen(out, a, pool):
+        if pool:
+            add("G", [a], [out], ("affine_select", out, a, [[0, 128]], OP.is_ge, 0.0, 1, 0))
+        else:
+            cp(out, a)
 
     nd = [0]
 
     def dma(q, out, a):
-        add(q, [a] if a[0] != "$" else [], [out] if out[0] != "$" else [], ("dma", out, a), sem="d%d" % nd[0])
+        load = a[0] == "$"
+        add(q, [] if load else [a], [out] if out[0] != "$" else [], ("dma", out, a), sem="d%d" % nd[0], behind=lastdma.get(q, []) * load)
+        lastdma[q] = [len(ops) - 1]
         nd[0] += 1
+
+    def repeat(name, lo, n, hi):
+        for a in range(lo + n, hi, n):
+            dma("S", vw(name, a, a + n), vw(name, lo, lo + n))
 
     def col(name, j):
         return vw(name, j, j + 1)
@@ -230,82 +215,97 @@ def build(rank, cores, topo):
     DC = vw("DC", 0, 8)
     ts(vw("IF"), vw("JF", 0, 128), col("CF", 0), OP.is_equal)
     ts(vw("MR"), vw("RF"), col("CF", 1), OP.is_equal)
-    for name, x in (("IB", 1.0), ("IH", 0.5), ("IN", -1.0), ("IK", 32768.0), ("IS", 2048.0), ("I4", 4.0), ("IN4", -4.0),
-                    ("IP", 1.0 / 32), ("IM", -1.0 / 32), ("IQ", -1.0 / 16), ("INF", -1.0), ("IF8", 1.0 / 8192), ("IN8", -1.0 / 8192)):
+    for name, x in (("IB", 1.0), ("IH", 0.5), ("IG", -0.5), ("IN", -1.0), ("IK", 32768.0), ("IS", 2048.0), ("I8", 8.0), ("J8", -8.0),
+                    ("IP", 1.0 / 32), ("IM", -0.25), ("IQ", 0.25), ("IU", 1.0 / UN), ("IF8", 1.0 / 8192), ("IN8", -1.0 / 8192),
+                    ("INH", -1.0 / 16), ("IF32", 32.0)):
         act(vw(name), vw("IF"), scale=x)
-    mset(vw("ONF"), 1.0)
-    mset(vw("ONB"), 1.0)
-    mset(vw("CQ"), -0.25)
-    mset(vw("CU"), -16.0)
-    mset(vw("CU", p1=1), -15.5)
-    mset(vw("CA"), -32.0)
-    mset(vw("CA", p1=1), -24.5)
-    mset(vw("CM"), MAGIC * W)
-    mset(col("CF", 12), 0.5 * RU)
-    mset(vw("VS", Z0, V0), 1 << 24)
-    mset(vw("C7"), -7.5)
-    for j, x in enumerate([64, V0 - Z0 - 64 + 7.5]):
-        mset(hv("CB", j, 8), x / 256)
-    iota(vw("CB", 16, 56), [[NS // 128, TS - 1], [0, 8]], (H0 - Z0) // 128, 0)
-    act(vw("CB", 16, 56), vw("CB", 16, 56), scale=0.5)
-    iota(vw("NB", 0, 4), [[0, 2], [128, 2]], made(-1) - Z0, 1)
-    iota(vw("NB", 4, 12), [[-NS, 4], [128, 2]], made(0) - Z0 + 2 * NS, 1)
-    act(vw("NB", 0, 12), vw("NB", 0, 12), scale=1.0 / 8192)
-    for name, x, y in (("MK0", 1.0, 0.0), ("MKB", 0.0, 256.0), ("MKN", 0.0, -256.0)):
+    for name, x in (("ONF", 1.0), ("ONB", 1.0), ("ONN", -1.0), ("CQ", -0.25), ("CM", MAGIC * W), ("C16", MAGIC * 16), ("C01", MAGIC),
+                    ("CR", MAGIC * 32 * RU), ("C15", -15.0 / 32), ("CT", 15.5 * RU), ("RP1", RU), ("RN1", -RU), ("C32", 32.0), ("C7", -7.5),
+                    ("CU", 16.0), ("CA", -32.0)):
         mset(vw(name), x)
-        mset(vw(name, step=16), y)
+    mset(vw("CU", p1=1), 15.5)
+    mset(vw("VS", Z0, V0), 1 << 24)
+    mset(vw("VB", 0, NS), float(W))
+    repeat("VB", 0, NS, UN)
+    for j, x in enumerate([(V0 - Z0) / 512, (H0 - Z0) / 256]):
+        mset(hv("CB", j, 8), x)
+    iota(vw("CE", 0, 32), [[NS, 2], [-128, 2], [0, 8]], slot(0), 0)
+    iota(vw("CE", 32, 40), [[0, 8]], 0, -1)
+    iota(vw("NB", 0, 2), [[128, 2]], made(-1) - Z0, 1)
+    act(vw("NB", 2, 4), vw("NB", 0, 2), scale=1.0 / 16384)
+    act(vw("NB", 4, 6), vw("NB", 0, 2), scale=1.0 / 8192)
+    for name, x, y in (("MK0", 1.0, 0.0), ("MKB", 0.0, 256.0), ("MKN", 0.0, -256.0)):
+        n = SB[name][0] // 2 if name != "MKN" else 128
+        mset(vw(name, 0, n), x)
+        mset(vw(name, 0, n, 16), y)
+        repeat(name, 0, n, SB[name][0])
     cp(vw("LS"), vw("JF", 0, 8))
     LC = vw("LS")
-    ts(vw("L15"), vw("JF", 0, 8), 16.0, OP.mult, 15.0, OP.add)
+    if PAR["xm"]:
+        ts(vw("L15"), vw("JF", 0, 8), 16.0, OP.mult, 15.0, OP.add)
     act(vw("W1"), DC, scale=2 * KU)
-    act(vw("DC8"), DC, scale=8192.0)
-    act(vw("DCM"), vw("DC"), scale=-1.0)
+    for j, x in enumerate((16384.0, 8192.0, float(UN))):
+        act(hv("DU", j, 8), DC, scale=x)
     ts(col("CF", 7), col("CF", 1), 8.0, OP.is_ge)
+    ts(col("CF", 12), col("MR", 2), 1.0 / 16, OP.mult)
     ts(col("CF", 13), col("CF", 7), RU, OP.mult)
     ts(col("CF", 14), col("CF", 1), 2.0, OP.is_lt, -KU, OP.mult)
     ts(col("CF", 15), col("CF", 7), -255.0, OP.mult)
     act(vw("BZ"), vw("BD"), scale=2 * KU)
-    for j, x in enumerate((-KU, RU, col("MR", 2), col("CF", 13), col("CF", 14))):
+    for j, x in enumerate((-KU, RU, col("CF", 12), col("CF", 13), col("CF", 14))):
         act(hv("WR", j, 8), DC, scale=x)
     ts(col("CF", 4), col("CF", 2), 16.0, OP.mult, 15.0, OP.add)
     ts(vw("WO"), vw("JF"), col("CF", 4), OP.is_equal)
-    tt(vw("WS"), vw("WO", 14, 142), vw("WO", 15, 143), OP.add)
+    tt(vw("WS"), vw("WO", 15, 143), vw("WO", 14, 142), OP.subtract)
     ts(col("CF", 17), col("CF", 3), 8.0, OP.add)
     ts(vw("TM2"), vw("RF"), col("CF", 17), OP.is_equal)
     tt(vw("AP"), vw("TM2"), vw("BD"), OP.mult)
     act(vw("AP2"), vw("AP"), scale=2.0)
     act(vw("APN"), vw("AP"), scale=-1.0)
-    for a in range(0, 2048, 512):
-        iota(vw("SEL", a, a + 512), [[0, 512]], 0, 0)
+    iota(vw("SEL", 0, 512), [[0, 512]], 0, 0)
+    repeat("SEL", 0, 512, 2048)
     asel(vw("SEL", 2, 2048, 16), vw("ONB"), [[-1, 16], [-16, 8]], OP.is_equal, 0, 1)
     for h in range(2):
         asel(vw("GS", 128 * h, 128 * h + 128, 1, 16), vw("ONB", p1=16), [[-1, 8], [0, 16]], OP.is_equal, -8 * h, 1)
     cp(col("CF", 5), col("TI", 0))
     cp(col("CF", 6), col("WI", 0))
-    for j in (8, 10):
-        ts(col("CF", j), col("CF", 1), 37.0 * 32, OP.mult, -2.0 ** 23, OP.add)
+    ts(col("CF", 8), col("IF", 2), 160.0, OP.mult)
+    ts(col("CF", 9), col("IF", 1), 1024.0, OP.mult, col("CF", 8), OP.add)
+    ts(col("CF", 10), col("IF", 0), -2.0 ** 23, OP.mult)
+    act(vw("CL"), vw("RF"), bias=col("CF", 10), scale=col("CF", 9))
     act(vw("WBD"), vw("BD"), scale=col("CF", 6))
-    act(vw("WB2"), vw("WBD"), scale=2.0)
-    act(vw("WBN"), vw("WBD"), scale=-1.0)
+    for name, x in (("WBN", -1.0), ("WB2", 2.0), ("WN2", -2.0))[:3 if any(PAR["zv"]) else 1]:
+        act(vw(name), vw("WBD"), scale=x)
+    ts(vw("TM2"), vw("RF"), 2.0, OP.is_equal)
+    tt(vw("W2"), vw("TM2"), vw("WBD"), OP.mult)
+    act(vw("W2N"), vw("W2"), scale=-1.0)
+    act(vw("C23"), vw("TM2"), scale=23.5 / 128)
+    act(vw("TM2"), vw("TM2"), scale=-16.0)
+    tt(vw("GL", p1=16), vw("TM2", p1=16), vw("GS", 128, 256, 1, 16), OP.mult)
     ts(vw("Q16"), vw("JF", 0, 16), 16.0, OP.mult, col("CF", 1), OP.add)
+    cp(vw("QB"), vw("Q16"))
     for h in range(2):
-        ts(hv("QP", 3 * h, 8), vw("Q16", 0, 8), 32.0, OP.mult, 16.0 * (1 - h) + 7.5, OP.add)
+        ts(hv("QP", 3 * h, 8), vw("Q16", 0, 8), 32.0, OP.mult, 16.0 * (1 - h), OP.add)
     act(vw("QP", 8, 24), vw("Q16"))
     iota(vw("QL"), [[-W // 2, 2], [0, 4]], 0, 0)
     act(vw("TMP"), vw("IF"), scale=col("CF", 5))
     mm([(vw("PF", 0, 128), vw("ONF"), vw("TMP"))])
-    act(vw("BI0"), vw("PF", 0, 128), scale=-RU)
+    act(vw("BI0"), vw("PF", 0, 128), scale=-RU, bias=-0.5 * RU)
     act(vw("BI1"), vw("BI0"), bias=8 * 255 * RU)
+    act(vw("BH"), vw("BI1"))
+    tt(vw("BL"), vw("BI1"), vw("BH"), OP.subtract)
     act(vw("BI"), vw("RF"), scale=-KU / 16)
-    ts(col("CF", 18), col("CF", 1), 0.0, OP.is_gt, -1.0 / 8192, OP.mult)
+    ts(col("CF", 18), col("CF", 1), 0.0, OP.is_gt, -1.0, OP.mult)
     ts(vw("TM2"), vw("JF", 1, 129), col("CF", 0), OP.is_equal, col("CF", 18), OP.mult)
-    tt(vw("DI"), vw("IF8"), vw("TM2"), OP.add)
-    act(vw("DJ"), vw("DI"), scale=1.0 / 16)
+    tt(vw("TMP"), vw("IF"), vw("TM2"), OP.add)
+    act(vw("DI"), vw("TMP"), scale=1.0 / 16384)
+    act(vw("DJ"), vw("TMP"), scale=1.0 / 8192)
+    act(vw("DK"), vw("TMP"), scale=1.0 / UN)
 
     for h in range(2):
         src = vw("SR", 1 - h, 256, 2)
         cp(hv("S16", h), src)
-        ts(hv("SF", h), src, -7.5, OP.add)
+        cp(hv("VB", h, 128, UN), src)
         cp(hv("VS", h, 128, made(-1)), src)
         cp(hv("ZA0", h), vw("ZR", 1 - h, 256, 2))
     for k in range(16):
@@ -323,18 +323,16 @@ def build(rank, cores, topo):
     for j in range(4):
         ts(hv("VS", j, 512, V0 + 2048), hv("VS", j, 512, V0), 12, OP.arith_shift_right)
 
-    def settle_lists(t):
-        ts(vw("SF"), ind(vw("VS", made(t), Z0), hv("LB", 1, 16, 64 * t)), 0.0 if t == TS - 1 else -7.5, OP.add)
-
     me = cores[rank]
     for t in range(TS):
         last = t == TS - 1
-        step[0] = t
-        nth.clear()
+        seen.clear()
         zx = "ZX%d" % (max(t - 1, 0) % 2)
         za, zb = "ZA%d" % (t % 2), "ZA%d" % ((t + 1) % 2)
         hs, hp = "HS%d" % (t % 2), "HS%d" % ((t + 1) % 2)
         sg, sp = "SG%d" % (t % 2), "SG%d" % ((t + 1) % 2)
+        ha, hb = "HA%d" % (t % 2), "HA%d" % ((t + 1) % 2)
+        count = vw(hb, 0, 128, 1, 16)
         wt = "WT%d" % (t % 2)
         dst = cores[(rank + 1 + t % 3) % NR]
         lands = [(hv("RY", t), hv("LB", 7, 8, 64 * t)), (hv("YB", 1, 128, 256 * t) if last else vw("YW", 0, 256, 2), hv("LB", 4, 8, 64 * t))]
@@ -350,15 +348,18 @@ def build(rank, cores, topo):
             else:
                 act(out, rows, AF.Copy)
 
-        for a, b in zip(PAR["mcut"][:-1], PAR["mcut"][1:] if t else ()):
-            rows = ind(vw("YW"), vw("S4", a // 16, b // 16))
-            if a // 512 in PAR["alt"]:
-                bank = vw(PAR["alt"][a // 512][a // 256 % 2], 0, 256)
-                act(vw("C2", a, b), rows, AF.Copy)
-                mm([(bank, vw("IN"), vw(zx, a, b)), (bank, vw("IB"), vw("C2", a, b))])
-                act(vw("M", a, b), bank, AF.Relu)
-            else:
-                tt(vw("M", a, b), rows, vw(zx, a, b), OP.max)
+        for j in range(8 if t else 0):
+            n = PAR["acut" if j in PAR["alt"] else "mcut"]
+            for a in range(512 * j, 512 * j + 512, n):
+                b = a + n
+                rows = ind(vw("YW"), vw("S4", a // 16, b // 16))
+                if j in PAR["alt"]:
+                    bank = vw(PAR["alt"][j], 0, n)
+                    act(vw("C2", a, b), rows, AF.Copy)
+                    mm([(bank, vw("IN"), vw(zx, a, b)), (bank, vw("IB"), vw("C2", a, b))])
+                    act(vw("M", a, b), bank, AF.Relu)
+                else:
+                    tt(vw("M", a, b), rows, vw(zx, a, b), OP.max)
         for h in range(2):
             pk, pa, pd = "PK%d" % h, "PA%d" % h, "PD%d" % h
             for j in range(4 * h, 4 * h + 4):
@@ -368,174 +369,192 @@ def build(rank, cores, topo):
                     continue
                 rows = ind(vw("X", 0, W), vw("S16", a // 16, b // 16))
                 gather(vw("G2", a, b), rows, j in PAR["c0v"])
-                if j in PAR["f0"]:
-                    tt(vw("M", a, b), rows, vw(zx, a, b), OP.max)
+                bank = ["PD0", "PD1", "PU", "PA1", "PF", "PD0", "PD1", "PU"][j]
+                mm([(vw(bank, k, 512, 16), vw("IN"), hv(za, j, 32)) for k in range(16)], stop=False)
+                mm([(vw(bank), vw("IB"), vw("G2", a, b))], start=False)
+                if j in PAR["r0v"]:
+                    ts(vw("M", a, b), vw(bank), 0.0, OP.max)
                 else:
-                    bank = vw(["PD0", "PD1", "PU", "PA1", "PD0", "PD1", "PU", "PD0"][j])
-                    mm([(bank, vw("IN"), vw(zx, a, b)), (bank, vw("IB"), vw("G2", a, b))])
-                    act(vw("M", a, b), bank, AF.Relu)
+                    act(vw("M", a, b), vw(bank), AF.Relu)
 
             def lanes(bank, c, n, name, wts, q0, q1):
                 return [(vw(bank, c + k, c + k + 16 * n - 15, 16, q1) + (q0, 1),
                          vw(name, 2048 * h + 16 * q0 + k, 2048 * h + 16 * q1, 16), wts) for k in range(16)]
-            dp, ends, uw = vw(pa, 256, 384), vw(pa, 271, 384, 16), hv("UW", h)
-            act(hv("NH0", h, 8), hv("THR", h, 8), bias=col("NB", 2 * t + h), scale=(made(t - 2) - made(t - 3)) / 4096)
+            uw, sf = hv("UW", h), hv("VB", h, 128, UN)
+            run = vw(pa, 256, 384)
             if t == 0:
-                key, rho, reset = vw(pk, 0, 128), vw(pk, 128, 256), vw("MKN")
+                key, rho, reset, thr = vw(pk, 0, 128), vw(pk, 128, 256), vw("MKN"), hv("THR", h, 8)
+                dp, ends = vw(pa, 0, 128), vw(pa, 15, 128, 16)
                 more = [(vw(pk, 0, 128, 1, 32 * j + 32) + (32 * j, 1), hv(za, 4 * h + j, 32), vw("BZ"))
-                        for j in range(4) if 4 * h + j not in PAR["alt"] and 4 * h + j not in PAR["f0"]]
+                        for j in range(4) if 4 * h + j not in PAR["alt"]]
                 mm([(key, vw("IB"), vw("BI")), (rho, vw("IF"), vw("BI0"))] + more, stop=False)
                 news = [(vw(pk, 128 + k, 256, 16), vw("IN"), hv(hp, h, 8)) for k in range(16)]
                 mm(news[:15], start=False, stop=False)
                 for q0, q1 in ((0, 96), (96, 128)):
                     mm(lanes(pk, 0, 16, "G2", vw("WR", 0, 16), q0, q1), start=False, stop=False)
                     mm(lanes(pk, 0, 8, "M", vw("W1"), q0, q1) + news[15:] * (q0 > 0), start=False, stop=q0 > 0)
-                ts(hv(sg, h), rho, col("CF", 12), OP.is_gt)
+                ts(hv(sg, h), rho, 0.0, OP.is_gt)
                 tt(hv("KEY", h), key, hv(sg, h), OP.add)
-                mm([(dp, hv("SF", h), vw("DI")), (ends, vw("IP"), hv("CB", 0, 8)), (ends, vw("IP"), hv("CB", 1, 8))])
+                mm([(dp, sf, vw("DI")), (ends, vw("IP"), hv("CB", 0, 8))])
             else:
-                diff, rho, key, ba = (hv(pd, j) for j in range(4))
-                reset, kept = hv(pk, 0), hv(pk, 1)
-                mm([(diff, hv("B16", h), vw("IB")), (diff, vw("IB"), vw("C7")), (rho, vw("IF"), vw("BI1")), (diff, hv("SF", h), vw("INF"))]
-                   + [(ba, hv("B16", h), vw("IQ")), (ba, vw("CA"), vw("ONB")), (ba, hv("SF", h), vw("IF"))] * (t == 1)
-                   + [(diff, vw("HT", p1=16), vw("GS", 128 * h, 128 * h + 128, 1, 16)), (key, vw("IB"), vw("BI"))], stop=False)
-                mm([(kept, vw("IF"), hv("KEY", h)), (kept, vw("ONB", p1=4), vw("ONB", p1=4))] + [(kept, vw("IN"), hv(sg, h))] * (t > 1)
-                   + [(reset, vw("IB"), vw("MKN"))] + [(kept, vw("I4"), uw)] * (t > 1), stop=False)
-                for x in PAR["sets"][h]:
-                    end = x == PAR["sets"][h][-1]
-                    mm((lanes(pd, 256, 8, "M", vw("W1"), *x[1:]) if x[0] == "M" else lanes(pd, 0, 24, "G2", vw("WR", 16, 40), *x[1:]))
-                       + [(key, vw("IB"), hv(sp, h))] * end, start=False, stop=end)
-                ts(uw, diff, 0.0, OP.not_equal, col("CF", 12), OP.max)
-                mm([(kept, vw("IN4"), uw), (kept, vw("IN4"), uw), (reset, vw("IN4"), uw),
-                    (vw(pk, 1, 128), vw("I4"), vw("UW", 128 * h, 128 * h + 127))], start=False)
+                diff, rho, ba = (hv(pd, j) for j in range(3))
+                key, dp, thr, reset = hv(pk, 0), hv(pk, 1), vw(pk, 256, 264), hv(pa, 0)
+                ends = vw(pk, 143, 256, 16)
+                new = [(hv(pd, j, 64), vw(hb, 128, 256, 1, 16), vw("GS", 128 * h + 64 * j, 128 * h + 64 * j + 64, 1, 16)) for j in range(2)]
+                blk = hv("B16", h)
+                mm([(diff, blk, vw("IB")), (diff, sf, vw("INH"))]
+                   + [(ba, sf, vw("IF")), (ba, vw("CA"), vw("ONB")), (ba, blk, vw("IN"))] * (t == 1), stop=False)
+                low = col(pd, 384)
+                mm([(low, count, vw("RN1", 0, 1, 1, 16)), (low, vw("IB"), col("CT", 0))] + whole(low, "CR", 1)
+                   + [(low, count, vw("RP1", 0, 1, 1, 16))], start=False, stop=False, pin=True)
+                mm([(rho, vw("IB"), vw("BH")), (rho, vw("IB"), vw("BL")), new[0]], start=False, stop=False)
+                for x in PAR["sg"][h]:
+                    end = x == PAR["sg"][h][-1]
+                    mm(lanes(pd, 0, 16, "G2", vw("WR", 16, 32), *x) + new[1:] * end, start=False, stop=end)
+                mm([(key, vw("IB"), vw("BI")), (key, vw("ONN", p1=t), vw("ONB", p1=t)), (dp, blk, vw("DJ" if t == 1 else "DK")),
+                    (thr, vw("IH"), vw("ONB", 0, 8)), (thr, vw("IH"), hv(hs, h, 8)), (thr, vw("IG"), hv(hp, h, 8))]
+                   + ([(ends, vw("IP"), hv("CB", 1, 8))] if t == 1 else
+                      [(ends, vw("IU"), hv("CE", 2 * ((t - 1) % 2) + h, 8)), (ends, vw("IU"), hv("CE", 4, 8))]), stop=False)
+                for x in PAR["sm"][h]:
+                    mm(lanes(pk, 0, 8, "M", vw("W1"), *x), start=False, stop=False)
+                for x in PAR["sl"][h]:
+                    mm(lanes(pk, 0, 8, "G2", vw("WR", 32, 40), *x), start=False, stop=False)
+                ts(uw, diff, 0.0, OP.not_equal, low, OP.max)
                 tt(hv(sg, h), rho, uw, OP.is_gt)
-                tt(hv("KS", h), key, hv(sg, h), OP.add)
-                tt(hv("KEY", h), kept, hv("KS", h), OP.min)
-                mm([(dp, hv("B16", h), vw("DJ")), (ends, vw("IP"), hv("CB", t + 1, 8))], stop=False)
-                name, plus, minus = ("C1", "IF8", "IN8") if t == 1 else ("UW", "IM", "IP")
+                name, plus, minus = ("C1", "IF8", "IN8") if t == 1 else ("UW", "IQ", "IM") if t % 2 else ("UW", "IM", "IQ")
                 if t == 1:
                     tt(hv("C1", h), ba, uw, OP.mult)
                 a = 128 * h
-                mm([(vw(pa, 256, 383), vw(minus), vw(name, a + 1, a + 128)), (vw(pa, 271, 368, 16), vw(plus), vw(name, a + 16, a + 128, 16)),
-                    (dp, vw(plus), hv(name, h))], start=False)
+                mm([(vw(pk, 128, 255), vw(minus), vw(name, a + 1, a + 128)), (vw(pk, 143, 240, 16), vw(plus), vw(name, a + 16, a + 128, 16)),
+                    (dp, vw(plus), hv(name, h)), (key, vw("I8"), uw)], start=False)
+                tt(hv("KEY", h), key, hv("KEY", h), OP.min)
+
+                def lack(name, down, up):
+                    return [(reset, vw(down), hv(name, h)), (vw(pa, 1, 128), vw(up), vw(name, a, a + 127))]
+                mm([(reset, vw("IB"), vw("MKN"))] + lack(sp, "J8", "I8"), stop=False)
+                mm(lack("UW", "IB", "IN") * (2 if t == 1 else 1), start=False, stop=False)
+                mm(lack(sg, "J8", "I8")[::-1], start=False)
             scan(hv("CN", h), vw("MK0", 0, 128), hv(sg, h), OP.mult, OP.add)
-            scan(vw(pk, 256, 384), reset, hv("KEY", h), OP.add, OP.max)
-            tt(hv("NE", h), vw(pk, 256, 384), hv("KEY", h), OP.not_equal)
+            scan(run, reset, hv("KEY", h), OP.add, OP.max)
+            tt(hv("NE", h), run, hv("KEY", h), OP.not_equal)
             scan(hv("SC", h), hv("NE", h), dp, OP.mult, OP.add)
             cn = vw("CN", 128 * h + 15, 128 * h + 128, 16)
-            tt(hv("BO", h, 8), cn, hv("THR", h, 8), OP.is_gt)
-            tt(hv(hs, h, 8), cn, hv("THR", h, 8), OP.not_equal)
-            tt(hv("NH", h, 8), hv(hs, h, 8), hv("NH0", h, 8), OP.mult)
-            tt(hv("XB", h, 8), hv("NH", h, 8), hv("BO", h, 8), OP.add)
+            tt(hv("BO", h, 8), cn, thr, OP.is_gt)
+            tt(hv(hs, h, 8), cn, thr, OP.not_equal)
+            if t < 2:
+                ts(hv("NH", h, 8), hv(hs, h, 8), col("NB", 2 + 2 * t + h), OP.mult)
+            tt(hv("XB", h, 8), hv("NH" if t < 2 else hs, h, 8), hv("BO", h, 8), OP.add)
             if h < PAR["xm"]:
                 tt(vw("XM"), ind(hv("XB", h, 8), LC), vw("MR"), OP.mult)
                 tt(hv("E1", h), ind(hv("SC", h), vw("L15")), vw("XM"), OP.min)
             else:
                 tt(hv("DB", h, 8), vw("SC", 128 * h + 15, 128 * h + 128, 16), hv("XB", h, 8), OP.min)
                 tt(hv("E1", h), ind(hv("DB", h, 8), LC), vw("MR"), OP.mult)
-            mm([(vw(pa, 0, 8), hv("E1", h), vw("DC8"))])
-            ts(hv("DL", h, 8), vw(pa, 0, 8), float(Z0 - made(t - 2)), OP.add)
-            rows, fb = ind(vw("VS", made(t - 2), H0 + NS * t), hv("DL", h, 8)), hv("FB", h, 128, 256 * t)
+            p8 = vw(pa, 408, 416)
+            mm([(p8, vw("IB"), vw("C15", 0, 8))] + [(p8, vw("IB"), hv("QB", h, 8))] * (t > 1), stop=False)
+            mm([(p8, hv("E1", h), hv("DU", min(t, 2), 8))], start=False)
+            ts(hv("DL", h, 8), p8, MAGIC, OP.add, MAGIC - (Z0 - made(-1)) * (t < 2), OP.subtract)
+            fb = hv("FB", h, 128, 256 * t)
             if t < 2:
-                ts(hv("FI", h), rows, LOW, OP.bitwise_and)
-                rows = hv("FI", h)
-            ts(fb, rows, float(W), OP.min)
-            ts(hv(wt, h, 8), vw(pa, 0, 8), 0.0, OP.is_equal, 0.125, OP.mult)
+                ts(hv("FI", h), ind(vw("VS", made(-1), H0 + NS * t), hv("DL", h, 8)), LOW, OP.bitwise_and)
+                ts(fb, hv("FI", h), float(W), OP.min)
+                ts(hv(wt, h, 8), p8, -15.0 / 32, OP.is_equal, 0.125, OP.mult)
+            else:
+                cp(fb, ind(vw("VB"), hv("DL", h, 8)))
+                ts(hv(wt, h, 8), p8, UN / 2, OP.is_lt, 0.125, OP.mult)
             if last:
                 tt(hv("WW", h, 8), hv("WT0", h, 8), hv("WT1", h, 8), OP.min)
             if h == 0 and not last:
                 send(hv("RV", t), fb, "rc")
-                cp(vw("VS", H0 + NS * t + 1, H0 + NS * t + 256, 2), hv("RV", t))
             if h == 0 or last:
-                cp(hv("FF", h), fb)
-                act(hv("PF", h, 128, 256), hv("FF", h), bias=col("CF", 10 + t % 2), scale=32.0)
-            else:
-                cp(vw("VS", H0 + NS * t, H0 + NS * t + 256, 2), fb)
-                ts(hv("PF", h, 128, 256), fb, 32.0, OP.mult, col("CF", 10 + t % 2), OP.add)
+                widen(hv("FF", h), fb, PAR["gp"][0])
+        for h in range(0 if last else 2):
+            view = hv("FB", 1, 128, 256 * t) if h else hv("RV", t)
+            widen(vw("VB", slot(t) + 1 - h, slot(t) + NS, 2), view, PAR["gp"][1 + h])
+            if t == 0:
+                cp(vw("VS", H0 + 1 - h, H0 + NS, 2), view)
         if not last:
             if t:
-                settle_lists(t - 1)
-            if PAR["ba"]:
-                act(vw("OS"), vw("SF"), bias=16 * MAGIC)
-                act(vw("B16"), vw("OS"), bias=-16 * MAGIC)
-            else:
-                ts(vw("B16"), vw("SF"), 16 * MAGIC, OP.add, -16 * MAGIC, OP.add)
-            ts(vw("S4"), vw("B16"), 1.0 / 16, OP.mult)
-            mm([(vw("PD0", 384, 400), vw("ONB"), vw("BO"))])
-            add("V", [vw("PD0", 384, 400)], [col("CF", 9)], ("tensor_reduce", col("CF", 9), vw("PD0", 384, 400)))
-            cp(col("AI", 0), col("CF", 9))
-            ts(col("AI", 1), col("AI", 0), 31, OP.bitwise_and)
-            ts(col("CF", 12), col("AI", 1), 0.5, OP.add, RU, OP.mult)
-            act(col("CF", 10 + (t + 1) % 2), col("CF", 9), bias=col("CF", 8), scale=32.0)
-            tt(vw("TH2"), vw(hp), vw(hs), OP.subtract)
-            act(vw("THR"), vw("TH2"), bias=0.5, scale=0.5)
-            mm([(vw("PU", 128, 256, 1, 16), vw(hs), vw("IB"))])
-            act(vw("HT", p1=16), vw("PU", 128, 256, 1, 16), scale=128.0)
+                cp(vw("VB", UN, UN + NS), ind(vw("VS", made(t - 1), Z0), hv("LB", 1, 16, 64 * (t - 1))))
+            ts(vw("S4"), vw("VB", UN, UN + NS), -7.5, OP.add, 1.0 / 16, OP.mult)
+            cp(vw("B16"), vw("S4"))
+            mm([(vw("PF", 256, 384, 1, 16), vw("BO"), vw("ONB")), (vw("PF", 384, 512, 1, 16), vw(hs), vw("IB"))])
+            act(vw(ha, p1=16), vw("PF", 256, 512, 1, 16), AF.Copy)
         for h in range(2):
             pa, pk = "PA%d" % h, "PK%d" % h
             yv = lands[1][0] if h else hv("YB", 0, 128, 256 * t)
+            av = hv(zb, h)
             cuts = [2048 * h + a for a in PAR["cuts"][h]]
             for a, b in zip(cuts[:-1], cuts[1:]):
-                gather(vw("D", a, b), ind(vw("X", 0, W + 16), vw("FB", 256 * t + a // 16, 256 * t + b // 16)), a in PAR["dvl" if last else "dv"])
+                gather(vw("D", a, b), ind(vw("X", 0, W + 16), vw("FB", 256 * t + a // 16, 256 * t + b // 16)), a in PAR["dv"])
             for a, b in zip(cuts[:-1], cuts[1:]):
                 scan(vw("MX", a, b), vw("MK0", 0, b - a), vw("D", a, b), OP.mult, OP.max)
                 scan(vw("MN", a, b), vw("MKB", 0, b - a), vw("D", a, b), OP.add, OP.min)
-            for p, n in ((0, 64), (1, 64)) if last else ((0, 128),):
+            for p, n in ((0, 64), (1, 64)) if last and h >= PAR["split"] else ((0, 128),):
                 def part(v, p=p, n=n):
                     return (v[0], v[1] + n * v[3] * p, min(v[2], v[1] + n * v[3] * (p + 1)), v[3], v[4])
 
                 def rows(v, p=p, n=n):
                     return v[:4] + (n * p + n, n * p, 1)
-                py = vw("PD%d" % h, 0, n) if p else vw(pa, 128, 128 + n)
-                mm([(py, vw("IB"), vw("CQ", 0, n))], stop=False)
-                mm([(py, vw("IH"), part(vw("MX", 2048 * h + 15, 2048 * h + 2048, 16)))], start=False, stop=False)
-                mm([(py, vw("IH"), part(vw("MN", 2048 * h + 15, 2048 * h + 2048, 16)))], start=False)
-                ts(part(yv), py, MAGIC, OP.add, MAGIC, OP.subtract)
+                py, pz = vw("PA%d" % h, 128, 128 + n), vw("PD%d" % h, 256, 256 + n)
+                mx, mn = (part(vw(x, 2048 * h + 15, 2048 * h + 2048, 16)) for x in ("MX", "MN"))
+                way = PAR["ya"][h]
+                for x in (py, pz)[way == 2:]:
+                    mm([(x, vw("IB"), vw("CQ", 0, n))] + [(x, vw("IN"), part(hv(za, h)))] * (x == pz) + [(x, vw("IH"), mx)], stop=False)
+                    mm([(x, vw("IH"), mn)] + whole(x, "C01", n) * (x == pz or way == 1), start=False, block=True)
+                if PAR["zv"][h]:
+                    ts(part(hv("MZ", h)), pz, 0.0, OP.max)
+                else:
+                    act(part(av), pz, AF.Abs)
+                if way == 2:
+                    tt(part(yv), pz, part(hv(za, h)), OP.add)
+                elif way == 1:
+                    act(part(yv), py, AF.Copy)
+                else:
+                    ts(part(yv), py, MAGIC, OP.add, MAGIC, OP.subtract)
                 if h == 0:
                     send(part(hv("RY", t)), part(yv), "rc" if p else "ra")
                 pu = rows(vw(pk, 384, 512))
-                tt(part(hv("MZ", h)), part(yv), part(hv(za, h)), OP.max)
-                mm([(pu, part(vw("IB")), vw("C7")), (pu, part(hv(za, h)), vw("WBN"))], stop=False)
-                mm([(pu, part(yv), vw("WBN"))], start=False, stop=False)
-                mm([(pu, part(hv("MZ", h)), vw("WB2"))], start=False)
+                big = [(pu, part(vw("IB")), vw("C16")), (pu, part(vw("IN")), vw("C16"))]
+                if PAR["zv"][h]:
+                    act(part(av), pz, AF.Abs)
+                    z, mz = part(hv(za, h)), part(hv("MZ", h))
+                    mm([(pu, part(vw("IN")), vw("C7")), (pu, z, vw("WBN")), (pu, part(yv), vw("WBD"))], stop=False)
+                    mm([(pu, mz, vw("WN2"))] + big + [(pu, mz, vw("WB2")), (pu, z, vw("WBD")), (pu, part(yv), vw("WBN"))], start=False, block=True)
+                else:
+                    mm([(pu, part(vw("IN")), vw("C7"))], stop=False)
+                    mm([(pu, part(av), vw("WBN"))] + big + [(pu, part(av), vw("WBD"))], start=False, block=True)
                 tt(rows(hv("E2", h)), pu, rows(vw("MR")), OP.mult)
-                ts(rows(hv("E3", h)), rows(hv("E2", h)), -16 * MAGIC, OP.add, 16 * MAGIC, OP.add)
+                pa = "PF" if last else "PU"
                 pi, pp, pc, both = vw(pa, 392, 400), hv(pa, h, 8, 384 + 8 * h), hv(pa, 1 - h, 8, 392 - 8 * h), hv(pa, 0, 16, 384 + 8 * h)
                 if last:
-                    both = hv(pa, p, 4, 392)
-                    mm([(both, vw("IF"), hv("QP", p, 4, 24 * h)), (both, vw("IK"), hv(wt, p, 4, 8 * h)), (both, vw("IB"), hv("QL", p, 4))]
-                       + [(pc, vw("IF"), hv("QP", 1 + h, 8)), (pc, vw("IS"), hv(wt, h, 8)), (pc, vw("IS"), hv("WW", h, 8))] * (p != h), stop=False)
-                    mm([(both, rows(hv("E2", h)), rows(hv("DC", p, 4)))], start=False, stop=False)
-                    mm([(both, rows(hv("E3", h)), rows(hv("DCM", p, 4)))], start=False)
-                    a, b = ((8, 12), (12, 24), (0, 12), (12, 16))[2 * h + p]
+                    m = n // 16
+                    both = hv(pa, p, m, 392)
+                    mm([(both, vw("IF"), hv("QP", p, m, 24 * h)), (both, vw("IK"), hv(wt, p, m, 8 * h)), (both, vw("IB"), hv("QL", p, m))]
+                       + [(pc, vw("IF"), hv("QP", 1 + h, 8)), (pc, vw("IS"), hv(wt, h, 8)), (pc, vw("IS"), hv("WW", h, 8))] * (p != h or m == 8),
+                       stop=False)
+                    mm([(both, rows(hv("E2", h)), rows(hv("DC", p, m)))], start=False)
+                    a, b = ((8, 12), (12, 24), (0, 12), (12, 16))[2 * h + p] if m == 4 else (8 - 8 * h, 24 - 8 * h)
                     cp(vw("LB", 64 * t + 24 * h + a, 64 * t + 24 * h + b), vw(pa, 384 + a, 384 + b))
                     if h == 0:
-                        send(hv("LB", p, 4, 64 * t + 56), hv("LB", p, 4, 64 * t + 8), "rd" if p else "rb")
+                        send(hv("LB", p, m, 64 * t + 56), hv("LB", p, m, 64 * t + 8), "rd" if p else "rb")
                     continue
-                mm([(hv(pa, 0, 16, 392 - 8 * h), vw("IF"), hv("QP", h, 16)), (pp, vw("IN"), vw("C7", 0, 8)), (pp, vw("IK"), hv(wt, h, 8)),
+                mm([(hv(pa, 0, 16, 392 - 8 * h), vw("IF"), hv("QP", h, 16)), (pp, vw("IK"), hv(wt, h, 8)),
                     (pi, vw("IK"), hv(wt, h, 8)), (pc, vw("IS"), hv(wt, h, 8))], stop=False)
-                mm([(both, hv("E2", h), vw("DC"))], start=False, stop=False)
-                mm([(both, hv("E3", h), vw("DCM"))], start=False)
+                mm([(both, hv("E2", h), vw("DC"))], start=False)
                 cp(hv("LB", h, 24, 64 * t), vw(pa, 384, 408))
                 if h == 0:
                     send(hv("LB", 3, 16, 64 * t), hv("LB", 0, 16, 64 * t), "rb")
-            pd, av = vw("PD%d" % h, 256, 384), hv(zb, h)
-            mm([(pd, vw("IN"), hv(za, h))], stop=False)
-            mm([(pd, vw("IB"), yv)], start=False)
-            act(av, pd, AF.Abs)
             if h and not last:
-                cp(vw("RP"), vw("LB", 64 * t + 40, 64 * t + 56))
-                for j in (1, 0):
-                    if j == 0:
-                        gather(vw("YW", 1, 256, 2), lands[0][0], not PAR["ya"])
-                    mm([(vw("PU", 0, 128), vw("WS"), lands[j][0])])
-                    act(hv("HI", j), vw("PU", 0, 128), scale=col("MR", 1))
-            u = hv("PU", h, 128, 256)
-            mm([(hv("PF", h), vw("CU"), vw("ONB")), (hv("PF", h), vw("WBD"), av)])
-            act(hv("UR", h), hv("PF", h), bias=MAGIC * W)
-            mm([(u, vw("INF"), hv("UR", h)), (u, vw("ONB", p1=1), vw("CM", p1=1)), (u, vw("WBD"), av)])
-            tt(hv("PR", h), hv("FF", h) if h == 0 or last else vw("VS", H0 + NS * t, H0 + NS * t + 256, 2), u, OP.mult)
-            tt(hv("PR2", h), hv("PR", h), hv("PF", h, 128, 256), OP.add)
+                cp(vw("RP", 0, 8), vw("LB", 64 * t + 48, 64 * t + 56))
+                gather(vw("YW", 1, 256, 2), lands[0][0], not PAR["yw"])
+            u, pf = hv("PU", 0), hv("PU", 1)
+            ff = hv("FF", h) if h == 0 or last else vw("VB", slot(t), slot(t) + NS, 2)
+            mm([(pf, vw("IF32"), ff), (pf, vw("CL"), vw("ONB")), (u, vw("CU"), vw("ONB"))]
+               + [(pf, vw("C32", p1=16), count)] * (t > 0), stop=False)
+            mm([(u, vw("WBN"), av)] + whole(u, "CM") + [(u, vw("WBD"), av)], start=False, pin=True)
+            tt(hv("PR", h), ff, u, OP.mult)
+            tt(hv("PR2", h), hv("PR", h), pf, OP.add)
             ts(hv("VS", h, 128, made(t)), hv("PR2", h), 5, OP.arith_shift_right, 4095, OP.bitwise_and)
 
         for j in range(0 if last else 2):
@@ -556,24 +575,23 @@ def build(rank, cores, topo):
             if last:
                 dma("S", ("$", "yx", a, a + W // 2), vw("X", a, a + W // 2))
         if not last:
+            for j in (0, 1):
+                tb, av, y = hv("PF", 1 - j), hv(zb, 1), lands[j][0]
+                mm([(tb, vw("C23"), vw("ONB")), (tb, vw("W2N"), av)] * j + [(tb, vw("WS"), y)] + whole(tb, "C16"), start=j == 0, stop=False, pin=True)
+                mm([(tb, vw("WO", 14, 142), y)] + [(tb, vw("APN"), y)] * PAR["old"][j] + [(tb, vw("W2"), av), (tb, vw("GL", p1=16), vw(ha, 128, 256, 1, 16))] * j, start=False, stop=False)
+            mm([(vw("PF", 128 + k, 256, 16), hv("SEL", k), vw("RP", 0, 8)) for k in range(16)], start=False, stop=False)
+            for j in (0, 1):
+                mm([(hv("PF", 1 - j), vw("APN"), hv("DD", j))], start=False, stop=False)
+                mm([(hv("PF", 1 - j), vw("AP2"), hv("DR", j))], start=False, stop=j == 1)
             for j in (1, 0):
-                mm([(hv("PA0", 1 - j), vw("WS"), lands[j][0])] + [(hv("PA0", 1 - j), vw("APN"), lands[j][0])] * PAR["old"][j]
-                   + [(hv("PA0", 1 - j), vw("IN"), hv("HI", j))], start=j == 1, stop=False)
-            for j in (1, 0):
-                if j == PAR["so"]:
-                    mm([(vw("PA0", k, 256, 16), hv("SEL", k), vw("RP")) for k in range(16)], start=False, stop=False)
-                mm([(hv("PA0", 1 - j), vw("APN"), hv("DD", j))], start=False, stop=False)
-                mm([(hv("PA0", 1 - j), vw("AP2"), hv("DR", j))], start=False, stop=j == 0)
-            for j in (1, 0):
-                act(vw("TB", 1 - j, 256, 2), hv("PA0", 1 - j), bias=col("CF", 15))
+                act(vw("TB", 1 - j, 256, 2), hv("PF", 1 - j), bias=col("CF", 15))
         if t < TS - 2:
             for k in range(16):
                 asel(vw("ZX%d" % ((t + 1) % 2), k, W, 16), vw(zb), [[0, 256]], OP.is_ge, 1, 0)
-    settle_lists(TS - 1)
     zf = "ZA%d" % (TS % 2)
     for h in range(2):
         act(vw("OZ", 1 - h, 256, 2), hv(zf, h), AF.Copy)
-        act(vw("OS", 1 - h, 256, 2), hv("SF", h), AF.Copy)
+        cp(vw("OS", 1 - h, 256, 2), ind(vw("VS", made(TS - 1), Z0), hv("LB", 2 + h, 8, 64 * (TS - 1))))
     dma("A", ("$", "yz", 0, 256), vw("OZ"))
     dma("A", ("$", "ys", 0, 256), vw("OS"))
     return ops
@@ -587,7 +605,12 @@ def depend(ops):
             for m, u, uw in seen.get(v[0], []):
                 if m == n:
                     continue
-                if v[0] in PS and (ops[m]["eng"] != o["eng"] or (o["eng"] == "P")):
+                if v[0] in PS and o["eng"] == ops[m]["eng"] == "P" and o["group"] == ops[m]["group"]:
+                    hit = clash(u, v)
+                    o["opens"] = o["opens"] and not hit
+                    if m == o["group"] or o["end"] or (hit and (o["pin"] or ops[m]["pin"] or ops[m]["opens"])):
+                        dep.add(m)
+                elif v[0] in PS and (ops[m]["eng"] != o["eng"] or (o["eng"] == "P")):
                     dep.add(m)
                 elif (w or uw) and clash(u, v):
                     dep.add(m)
@@ -600,25 +623,198 @@ def depend(ops):
             lst.append((n, v, w))
 
 
-def schedule(ops):
-    calls = STEP.split()
-    step = {x.strip("+-"): k + len(calls) * (x.count("+") - x.count("-")) for k, x in enumerate(calls)}
-    first = {x: k - 10000 for k, x in enumerate(FIRST.split())}
-    last = {x: k + 10000 for k, x in enumerate(LAST.split())}
-    rank = []
+def size(v):
+    return 16 * size(v[2]) if v[0] == "@" else len(range(v[1], v[2], v[3]))
+
+
+def narrow(v):
+    return v[0] not in PS and SB[v[0]][1] in (B, U)
+
+
+def cost(o, plan):
+    c, e, f = o["call"], o["eng"], plan["slow"]
+    cycle = 0.83e-3 * f
+    if c is None:
+        return 128 / o["cnt"] * (plan["row"] + 2 * size(o["w"][0]) / plan["link"]), plan["land"]
+    if c[0] == "send":
+        return plan["send"], 0.0
+    if c[0] == "dma":
+        v = c[2] if c[1][0] == "$" else c[1]
+        return 0.05, size(v) * v[4] * (2 if narrow(v) else 4) / plan["bytes"]
+    if c[0] == "mm":
+        return f * sum(max(min(64, size(t[1])), size(t[2])) * (1 if narrow(t[1]) else 4) * plan["pe"] + plan["mm"] for t in c[1]), plan["pelag"]
+    vs = [x for x in c[1:] if isinstance(x, tuple)]
+    n = max(size(x) for x in vs)
+    if e == "G":
+        return (0.13 if c[0] == "iota" else 0.17) * f + 2 * n * cycle, 0.0
+    if any(x[0] == "@" for x in vs):
+        return 0.06 * f + plan["scatter" if vs[0][0] == "@" else "gather"] * n * cycle, 0.0
+    if e == "A":
+        return plan["act"] * f + max(64, n) * cycle, 0.0
+    if c[0] == "tensor_tensor":
+        k = 1 if vs[1][0] in PS or vs[2][0] in PS else 2
+    else:
+        k = 0.5 if all(narrow(x) for x in vs if size(x) == n) else 1
+    return max(64, k * n) * cycle, 0.0
+
+
+def place(eng, dur, nexts, urgency):
+    left = [0] * len(eng)
+    for x in nexts:
+        for j, _ in x:
+            left[j] += 1
+    ready, start = [0.0] * len(eng), [0.0] * len(eng)
+    free, todo = {e: 0.0 for e in eng}, {e: [] for e in eng}
+    for i, e in enumerate(eng):
+        if not left[i]:
+            todo[e].append(i)
+    for _ in eng:
+        t, e = min((max(free[e], min(ready[i] for i in x)), e) for e, x in todo.items() if x)
+        now = [i for i in todo[e] if ready[i] <= t + 1e-9]
+        i = min(now, key=lambda k: (ready[k] if e == "D" else urgency[k], k))
+        soon = [j for j in todo[e] if t < ready[j] < t + dur[i] and urgency[j] < urgency[i] and e != "D"]
+        if soon:
+            j = min(soon, key=lambda k: (urgency[k], k))
+            fit = [k for k in now if t + dur[k] <= ready[j] + 0.02]
+            if fit:
+                i = min(fit, key=lambda k: (urgency[k], k))
+            elif (max(ready[j] - urgency[j], ready[j] + dur[j] - urgency[i]) + PLAN["look"] * (ready[j] - t)
+                  < max(t - urgency[i], t + dur[i] - urgency[j])):
+                i, t = j, ready[j]
+        todo[e].remove(i)
+        start[i] = t
+        free[e] = t + dur[i]
+        for j, w in nexts[i]:
+            ready[j] = max(ready[j], t + dur[i] + w)
+            left[j] -= 1
+            if not left[j]:
+                todo[eng[j]].append(j)
+    return start
+
+
+def graph(ops, plan):
+    eng = [o["eng"] for o in ops]
+    dur, lag = (list(x) for x in zip(*[cost(o, plan) for o in ops]))
+    dur[eng.index("R") - 1] += plan["first"]
+    after, before = [[] for _ in ops], [[] for _ in ops]
+    data = {}
     for i, o in enumerate(ops):
-        if "sem" in o and not o["dep"]:
-            rank.append(i - 20000)
-        elif o["step"] <= 1 and o["key"] in first:
-            rank.append(first[o["key"]])
-        elif o["step"] >= 4 and o["key"] in last:
-            rank.append(last[o["key"]])
-        else:
-            rank.append(len(calls) * o["step"] + step.get(o["key"], 30000))
+        if o["call"] and o["call"][0] == "dma":
+            data[i] = len(eng)
+            eng.append("D")
+            dur.append(lag[i])
+            lag.append(0.0)
+            after.append([])
+            before.append([(i, plan["dma"])])
+            after[i].append((data[i], plan["dma"]))
+    for i, o in enumerate(ops):
+        for d in o["next"]:
+            w = 0.0
+            if d not in o["soft"] and o["call"] is not None:
+                d = data.get(d, d)
+                w = lag[d] + plan["wake"] + plan["lag"] * (eng[d] == "V") + plan["own"] * (eng[d] == eng[i])
+            before[i].append((d, w))
+            after[d].append((i, w))
+    return eng, dur, before, after
+
+
+def replay(order, eng, dur, before, after):
+    end, free = [0.0] * len(eng), {}
+    for i in order:
+        end[i] = free[eng[i]] = max([free.get(eng[i], 0.0)] + [end[d] + w for d, w in before[i]]) + dur[i]
+    return max(end)
+
+
+def schedule(ops):
+    reach = []
+    for o in ops:
+        far = 0
+        for d in o["dep"]:
+            if d not in o["soft"] or o["eng"] == "P":
+                far |= reach[d]
+        o["next"] = sorted(d for d in o["dep"] if not far >> d & 1)
+        reach.append(far | sum(1 << d for d in o["next"] if d not in o["soft"] or o["eng"] == "P"))
+    cases = [graph(ops, dict(PLAN, **x)) for x in RANGE]
+    eng, dur, before, after = cases[0]
+    tail = [0.0] * len(eng)
     for i in range(len(ops) - 1, -1, -1):
-        for d in ops[i]["dep"]:
-            rank[d] = min(rank[d], rank[i])
-    return sorted(range(len(ops)), key=lambda i: (rank[i], i))
+        for k in [j for j, _ in after[i] if j >= len(ops)] + [i]:
+            tail[k] = dur[k] + max([w + tail[j] for j, w in after[k]] + [0.0])
+    urgency, best, scale = [-x for x in tail], None, None
+    shake = np.random.RandomState(0)
+    names = {}
+    kin = np.array([names.setdefault(o["name"], len(names)) for o in ops] + [0] * (len(eng) - len(ops)))
+    for k in range(PLAN["passes"]):
+        if k > 5 and k % 2 == 0:
+            move = shake.normal(0, PLAN["shake"], len(names)) * (shake.rand(len(names)) < PLAN["some"])
+            urgency = (np.array(best[2]) + move[kin]).tolist()
+        eng, dur, before, after = cases[k // 2 % len(cases) if PLAN["turn"] else 0]
+        start = place(eng, dur, after, urgency)
+        order = sorted(range(len(eng)), key=lambda i: (start[i], i))
+        ends = [replay(order, *x) for x in cases]
+        scale = scale or ends
+        score = sum(a / b for a, b in zip(ends, scale))
+        back = place(eng, dur, before, [-s - d for s, d in zip(start, dur)])
+        urgency = [-s - d for s, d in zip(back, dur)]
+        if best is None or score < best[0]:
+            best = (score, order, urgency, ends)
+    order, ends = polish(best[1], cases, scale, kin.tolist(), shake)
+    return [i for i in order if i < len(ops)], ends
+
+
+def polish(order, cases, scale, kin, shake):
+    eng, n = cases[0][0], len(order)
+
+    def run(order):
+        ends, links = [], []
+        for _, dur, before, _ in cases:
+            end, free, why = [0.0] * n, {}, [None] * n
+            for i in order:
+                t, k = free.get(eng[i], (0.0, None))
+                for d, w in before[i]:
+                    if end[d] + w >= t:
+                        t, k = end[d] + w, -1 - d
+                why[i] = k
+                end[i] = t + dur[i]
+                free[eng[i]] = (end[i], i)
+            i = end.index(max(end))
+            ends.append(end[i])
+            while why[i] is not None:
+                if why[i] >= 0 and eng[i] not in "DR":
+                    links.append((why[i], i))
+                i = why[i] if why[i] >= 0 else -1 - why[i]
+        return sum(a / b for a, b in zip(ends, scale)), ends, links
+
+    def ahead(order, a, b):
+        order = list(order)
+        for j in [i for i in order if kin[i] == kin[b] and eng[i] == eng[b]]:
+            q = order.index(j)
+            p = next((x for x in range(q - 1, max(q - 400, -1), -1) if kin[order[x]] == kin[a] and eng[order[x]] == eng[a]), None)
+            if p is None:
+                continue
+            need = {j}
+            for x in range(q, p - 1, -1):
+                if order[x] in need:
+                    need.update(d for d, _ in cases[0][2][order[x]])
+                    if x < q:
+                        need.update(y for y in order[p:x] if eng[y] == eng[order[x]])
+            if order[p] not in need:
+                order[p:q + 1] = [y for y in order[p:q + 1] if y in need] + [y for y in order[p:q + 1] if y not in need]
+        return order
+    score, ends, links = run(order)
+    best = (score, order, ends)
+    for k in range(PLAN["moves"]):
+        a, b = links[shake.randint(len(links))]
+        other = ahead(order, a, b)
+        s, e, x = run(other)
+        if s < score + PLAN["give"] * (1 - k / PLAN["moves"]) * shake.rand():
+            score, ends, links, order = s, e, x, other
+            if s < best[0]:
+                best = (s, order, e)
+    return best[1:]
+
+
+ORDER = []
 
 
 def rank_program(g, core, T, topo):
@@ -627,7 +823,9 @@ def rank_program(g, core, T, topo):
         return
     ops = build(rank, list(T.cores), topo)
     depend(ops)
-    order = schedule(ops)
+    if not ORDER:
+        ORDER.extend(schedule(ops))
+    order = ORDER[0]
     pos = {i: k for k, i in enumerate(order)}
     known = {}
     for i in order:
@@ -700,8 +898,6 @@ def rank_program(g, core, T, topo):
                 ins = q.activation(ap(c[1]), ap(c[2]), c[3])
             else:
                 ins = q.activation(ap(c[1]), ap(c[2]), c[3], bias=ap(c[4]), scale=ap(c[5]))
-        elif c[0] == "tensor_reduce":
-            ins = q.tensor_reduce(ap(c[1]), ap(c[2]), AxisListType.X, OP.add)
         elif c[0] == "iota":
             if SB[c[1][0]][1] == I:
                 ins = q.iota(ap(c[1]), c[2], c[3], c[4])

@@ -8,7 +8,7 @@ WD = 2 * W
 Z0 = NS * (TS + 1)
 V0 = Z0 + 128
 H0 = V0 + W
-UN = 1024
+UN = 4096
 MAGIC = 12582912.0
 KU = 2.0 ** -14
 RU = 2.0 ** -34
@@ -16,27 +16,28 @@ LOW = -(4095 << 12) - 1
 
 B, F, I, U = "bfloat16", "float32", "int32", "uint16"
 SB = {
-    "X": (WD, B), "VS": (H0 + NS, I), "VB": (UN + 3 * NS, F), "TB": (256, B), "YW": (256, B), "SEL": (2048, B),
+    "X": (WD, B), "VS": (H0 + NS, I), "VB": (UN + NS * TS, F), "TB": (256, B), "YW": (256, B), "PT": (32, B),
     "M": (W, B), "G2": (W, B), "D": (W, B), "MX": (W, B), "MN": (W, B), "ZX0": (W, B), "ZX1": (W, B), "C2": (W, B),
-    "ZA0": (256, B), "ZA1": (256, B), "ZR": (256, B), "SR": (256, I), "S16": (256, U), "S4": (256, U),
-    "WI": (8, I), "TI": (8, I), "WM": (256, I), "WMF": (256, F), "CF": (32, F), "PI": (16, I),
+    "ZA0": (256, B), "ZA1": (256, B), "ZR": (256, B), "SR": (256, I), "S16": (256, U),
+    "SF0": (256, F), "SF1": (256, F), "SQ0": (256, U), "SQ1": (256, U), "BQ0": (256, B), "BQ1": (256, B),
+    "WI": (8, I), "TI": (8, I), "WM": (256, I), "WN": (256, B), "CF": (32, F), "PI": (16, I),
     "JF": (144, F), "RF": (128, F), "GF": (128, F), "IF": (128, F), "IF8": (128, F), "IN8": (128, F), "INH": (128, F), "IF32": (128, F),
-    "IB": (128, B), "IH": (128, B), "IG": (128, B), "IN": (128, B), "IK": (128, B), "IS": (128, B), "I8": (128, B), "J8": (128, B),
-    "IP": (128, B), "IM": (128, B), "IQ": (128, B), "IU": (128, B),
-    "BD": (128, B), "MR": (128, F), "WBD": (128, B), "ONF": (128, F), "ONB": (128, B), "ONN": (128, B), "CQ": (128, B), "CU": (128, B),
-    "CA": (128, B), "CM": (128, B), "C16": (128, B), "C01": (128, B), "CR": (8, B), "C15": (128, B), "CT": (8, B), "RP1": (8, B),
+    "IB": (128, B), "IH": (128, B), "IG": (128, B), "IN": (128, B), "I8": (128, B), "J8": (128, B),
+    "IM": (128, B), "IQ": (128, B), "IU": (128, B), "IL": (128, B), "I2": (128, B), "PL": (128, B),
+    "BD": (128, B), "MR": (128, F), "WBD": (128, B), "ONF": (128, F), "ONB": (128, B), "ONN": (128, B), "CU": (128, B),
+    "CA": (128, B), "CM": (128, B), "C16": (128, B), "C01": (128, B), "CR": (8, B), "CT": (8, B), "RP1": (8, B),
     "RN1": (8, B), "BH": (128, B), "BL": (128, B), "C32": (128, B), "CL": (128, B), "W2": (128, B), "W2N": (128, B), "C23": (128, B), "GL": (128, B),
-    "C7": (128, B), "CB": (24, B), "CE": (40, B), "TMP": (128, F), "TM2": (128, F), "DI": (128, F), "DJ": (128, B), "DK": (128, B), "B16": (256, B),
-    "WO": (144, B), "WS": (128, B), "AP": (128, B), "AP2": (128, B), "APN": (128, B), "L15": (8, U), "LS": (8, U),
+    "C7": (128, B), "CB": (24, B), "CE": (72, B), "C2K": (16, B), "SN": (16, B), "TMP": (128, F), "TM2": (128, F), "DI": (128, F), "DJ": (128, B), "DK": (128, B),
+    "WO": (144, B), "WS": (128, B), "AP2": (128, B), "APN": (128, B), "L15": (8, U), "LS": (8, U),
     "BZ": (128, B), "XM": (128, F), "WBN": (128, B), "WB2": (128, B), "WN2": (128, B), "MZ": (256, B), "HA0": (256, B), "HA1": (256, B), "GS": (256, B),
-    "DC": (16, B), "DU": (24, F), "W1": (8, B), "WR": (40, B),
+    "DC": (16, B), "DU": (32, F), "W1": (8, B), "WR": (40, B),
     "BI0": (128, F), "BI1": (128, F), "BI": (128, B), "QP": (32, F), "QL": (8, B), "Q16": (16, F), "QB": (16, B),
     "MK0": (512, B), "MKB": (512, B), "MKN": (128, B),
     "UW": (256, B), "SG0": (256, B), "SG1": (256, B), "KEY": (256, F), "NE": (256, F), "SC": (256, F), "CN": (256, B),
     "C1": (256, F), "NH": (16, F), "XB": (16, F), "BO": (16, B), "HS0": (16, B), "HS1": (16, B), "THR": (16, F),
     "DB": (16, F), "E1": (256, F), "E2": (256, B), "WT0": (16, B), "WT1": (16, B), "WW": (16, B), "DL": (16, U),
     "NB": (8, F), "FI": (256, I), "FB": (256 * TS, U), "FF": (256, F), "YB": (256 * TS, B), "LB": (64 * TS, U),
-    "RY": (128 * TS, B), "RP": (16, B), "RV": (128 * TS, U), "DD": (256, B), "DR": (256, B),
+    "RY": (128 * TS, B), "RV": (128 * TS, U), "DD": (256, B), "DR": (256, B),
     "PR": (256, F), "PR2": (256, I), "OS": (256, F), "OZ": (256, B),
 }
 PS = ["PK0", "PK1", "PU", "PA0", "PA1", "PD0", "PD1", "PF"]
@@ -47,33 +48,38 @@ for _k, _v in SB.items():
 SCRATCH = {k: ("sbuf", [128, v[0]], v[1]) for k, v in SB.items() if k not in SHARE}
 SCRATCH.update({"K" + d: ("sbuf", [128, 128 * sum(x[0] == "K" + d for x in SHARE.values())], d) for d in (B, F)})
 SCRATCH.update({k: ("psum", [128, 512], F) for k in PS})
-NDMA = 24
+NDMA = 34
 SEMAPHORES = (["qV", "qA", "qP", "qG", "sent"] + ["d%d" % k for k in range(NDMA)]
-              + ["r%s%d" % (x, t) for x in "abc" for t in range(TS)] + ["rd%d" % (TS - 1)])
+              + ["r%s%d" % (x, t) for x in "abc" for t in range(TS)])
 
 PAR = {
-    "alt": {0: "PA0", 7: "PA1"},
-    "acut": 256, "mcut": 256,
-    "gv": (0,),
+    "alt": {0: "PA0", 1: "PA1", 14: "PA0", 15: "PA1"},
+    "wide": (),
+    "gv": {0: 512},
     "cuts": ([0, 512, 1024, 1536, 1856, 2048], [0, 512, 1024, 1536, 2048]),
-    "dv": (),
+    "dv": (3072,),
     "run": 4,
-    "split": 1,
-    "xm": 2,
+    "cut": 64,
+    "tb": ("PD1", "PF"), "tv": (0, 0),
+    "xm": 1,
     "ya": (0, 0),
     "c0v": (1, 3), "r0v": (0, 2, 5),
     "old": (1, 1), "yw": 1,
-    "zi": (0, 16),
-    "zv": (0, 0), "gp": (0, 0, 0), "sg": (((0, 128),), ((0, 128),)), "sm": (((0, 128),), ((0, 128),)), "sl": (((0, 128),), ((0, 128),)),
+    "fill": ("C2K", "CR", "CT", "RP1", "RN1", "ONN", "C32", "CA"),
+    "pv": 1, "eal": (0, 1), "yal": (0, 1), "ea": (0, 0), "gate": "A", "late": 0, "s0": ((0, 128),), "fa": (1, 1), "gvl": {0: 512}, "dvl": (3072,),
+    "zi": (4, 4),
+    "zv": (0, 0), "gp": (0, 1, 0, 1), "gi": (0, 1, 1), "sg": (((0, 128),), ((0, 128),)), "sm": (((0, 128),), ((0, 128),)), "sl": (((0, 128),), ((0, 128),)),
 }
 PLAN = {"slow": 1.25, "gather": 1.56, "scatter": 3.8, "wake": 0.14, "lag": 0.09, "own": 0.02, "act": 0.02, "pe": 0.43e-3, "mm": 0.005, "pelag": 0.03,
-        "send": 0.7, "row": 0.04, "link": 1.0e4, "land": 1.9, "first": 4.0, "dma": 1.5, "bytes": 4.5e5, "look": 2.0, "passes": 400, "shake": 0.3,
-        "some": 0.3, "turn": 0, "moves": 2000, "give": 0.002}
-RANGE = [{}, {"slow": 1.0, "gather": 1.56}, {"slow": 1.1, "gather": 1.15, "scatter": 2.5, "lag": 0.0, "own": 0.11},
-         {"slow": 1.4, "gather": 1.95, "scatter": 5.0}]
+        "send": 0.7, "row": 0.04, "link": 1.0e4, "land": 1.5, "first": 4.0, "dma": 1.5, "bytes": 4.5e5, "look": 2.0, "passes": 60, "shake": 0.3,
+        "some": 0.3, "turn": 0, "moves": 10000, "give": 0.001, "ease": 0.0, "seed": 12, "aim": 0.0, "power": 20}
+RANGE = [{"slow": 1.27, "gather": 1.62, "scatter": 4.0, "par": 149}, {"slow": 1.0, "gather": 1.56, "par": 125},
+         {"slow": 1.1, "gather": 1.15, "scatter": 2.5, "lag": 0.0, "own": 0.11, "par": 124},
+         {"slow": 1.4, "gather": 1.95, "scatter": 5.0, "par": 179}, {"slow": 1.2, "gather": 2.0, "scatter": 2.5, "par": 158},
+         {"slow": 1.3, "gather": 1.2, "scatter": 5.5, "land": 2.1, "par": 145}]
 
 
-EVERY = {"YB": 256, "LB": 64, "RY": 128, "RV": 128, "FB": 256, "VS": 256, "VB": 256, "CE": 8, "DU": 8}
+EVERY = {"YB": 256, "LB": 64, "RY": 128, "RV": 128, "FB": 256, "VS": 256, "VB": 256, "CE": 16, "DU": 8}
 
 
 def vw(name, lo=0, hi=None, step=1, p1=128):
@@ -87,7 +93,7 @@ def made(t):
 
 
 def slot(t):
-    return UN + NS * (1 + t % 2)
+    return UN + NS * (1 + t)
 
 
 def ind(win, off):
@@ -105,7 +111,7 @@ def clash(a, b):
 def build(rank, cores, topo):
     ops = []
     pool = []
-    lastdma, group, seen = {}, {}, {}
+    lastdma, group, seen, gate = {}, {}, {}, {}
 
     def add(eng, rd, wr, call, **kw):
         r, w = [], []
@@ -120,6 +126,8 @@ def build(rank, cores, topo):
                 w.append(v)
         o = {"eng": eng, "r": r, "w": w, "call": call}
         o.update(kw)
+        if eng in gate and any(x[0] in ("RY", "RV", "RP") or (x[0] == "LB" and x[1] % 64 >= 48) for x in r):
+            o["behind"] = [gate[eng]]
         name = (eng,) + tuple((x[0].rstrip("01") if x[0] not in PS else x[0], x[1] % EVERY.get(x[0], WD)) for x in (w + r)[:3])
         seen[name] = seen.get(name, 0) + 1
         o["name"] = name + (seen[name],)
@@ -167,15 +175,15 @@ def build(rank, cores, topo):
 
     def widen(out, a, pool):
         if pool:
-            add("G", [a], [out], ("affine_select", out, a, [[0, 128]], OP.is_ge, 0.0, 1, 0))
+            add("G", [a], [out], ("affine_select", out, a, [[0, size(a)]], OP.is_ge, 0.0, 1, 0))
         else:
             cp(out, a)
 
     nd = [0]
 
-    def dma(q, out, a):
+    def dma(q, out, a, *then):
         load = a[0] == "$"
-        add(q, [] if load else [a], [out] if out[0] != "$" else [], ("dma", out, a), sem="d%d" % nd[0], behind=lastdma.get(q, []) * load)
+        add(q, [] if load else [a, *then], [out] if out[0] != "$" else [], ("dma", out, a), sem="d%d" % nd[0], behind=lastdma.get(q, []) * load)
         lastdma[q] = [len(ops) - 1]
         nd[0] += 1
 
@@ -203,8 +211,8 @@ def build(rank, cores, topo):
     iota(vw("GF"), [[1, 8], [0, 16]], 0, 0)
     iota(vw("RF"), [[0, 8], [1, 16]], 0, 0)
     iota(vw("JF"), [[1, 144]], 0, 0)
-    mset(vw("X", W, W + 16), 0.0)
-    dma("S", vw("X", W + 16, WD), vw("X", 16, W))
+    iota(vw("X", W, W + 16), [[0, 16]], 0, 0)
+    dma("S", vw("X", W + 16, WD), vw("X", 16, W), vw("VS", V0, V0 + 2048))
     ts(vw("PI", 1, 2), vw("PI", 0, 1), 15, OP.bitwise_and)
     ts(vw("PI", 2, 3), vw("PI", 0, 1), 4, OP.arith_shift_right)
     ts(vw("PI", 3, 4), vw("PI", 0, 1), 1, OP.arith_shift_right, 7, OP.bitwise_and)
@@ -215,22 +223,26 @@ def build(rank, cores, topo):
     DC = vw("DC", 0, 8)
     ts(vw("IF"), vw("JF", 0, 128), col("CF", 0), OP.is_equal)
     ts(vw("MR"), vw("RF"), col("CF", 1), OP.is_equal)
-    for name, x in (("IB", 1.0), ("IH", 0.5), ("IG", -0.5), ("IN", -1.0), ("IK", 32768.0), ("IS", 2048.0), ("I8", 8.0), ("J8", -8.0),
-                    ("IP", 1.0 / 32), ("IM", -0.25), ("IQ", 0.25), ("IU", 1.0 / UN), ("IF8", 1.0 / 8192), ("IN8", -1.0 / 8192),
+    for name, x in (("IB", 1.0), ("IH", 0.5), ("IG", -0.5), ("IN", -1.0), ("IL", 128.0), ("I8", 8.0), ("J8", -8.0),
+                    ("IM", -NS / UN), ("IQ", NS / UN), ("IU", 1.0 / UN), ("IF8", 1.0 / 8192), ("IN8", -1.0 / 8192),
                     ("INH", -1.0 / 16), ("IF32", 32.0)):
         act(vw(name), vw("IF"), scale=x)
-    for name, x in (("ONF", 1.0), ("ONB", 1.0), ("ONN", -1.0), ("CQ", -0.25), ("CM", MAGIC * W), ("C16", MAGIC * 16), ("C01", MAGIC),
-                    ("CR", MAGIC * 32 * RU), ("C15", -15.0 / 32), ("CT", 15.5 * RU), ("RP1", RU), ("RN1", -RU), ("C32", 32.0), ("C7", -7.5),
-                    ("CU", 16.0), ("CA", -32.0)):
-        mset(vw(name), x)
+    for name, x in (("ONF", 1.0), ("ONB", 1.0), ("CU", 16.0), ("C16", MAGIC * 16), ("C01", MAGIC), ("CM", MAGIC * W),
+                    ("ONN", -1.0), ("C32", 16.0), ("CA", -32.0), ("C2K", UN / 2),
+                    ("CR", MAGIC * 32 * RU), ("CT", 15.5 * RU), ("RP1", RU / 2), ("RN1", -RU / 2)):
+        if name in PAR["fill"]:
+            n = SB[name][0]
+            add("G", [vw("RF", 0, n)], [vw(name)], ("affine_select", vw(name), vw("RF", 0, n), [[0, n]], OP.is_gt, x, 0, 0))
+        else:
+            mset(vw(name), x)
     mset(vw("CU", p1=1), 15.5)
     mset(vw("VS", Z0, V0), 1 << 24)
-    mset(vw("VB", 0, NS), float(W))
-    repeat("VB", 0, NS, UN)
-    for j, x in enumerate([(V0 - Z0) / 512, (H0 - Z0) / 256]):
-        mset(hv("CB", j, 8), x)
-    iota(vw("CE", 0, 32), [[NS, 2], [-128, 2], [0, 8]], slot(0), 0)
-    iota(vw("CE", 32, 40), [[0, 8]], 0, -1)
+    iota(vw("VB", UN, UN + NS), [[0, NS]], W, 0)
+    for a, b, n in ((1, 16, 1), (2, 16, 1), (7, 16, 1), (3, 1, 2), (5, 1, 2), (9, 1, 7)):
+        dma("S", vw("VB", NS * a, NS * (a + n)), vw("VB", NS * b, NS * (b + n)), vw("VS", V0, V0 + 2048))
+    iota(vw("CB", 0, 16), [[(H0 - Z0) // 2 - (V0 - Z0) // 4, 2], [0, 8]], (V0 - Z0) // 4, 0)
+    iota(vw("CE", 0, 64), [[NS, 4], [-128, 2], [0, 8]], slot(1) - UN // 2, 0)
+    iota(vw("CE", 64, 72), [[0, 8]], 0, -1)
     iota(vw("NB", 0, 2), [[128, 2]], made(-1) - Z0, 1)
     act(vw("NB", 2, 4), vw("NB", 0, 2), scale=1.0 / 16384)
     act(vw("NB", 4, 6), vw("NB", 0, 2), scale=1.0 / 8192)
@@ -244,8 +256,9 @@ def build(rank, cores, topo):
     if PAR["xm"]:
         ts(vw("L15"), vw("JF", 0, 8), 16.0, OP.mult, 15.0, OP.add)
     act(vw("W1"), DC, scale=2 * KU)
-    for j, x in enumerate((16384.0, 8192.0, float(UN))):
+    for j, x in enumerate((16384.0, 8192.0)):
         act(hv("DU", j, 8), DC, scale=x)
+    act(vw("DU", 16, 32), vw("DC"), scale=float(UN))
     ts(col("CF", 7), col("CF", 1), 8.0, OP.is_ge)
     ts(col("CF", 12), col("MR", 2), 1.0 / 16, OP.mult)
     ts(col("CF", 13), col("CF", 7), RU, OP.mult)
@@ -258,13 +271,12 @@ def build(rank, cores, topo):
     ts(vw("WO"), vw("JF"), col("CF", 4), OP.is_equal)
     tt(vw("WS"), vw("WO", 15, 143), vw("WO", 14, 142), OP.subtract)
     ts(col("CF", 17), col("CF", 3), 8.0, OP.add)
-    ts(vw("TM2"), vw("RF"), col("CF", 17), OP.is_equal)
-    tt(vw("AP"), vw("TM2"), vw("BD"), OP.mult)
-    act(vw("AP2"), vw("AP"), scale=2.0)
-    act(vw("APN"), vw("AP"), scale=-1.0)
-    iota(vw("SEL", 0, 512), [[0, 512]], 0, 0)
-    repeat("SEL", 0, 512, 2048)
-    asel(vw("SEL", 2, 2048, 16), vw("ONB"), [[-1, 16], [-16, 8]], OP.is_equal, 0, 1)
+    ts(vw("TM2"), vw("RF"), col("CF", 17), OP.is_equal, 2.0, OP.mult)
+    tt(vw("AP2"), vw("TM2"), vw("BD"), OP.mult)
+    act(vw("APN"), vw("AP2"), scale=-0.5)
+    act(vw("C7"), vw("MR"), scale=16.0, bias=-8.5)
+    iota(vw("PT"), [[1, 32]], 0, 0)
+    act(vw("I2"), vw("IF"), scale=col("MR", 2))
     for h in range(2):
         asel(vw("GS", 128 * h, 128 * h + 128, 1, 16), vw("ONB", p1=16), [[-1, 8], [0, 16]], OP.is_equal, -8 * h, 1)
     cp(col("CF", 5), col("TI", 0))
@@ -287,7 +299,9 @@ def build(rank, cores, topo):
     for h in range(2):
         ts(hv("QP", 3 * h, 8), vw("Q16", 0, 8), 32.0, OP.mult, 16.0 * (1 - h), OP.add)
     act(vw("QP", 8, 24), vw("Q16"))
-    iota(vw("QL"), [[-W // 2, 2], [0, 4]], 0, 0)
+    cut = PAR["cut"]
+    iota(vw("QL", 0, cut // 16), [[0, cut // 16]], 0, 0)
+    iota(vw("QL", cut // 16, 8), [[0, 8 - cut // 16]], -32 * cut, 0)
     act(vw("TMP"), vw("IF"), scale=col("CF", 5))
     mm([(vw("PF", 0, 128), vw("ONF"), vw("TMP"))])
     act(vw("BI0"), vw("PF", 0, 128), scale=-RU, bias=-0.5 * RU)
@@ -304,29 +318,33 @@ def build(rank, cores, topo):
 
     for h in range(2):
         src = vw("SR", 1 - h, 256, 2)
-        cp(hv("S16", h), src)
-        cp(hv("VB", h, 128, UN), src)
-        cp(hv("VS", h, 128, made(-1)), src)
+        widen(hv("S16", h), src, PAR["gi"][0])
+        widen(hv("SF1", h), src, PAR["gi"][1])
+        widen(hv("VS", h, 128, made(-1)), src, PAR["gi"][2])
         cp(hv("ZA0", h), vw("ZR", 1 - h, 256, 2))
     for k in range(16):
+        asel(vw("ZX0", k, W // 2, 16), hv("ZA0", 0), [[0, 128]], OP.is_ge, 1, 0)
         if k < PAR["zi"][0]:
-            act(vw("ZX0", k, W, 16), vw("ZA0"), AF.Copy)
+            act(vw("ZX0", W // 2 + k, W, 16), hv("ZA0", 1), AF.Copy)
         elif k < sum(PAR["zi"]):
-            asel(vw("ZX0", k, W, 16), vw("ZA0"), [[0, 256]], OP.is_ge, 1, 0)
+            asel(vw("ZX0", W // 2 + k, W, 16), hv("ZA0", 1), [[0, 128]], OP.is_ge, 1, 0)
         else:
-            cp(vw("ZX0", k, W, 16), vw("ZA0"))
-    cp(vw("WMF", p1=8), vw("WM", p1=8))
-    for h in range(2):
-        mm([(vw("PD1", 8 * h, 8 * h + 8), vw("WMF", 1 - h, 256, 2, 8), vw("IF", 0, 8, 1, 8))])
-    ts(vw("HS1"), vw("PD1", 0, 16), -1.0, OP.mult, 1.0, OP.add)
-    cp(vw("THR"), vw("PD1", 0, 16))
-    for j in range(4):
-        ts(hv("VS", j, 512, V0 + 2048), hv("VS", j, 512, V0), 12, OP.arith_shift_right)
+            cp(vw("ZX0", W // 2 + k, W, 16), hv("ZA0", 1))
+    act(vw("OZ"), vw("ZA0"), AF.Copy)
+    for j in PAR["alt"]:
+        act(hv("OZ", j, 16), hv("OZ", j, 16), scale=0.0)
+    ts(vw("WN", p1=8), vw("WM", p1=8), -1.0, OP.add)
+    mm([(vw("PF", 256 + 8 * h, 264 + 8 * h), vw("WN", 1 - h, 256, 2, 8), vw("IB", 0, 8, 1, 8)) for h in range(2)])
+    act(vw("HS1"), vw("PF", 256, 272), scale=-1.0)
+    act(vw("THR"), vw("PF", 256, 272), bias=1.0)
+    for j in range(8):
+        ts(hv("VS", j, 256, V0 + 2048), hv("VS", j, 256, V0), 12, OP.arith_shift_right)
 
     me = cores[rank]
     for t in range(TS):
         last = t == TS - 1
         seen.clear()
+        gate.clear()
         zx = "ZX%d" % (max(t - 1, 0) % 2)
         za, zb = "ZA%d" % (t % 2), "ZA%d" % ((t + 1) % 2)
         hs, hp = "HS%d" % (t % 2), "HS%d" % ((t + 1) % 2)
@@ -334,6 +352,7 @@ def build(rank, cores, topo):
         ha, hb = "HA%d" % (t % 2), "HA%d" % ((t + 1) % 2)
         count = vw(hb, 0, 128, 1, 16)
         wt = "WT%d" % (t % 2)
+        it, nx = str(max(t, 1) % 2), str((t + 1) % 2)
         dst = cores[(rank + 1 + t % 3) % NR]
         lands = [(hv("RY", t), hv("LB", 7, 8, 64 * t)), (hv("YB", 1, 128, 256 * t) if last else vw("YW", 0, 256, 2), hv("LB", 4, 8, 64 * t))]
 
@@ -348,11 +367,11 @@ def build(rank, cores, topo):
             else:
                 act(out, rows, AF.Copy)
 
-        for j in range(8 if t else 0):
-            n = PAR["acut" if j in PAR["alt"] else "mcut"]
-            for a in range(512 * j, 512 * j + 512, n):
+        for j in range(16 if t else 0):
+            n = 512 if j in PAR["wide"] else 256
+            for a in [256 * j] * (j - 1 not in PAR["wide"]):
                 b = a + n
-                rows = ind(vw("YW"), vw("S4", a // 16, b // 16))
+                rows = ind(vw("YW"), vw("SQ" + it, a // 16, b // 16))
                 if j in PAR["alt"]:
                     bank = vw(PAR["alt"][j], 0, n)
                     act(vw("C2", a, b), rows, AF.Copy)
@@ -365,12 +384,15 @@ def build(rank, cores, topo):
             for j in range(4 * h, 4 * h + 4):
                 a, b = 512 * j, 512 * j + 512
                 if t:
-                    gather(vw("G2", a, b), ind(vw("TB"), vw("S4", a // 16, b // 16)), j in PAR["gv"])
+                    n = PAR["gvl" if last else "gv"].get(j, 0)
+                    for x, y in ((a, a + n), (a + n, b)):
+                        if x < y:
+                            gather(vw("G2", x, y), ind(vw("TB"), vw("SQ" + it, x // 16, y // 16)), x == a and n > 0)
                     continue
                 rows = ind(vw("X", 0, W), vw("S16", a // 16, b // 16))
                 gather(vw("G2", a, b), rows, j in PAR["c0v"])
                 bank = ["PD0", "PD1", "PU", "PA1", "PF", "PD0", "PD1", "PU"][j]
-                mm([(vw(bank, k, 512, 16), vw("IN"), hv(za, j, 32)) for k in range(16)], stop=False)
+                mm([(vw(bank), vw("IN"), vw(zx, a, b))] if h else [(vw(bank, k, 512, 16), vw("IN"), hv(za, j, 32)) for k in range(16)], stop=False)
                 mm([(vw(bank), vw("IB"), vw("G2", a, b))], start=False)
                 if j in PAR["r0v"]:
                     ts(vw("M", a, b), vw(bank), 0.0, OP.max)
@@ -380,28 +402,27 @@ def build(rank, cores, topo):
             def lanes(bank, c, n, name, wts, q0, q1):
                 return [(vw(bank, c + k, c + k + 16 * n - 15, 16, q1) + (q0, 1),
                          vw(name, 2048 * h + 16 * q0 + k, 2048 * h + 16 * q1, 16), wts) for k in range(16)]
-            uw, sf = hv("UW", h), hv("VB", h, 128, UN)
+            uw, sf = hv("UW", h), hv("SF" + it, h)
             run = vw(pa, 256, 384)
             if t == 0:
                 key, rho, reset, thr = vw(pk, 0, 128), vw(pk, 128, 256), vw("MKN"), hv("THR", h, 8)
                 dp, ends = vw(pa, 0, 128), vw(pa, 15, 128, 16)
-                more = [(vw(pk, 0, 128, 1, 32 * j + 32) + (32 * j, 1), hv(za, 4 * h + j, 32), vw("BZ"))
-                        for j in range(4) if 4 * h + j not in PAR["alt"]]
-                mm([(key, vw("IB"), vw("BI")), (rho, vw("IF"), vw("BI0"))] + more, stop=False)
-                news = [(vw(pk, 128 + k, 256, 16), vw("IN"), hv(hp, h, 8)) for k in range(16)]
-                mm(news[:15], start=False, stop=False)
-                for q0, q1 in ((0, 96), (96, 128)):
-                    mm(lanes(pk, 0, 16, "G2", vw("WR", 0, 16), q0, q1), start=False, stop=False)
-                    mm(lanes(pk, 0, 8, "M", vw("W1"), q0, q1) + news[15:] * (q0 > 0), start=False, stop=q0 > 0)
+                mm([(key, vw("IB"), vw("BI")), (rho, vw("IF"), vw("BI0")), (key, hv("OZ", h), vw("BZ"))], stop=False)
+                new = [(hv(pk, j, 64, 128), vw("WN", 1 - h, 256, 2, 8), vw("GS", 64 * j, 64 * j + 64, 1, 8)) for j in range(2)]
+                mm(new[:1], start=False, stop=False)
+                for x in PAR["s0"]:
+                    mm(lanes(pk, 0, 16, "G2", vw("WR", 0, 16), *x), start=False, stop=False)
+                    mm(lanes(pk, 0, 8, "M", vw("W1"), *x), start=False, stop=False)
+                mm(new[1:], start=False)
                 ts(hv(sg, h), rho, 0.0, OP.is_gt)
                 tt(hv("KEY", h), key, hv(sg, h), OP.add)
-                mm([(dp, sf, vw("DI")), (ends, vw("IP"), hv("CB", 0, 8))])
+                mm([(dp, sf, vw("DI")), (ends, vw("IU"), hv("CB", 0, 8))])
             else:
                 diff, rho, ba = (hv(pd, j) for j in range(3))
                 key, dp, thr, reset = hv(pk, 0), hv(pk, 1), vw(pk, 256, 264), hv(pa, 0)
                 ends = vw(pk, 143, 256, 16)
                 new = [(hv(pd, j, 64), vw(hb, 128, 256, 1, 16), vw("GS", 128 * h + 64 * j, 128 * h + 64 * j + 64, 1, 16)) for j in range(2)]
-                blk = hv("B16", h)
+                blk = hv("BQ" + it, h)
                 mm([(diff, blk, vw("IB")), (diff, sf, vw("INH"))]
                    + [(ba, sf, vw("IF")), (ba, vw("CA"), vw("ONB")), (ba, blk, vw("IN"))] * (t == 1), stop=False)
                 low = col(pd, 384)
@@ -412,16 +433,16 @@ def build(rank, cores, topo):
                     end = x == PAR["sg"][h][-1]
                     mm(lanes(pd, 0, 16, "G2", vw("WR", 16, 32), *x) + new[1:] * end, start=False, stop=end)
                 mm([(key, vw("IB"), vw("BI")), (key, vw("ONN", p1=t), vw("ONB", p1=t)), (dp, blk, vw("DJ" if t == 1 else "DK")),
-                    (thr, vw("IH"), vw("ONB", 0, 8)), (thr, vw("IH"), hv(hs, h, 8)), (thr, vw("IG"), hv(hp, h, 8))]
-                   + ([(ends, vw("IP"), hv("CB", 1, 8))] if t == 1 else
-                      [(ends, vw("IU"), hv("CE", 2 * ((t - 1) % 2) + h, 8)), (ends, vw("IU"), hv("CE", 4, 8))]), stop=False)
+                    (thr, vw("IH"), hv(hs, h, 8)), (thr, vw("IG"), hv(hp, h, 8))]
+                   + ([(ends, vw("IU"), hv("CB", 1, 8)), (thr, vw("IH"), vw("ONB", 0, 8))] if t == 1 else
+                      [(ends, vw("IU"), hv("CE", 2 * t - 4 + h, 8)), (ends, vw("IU"), hv("CE", 8, 8))]), stop=False)
                 for x in PAR["sm"][h]:
                     mm(lanes(pk, 0, 8, "M", vw("W1"), *x), start=False, stop=False)
                 for x in PAR["sl"][h]:
                     mm(lanes(pk, 0, 8, "G2", vw("WR", 32, 40), *x), start=False, stop=False)
                 ts(uw, diff, 0.0, OP.not_equal, low, OP.max)
                 tt(hv(sg, h), rho, uw, OP.is_gt)
-                name, plus, minus = ("C1", "IF8", "IN8") if t == 1 else ("UW", "IQ", "IM") if t % 2 else ("UW", "IM", "IQ")
+                name, plus, minus = ("C1", "IF8", "IN8") if t == 1 else ("UW", "IM", "IQ")
                 if t == 1:
                     tt(hv("C1", h), ba, uw, OP.mult)
                 a = 128 * h
@@ -439,11 +460,13 @@ def build(rank, cores, topo):
             tt(hv("NE", h), run, hv("KEY", h), OP.not_equal)
             scan(hv("SC", h), hv("NE", h), dp, OP.mult, OP.add)
             cn = vw("CN", 128 * h + 15, 128 * h + 128, 16)
-            tt(hv("BO", h, 8), cn, thr, OP.is_gt)
-            tt(hv(hs, h, 8), cn, thr, OP.not_equal)
             if t < 2:
+                tt(hv("BO", h, 8), cn, thr, OP.is_gt)
+                tt(hv(hs, h, 8), cn, thr, OP.not_equal)
                 ts(hv("NH", h, 8), hv(hs, h, 8), col("NB", 2 + 2 * t + h), OP.mult)
-            tt(hv("XB", h, 8), hv("NH" if t < 2 else hs, h, 8), hv("BO", h, 8), OP.add)
+                tt(hv("XB", h, 8), hv("NH", h, 8), hv("BO", h, 8), OP.add)
+            else:
+                tt(hv("XB", h, 8), cn, thr, OP.subtract)
             if h < PAR["xm"]:
                 tt(vw("XM"), ind(hv("XB", h, 8), LC), vw("MR"), OP.mult)
                 tt(hv("E1", h), ind(hv("SC", h), vw("L15")), vw("XM"), OP.min)
@@ -451,34 +474,40 @@ def build(rank, cores, topo):
                 tt(hv("DB", h, 8), vw("SC", 128 * h + 15, 128 * h + 128, 16), hv("XB", h, 8), OP.min)
                 tt(hv("E1", h), ind(hv("DB", h, 8), LC), vw("MR"), OP.mult)
             p8 = vw(pa, 408, 416)
-            mm([(p8, vw("IB"), vw("C15", 0, 8))] + [(p8, vw("IB"), hv("QB", h, 8))] * (t > 1), stop=False)
-            mm([(p8, hv("E1", h), hv("DU", min(t, 2), 8))], start=False)
-            ts(hv("DL", h, 8), p8, MAGIC, OP.add, MAGIC - (Z0 - made(-1)) * (t < 2), OP.subtract)
             fb = hv("FB", h, 128, 256 * t)
+            wide = hv("FF", h) if h == 0 or last else vw("VB", slot(t), slot(t) + NS, 2)
             if t < 2:
+                mm([(p8, hv("E1", h), hv("DU", t, 8))])
+                ts(hv("DL", h, 8), p8, float(Z0 - made(-1)), OP.add)
                 ts(hv("FI", h), ind(vw("VS", made(-1), H0 + NS * t), hv("DL", h, 8)), LOW, OP.bitwise_and)
                 ts(fb, hv("FI", h), float(W), OP.min)
-                ts(hv(wt, h, 8), p8, -15.0 / 32, OP.is_equal, 0.125, OP.mult)
+                ts(hv(wt, h, 8), p8, 0.0, OP.is_equal, 32.0, OP.mult)
             else:
-                cp(fb, ind(vw("VB"), hv("DL", h, 8)))
-                ts(hv(wt, h, 8), p8, UN / 2, OP.is_lt, 0.125, OP.mult)
+                mm([(vw(pa, 408, 424), vw("IB"), vw("C2K")), (p8, vw("IB"), hv("QB", h, 8))], stop=False)
+                mm([(vw(pa, 408, 424), hv("E1", h), vw("DU", 16, 32))], start=False)
+                cp(hv("DL", h, 8), p8)
+                cp(fb, ind(vw("VB", 0, slot(t)), hv("DL", h, 8)))
+                ts(hv(wt, h, 8), vw(pa, 416, 424), float(UN), OP.is_equal, 32.0, OP.mult)
             if last:
                 tt(hv("WW", h, 8), hv("WT0", h, 8), hv("WT1", h, 8), OP.min)
             if h == 0 and not last:
                 send(hv("RV", t), fb, "rc")
-            if h == 0 or last:
-                widen(hv("FF", h), fb, PAR["gp"][0])
-        for h in range(0 if last else 2):
-            view = hv("FB", 1, 128, 256 * t) if h else hv("RV", t)
-            widen(vw("VB", slot(t) + 1 - h, slot(t) + NS, 2), view, PAR["gp"][1 + h])
-            if t == 0:
-                cp(vw("VS", H0 + 1 - h, H0 + NS, 2), view)
+            if t > 1 and PAR["fa"][h]:
+                act(wide, ind(vw("VB", 0, slot(t)), hv("DL", h, 8)), AF.Copy)
+            else:
+                widen(wide, fb, PAR["gp"][2 * h])
         if not last:
-            if t:
-                cp(vw("VB", UN, UN + NS), ind(vw("VS", made(t - 1), Z0), hv("LB", 1, 16, 64 * (t - 1))))
-            ts(vw("S4"), vw("VB", UN, UN + NS), -7.5, OP.add, 1.0 / 16, OP.mult)
-            cp(vw("B16"), vw("S4"))
-            mm([(vw("PF", 256, 384, 1, 16), vw("BO"), vw("ONB")), (vw("PF", 384, 512, 1, 16), vw(hs), vw("IB"))])
+            if t == 0:
+                cp(vw("VS", H0, H0 + NS, 2), hv("FB", 1))
+            else:
+                cp(vw("SF" + nx), ind(vw("VS", made(t - 1), Z0), hv("LB", 1, 16, 64 * (t - 1))))
+            ts(vw("SQ" + nx), vw("SF" + nx), -7.5, OP.add, 1.0 / 16, OP.mult)
+            widen(vw("BQ" + nx), vw("SQ" + nx), PAR["gp"][3])
+            if t > 1:
+                act(vw("SN"), vw("XB"), AF.Sign, bias=-0.5)
+                act(vw(hs), vw("SN"), AF.Abs)
+            mm([(vw("PF", 256, 384, 1, 16), vw(x), vw("ONB")) for x in ((hs, "SN") if t > 1 else ("BO", "BO"))]
+               + [(vw("PF", 384, 512, 1, 16), vw(hs), vw("IB"))])
             act(vw(ha, p1=16), vw("PF", 256, 512, 1, 16), AF.Copy)
         for h in range(2):
             pa, pk = "PA%d" % h, "PK%d" % h
@@ -486,26 +515,29 @@ def build(rank, cores, topo):
             av = hv(zb, h)
             cuts = [2048 * h + a for a in PAR["cuts"][h]]
             for a, b in zip(cuts[:-1], cuts[1:]):
-                gather(vw("D", a, b), ind(vw("X", 0, W + 16), vw("FB", 256 * t + a // 16, 256 * t + b // 16)), a in PAR["dv"])
+                gather(vw("D", a, b), ind(vw("X", 0, W + 16), vw("FB", 256 * t + a // 16, 256 * t + b // 16)), a in PAR["dvl" if last else "dv"])
             for a, b in zip(cuts[:-1], cuts[1:]):
                 scan(vw("MX", a, b), vw("MK0", 0, b - a), vw("D", a, b), OP.mult, OP.max)
                 scan(vw("MN", a, b), vw("MKB", 0, b - a), vw("D", a, b), OP.add, OP.min)
-            for p, n in ((0, 64), (1, 64)) if last and h >= PAR["split"] else ((0, 128),):
+            for p, n in ((0, cut), (cut, 128 - cut)) if last and h else ((0, 128),):
                 def part(v, p=p, n=n):
-                    return (v[0], v[1] + n * v[3] * p, min(v[2], v[1] + n * v[3] * (p + 1)), v[3], v[4])
+                    return (v[0], v[1] + v[3] * p, min(v[2], v[1] + v[3] * (p + n)), v[3], v[4])
 
                 def rows(v, p=p, n=n):
-                    return v[:4] + (n * p + n, n * p, 1)
-                py, pz = vw("PA%d" % h, 128, 128 + n), vw("PD%d" % h, 256, 256 + n)
+                    return v[:4] + (p + n, p, 1)
+                bank = 0 if p else h
+                py, pz = vw("PA%d" % bank, 128, 128 + n), vw("PD%d" % bank, 256, 256 + n)
                 mx, mn = (part(vw(x, 2048 * h + 15, 2048 * h + 2048, 16)) for x in ("MX", "MN"))
-                way = PAR["ya"][h]
+                way = PAR["yal" if last else "ya"][h]
                 for x in (py, pz)[way == 2:]:
-                    mm([(x, vw("IB"), vw("CQ", 0, n))] + [(x, vw("IN"), part(hv(za, h)))] * (x == pz) + [(x, vw("IH"), mx)], stop=False)
+                    mm([(x, vw("IM"), vw("ONB", 0, n))] + [(x, vw("IN"), part(hv(za, h)))] * (x == pz) + [(x, vw("IH"), mx)], stop=False)
                     mm([(x, vw("IH"), mn)] + whole(x, "C01", n) * (x == pz or way == 1), start=False, block=True)
                 if PAR["zv"][h]:
                     ts(part(hv("MZ", h)), pz, 0.0, OP.max)
                 else:
                     act(part(av), pz, AF.Abs)
+                    if "A" in PAR["gate"]:
+                        gate["A"] = len(ops) - 1
                 if way == 2:
                     tt(part(yv), pz, part(hv(za, h)), OP.add)
                 elif way == 1:
@@ -513,40 +545,53 @@ def build(rank, cores, topo):
                 else:
                     ts(part(yv), py, MAGIC, OP.add, MAGIC, OP.subtract)
                 if h == 0:
-                    send(part(hv("RY", t)), part(yv), "rc" if p else "ra")
-                pu = rows(vw(pk, 384, 512))
+                    send(hv("RY", t), yv, "ra")
+                pu = rows(vw("PK%d" % bank, 384, 512))
                 big = [(pu, part(vw("IB")), vw("C16")), (pu, part(vw("IN")), vw("C16"))]
                 if PAR["zv"][h]:
                     act(part(av), pz, AF.Abs)
                     z, mz = part(hv(za, h)), part(hv("MZ", h))
-                    mm([(pu, part(vw("IN")), vw("C7")), (pu, z, vw("WBN")), (pu, part(yv), vw("WBD"))], stop=False)
+                    mm([(pu, part(vw("IB")), vw("C7")), (pu, z, vw("WBN")), (pu, part(yv), vw("WBD"))], stop=False)
                     mm([(pu, mz, vw("WN2"))] + big + [(pu, mz, vw("WB2")), (pu, z, vw("WBD")), (pu, part(yv), vw("WBN"))], start=False, block=True)
                 else:
-                    mm([(pu, part(vw("IN")), vw("C7"))], stop=False)
+                    mm([(pu, part(vw("IB")), vw("C7"))], stop=False)
                     mm([(pu, part(av), vw("WBN"))] + big + [(pu, part(av), vw("WBD"))], start=False, block=True)
-                tt(rows(hv("E2", h)), pu, rows(vw("MR")), OP.mult)
-                pa = "PF" if last else "PU"
+                if PAR["eal" if last else "ea"][h]:
+                    act(rows(hv("E2", h)), pu, AF.Relu)
+                else:
+                    ts(rows(hv("E2", h)), pu, 0.0, OP.max)
+                pa = "PD1" if p else "PF" if last else "PU"
                 pi, pp, pc, both = vw(pa, 392, 400), hv(pa, h, 8, 384 + 8 * h), hv(pa, 1 - h, 8, 392 - 8 * h), hv(pa, 0, 16, 384 + 8 * h)
                 if last:
-                    m = n // 16
-                    both = hv(pa, p, m, 392)
-                    mm([(both, vw("IF"), hv("QP", p, m, 24 * h)), (both, vw("IK"), hv(wt, p, m, 8 * h)), (both, vw("IB"), hv("QL", p, m))]
-                       + [(pc, vw("IF"), hv("QP", 1 + h, 8)), (pc, vw("IS"), hv(wt, h, 8)), (pc, vw("IS"), hv("WW", h, 8))] * (p != h or m == 8),
-                       stop=False)
-                    mm([(both, rows(hv("E2", h)), rows(hv("DC", p, m)))], start=False)
-                    a, b = ((8, 12), (12, 24), (0, 12), (12, 16))[2 * h + p] if m == 4 else (8 - 8 * h, 24 - 8 * h)
+                    def cols(name, base=0, p=p, n=n):
+                        return vw(name, base + p // 16, base + (p + n) // 16)
+                    both = cols(pa, 392)
+                    mm([(both, vw("IF"), cols("QP", 24 * h)), (both, vw("IL"), cols(wt, 8 * h)), (both, vw("IB"), cols("QL"))]
+                       + [(pc, vw("IF"), hv("QP", 1 + h, 8)), (pc, vw("I8"), hv(wt, h, 8)), (pc, vw("I8"), hv("WW", h, 8))] * (p == 0), stop=False)
+                    mm([(both, rows(hv("E2", h)), rows(cols("DC")))], start=False)
+                    a, b = (8 + p // 16 if p else 0, 8 + (p + n) // 16) if h else (8, 24)
                     cp(vw("LB", 64 * t + 24 * h + a, 64 * t + 24 * h + b), vw(pa, 384 + a, 384 + b))
                     if h == 0:
-                        send(hv("LB", p, m, 64 * t + 56), hv("LB", p, m, 64 * t + 8), "rd" if p else "rb")
+                        send(hv("LB", 7, 8, 64 * t), hv("LB", 1, 8, 64 * t), "rb")
                     continue
-                mm([(hv(pa, 0, 16, 392 - 8 * h), vw("IF"), hv("QP", h, 16)), (pp, vw("IK"), hv(wt, h, 8)),
-                    (pi, vw("IK"), hv(wt, h, 8)), (pc, vw("IS"), hv(wt, h, 8))], stop=False)
+                mm([(hv(pa, 0, 16, 392 - 8 * h), vw("IF"), hv("QP", h, 16)), (pp, vw("IH"), hv(wt, h, 8)),
+                    (pi, vw("IL"), hv(wt, h, 8)), (pc, vw("I8"), hv(wt, h, 8))], stop=False)
                 mm([(both, hv("E2", h), vw("DC"))], start=False)
+                if "P" in PAR["gate"]:
+                    gate["P"] = len(ops) - 1
                 cp(hv("LB", h, 24, 64 * t), vw(pa, 384, 408))
+                gate["V"] = len(ops) - 1
                 if h == 0:
                     send(hv("LB", 3, 16, 64 * t), hv("LB", 0, 16, 64 * t), "rb")
+                    gate["G"] = pool[0]
+                if h == (t == 0 or PAR["late"]):
+                    widen(vw("VB", slot(t) + 1, slot(t) + NS, 2), hv("RV", t), PAR["gp"][1])
+                    if t == 0:
+                        cp(vw("VS", H0 + 1, H0 + NS, 2), hv("RV", t))
+                if "V" not in PAR["gate"]:
+                    gate.pop("V")
             if h and not last:
-                cp(vw("RP", 0, 8), vw("LB", 64 * t + 48, 64 * t + 56))
+                gather(vw("PL"), ind(vw("PT"), vw("LB", 64 * t + 48, 64 * t + 56)), PAR["pv"])
                 gather(vw("YW", 1, 256, 2), lands[0][0], not PAR["yw"])
             u, pf = hv("PU", 0), hv("PU", 1)
             ff = hv("FF", h) if h == 0 or last else vw("VB", slot(t), slot(t) + NS, 2)
@@ -564,27 +609,28 @@ def build(rank, cores, topo):
             else:
                 tt(hv("DD", j), ind(vw("X"), lands[j][1]), lands[j][0], OP.subtract)
                 ts(hv("DR", j), hv("DD", j), 0.0, OP.max)
-        for p in range(2 if last else 1):
-            a = W // 2 * p
-            for j in (1, 0):
+        for p, n in ((0, cut), (cut, 128 - cut)) if last else ((0, 128),):
+            for j in (0, 1) if p else (1, 0):
                 ys, ls = lands[j]
                 if last:
-                    cp(ind(vw("X", a, a + W + W // 2), hv(ls[0], p, 4, ls[1])), hv(ys[0], p, 64, ys[1]))
+                    cp(ind(vw("X", 32 * p, W + 32 * (p + n)), vw(ls[0], ls[1] + p // 16, ls[1] + (p + n) // 16)), vw(ys[0], ys[1] + p, ys[1] + p + n))
                 else:
                     cp(ind(vw("X"), ls), ys)
             if last:
-                dma("S", ("$", "yx", a, a + W // 2), vw("X", a, a + W // 2))
-        if not last:
-            for j in (0, 1):
-                tb, av, y = hv("PF", 1 - j), hv(zb, 1), lands[j][0]
-                mm([(tb, vw("C23"), vw("ONB")), (tb, vw("W2N"), av)] * j + [(tb, vw("WS"), y)] + whole(tb, "C16"), start=j == 0, stop=False, pin=True)
-                mm([(tb, vw("WO", 14, 142), y)] + [(tb, vw("APN"), y)] * PAR["old"][j] + [(tb, vw("W2"), av), (tb, vw("GL", p1=16), vw(ha, 128, 256, 1, 16))] * j, start=False, stop=False)
-            mm([(vw("PF", 128 + k, 256, 16), hv("SEL", k), vw("RP", 0, 8)) for k in range(16)], start=False, stop=False)
-            for j in (0, 1):
-                mm([(hv("PF", 1 - j), vw("APN"), hv("DD", j))], start=False, stop=False)
-                mm([(hv("PF", 1 - j), vw("AP2"), hv("DR", j))], start=False, stop=j == 1)
-            for j in (1, 0):
-                act(vw("TB", 1 - j, 256, 2), hv("PF", 1 - j), bias=col("CF", 15))
+                dma("S", ("$", "yx", 32 * p, 32 * (p + n)), vw("X", 32 * p, 32 * (p + n)))
+        for j in range(0 if last else 2):
+            tb, av, y = hv(PAR["tb"][j], 0), hv(zb, 1), lands[j][0]
+            mm([(tb, vw("C23"), vw("ONB")), (tb, vw("W2N"), av)] * j + [(tb, vw("WS"), y)] + whole(tb, "C16"), stop=False, pin=True)
+            mm([(tb, vw("WO", 14, 142), y)] + [(tb, vw("APN"), y)] * PAR["old"][j]
+               + ([(tb, vw("W2"), av), (tb, vw("GL", p1=16), vw(ha, 128, 256, 1, 16))] if j else [(tb, vw("I2"), vw("PL"))])
+               + [(tb, vw("APN"), hv("DD", j))], start=False, stop=False)
+            mm([(tb, vw("AP2"), hv("DR", j))], start=False)
+            if PAR["tv"][j]:
+                ts(vw("TB", 1 - j, 256, 2), tb, col("CF", 15), OP.add)
+            else:
+                act(vw("TB", 1 - j, 256, 2), tb, bias=col("CF", 15))
+        for a in (0, UN // 2) if 0 < t < TS - 1 else ():
+            dma("S", vw("VB", a, a + NS), vw("SF" + nx), hv("DR", 0))
         if t < TS - 2:
             for k in range(16):
                 asel(vw("ZX%d" % ((t + 1) % 2), k, W, 16), vw(zb), [[0, 256]], OP.is_ge, 1, 0)
@@ -719,10 +765,36 @@ def graph(ops, plan):
 
 
 def replay(order, eng, dur, before, after):
-    end, free = [0.0] * len(eng), {}
+    end, free = [0.0] * len(eng), dict.fromkeys(eng, 0.0)
     for i in order:
-        end[i] = free[eng[i]] = max([free.get(eng[i], 0.0)] + [end[d] + w for d, w in before[i]]) + dur[i]
+        e = eng[i]
+        t = free[e]
+        for d, w in before[i]:
+            if end[d] + w > t:
+                t = end[d] + w
+        end[i] = free[e] = t + dur[i]
     return max(end)
+
+
+def judge(ends, scale):
+    return len(ends) * (sum((a / b) ** PLAN["power"] for a, b in zip(ends, scale)) / len(ends)) ** (1 / PLAN["power"])
+
+
+def chain(order, eng, dur, before, after):
+    end, free, why = [0.0] * len(eng), {}, [None] * len(eng)
+    for i in order:
+        t, k = free.get(eng[i], (0.0, None))
+        for d, w in before[i]:
+            if end[d] + w >= t:
+                t, k = end[d] + w, -1 - d
+        why[i], end[i] = k, t + dur[i]
+        free[eng[i]] = (end[i], i)
+    i, links = end.index(max(end)), []
+    while why[i] is not None:
+        if why[i] >= 0 and eng[i] not in "DR":
+            links.append((why[i], i))
+        i = why[i] if why[i] >= 0 else -1 - why[i]
+    return links
 
 
 def schedule(ops):
@@ -740,77 +812,77 @@ def schedule(ops):
     for i in range(len(ops) - 1, -1, -1):
         for k in [j for j, _ in after[i] if j >= len(ops)] + [i]:
             tail[k] = dur[k] + max([w + tail[j] for j, w in after[k]] + [0.0])
-    urgency, best, scale = [-x for x in tail], None, None
-    shake = np.random.RandomState(0)
+    urgency, best, now, scale = [-x for x in tail], None, None, None
+    shake = np.random.RandomState(PLAN["seed"])
     names = {}
     kin = np.array([names.setdefault(o["name"], len(names)) for o in ops] + [0] * (len(eng) - len(ops)))
     for k in range(PLAN["passes"]):
         if k > 5 and k % 2 == 0:
             move = shake.normal(0, PLAN["shake"], len(names)) * (shake.rand(len(names)) < PLAN["some"])
-            urgency = (np.array(best[2]) + move[kin]).tolist()
+            if shake.rand() < PLAN["aim"]:
+                move *= 0.2
+                links = chain(now[2], *cases[shake.randint(len(cases))])
+                for a, b in [links[x] for x in shake.randint(len(links), size=4)]:
+                    gap = abs(now[1][a] - now[1][b]) / 2 + 0.1
+                    move[kin[a]] += gap
+                    move[kin[b]] -= gap
+            urgency = (np.array(now[1]) + move[kin]).tolist()
         eng, dur, before, after = cases[k // 2 % len(cases) if PLAN["turn"] else 0]
         start = place(eng, dur, after, urgency)
         order = sorted(range(len(eng)), key=lambda i: (start[i], i))
         ends = [replay(order, *x) for x in cases]
-        scale = scale or ends
-        score = sum(a / b for a, b in zip(ends, scale))
+        scale = [r["par"] for r in RANGE]
+        score = judge(ends, scale)
         back = place(eng, dur, before, [-s - d for s, d in zip(start, dur)])
         urgency = [-s - d for s, d in zip(back, dur)]
         if best is None or score < best[0]:
             best = (score, order, urgency, ends)
+        if now is None or score < now[0] + PLAN["ease"] * (1 - k / PLAN["passes"]) * shake.rand():
+            now = (score, urgency, order)
     order, ends = polish(best[1], cases, scale, kin.tolist(), shake)
     return [i for i in order if i < len(ops)], ends
 
 
 def polish(order, cases, scale, kin, shake):
-    eng, n = cases[0][0], len(order)
+    eng = cases[0][0]
 
-    def run(order):
-        ends, links = [], []
-        for _, dur, before, _ in cases:
-            end, free, why = [0.0] * n, {}, [None] * n
-            for i in order:
-                t, k = free.get(eng[i], (0.0, None))
-                for d, w in before[i]:
-                    if end[d] + w >= t:
-                        t, k = end[d] + w, -1 - d
-                why[i] = k
-                end[i] = t + dur[i]
-                free[eng[i]] = (end[i], i)
-            i = end.index(max(end))
-            ends.append(end[i])
-            while why[i] is not None:
-                if why[i] >= 0 and eng[i] not in "DR":
-                    links.append((why[i], i))
-                i = why[i] if why[i] >= 0 else -1 - why[i]
-        return sum(a / b for a, b in zip(ends, scale)), ends, links
-
-    def ahead(order, a, b):
+    def ahead(order, a, b, way, every):
         order = list(order)
         for j in [i for i in order if kin[i] == kin[b] and eng[i] == eng[b]]:
             q = order.index(j)
             p = next((x for x in range(q - 1, max(q - 400, -1), -1) if kin[order[x]] == kin[a] and eng[order[x]] == eng[a]), None)
             if p is None:
                 continue
-            need = {j}
-            for x in range(q, p - 1, -1):
-                if order[x] in need:
-                    need.update(d for d, _ in cases[0][2][order[x]])
-                    if x < q:
-                        need.update(y for y in order[p:x] if eng[y] == eng[order[x]])
-            if order[p] not in need:
-                order[p:q + 1] = [y for y in order[p:q + 1] if y in need] + [y for y in order[p:q + 1] if y not in need]
+            if every < 1 and shake.rand() > every and j != b:
+                continue
+            span = order[p:q + 1] if way else order[p:q + 1][::-1]
+            need = {span[-1]}
+            for x in range(len(span) - 1, -1, -1):
+                if span[x] in need:
+                    need.update(d for d, _ in cases[0][2 if way else 3][span[x]])
+            if span[0] not in need:
+                span = [y for y in span if y in need] + [y for y in span if y not in need]
+                order[p:q + 1] = span if way else span[::-1]
         return order
-    score, ends, links = run(order)
+    ends = [replay(order, *x) for x in cases]
+    score, links = judge(ends, scale), {}
     best = (score, order, ends)
     for k in range(PLAN["moves"]):
-        a, b = links[shake.randint(len(links))]
-        other = ahead(order, a, b)
-        s, e, x = run(other)
-        if s < score + PLAN["give"] * (1 - k / PLAN["moves"]) * shake.rand():
-            score, ends, links, order = s, e, x, other
-            if s < best[0]:
-                best = (s, order, e)
+        c = shake.randint(len(cases))
+        if c not in links:
+            links[c] = chain(order, *cases[c])
+        a, b = links[c][shake.randint(len(links[c]))]
+        other = ahead(order, a, b, shake.randint(2), shake.randint(3) > 0)
+        bar = score + PLAN["give"] * (1 - k / PLAN["moves"]) * shake.rand()
+        trial = [x * 0.997 for x in ends]
+        for x in list(range(c, len(cases))) + list(range(c)):
+            trial[x] = replay(other, *cases[x])
+            if other == order or judge(trial, scale) >= bar:
+                break
+        else:
+            score, ends, links, order = judge(trial, scale), trial, {}, other
+            if score < best[0]:
+                best = (score, order, ends)
     return best[1:]
 
 

import numpy as np
from concourse.mybir import AluOpType, AxisListType, ActivationFunctionType

OP = AluOpType
AF = ActivationFunctionType
W, NS, TS, NR = 4096, 256, 6, 4
WD = 2 * W
Z0 = NS * (TS + 1)
V0 = Z0 + 128
H0 = V0 + W
UN = 4096
MAGIC = 12582912.0
KU = 2.0 ** -14
RU = 2.0 ** -34
LOW = -(4095 << 12) - 1

B, F, I, U = "bfloat16", "float32", "int32", "uint16"
SB = {
    "X": (WD, B), "VS": (H0 + NS, I), "VB": (UN + NS * TS, F), "TB": (256, B), "YW": (256, B), "PT": (32, B),
    "M": (W, B), "G2": (W, B), "D": (W, B), "MX": (W, B), "MN": (W, B), "ZX0": (W, B), "ZX1": (W, B), "C2": (W, B),
    "ZA0": (256, B), "ZA1": (256, B), "ZR": (256, B), "SR": (256, I), "S16": (256, U),
    "SF0": (256, F), "SF1": (256, F), "SQ0": (256, U), "SQ1": (256, U), "BQ0": (256, B), "BQ1": (256, B),
    "WI": (8, I), "TI": (8, I), "WM": (256, I), "WN": (256, B), "CF": (32, F), "PI": (16, I),
    "JF": (144, F), "RF": (128, F), "GF": (128, F), "IF": (128, F), "IF8": (128, F), "IN8": (128, F), "INH": (128, F), "IF32": (128, F),
    "IB": (128, B), "IH": (128, B), "IG": (128, B), "IN": (128, B), "I8": (128, B), "J8": (128, B),
    "IM": (128, B), "IQ": (128, B), "IU": (128, B), "IL": (128, B), "I2": (128, B), "PL": (128, B),
    "BD": (128, B), "MR": (128, F), "WBD": (128, B), "ONF": (128, F), "ONB": (128, B), "ONN": (128, B), "CU": (128, B),
    "CA": (128, B), "CM": (128, B), "C16": (128, B), "C01": (128, B), "CR": (8, B), "CT": (8, B), "RP1": (8, B),
    "RN1": (8, B), "BH": (128, B), "BL": (128, B), "C32": (128, B), "CL": (128, B), "W2": (128, B), "W2N": (128, B), "C23": (128, B), "GL": (128, B),
    "C7": (128, B), "CB": (24, B), "CE": (72, B), "C2K": (16, B), "SN": (16, B), "TMP": (128, F), "TM2": (128, F), "DI": (128, F), "DJ": (128, B), "DK": (128, B),
    "WO": (144, B), "WS": (128, B), "AP2": (128, B), "APN": (128, B), "L15": (8, U), "LS": (8, U),
    "BZ": (128, B), "XM": (128, F), "WBN": (128, B), "WB2": (128, B), "WN2": (128, B), "MZ": (256, B), "HA0": (256, B), "HA1": (256, B), "GS": (256, B),
    "DC": (16, B), "DU": (32, F), "W1": (8, B), "WR": (40, B),
    "BI0": (128, F), "BI1": (128, F), "BI": (128, B), "QP": (32, F), "QL": (8, B), "Q16": (16, F), "QB": (16, B),
    "MK0": (512, B), "MKB": (512, B), "MKN": (128, B),
    "UW": (256, B), "SG0": (256, B), "SG1": (256, B), "KEY": (256, F), "NE": (256, F), "SC": (256, F), "CN": (256, B),
    "C1": (256, F), "NH": (16, F), "XB": (16, F), "BO": (16, B), "HS0": (16, B), "HS1": (16, B), "THR": (16, F),
    "DB": (16, F), "E1": (256, F), "E2": (256, B), "WT0": (16, B), "WT1": (16, B), "WW": (16, B), "DL": (16, U),
    "NB": (8, F), "FI": (256, I), "FB": (256 * TS, U), "FF": (256, F), "YB": (256 * TS, B), "LB": (64 * TS, U),
    "RY": (128 * TS, B), "RV": (128 * TS, U), "DD": (256, B), "DR": (256, B),
    "PR": (256, F), "PR2": (256, I), "OS": (256, F), "OZ": (256, B),
}
PS = ["PK0", "PK1", "PU", "PA0", "PA1", "PD0", "PD1", "PF"]
SHARE = {}
for _k, _v in SB.items():
    if _v[0] == 128 and _v[1] in (B, F) and _k != "XM":
        SHARE[_k] = ("K" + _v[1], 128 * sum(x[0] == "K" + _v[1] for x in SHARE.values()))
SCRATCH = {k: ("sbuf", [128, v[0]], v[1]) for k, v in SB.items() if k not in SHARE}
SCRATCH.update({"K" + d: ("sbuf", [128, 128 * sum(x[0] == "K" + d for x in SHARE.values())], d) for d in (B, F)})
SCRATCH.update({k: ("psum", [128, 512], F) for k in PS})
NDMA = 34
SEMAPHORES = (["qV", "qA", "qP", "qG", "sent"] + ["d%d" % k for k in range(NDMA)]
              + ["r%s%d" % (x, t) for x in "abc" for t in range(TS)])

PAR = {
    "alt": {0: "PA0", 1: "PA1", 14: "PA0", 15: "PA1"},
    "wide": (),
    "gv": {0: 512},
    "cuts": ([0, 512, 1024, 1536, 1856, 2048], [0, 512, 1024, 1536, 2048]),
    "dv": (3072,),
    "run": 4,
    "cut": 64,
    "tb": ("PD1", "PF"), "tv": (0, 0),
    "xm": 1,
    "ya": (0, 0),
    "c0v": (1, 3), "r0v": (0, 2, 5),
    "old": (1, 1), "yw": 1,
    "fill": ("C2K", "CR", "CT", "RP1", "RN1", "ONN", "C32", "CA"),
    "pv": 1, "eal": (0, 1), "yal": (0, 1), "ea": (0, 0), "gate": "A", "late": 0, "s0": ((0, 128),), "fa": (1, 1), "gvl": {0: 512}, "dvl": (3072,),
    "zi": (4, 4),
    "zv": (0, 0), "gp": (0, 1, 0, 1), "gi": (0, 1, 1), "sg": (((0, 128),), ((0, 128),)), "sm": (((0, 128),), ((0, 128),)), "sl": (((0, 128),), ((0, 128),)),
}
PLAN = {"slow": 1.25, "gather": 1.56, "scatter": 3.8, "wake": 0.14, "lag": 0.09, "own": 0.02, "act": 0.02, "pe": 0.43e-3, "mm": 0.005, "pelag": 0.03,
        "send": 0.7, "row": 0.04, "link": 1.0e4, "land": 1.5, "first": 4.0, "dma": 1.5, "bytes": 4.5e5, "look": 2.0, "passes": 60, "shake": 0.3,
        "some": 0.3, "turn": 0, "moves": 10000, "give": 0.001, "ease": 0.0, "seed": 12, "aim": 0.0, "power": 20}
RANGE = [{"slow": 1.27, "gather": 1.62, "scatter": 4.0, "par": 149}, {"slow": 1.0, "gather": 1.56, "par": 125},
         {"slow": 1.1, "gather": 1.15, "scatter": 2.5, "lag": 0.0, "own": 0.11, "par": 124},
         {"slow": 1.4, "gather": 1.95, "scatter": 5.0, "par": 179}, {"slow": 1.2, "gather": 2.0, "scatter": 2.5, "par": 158},
         {"slow": 1.3, "gather": 1.2, "scatter": 5.5, "land": 2.1, "par": 145}]


EVERY = {"YB": 256, "LB": 64, "RY": 128, "RV": 128, "FB": 256, "VS": 256, "VB": 256, "CE": 16, "DU": 8}


def vw(name, lo=0, hi=None, step=1, p1=128):
    if hi is None:
        hi = SB[name][0] if name in SB else 512
    return (name, lo, hi, step, p1)


def made(t):
    return NS * (TS - 1 - max(t, -1))


def slot(t):
    return UN + NS * (1 + t)


def ind(win, off):
    return ("@", win, off)


def clash(a, b):
    if a[2] <= b[1] or b[2] <= a[1]:
        return False
    if a[3] > 1 and a[3] == b[3] and (a[1] - b[1]) % a[3] != 0:
        return False
    return True


def build(rank, cores, topo):
    ops = []
    pool = []
    lastdma, group, seen, gate = {}, {}, {}, {}

    def add(eng, rd, wr, call, **kw):
        r, w = [], []
        for v in rd:
            if isinstance(v, tuple):
                r += [v[1], v[2]] if v[0] == "@" else [v]
        for v in wr:
            if v[0] == "@":
                w.append(v[1])
                r.append(v[2])
            else:
                w.append(v)
        o = {"eng": eng, "r": r, "w": w, "call": call}
        o.update(kw)
        if eng in gate and any(x[0] in ("RY", "RV", "RP") or (x[0] == "LB" and x[1] % 64 >= 48) for x in r):
            o["behind"] = [gate[eng]]
        name = (eng,) + tuple((x[0].rstrip("01") if x[0] not in PS else x[0], x[1] % EVERY.get(x[0], WD)) for x in (w + r)[:3])
        seen[name] = seen.get(name, 0) + 1
        o["name"] = name + (seen[name],)
        ops.append(o)

    def cp(out, a):
        add("V", [a], [out], ("tensor_copy", out, a))

    def tt(out, a, b, op):
        add("V", [a, b], [out], ("tensor_tensor", out, a, b, op))

    def ts(out, a, s1, op0, s2=None, op1=None):
        add("V", [a, s1, s2], [out], ("tensor_scalar", out, a, s1, s2, op0) + ((op1,) if op1 is not None else ()))

    def scan(out, d0, d1, op0, op1):
        add("V", [d0, d1], [out], ("tensor_tensor_scan", out, d0, d1, 0.0, op0, op1))

    def mset(out, val):
        add("V", [], [out], ("memset", out, val))

    def act(out, a, func=AF.Identity, bias=0.0, scale=1.0):
        add("A", [a, bias, scale], [out], ("activation", out, a, func, bias, scale))

    def mm(terms, start=True, stop=True, pin=False, block=False):
        bank = terms[0][0][0]
        step = PAR["run"] if len(terms) >= 16 else len(terms) if block else 1
        for k in range(0, len(terms), step):
            some = terms[k:k + step]
            first, end = start and k == 0, stop and k + step >= len(terms)
            if first:
                group[bank] = len(ops)
            add("P", [x for t in some for x in t[1:]], [t[0] for t in some], ("mm", some, first, end), goon=not first,
                group=group[bank], end=end, pin=pin, opens=True)

    def whole(out, big, n=128):
        return [(out, x, vw(big, 0, n)) for x in (vw("IB"), vw("IN"))]

    def iota(out, pat, base, cm):
        add("G", [], [out], ("iota", out, pat, base, cm))

    def asel(out, a, pat, op, base, cm):
        add("G", [a], [out], ("affine_select", out, a, pat, op, 0.0, base, cm), behind=pool[:1])
        if pool:
            pool.append(len(ops) - 1)

    def widen(out, a, pool):
        if pool:
            add("G", [a], [out], ("affine_select", out, a, [[0, size(a)]], OP.is_ge, 0.0, 1, 0))
        else:
            cp(out, a)

    nd = [0]

    def dma(q, out, a, *then):
        load = a[0] == "$"
        add(q, [] if load else [a, *then], [out] if out[0] != "$" else [], ("dma", out, a), sem="d%d" % nd[0], behind=lastdma.get(q, []) * load)
        lastdma[q] = [len(ops) - 1]
        nd[0] += 1

    def repeat(name, lo, n, hi):
        for a in range(lo + n, hi, n):
            dma("S", vw(name, a, a + n), vw(name, lo, lo + n))

    def col(name, j):
        return vw(name, j, j + 1)

    def hv(name, h, n=128, base=0):
        return vw(name, base + n * h, base + n * h + n)

    dma("S", vw("ZR"), ("$", "z0", 0, 256))
    dma("A", col("TI", 0), ("$", "th", 0, 1))
    dma("S", vw("SR"), ("$", "scan", 0, 256))
    dma("A", vw("WM", p1=8), ("$", "warm", 0, 256))
    dma("A", col("WI", 0), ("$", "wt", 0, 1))
    for j in range(2):
        dma("S", hv("X", j, 2048), ("$", "reg", 2048 * j, 2048 * j + 2048))
    for j in range(2):
        dma("S", hv("VS", j, 1024, V0), ("$", "vw", 1024 * j, 1024 * j + 1024))

    iota(vw("PI", 0, 1), [[0, 1]], 0, 1)
    iota(vw("GF"), [[1, 8], [0, 16]], 0, 0)
    iota(vw("RF"), [[0, 8], [1, 16]], 0, 0)
    iota(vw("JF"), [[1, 144]], 0, 0)
    iota(vw("X", W, W + 16), [[0, 16]], 0, 0)
    dma("S", vw("X", W + 16, WD), vw("X", 16, W), vw("VS", V0, V0 + 2048))
    ts(vw("PI", 1, 2), vw("PI", 0, 1), 15, OP.bitwise_and)
    ts(vw("PI", 2, 3), vw("PI", 0, 1), 4, OP.arith_shift_right)
    ts(vw("PI", 3, 4), vw("PI", 0, 1), 1, OP.arith_shift_right, 7, OP.bitwise_and)
    cp(vw("CF", 0, 4), vw("PI", 0, 4))
    ts(vw("BD"), vw("GF"), col("CF", 2), OP.is_equal)
    for j in range(2):
        ts(hv("DC", j, 8), vw("GF", 0, 128, 16), 0.0, OP.add, col("CF", 2), OP.is_equal)
    DC = vw("DC", 0, 8)
    ts(vw("IF"), vw("JF", 0, 128), col("CF", 0), OP.is_equal)
    ts(vw("MR"), vw("RF"), col("CF", 1), OP.is_equal)
    for name, x in (("IB", 1.0), ("IH", 0.5), ("IG", -0.5), ("IN", -1.0), ("IL", 128.0), ("I8", 8.0), ("J8", -8.0),
                    ("IM", -NS / UN), ("IQ", NS / UN), ("IU", 1.0 / UN), ("IF8", 1.0 / 8192), ("IN8", -1.0 / 8192),
                    ("INH", -1.0 / 16), ("IF32", 32.0)):
        act(vw(name), vw("IF"), scale=x)
    for name, x in (("ONF", 1.0), ("ONB", 1.0), ("CU", 16.0), ("C16", MAGIC * 16), ("C01", MAGIC), ("CM", MAGIC * W),
                    ("ONN", -1.0), ("C32", 16.0), ("CA", -32.0), ("C2K", UN / 2),
                    ("CR", MAGIC * 32 * RU), ("CT", 15.5 * RU), ("RP1", RU / 2), ("RN1", -RU / 2)):
        if name in PAR["fill"]:
            n = SB[name][0]
            add("G", [vw("RF", 0, n)], [vw(name)], ("affine_select", vw(name), vw("RF", 0, n), [[0, n]], OP.is_gt, x, 0, 0))
        else:
            mset(vw(name), x)
    mset(vw("CU", p1=1), 15.5)
    mset(vw("VS", Z0, V0), 1 << 24)
    iota(vw("VB", UN, UN + NS), [[0, NS]], W, 0)
    for a, b, n in ((1, 16, 1), (2, 16, 1), (7, 16, 1), (3, 1, 2), (5, 1, 2), (9, 1, 7)):
        dma("S", vw("VB", NS * a, NS * (a + n)), vw("VB", NS * b, NS * (b + n)), vw("VS", V0, V0 + 2048))
    iota(vw("CB", 0, 16), [[(H0 - Z0) // 2 - (V0 - Z0) // 4, 2], [0, 8]], (V0 - Z0) // 4, 0)
    iota(vw("CE", 0, 64), [[NS, 4], [-128, 2], [0, 8]], slot(1) - UN // 2, 0)
    iota(vw("CE", 64, 72), [[0, 8]], 0, -1)
    iota(vw("NB", 0, 2), [[128, 2]], made(-1) - Z0, 1)
    act(vw("NB", 2, 4), vw("NB", 0, 2), scale=1.0 / 16384)
    act(vw("NB", 4, 6), vw("NB", 0, 2), scale=1.0 / 8192)
    for name, x, y in (("MK0", 1.0, 0.0), ("MKB", 0.0, 256.0), ("MKN", 0.0, -256.0)):
        n = SB[name][0] // 2 if name != "MKN" else 128
        mset(vw(name, 0, n), x)
        mset(vw(name, 0, n, 16), y)
        repeat(name, 0, n, SB[name][0])
    cp(vw("LS"), vw("JF", 0, 8))
    LC = vw("LS")
    if PAR["xm"]:
        ts(vw("L15"), vw("JF", 0, 8), 16.0, OP.mult, 15.0, OP.add)
    act(vw("W1"), DC, scale=2 * KU)
    for j, x in enumerate((16384.0, 8192.0)):
        act(hv("DU", j, 8), DC, scale=x)
    act(vw("DU", 16, 32), vw("DC"), scale=float(UN))
    ts(col("CF", 7), col("CF", 1), 8.0, OP.is_ge)
    ts(col("CF", 12), col("MR", 2), 1.0 / 16, OP.mult)
    ts(col("CF", 13), col("CF", 7), RU, OP.mult)
    ts(col("CF", 14), col("CF", 1), 2.0, OP.is_lt, -KU, OP.mult)
    ts(col("CF", 15), col("CF", 7), -255.0, OP.mult)
    act(vw("BZ"), vw("BD"), scale=2 * KU)
    for j, x in enumerate((-KU, RU, col("CF", 12), col("CF", 13), col("CF", 14))):
        act(hv("WR", j, 8), DC, scale=x)
    ts(col("CF", 4), col("CF", 2), 16.0, OP.mult, 15.0, OP.add)
    ts(vw("WO"), vw("JF"), col("CF", 4), OP.is_equal)
    tt(vw("WS"), vw("WO", 15, 143), vw("WO", 14, 142), OP.subtract)
    ts(col("CF", 17), col("CF", 3), 8.0, OP.add)
    ts(vw("TM2"), vw("RF"), col("CF", 17), OP.is_equal, 2.0, OP.mult)
    tt(vw("AP2"), vw("TM2"), vw("BD"), OP.mult)
    act(vw("APN"), vw("AP2"), scale=-0.5)
    act(vw("C7"), vw("MR"), scale=16.0, bias=-8.5)
    iota(vw("PT"), [[1, 32]], 0, 0)
    act(vw("I2"), vw("IF"), scale=col("MR", 2))
    for h in range(2):
        asel(vw("GS", 128 * h, 128 * h + 128, 1, 16), vw("ONB", p1=16), [[-1, 8], [0, 16]], OP.is_equal, -8 * h, 1)
    cp(col("CF", 5), col("TI", 0))
    cp(col("CF", 6), col("WI", 0))
    ts(col("CF", 8), col("IF", 2), 160.0, OP.mult)
    ts(col("CF", 9), col("IF", 1), 1024.0, OP.mult, col("CF", 8), OP.add)
    ts(col("CF", 10), col("IF", 0), -2.0 ** 23, OP.mult)
    act(vw("CL"), vw("RF"), bias=col("CF", 10), scale=col("CF", 9))
    act(vw("WBD"), vw("BD"), scale=col("CF", 6))
    for name, x in (("WBN", -1.0), ("WB2", 2.0), ("WN2", -2.0))[:3 if any(PAR["zv"]) else 1]:
        act(vw(name), vw("WBD"), scale=x)
    ts(vw("TM2"), vw("RF"), 2.0, OP.is_equal)
    tt(vw("W2"), vw("TM2"), vw("WBD"), OP.mult)
    act(vw("W2N"), vw("W2"), scale=-1.0)
    act(vw("C23"), vw("TM2"), scale=23.5 / 128)
    act(vw("TM2"), vw("TM2"), scale=-16.0)
    tt(vw("GL", p1=16), vw("TM2", p1=16), vw("GS", 128, 256, 1, 16), OP.mult)
    ts(vw("Q16"), vw("JF", 0, 16), 16.0, OP.mult, col("CF", 1), OP.add)
    cp(vw("QB"), vw("Q16"))
    for h in range(2):
        ts(hv("QP", 3 * h, 8), vw("Q16", 0, 8), 32.0, OP.mult, 16.0 * (1 - h), OP.add)
    act(vw("QP", 8, 24), vw("Q16"))
    cut = PAR["cut"]
    iota(vw("QL", 0, cut // 16), [[0, cut // 16]], 0, 0)
    iota(vw("QL", cut // 16, 8), [[0, 8 - cut // 16]], -32 * cut, 0)
    act(vw("TMP"), vw("IF"), scale=col("CF", 5))
    mm([(vw("PF", 0, 128), vw("ONF"), vw("TMP"))])
    act(vw("BI0"), vw("PF", 0, 128), scale=-RU, bias=-0.5 * RU)
    act(vw("BI1"), vw("BI0"), bias=8 * 255 * RU)
    act(vw("BH"), vw("BI1"))
    tt(vw("BL"), vw("BI1"), vw("BH"), OP.subtract)
    act(vw("BI"), vw("RF"), scale=-KU / 16)
    ts(col("CF", 18), col("CF", 1), 0.0, OP.is_gt, -1.0, OP.mult)
    ts(vw("TM2"), vw("JF", 1, 129), col("CF", 0), OP.is_equal, col("CF", 18), OP.mult)
    tt(vw("TMP"), vw("IF"), vw("TM2"), OP.add)
    act(vw("DI"), vw("TMP"), scale=1.0 / 16384)
    act(vw("DJ"), vw("TMP"), scale=1.0 / 8192)
    act(vw("DK"), vw("TMP"), scale=1.0 / UN)

    for h in range(2):
        src = vw("SR", 1 - h, 256, 2)
        widen(hv("S16", h), src, PAR["gi"][0])
        widen(hv("SF1", h), src, PAR["gi"][1])
        widen(hv("VS", h, 128, made(-1)), src, PAR["gi"][2])
        cp(hv("ZA0", h), vw("ZR", 1 - h, 256, 2))
    for k in range(16):
        asel(vw("ZX0", k, W // 2, 16), hv("ZA0", 0), [[0, 128]], OP.is_ge, 1, 0)
        if k < PAR["zi"][0]:
            act(vw("ZX0", W // 2 + k, W, 16), hv("ZA0", 1), AF.Copy)
        elif k < sum(PAR["zi"]):
            asel(vw("ZX0", W // 2 + k, W, 16), hv("ZA0", 1), [[0, 128]], OP.is_ge, 1, 0)
        else:
            cp(vw("ZX0", W // 2 + k, W, 16), hv("ZA0", 1))
    act(vw("OZ"), vw("ZA0"), AF.Copy)
    for j in PAR["alt"]:
        act(hv("OZ", j, 16), hv("OZ", j, 16), scale=0.0)
    ts(vw("WN", p1=8), vw("WM", p1=8), -1.0, OP.add)
    mm([(vw("PF", 256 + 8 * h, 264 + 8 * h), vw("WN", 1 - h, 256, 2, 8), vw("IB", 0, 8, 1, 8)) for h in range(2)])
    act(vw("HS1"), vw("PF", 256, 272), scale=-1.0)
    act(vw("THR"), vw("PF", 256, 272), bias=1.0)
    for j in range(8):
        ts(hv("VS", j, 256, V0 + 2048), hv("VS", j, 256, V0), 12, OP.arith_shift_right)

    me = cores[rank]
    for t in range(TS):
        last = t == TS - 1
        seen.clear()
        gate.clear()
        zx = "ZX%d" % (max(t - 1, 0) % 2)
        za, zb = "ZA%d" % (t % 2), "ZA%d" % ((t + 1) % 2)
        hs, hp = "HS%d" % (t % 2), "HS%d" % ((t + 1) % 2)
        sg, sp = "SG%d" % (t % 2), "SG%d" % ((t + 1) % 2)
        ha, hb = "HA%d" % (t % 2), "HA%d" % ((t + 1) % 2)
        count = vw(hb, 0, 128, 1, 16)
        wt = "WT%d" % (t % 2)
        it, nx = str(max(t, 1) % 2), str((t + 1) % 2)
        dst = cores[(rank + 1 + t % 3) % NR]
        lands = [(hv("RY", t), hv("LB", 7, 8, 64 * t)), (hv("YB", 1, 128, 256 * t) if last else vw("YW", 0, 256, 2), hv("LB", 4, 8, 64 * t))]

        def send(there, here, sem):
            add("G", [here], [], ("send", dst, there, here, sem + str(t)), behind=list(pool))
            pool[:] = [len(ops) - 1]
            add("R", [], [there], None, sem=sem + str(t), after=[len(ops) - 1], cnt=len(topo.engines(me, dst)))

        def gather(out, rows, vector):
            if vector:
                cp(out, rows)
            else:
                act(out, rows, AF.Copy)

        for j in range(16 if t else 0):
            n = 512 if j in PAR["wide"] else 256
            for a in [256 * j] * (j - 1 not in PAR["wide"]):
                b = a + n
                rows = ind(vw("YW"), vw("SQ" + it, a // 16, b // 16))
                if j in PAR["alt"]:
                    bank = vw(PAR["alt"][j], 0, n)
                    act(vw("C2", a, b), rows, AF.Copy)
                    mm([(bank, vw("IN"), vw(zx, a, b)), (bank, vw("IB"), vw("C2", a, b))])
                    act(vw("M", a, b), bank, AF.Relu)
                else:
                    tt(vw("M", a, b), rows, vw(zx, a, b), OP.max)
        for h in range(2):
            pk, pa, pd = "PK%d" % h, "PA%d" % h, "PD%d" % h
            for j in range(4 * h, 4 * h + 4):
                a, b = 512 * j, 512 * j + 512
                if t:
                    n = PAR["gvl" if last else "gv"].get(j, 0)
                    for x, y in ((a, a + n), (a + n, b)):
                        if x < y:
                            gather(vw("G2", x, y), ind(vw("TB"), vw("SQ" + it, x // 16, y // 16)), x == a and n > 0)
                    continue
                rows = ind(vw("X", 0, W), vw("S16", a // 16, b // 16))
                gather(vw("G2", a, b), rows, j in PAR["c0v"])
                bank = ["PD0", "PD1", "PU", "PA1", "PF", "PD0", "PD1", "PU"][j]
                mm([(vw(bank), vw("IN"), vw(zx, a, b))] if h else [(vw(bank, k, 512, 16), vw("IN"), hv(za, j, 32)) for k in range(16)], stop=False)
                mm([(vw(bank), vw("IB"), vw("G2", a, b))], start=False)
                if j in PAR["r0v"]:
                    ts(vw("M", a, b), vw(bank), 0.0, OP.max)
                else:
                    act(vw("M", a, b), vw(bank), AF.Relu)

            def lanes(bank, c, n, name, wts, q0, q1):
                return [(vw(bank, c + k, c + k + 16 * n - 15, 16, q1) + (q0, 1),
                         vw(name, 2048 * h + 16 * q0 + k, 2048 * h + 16 * q1, 16), wts) for k in range(16)]
            uw, sf = hv("UW", h), hv("SF" + it, h)
            run = vw(pa, 256, 384)
            if t == 0:
                key, rho, reset, thr = vw(pk, 0, 128), vw(pk, 128, 256), vw("MKN"), hv("THR", h, 8)
                dp, ends = vw(pa, 0, 128), vw(pa, 15, 128, 16)
                mm([(key, vw("IB"), vw("BI")), (rho, vw("IF"), vw("BI0")), (key, hv("OZ", h), vw("BZ"))], stop=False)
                new = [(hv(pk, j, 64, 128), vw("WN", 1 - h, 256, 2, 8), vw("GS", 64 * j, 64 * j + 64, 1, 8)) for j in range(2)]
                mm(new[:1], start=False, stop=False)
                for x in PAR["s0"]:
                    mm(lanes(pk, 0, 16, "G2", vw("WR", 0, 16), *x), start=False, stop=False)
                    mm(lanes(pk, 0, 8, "M", vw("W1"), *x), start=False, stop=False)
                mm(new[1:], start=False)
                ts(hv(sg, h), rho, 0.0, OP.is_gt)
                tt(hv("KEY", h), key, hv(sg, h), OP.add)
                mm([(dp, sf, vw("DI")), (ends, vw("IU"), hv("CB", 0, 8))])
            else:
                diff, rho, ba = (hv(pd, j) for j in range(3))
                key, dp, thr, reset = hv(pk, 0), hv(pk, 1), vw(pk, 256, 264), hv(pa, 0)
                ends = vw(pk, 143, 256, 16)
                new = [(hv(pd, j, 64), vw(hb, 128, 256, 1, 16), vw("GS", 128 * h + 64 * j, 128 * h + 64 * j + 64, 1, 16)) for j in range(2)]
                blk = hv("BQ" + it, h)
                mm([(diff, blk, vw("IB")), (diff, sf, vw("INH"))]
                   + [(ba, sf, vw("IF")), (ba, vw("CA"), vw("ONB")), (ba, blk, vw("IN"))] * (t == 1), stop=False)
                low = col(pd, 384)
                mm([(low, count, vw("RN1", 0, 1, 1, 16)), (low, vw("IB"), col("CT", 0))] + whole(low, "CR", 1)
                   + [(low, count, vw("RP1", 0, 1, 1, 16))], start=False, stop=False, pin=True)
                mm([(rho, vw("IB"), vw("BH")), (rho, vw("IB"), vw("BL")), new[0]], start=False, stop=False)
                for x in PAR["sg"][h]:
                    end = x == PAR["sg"][h][-1]
                    mm(lanes(pd, 0, 16, "G2", vw("WR", 16, 32), *x) + new[1:] * end, start=False, stop=end)
                mm([(key, vw("IB"), vw("BI")), (key, vw("ONN", p1=t), vw("ONB", p1=t)), (dp, blk, vw("DJ" if t == 1 else "DK")),
                    (thr, vw("IH"), hv(hs, h, 8)), (thr, vw("IG"), hv(hp, h, 8))]
                   + ([(ends, vw("IU"), hv("CB", 1, 8)), (thr, vw("IH"), vw("ONB", 0, 8))] if t == 1 else
                      [(ends, vw("IU"), hv("CE", 2 * t - 4 + h, 8)), (ends, vw("IU"), hv("CE", 8, 8))]), stop=False)
                for x in PAR["sm"][h]:
                    mm(lanes(pk, 0, 8, "M", vw("W1"), *x), start=False, stop=False)
                for x in PAR["sl"][h]:
                    mm(lanes(pk, 0, 8, "G2", vw("WR", 32, 40), *x), start=False, stop=False)
                ts(uw, diff, 0.0, OP.not_equal, low, OP.max)
                tt(hv(sg, h), rho, uw, OP.is_gt)
                name, plus, minus = ("C1", "IF8", "IN8") if t == 1 else ("UW", "IM", "IQ")
                if t == 1:
                    tt(hv("C1", h), ba, uw, OP.mult)
                a = 128 * h
                mm([(vw(pk, 128, 255), vw(minus), vw(name, a + 1, a + 128)), (vw(pk, 143, 240, 16), vw(plus), vw(name, a + 16, a + 128, 16)),
                    (dp, vw(plus), hv(name, h)), (key, vw("I8"), uw)], start=False)
                tt(hv("KEY", h), key, hv("KEY", h), OP.min)

                def lack(name, down, up):
                    return [(reset, vw(down), hv(name, h)), (vw(pa, 1, 128), vw(up), vw(name, a, a + 127))]
                mm([(reset, vw("IB"), vw("MKN"))] + lack(sp, "J8", "I8"), stop=False)
                mm(lack("UW", "IB", "IN") * (2 if t == 1 else 1), start=False, stop=False)
                mm(lack(sg, "J8", "I8")[::-1], start=False)
            scan(hv("CN", h), vw("MK0", 0, 128), hv(sg, h), OP.mult, OP.add)
            scan(run, reset, hv("KEY", h), OP.add, OP.max)
            tt(hv("NE", h), run, hv("KEY", h), OP.not_equal)
            scan(hv("SC", h), hv("NE", h), dp, OP.mult, OP.add)
            cn = vw("CN", 128 * h + 15, 128 * h + 128, 16)
            if t < 2:
                tt(hv("BO", h, 8), cn, thr, OP.is_gt)
                tt(hv(hs, h, 8), cn, thr, OP.not_equal)
                ts(hv("NH", h, 8), hv(hs, h, 8), col("NB", 2 + 2 * t + h), OP.mult)
                tt(hv("XB", h, 8), hv("NH", h, 8), hv("BO", h, 8), OP.add)
            else:
                tt(hv("XB", h, 8), cn, thr, OP.subtract)
            if h < PAR["xm"]:
                tt(vw("XM"), ind(hv("XB", h, 8), LC), vw("MR"), OP.mult)
                tt(hv("E1", h), ind(hv("SC", h), vw("L15")), vw("XM"), OP.min)
            else:
                tt(hv("DB", h, 8), vw("SC", 128 * h + 15, 128 * h + 128, 16), hv("XB", h, 8), OP.min)
                tt(hv("E1", h), ind(hv("DB", h, 8), LC), vw("MR"), OP.mult)
            p8 = vw(pa, 408, 416)
            fb = hv("FB", h, 128, 256 * t)
            wide = hv("FF", h) if h == 0 or last else vw("VB", slot(t), slot(t) + NS, 2)
            if t < 2:
                mm([(p8, hv("E1", h), hv("DU", t, 8))])
                ts(hv("DL", h, 8), p8, float(Z0 - made(-1)), OP.add)
                ts(hv("FI", h), ind(vw("VS", made(-1), H0 + NS * t), hv("DL", h, 8)), LOW, OP.bitwise_and)
                ts(fb, hv("FI", h), float(W), OP.min)
                ts(hv(wt, h, 8), p8, 0.0, OP.is_equal, 32.0, OP.mult)
            else:
                mm([(vw(pa, 408, 424), vw("IB"), vw("C2K")), (p8, vw("IB"), hv("QB", h, 8))], stop=False)
                mm([(vw(pa, 408, 424), hv("E1", h), vw("DU", 16, 32))], start=False)
                cp(hv("DL", h, 8), p8)
                cp(fb, ind(vw("VB", 0, slot(t)), hv("DL", h, 8)))
                ts(hv(wt, h, 8), vw(pa, 416, 424), float(UN), OP.is_equal, 32.0, OP.mult)
            if last:
                tt(hv("WW", h, 8), hv("WT0", h, 8), hv("WT1", h, 8), OP.min)
            if h == 0 and not last:
                send(hv("RV", t), fb, "rc")
            if t > 1 and PAR["fa"][h]:
                act(wide, ind(vw("VB", 0, slot(t)), hv("DL", h, 8)), AF.Copy)
            else:
                widen(wide, fb, PAR["gp"][2 * h])
        if not last:
            if t == 0:
                cp(vw("VS", H0, H0 + NS, 2), hv("FB", 1))
            else:
                cp(vw("SF" + nx), ind(vw("VS", made(t - 1), Z0), hv("LB", 1, 16, 64 * (t - 1))))
            ts(vw("SQ" + nx), vw("SF" + nx), -7.5, OP.add, 1.0 / 16, OP.mult)
            widen(vw("BQ" + nx), vw("SQ" + nx), PAR["gp"][3])
            if t > 1:
                act(vw("SN"), vw("XB"), AF.Sign, bias=-0.5)
                act(vw(hs), vw("SN"), AF.Abs)
            mm([(vw("PF", 256, 384, 1, 16), vw(x), vw("ONB")) for x in ((hs, "SN") if t > 1 else ("BO", "BO"))]
               + [(vw("PF", 384, 512, 1, 16), vw(hs), vw("IB"))])
            act(vw(ha, p1=16), vw("PF", 256, 512, 1, 16), AF.Copy)
        for h in range(2):
            pa, pk = "PA%d" % h, "PK%d" % h
            yv = lands[1][0] if h else hv("YB", 0, 128, 256 * t)
            av = hv(zb, h)
            cuts = [2048 * h + a for a in PAR["cuts"][h]]
            for a, b in zip(cuts[:-1], cuts[1:]):
                gather(vw("D", a, b), ind(vw("X", 0, W + 16), vw("FB", 256 * t + a // 16, 256 * t + b // 16)), a in PAR["dvl" if last else "dv"])
            for a, b in zip(cuts[:-1], cuts[1:]):
                scan(vw("MX", a, b), vw("MK0", 0, b - a), vw("D", a, b), OP.mult, OP.max)
                scan(vw("MN", a, b), vw("MKB", 0, b - a), vw("D", a, b), OP.add, OP.min)
            for p, n in ((0, cut), (cut, 128 - cut)) if last and h else ((0, 128),):
                def part(v, p=p, n=n):
                    return (v[0], v[1] + v[3] * p, min(v[2], v[1] + v[3] * (p + n)), v[3], v[4])

                def rows(v, p=p, n=n):
                    return v[:4] + (p + n, p, 1)
                bank = 0 if p else h
                py, pz = vw("PA%d" % bank, 128, 128 + n), vw("PD%d" % bank, 256, 256 + n)
                mx, mn = (part(vw(x, 2048 * h + 15, 2048 * h + 2048, 16)) for x in ("MX", "MN"))
                way = PAR["yal" if last else "ya"][h]
                for x in (py, pz)[way == 2:]:
                    mm([(x, vw("IM"), vw("ONB", 0, n))] + [(x, vw("IN"), part(hv(za, h)))] * (x == pz) + [(x, vw("IH"), mx)], stop=False)
                    mm([(x, vw("IH"), mn)] + whole(x, "C01", n) * (x == pz or way == 1), start=False, block=True)
                if PAR["zv"][h]:
                    ts(part(hv("MZ", h)), pz, 0.0, OP.max)
                else:
                    act(part(av), pz, AF.Abs)
                    if "A" in PAR["gate"]:
                        gate["A"] = len(ops) - 1
                if way == 2:
                    tt(part(yv), pz, part(hv(za, h)), OP.add)
                elif way == 1:
                    act(part(yv), py, AF.Copy)
                else:
                    ts(part(yv), py, MAGIC, OP.add, MAGIC, OP.subtract)
                if h == 0:
                    send(hv("RY", t), yv, "ra")
                pu = rows(vw("PK%d" % bank, 384, 512))
                big = [(pu, part(vw("IB")), vw("C16")), (pu, part(vw("IN")), vw("C16"))]
                if PAR["zv"][h]:
                    act(part(av), pz, AF.Abs)
                    z, mz = part(hv(za, h)), part(hv("MZ", h))
                    mm([(pu, part(vw("IB")), vw("C7")), (pu, z, vw("WBN")), (pu, part(yv), vw("WBD"))], stop=False)
                    mm([(pu, mz, vw("WN2"))] + big + [(pu, mz, vw("WB2")), (pu, z, vw("WBD")), (pu, part(yv), vw("WBN"))], start=False, block=True)
                else:
                    mm([(pu, part(vw("IB")), vw("C7"))], stop=False)
                    mm([(pu, part(av), vw("WBN"))] + big + [(pu, part(av), vw("WBD"))], start=False, block=True)
                if PAR["eal" if last else "ea"][h]:
                    act(rows(hv("E2", h)), pu, AF.Relu)
                else:
                    ts(rows(hv("E2", h)), pu, 0.0, OP.max)
                pa = "PD1" if p else "PF" if last else "PU"
                pi, pp, pc, both = vw(pa, 392, 400), hv(pa, h, 8, 384 + 8 * h), hv(pa, 1 - h, 8, 392 - 8 * h), hv(pa, 0, 16, 384 + 8 * h)
                if last:
                    def cols(name, base=0, p=p, n=n):
                        return vw(name, base + p // 16, base + (p + n) // 16)
                    both = cols(pa, 392)
                    mm([(both, vw("IF"), cols("QP", 24 * h)), (both, vw("IL"), cols(wt, 8 * h)), (both, vw("IB"), cols("QL"))]
                       + [(pc, vw("IF"), hv("QP", 1 + h, 8)), (pc, vw("I8"), hv(wt, h, 8)), (pc, vw("I8"), hv("WW", h, 8))] * (p == 0), stop=False)
                    mm([(both, rows(hv("E2", h)), rows(cols("DC")))], start=False)
                    a, b = (8 + p // 16 if p else 0, 8 + (p + n) // 16) if h else (8, 24)
                    cp(vw("LB", 64 * t + 24 * h + a, 64 * t + 24 * h + b), vw(pa, 384 + a, 384 + b))
                    if h == 0:
                        send(hv("LB", 7, 8, 64 * t), hv("LB", 1, 8, 64 * t), "rb")
                    continue
                mm([(hv(pa, 0, 16, 392 - 8 * h), vw("IF"), hv("QP", h, 16)), (pp, vw("IH"), hv(wt, h, 8)),
                    (pi, vw("IL"), hv(wt, h, 8)), (pc, vw("I8"), hv(wt, h, 8))], stop=False)
                mm([(both, hv("E2", h), vw("DC"))], start=False)
                if "P" in PAR["gate"]:
                    gate["P"] = len(ops) - 1
                cp(hv("LB", h, 24, 64 * t), vw(pa, 384, 408))
                gate["V"] = len(ops) - 1
                if h == 0:
                    send(hv("LB", 3, 16, 64 * t), hv("LB", 0, 16, 64 * t), "rb")
                    gate["G"] = pool[0]
                if h == (t == 0 or PAR["late"]):
                    widen(vw("VB", slot(t) + 1, slot(t) + NS, 2), hv("RV", t), PAR["gp"][1])
                    if t == 0:
                        cp(vw("VS", H0 + 1, H0 + NS, 2), hv("RV", t))
                if "V" not in PAR["gate"]:
                    gate.pop("V")
            if h and not last:
                gather(vw("PL"), ind(vw("PT"), vw("LB", 64 * t + 48, 64 * t + 56)), PAR["pv"])
                gather(vw("YW", 1, 256, 2), lands[0][0], not PAR["yw"])
            u, pf = hv("PU", 0), hv("PU", 1)
            ff = hv("FF", h) if h == 0 or last else vw("VB", slot(t), slot(t) + NS, 2)
            mm([(pf, vw("IF32"), ff), (pf, vw("CL"), vw("ONB")), (u, vw("CU"), vw("ONB"))]
               + [(pf, vw("C32", p1=16), count)] * (t > 0), stop=False)
            mm([(u, vw("WBN"), av)] + whole(u, "CM") + [(u, vw("WBD"), av)], start=False, pin=True)
            tt(hv("PR", h), ff, u, OP.mult)
            tt(hv("PR2", h), hv("PR", h), pf, OP.add)
            ts(hv("VS", h, 128, made(t)), hv("PR2", h), 5, OP.arith_shift_right, 4095, OP.bitwise_and)

        for j in range(0 if last else 2):
            if PAR["old"][j]:
                act(hv("DD", j), ind(vw("X"), lands[j][1]), AF.Copy)
                tt(hv("DR", j), ind(vw("X"), lands[j][1]), lands[j][0], OP.max)
            else:
                tt(hv("DD", j), ind(vw("X"), lands[j][1]), lands[j][0], OP.subtract)
                ts(hv("DR", j), hv("DD", j), 0.0, OP.max)
        for p, n in ((0, cut), (cut, 128 - cut)) if last else ((0, 128),):
            for j in (0, 1) if p else (1, 0):
                ys, ls = lands[j]
                if last:
                    cp(ind(vw("X", 32 * p, W + 32 * (p + n)), vw(ls[0], ls[1] + p // 16, ls[1] + (p + n) // 16)), vw(ys[0], ys[1] + p, ys[1] + p + n))
                else:
                    cp(ind(vw("X"), ls), ys)
            if last:
                dma("S", ("$", "yx", 32 * p, 32 * (p + n)), vw("X", 32 * p, 32 * (p + n)))
        for j in range(0 if last else 2):
            tb, av, y = hv(PAR["tb"][j], 0), hv(zb, 1), lands[j][0]
            mm([(tb, vw("C23"), vw("ONB")), (tb, vw("W2N"), av)] * j + [(tb, vw("WS"), y)] + whole(tb, "C16"), stop=False, pin=True)
            mm([(tb, vw("WO", 14, 142), y)] + [(tb, vw("APN"), y)] * PAR["old"][j]
               + ([(tb, vw("W2"), av), (tb, vw("GL", p1=16), vw(ha, 128, 256, 1, 16))] if j else [(tb, vw("I2"), vw("PL"))])
               + [(tb, vw("APN"), hv("DD", j))], start=False, stop=False)
            mm([(tb, vw("AP2"), hv("DR", j))], start=False)
            if PAR["tv"][j]:
                ts(vw("TB", 1 - j, 256, 2), tb, col("CF", 15), OP.add)
            else:
                act(vw("TB", 1 - j, 256, 2), tb, bias=col("CF", 15))
        for a in (0, UN // 2) if 0 < t < TS - 1 else ():
            dma("S", vw("VB", a, a + NS), vw("SF" + nx), hv("DR", 0))
        if t < TS - 2:
            for k in range(16):
                asel(vw("ZX%d" % ((t + 1) % 2), k, W, 16), vw(zb), [[0, 256]], OP.is_ge, 1, 0)
    zf = "ZA%d" % (TS % 2)
    for h in range(2):
        act(vw("OZ", 1 - h, 256, 2), hv(zf, h), AF.Copy)
        cp(vw("OS", 1 - h, 256, 2), ind(vw("VS", made(TS - 1), Z0), hv("LB", 2 + h, 8, 64 * (TS - 1))))
    dma("A", ("$", "yz", 0, 256), vw("OZ"))
    dma("A", ("$", "ys", 0, 256), vw("OS"))
    return ops


def depend(ops):
    seen = {}
    for n, o in enumerate(ops):
        dep = set(o.get("after", ()))
        for v, w in [(v, False) for v in o["r"]] + [(v, True) for v in o["w"]]:
            for m, u, uw in seen.get(v[0], []):
                if m == n:
                    continue
                if v[0] in PS and o["eng"] == ops[m]["eng"] == "P" and o["group"] == ops[m]["group"]:
                    hit = clash(u, v)
                    o["opens"] = o["opens"] and not hit
                    if m == o["group"] or o["end"] or (hit and (o["pin"] or ops[m]["pin"] or ops[m]["opens"])):
                        dep.add(m)
                elif v[0] in PS and (ops[m]["eng"] != o["eng"] or (o["eng"] == "P")):
                    dep.add(m)
                elif (w or uw) and clash(u, v):
                    dep.add(m)
        o["soft"] = {m for m in dep if ops[m]["eng"] == o["eng"] and o.get("goon")} | (set(o.get("behind", ())) - dep)
        o["dep"] = dep | o["soft"]
        for v, w in [(v, False) for v in o["r"]] + [(v, True) for v in o["w"]]:
            lst = seen.setdefault(v[0], [])
            if w and v[0] not in PS:
                lst[:] = [e for e in lst if not (v[3] == 1 and v[4] == 128 and len(v) == 5 and v[1] <= e[1][1] and e[1][2] <= v[2])]
            lst.append((n, v, w))


def size(v):
    return 16 * size(v[2]) if v[0] == "@" else len(range(v[1], v[2], v[3]))


def narrow(v):
    return v[0] not in PS and SB[v[0]][1] in (B, U)


def cost(o, plan):
    c, e, f = o["call"], o["eng"], plan["slow"]
    cycle = 0.83e-3 * f
    if c is None:
        return 128 / o["cnt"] * (plan["row"] + 2 * size(o["w"][0]) / plan["link"]), plan["land"]
    if c[0] == "send":
        return plan["send"], 0.0
    if c[0] == "dma":
        v = c[2] if c[1][0] == "$" else c[1]
        return 0.05, size(v) * v[4] * (2 if narrow(v) else 4) / plan["bytes"]
    if c[0] == "mm":
        return f * sum(max(min(64, size(t[1])), size(t[2])) * (1 if narrow(t[1]) else 4) * plan["pe"] + plan["mm"] for t in c[1]), plan["pelag"]
    vs = [x for x in c[1:] if isinstance(x, tuple)]
    n = max(size(x) for x in vs)
    if e == "G":
        return (0.13 if c[0] == "iota" else 0.17) * f + 2 * n * cycle, 0.0
    if any(x[0] == "@" for x in vs):
        return 0.06 * f + plan["scatter" if vs[0][0] == "@" else "gather"] * n * cycle, 0.0
    if e == "A":
        return plan["act"] * f + max(64, n) * cycle, 0.0
    if c[0] == "tensor_tensor":
        k = 1 if vs[1][0] in PS or vs[2][0] in PS else 2
    else:
        k = 0.5 if all(narrow(x) for x in vs if size(x) == n) else 1
    return max(64, k * n) * cycle, 0.0


def place(eng, dur, nexts, urgency):
    left = [0] * len(eng)
    for x in nexts:
        for j, _ in x:
            left[j] += 1
    ready, start = [0.0] * len(eng), [0.0] * len(eng)
    free, todo = {e: 0.0 for e in eng}, {e: [] for e in eng}
    for i, e in enumerate(eng):
        if not left[i]:
            todo[e].append(i)
    for _ in eng:
        t, e = min((max(free[e], min(ready[i] for i in x)), e) for e, x in todo.items() if x)
        now = [i for i in todo[e] if ready[i] <= t + 1e-9]
        i = min(now, key=lambda k: (ready[k] if e == "D" else urgency[k], k))
        soon = [j for j in todo[e] if t < ready[j] < t + dur[i] and urgency[j] < urgency[i] and e != "D"]
        if soon:
            j = min(soon, key=lambda k: (urgency[k], k))
            fit = [k for k in now if t + dur[k] <= ready[j] + 0.02]
            if fit:
                i = min(fit, key=lambda k: (urgency[k], k))
            elif (max(ready[j] - urgency[j], ready[j] + dur[j] - urgency[i]) + PLAN["look"] * (ready[j] - t)
                  < max(t - urgency[i], t + dur[i] - urgency[j])):
                i, t = j, ready[j]
        todo[e].remove(i)
        start[i] = t
        free[e] = t + dur[i]
        for j, w in nexts[i]:
            ready[j] = max(ready[j], t + dur[i] + w)
            left[j] -= 1
            if not left[j]:
                todo[eng[j]].append(j)
    return start


def graph(ops, plan):
    eng = [o["eng"] for o in ops]
    dur, lag = (list(x) for x in zip(*[cost(o, plan) for o in ops]))
    dur[eng.index("R") - 1] += plan["first"]
    after, before = [[] for _ in ops], [[] for _ in ops]
    data = {}
    for i, o in enumerate(ops):
        if o["call"] and o["call"][0] == "dma":
            data[i] = len(eng)
            eng.append("D")
            dur.append(lag[i])
            lag.append(0.0)
            after.append([])
            before.append([(i, plan["dma"])])
            after[i].append((data[i], plan["dma"]))
    for i, o in enumerate(ops):
        for d in o["next"]:
            w = 0.0
            if d not in o["soft"] and o["call"] is not None:
                d = data.get(d, d)
                w = lag[d] + plan["wake"] + plan["lag"] * (eng[d] == "V") + plan["own"] * (eng[d] == eng[i])
            before[i].append((d, w))
            after[d].append((i, w))
    return eng, dur, before, after


def replay(order, eng, dur, before, after):
    end, free = [0.0] * len(eng), dict.fromkeys(eng, 0.0)
    for i in order:
        e = eng[i]
        t = free[e]
        for d, w in before[i]:
            if end[d] + w > t:
                t = end[d] + w
        end[i] = free[e] = t + dur[i]
    return max(end)


def judge(ends, scale):
    return len(ends) * (sum((a / b) ** PLAN["power"] for a, b in zip(ends, scale)) / len(ends)) ** (1 / PLAN["power"])


def chain(order, eng, dur, before, after):
    end, free, why = [0.0] * len(eng), {}, [None] * len(eng)
    for i in order:
        t, k = free.get(eng[i], (0.0, None))
        for d, w in before[i]:
            if end[d] + w >= t:
                t, k = end[d] + w, -1 - d
        why[i], end[i] = k, t + dur[i]
        free[eng[i]] = (end[i], i)
    i, links = end.index(max(end)), []
    while why[i] is not None:
        if why[i] >= 0 and eng[i] not in "DR":
            links.append((why[i], i))
        i = why[i] if why[i] >= 0 else -1 - why[i]
    return links


def schedule(ops):
    reach = []
    for o in ops:
        far = 0
        for d in o["dep"]:
            if d not in o["soft"] or o["eng"] == "P":
                far |= reach[d]
        o["next"] = sorted(d for d in o["dep"] if not far >> d & 1)
        reach.append(far | sum(1 << d for d in o["next"] if d not in o["soft"] or o["eng"] == "P"))
    cases = [graph(ops, dict(PLAN, **x)) for x in RANGE]
    eng, dur, before, after = cases[0]
    tail = [0.0] * len(eng)
    for i in range(len(ops) - 1, -1, -1):
        for k in [j for j, _ in after[i] if j >= len(ops)] + [i]:
            tail[k] = dur[k] + max([w + tail[j] for j, w in after[k]] + [0.0])
    urgency, best, now, scale = [-x for x in tail], None, None, None
    shake = np.random.RandomState(PLAN["seed"])
    names = {}
    kin = np.array([names.setdefault(o["name"], len(names)) for o in ops] + [0] * (len(eng) - len(ops)))
    for k in range(PLAN["passes"]):
        if k > 5 and k % 2 == 0:
            move = shake.normal(0, PLAN["shake"], len(names)) * (shake.rand(len(names)) < PLAN["some"])
            if shake.rand() < PLAN["aim"]:
                move *= 0.2
                links = chain(now[2], *cases[shake.randint(len(cases))])
                for a, b in [links[x] for x in shake.randint(len(links), size=4)]:
                    gap = abs(now[1][a] - now[1][b]) / 2 + 0.1
                    move[kin[a]] += gap
                    move[kin[b]] -= gap
            urgency = (np.array(now[1]) + move[kin]).tolist()
        eng, dur, before, after = cases[k // 2 % len(cases) if PLAN["turn"] else 0]
        start = place(eng, dur, after, urgency)
        order = sorted(range(len(eng)), key=lambda i: (start[i], i))
        ends = [replay(order, *x) for x in cases]
        scale = [r["par"] for r in RANGE]
        score = judge(ends, scale)
        back = place(eng, dur, before, [-s - d for s, d in zip(start, dur)])
        urgency = [-s - d for s, d in zip(back, dur)]
        if best is None or score < best[0]:
            best = (score, order, urgency, ends)
        if now is None or score < now[0] + PLAN["ease"] * (1 - k / PLAN["passes"]) * shake.rand():
            now = (score, urgency, order)
    order, ends = polish(best[1], cases, scale, kin.tolist(), shake)
    return [i for i in order if i < len(ops)], ends


def polish(order, cases, scale, kin, shake):
    eng = cases[0][0]

    def ahead(order, a, b, way, every):
        order = list(order)
        for j in [i for i in order if kin[i] == kin[b] and eng[i] == eng[b]]:
            q = order.index(j)
            p = next((x for x in range(q - 1, max(q - 400, -1), -1) if kin[order[x]] == kin[a] and eng[order[x]] == eng[a]), None)
            if p is None:
                continue
            if every < 1 and shake.rand() > every and j != b:
                continue
            span = order[p:q + 1] if way else order[p:q + 1][::-1]
            need = {span[-1]}
            for x in range(len(span) - 1, -1, -1):
                if span[x] in need:
                    need.update(d for d, _ in cases[0][2 if way else 3][span[x]])
            if span[0] not in need:
                span = [y for y in span if y in need] + [y for y in span if y not in need]
                order[p:q + 1] = span if way else span[::-1]
        return order
    ends = [replay(order, *x) for x in cases]
    score, links = judge(ends, scale), {}
    best = (score, order, ends)
    for k in range(PLAN["moves"]):
        c = shake.randint(len(cases))
        if c not in links:
            links[c] = chain(order, *cases[c])
        a, b = links[c][shake.randint(len(links[c]))]
        other = ahead(order, a, b, shake.randint(2), shake.randint(3) > 0)
        bar = score + PLAN["give"] * (1 - k / PLAN["moves"]) * shake.rand()
        trial = [x * 0.997 for x in ends]
        for x in list(range(c, len(cases))) + list(range(c)):
            trial[x] = replay(other, *cases[x])
            if other == order or judge(trial, scale) >= bar:
                break
        else:
            score, ends, links, order = judge(trial, scale), trial, {}, other
            if score < best[0]:
                best = (score, order, ends)
    return best[1:]


ORDER = []


def rank_program(g, core, T, topo):
    rank = T.rank_of(core)
    if rank is None:
        return
    ops = build(rank, list(T.cores), topo)
    depend(ops)
    if not ORDER:
        ORDER.extend(schedule(ops))
    order = ORDER[0]
    pos = {i: k for k, i in enumerate(order)}
    known = {}
    for i in order:
        o = ops[i]
        o["wait"] = []
        if o["call"] is None:
            continue
        need = {}
        for d in o["dep"] - o["soft"]:
            key = ops[d].get("sem") or ops[d]["eng"]
            if key not in need or pos[d] > pos[need[key]]:
                need[key] = d
        mine = known.setdefault(o["eng"], {})
        for key, d in sorted(need.items(), key=lambda x: -pos[x[1]]):
            if mine.get(key, -1) < pos[d]:
                mine[key] = pos[d]
                o["wait"].append(d)
                ops[d]["mark"] = True
                for k, x in ops[d].get("knew", {}).items():
                    mine[k] = max(mine.get(k, -1), x)
        o["knew"] = dict(mine)
    queue = {"V": g.vector, "A": g.scalar, "P": g.tensor, "G": g, "S": g.sync}
    count = {}
    sent = 0

    def ap(v):
        if not isinstance(v, tuple):
            return v
        if v[0] == "@":
            return ap(v[1]).indirect(ap(v[2]))
        if v[0] == "$":
            t = T[v[1]]
            return t[:] if v[3] - v[2] == t.shape[1] else t[:, v[2]:v[3]]
        if v[0] in SHARE:
            name, a = SHARE[v[0]]
            v = (name, v[1] + a, v[2] + a) + v[3:]
        t = T[v[0]]
        if len(v) > 5:
            return t[v[5]:v[4]:v[6], v[1]:v[2]:v[3]]
        if v[3] == 1:
            return t[0:v[4], v[1]:v[2]]
        return t[0:v[4], v[1]:v[2]:v[3]]

    tail = []
    for i in order:
        o = ops[i]
        e, c = o["eng"], o["call"]
        if c is None:
            o["sig"] = (o["sem"], o["cnt"])
            continue
        q = queue[e]
        for d in o["wait"]:
            q.wait_ge(T.sem[ops[d]["sig"][0]], ops[d]["sig"][1])
        if c[0] == "send":
            rid, pid = topo.addr(c[1])[:2]
            g.remote_dma(ap(c[2]), ap(c[3]), T.sem[c[4]], T.sem["sent"], pid, rid, topo.mask(core, c[1]))
            sent += len(topo.engines(core, c[1]))
            continue
        if c[0] == "dma":
            q.dma_start(ap(c[1]), ap(c[2])).then_inc(T.sem[o["sem"]], 16)
            o["sig"] = (o["sem"], 16)
            if not o.get("mark"):
                tail.append(o["sem"])
            continue
        if c[0] == "mm":
            for k, t in enumerate(c[1]):
                ins = q.matmul(ap(t[0]), ap(t[1]), ap(t[2]), c[2] and k == 0, c[3] and k == len(c[1]) - 1)
        elif c[0] == "activation":
            if c[3] == AF.Copy:
                ins = q.activation(ap(c[1]), ap(c[2]), c[3])
            else:
                ins = q.activation(ap(c[1]), ap(c[2]), c[3], bias=ap(c[4]), scale=ap(c[5]))
        elif c[0] == "iota":
            if SB[c[1][0]][1] == I:
                ins = q.iota(ap(c[1]), c[2], c[3], c[4])
            else:
                ins = q.iota(ap(c[1]), c[2], c[3], c[4], allow_small_or_imprecise_dtypes=True)
        elif c[0] == "affine_select":
            ins = q.affine_select(ap(c[1]), ap(c[2]), c[3], c[4], c[5], c[6], c[7])
        elif c[0] == "tensor_copy":
            ins = q.tensor_copy(ap(c[1]), ap(c[2]))
        elif c[0] == "tensor_tensor":
            ins = q.tensor_tensor(ap(c[1]), ap(c[2]), ap(c[3]), c[4])
        elif c[0] == "tensor_scalar":
            ins = q.tensor_scalar(*[ap(x) for x in c[1:]])
        elif c[0] == "tensor_tensor_scan":
            ins = q.tensor_tensor_scan(*[ap(x) for x in c[1:]])
        else:
            ins = q.memset(ap(c[1]), c[2])
        if o.get("mark"):
            count[e] = count.get(e, 0) + 1
            ins.then_inc(T.sem["q" + e], 1)
            o["sig"] = ("q" + e, count[e])
    g.wait_ge(T.sem["sent"], sent)
    for s in tail:
        g.sync.wait_ge(T.sem[s], 16)
